import numpy as np, ml_dtypes
CORES = [48,51,52,55]
N = 4
BF = ml_dtypes.bfloat16
def gentries(a):
    return np.ascontiguousarray(a.reshape(8, 16, -1).transpose(0, 2, 1)).reshape(8, -1)
def gtable(e):
    e = np.asarray(e); return np.ascontiguousarray(e.reshape(8, -1, 16).transpose(0, 2, 1)).reshape(128, -1).astype(np.int32)
W, UM, O, T, ST = 4096, 4096, 256, 5, 1
def parts(rng):
    x = rng.integers(0, 256, (N, 128, W), dtype=np.int16)
    p = rng.integers(0, W, (N, 8, W)); v = rng.integers(0, W, (N, 8, O, 16)); y = rng.integers(0, 256, (N, 128, O)); w = rng.integers(0, 256, (N, 128, 1))
    lm = np.zeros((N, 8, 2), np.int64)
    for q in range(N):
        lm[q, :, 0] = rng.permutation(np.array([400, 1000, 1150, 1300, 1400, 1550, 1700, 2600])) + rng.integers(-50, 51, 8)
        lm[q, :, 1] = rng.permutation(np.array([1100, 1200, 1300, 1400, 1500, 1600, 1700, 1800])) + rng.integers(-50, 51, 8)
    return x, p, v, y, w, lm
def pack(x, p, v, y, w, lm):
    return {"claim": np.ascontiguousarray(x).astype(np.float32).astype(BF), "par": np.ascontiguousarray(p).astype(np.int32), "who": np.stack([gtable(a.reshape(8, -1)) for a in v]),
            "est": np.ascontiguousarray(y).astype(np.float32).astype(BF), "wt": np.ascontiguousarray(w).astype(np.int32), "lim": np.ascontiguousarray(lm).astype(np.int32)}
def setup_inputs(rng):
    return pack(*parts(rng))
def setup_inputs_spread(rng):
    x, p, v, y, w, lm = parts(rng)
    x = (x.reshape(N, 8, 16, W) >> rng.integers(0, 9, (N, 8, 1, W)).astype(np.int16)).reshape(N, 128, W)
    p = np.minimum((W * rng.random(p.shape) ** 2).astype(np.int64), W - 1); v = np.minimum((W * rng.random(v.shape) ** 3).astype(np.int64), W - 1)
    y = (y.reshape(N, 8, 16, O) >> rng.integers(0, 9, (N, 8, 1, O))).reshape(N, 128, O); w = w >> rng.integers(0, 8, w.shape)
    lm = np.minimum(np.exp2(5 + 7 * rng.random(lm.shape)).astype(np.int64), 4080)
    return pack(x, p, v, y, w, lm)
def setup_inputs_ends(rng):
    c = rng.integers(0, 4, (N, 8, 1, W), dtype=np.int16); x = (255 * np.where(c < 2, c, rng.integers(0, 2, (N, 8, 16, W), dtype=np.int16))).reshape(N, 128, W)
    p = (W - 1) * rng.integers(0, 2, (N, 8, W))
    v = np.where(rng.random((N, 8, O, 1)) < 0.2, rng.integers(0, W, (N, 8, O, 16)), (W - 1) * rng.integers(0, 2, (N, 8, O, 16)))
    c = rng.integers(0, 4, (N, 8, 1, O)); y = (255 * np.where(c < 2, c, rng.integers(0, 2, (N, 8, 16, O)))).reshape(N, 128, O)
    w = 255 * rng.integers(0, 2, (N, 8, 16)); w[:, 3] = 0; w[:, 7] = 255; w = w.reshape(N, 128, 1)
    lm = np.full((N, 8, 2), 4080, np.int64)
    for q in range(N):
        for b in range(2): lm[q, :7, b] = 4080 * rng.permutation(np.array([0, 0, 0, 0, 1, 1, 1]))
    u = (16 * 255 * 255) & (UM - 1); hl = ((((W - 1) * u) >> 5) + W - 1) & (W - 1); h1 = ((u >> 5) + 1) & (W - 1)
    x[:, 112:, 0] = 0; x[:, 112:, hl] = 255; x[:, 112:, h1] = 255
    p[:, 7, 0] = W - 1; p[:, 7, 1] = 0; p[:, 7, W - 1] = 0
    y[:, 112:, O - 1] = 255; y[:, 112:, 3] = 255
    v[:, 7, O - 1] = 0; v[:, 7, O - 1, 14] = W - 1; v[:, 7, O - 1, 15] = 1
    v[:, 7, 3] = 0; v[:, 7, 3, 1] = W - 1; v[:, 7, 3, 2] = W - 1
    return pack(x, p, v, y, w, lm)
def setup_inputs_corners(rng):
    x, p, v, y, w, lm = parts(rng); sh = int(rng.integers(0, 8)); a = np.arange(W)
    for q in range(N):
        for g in range(8):
            m = (g + q + sh) % 8; lo, hi = 16 * g, 16 * g + 16
            if m == 0:
                p[q, g] = np.minimum(a + 1, W - 1); lm[q, g] = (4080, 1500); v[q, g, 0] = W - 1; v[q, g, 1] = 0; v[q, g, O - 1, 15] = W - 2
            elif m == 1:
                p[q, g] = a; lm[q, g] = (1, 0)
            elif m == 2:
                p[q, g] = 0; lm[q, g] = (0, 0); v[q, g] = rng.integers(0, W, (O, 1)); v[q, g, ::2] = W - 1
            elif m == 3:
                pool = np.concatenate([np.array([0, W - 1]), 1 + rng.permutation(W - 2)[:6]]); v[q, g] = pool[rng.integers(0, 8, (O, 16))]; p[q, g] = W - 1; lm[q, g] = (1300, 0)
            elif m == 4:
                w[q, lo:hi] = 0; lm[q, g] = (1, 0)
                e = rng.permutation(W)[:19]; c = x[q, lo:hi]
                c[:, e[:16]] = 255; c[np.arange(14), e[1:15]] = 0; c[14:, e[15]] = 0
                c[:, e[16:18]] = 0; c[:, e[18]] = 127
                p[q, g, e[:16]] = e[16]; p[q, g, e[16:18]] = e[1]; p[q, g, e[18]] = e[18]
                v[q, g, O - 1] = e[:16]
                v[q, g, O - 2] = e[:16]; v[q, g, O - 2, 0] = e[18]
                v[q, g, 0] = e[16]; v[q, g, 0, 0] = e[0]; v[q, g, O - 3] = e[17]; v[q, g, O - 3, 0] = e[0]
            elif m == 5:
                w[q, lo:hi] = 255; y[q, lo:hi] = 255; lm[q, g] = (1300, 4080)
            elif m == 6:
                v[q, g] = rng.permutation(W)[:16 * O].reshape(O, 16); lm[q, g] = (1200, 0)
            else:
                p[q, g] = W - 1 - a; w[q, lo:hi] = 0; w[q, lo + int(rng.integers(0, 16))] = 1; y[q, lo:hi, 0] = 0; lm[q, g] = (4080, 0)
    return pack(x, p, v, y, w, lm)
def setup_inputs_counts(rng):
    x, p, v, y, w, lm = parts(rng); a = int(rng.integers(0, N)); b = (a - ST) % N; d = (a - 2 * ST) % N; s = np.arange(W)
    p[d, :, :64] = np.arange(64); v[d] = rng.integers(0, 63, (8, O, 16)); lm[d, :, 0] = 1360 + rng.integers(-50, 51, 8)
    lm[b, :, 0] = 0; v[b] = rng.integers(64, W, (8, O, 16))
    w[a] = 0; x[a] = (x[a] & 63) + 191 * (s & 1)
    p[a] = (p[a] - (p[a] & 1)) + ((s + (s >= 64)) & 1); p[a, :, 63] = 63
    lm[a, :, 0] = 340 + rng.integers(-20, 21, 8); lm[a, :, 1] = 4080
    v[a] = rng.integers(64, W, (8, O, 16)); v[a, 7, O - 1] = 63; v[a, 0, 0, :15] = 63
    return pack(x, p, v, y, w, lm)
def setup_inputs_ties(rng):
    x, p, v, y, w, lm = parts(rng)
    z = np.stack([rng.permutation(np.array([1, 1, 3, 3, 8, 31, 64, 85])) for q in range(N)])
    x = ((x & 3).reshape(N, 8, 16, W) * z[:, :, None, None]).reshape(N, 128, W)
    lm = np.stack([z * rng.integers(17, 23, (N, 8)), z * rng.integers(18, 27, (N, 8))], axis=2)
    v[:, ::3] = v[:, ::3] & 63
    return pack(x, p, v, y, w, lm)
def check_inputs(d):
    bad = []
    for k, lo, hi in (("claim", 0, 255), ("par", 0, W - 1), ("who", 0, W - 1), ("est", 0, 255), ("wt", 0, 255), ("lim", 0, 4080)):
        a = np.asarray(d[k]).astype(np.float32)
        if not (np.min(a) >= lo and np.max(a) <= hi): bad.append("range of " + k)
        elif not np.all(np.floor(a) == a): bad.append("whole numbers of " + k)
    return bad
def place(s, u, t):
    return (((s * u[:, :, None]) >> 5) + s + 77 * t) & (W - 1)
def reference(claim, par, who, est, wt, lim):
    X = np.ascontiguousarray(np.asarray(claim).astype(np.float32).astype(np.int32).reshape(N, 8, 16, W).transpose(0, 1, 3, 2))
    P = np.asarray(par).astype(np.int64); V = np.stack([gentries(a) for a in who]).astype(np.int64).reshape(N, 8, O, 16)
    Y = np.ascontiguousarray(np.asarray(est).astype(np.float32).astype(np.int64).reshape(N, 8, 16, O).transpose(0, 1, 3, 2))
    wq = np.asarray(wt).astype(np.int64).reshape(N, 8, 1, 16); lm = np.asarray(lim).astype(np.int64)
    G = np.arange(8)[:, None]; cnt = [0] * N
    for t in range(T):
        for q in range(N):
            r = (q - ST * t) % N; v = V[r]; y0 = Y[r]
            u = np.add.reduce(wq[q] * y0, axis=2) & (UM - 1)
            p = P[q][G, v.reshape(8, -1)].reshape(8, O, 16)
            x = X[q][G, place(v, u, t).reshape(8, -1)].reshape(8, O, 16, 16)
            z = X[q][G, place(p, u, t).reshape(8, -1)].reshape(8, O, 16, 16)
            dep = np.add.reduce(np.abs(x - z), axis=3) < lm[q, :, 0][:, None, None] + cnt[q]
            cand = ~dep | np.all(dep, axis=2, keepdims=True)
            M = (np.max(np.where(cand[..., None], x, -1), axis=2) + np.min(np.where(cand[..., None], x, 256), axis=2)) >> 1
            far = np.where(cand, np.add.reduce(np.abs(x - M[:, :, None, :]), axis=3), 1 << 20)
            y = np.take_along_axis(x, np.argmin(far, axis=2)[:, :, None, None], 2)[:, :, 0, :]
            err = np.add.reduce(np.abs(x - y[:, :, None, :]), axis=3)
            j = np.argmax(err, axis=2)[:, :, None]; rest = np.where(np.arange(16) == j, -1, err); k = np.argmax(rest, axis=2)[:, :, None]
            ask = np.take_along_axis(rest, k, 2)[:, :, 0] >= lm[q, :, 1][:, None]
            vj = np.take_along_axis(v, j, 2)[:, :, 0]; vk = np.take_along_axis(v, k, 2)[:, :, 0]
            for g in range(8):
                o = np.nonzero(ask[g])[0]
                if len(o):
                    s, first = np.unique(vk[g, o], return_index=True)
                    P[q, g, s] = vj[g, o[first]]
            V[r] = np.where(dep, p, v); Y[r] = (y0 + y) >> 1
            cnt[q] = int(np.count_nonzero(dep)) & 31
    return {"yv": np.stack([gtable(a.reshape(8, -1)) for a in V]).astype(np.float32), "ye": np.ascontiguousarray(Y.transpose(0, 1, 3, 2)).reshape(N, 128, O).astype(np.float32).astype(BF), "yp": P.astype(np.float32)}

@@ -1,0 +1,729 @@
+import numpy as np
+from concourse.mybir import AluOpType, AxisListType, ActivationFunctionType
+
+A = AluOpType
+AF = ActivationFunctionType
+VIS = 5
+BLOCKS = [(0, 64), (64, 128), (128, 192), (192, 256)]
+BUF = {}
+SEMAPHORES = ["vv", "ss", "pp", "gg"]
+
+
+def _b(name, shape, dtype="float32", where="sbuf"):
+    BUF[name] = (where, shape, dtype)
+
+
+BF, F32, I32, U16 = "bfloat16", "float32", "int32", "uint16"
+_b("claimw", [128, 4096], BF)
+_b("parw", [128, 4368], BF)
+for _t in range(VIS):
+    _b("yb%d" % _t, [128, 256], BF)
+    _b("vb%d" % _t, [128, 256], F32)
+    _b("yn%d" % _t, [128, 256], BF)
+    _b("vn%d" % _t, [128, 256], F32)
+    _b("thc%d" % _t, [128, 8], F32)
+for _n in ("x0", "x1", "xs", "pr", "d", "ad", "af", "ae", "mx", "mn"):
+    _b(_n, [128, 4096], BF)
+for _n in ("um0", "um1", "hi0", "hi1", "t1", "t2", "t3", "msum", "mhalf", "yhalf", "aint"):
+    _b(_n, [128, 256], I32)
+for _n in ("hl", "zl", "vl", "h2l"):
+    _b(_n, [128, 256], U16)
+for _n in ("q1", "q2", "dif", "vm", "fh", "dlt", "h2f", "sa", "sb", "cr", "dg", "cs", "tt_"):
+    _b(_n, [128, 256], F32)
+for _n in ("dep", "mm_", "yy", "ohb", "adat", "oc"):
+    _b(_n, [128, 256], BF)
+_b("tr", [128, 512], F32)
+_b("kint", [128, 64], I32)
+_b("yl", [128, 16], U16)
+_b("pm", [128, 512], F32)
+_b("code", [128, 64], I32)
+_b("ask", [128, 32], F32)
+_b("kk", [128, 32], BF)
+_b("ktb", [16, 256], BF)
+_b("bia", [128, 16], F32)
+_b("sint", [128, 32], I32)
+_b("dd", [128, 3072], BF)
+_b("dso", [128, 3072], BF)
+_b("rs0", [128, 512], BF)
+_b("rs1", [128, 1024], BF)
+_b("px32", [128, 2048], BF)
+_b("cb", [128, 64], BF)
+for _t in range(VIS):
+    _b("ct%d" % _t, [128, 64], BF)
+_b("dfl", [128, 64], F32)
+_b("ol", [128, 16], U16)
+_b("dsum", [128, 2], F32)
+_b("cint", [128, 2], I32)
+for _n in ("ones", "eye", "neye", "blk", "blk1", "blk8k", "tri", "trim", "dm32", "wmat", "j1", "j2", "kt", "r2"):
+    _b(_n, [128, 128], BF)
+for _n in ("sx", "px", "r1", "rm"):
+    _b(_n, [128, 2048], BF)
+for _n in ("blkf", "blk512", "onesf", "dmask"):
+    _b(_n, [128, 128], F32)
+_b("exs", [16, 512], BF)
+_b("exf", [16, 128], F32)
+_b("eyef", [16, 16], F32)
+_b("io1", [128, 128], I32)
+_b("io2", [128, 128], I32)
+_b("pcol", [128, 4], I32)
+_b("cols", [128, 16], F32)
+_b("wti", [128, 1], I32)
+_b("wtf", [128, 1], F32)
+_b("limi", [8, 2], I32)
+_b("limf", [8, 2], F32)
+_b("limd", [8, 8], F32)
+_b("tht", [128, 16], F32)
+_b("thb", [128, 2], F32)
+_b("dcon", [128, 16], F32)
+_b("iod", [128, 16], I32)
+_b("whoi", [128, 256], I32)
+_b("pari", [128, 256], I32)
+_b("parlh", [128, 512], I32)
+_b("parb", [128, 512], BF)
+_b("ypf", [128, 256], F32)
+_b("dlo", [8, 4096], BF, "dram")
+_b("dhi", [8, 4096], BF, "dram")
+for _n in ("pz0", "pz1", "pz2", "pz3", "pk0", "pk1", "pf0", "pf1"):
+    _b(_n, [128, 512], F32, "psum")
+
+for _n in ("who", "est", "wt", "lim", "par", "claim0", "claim1", "plo", "phi", "pwin", "yv0", "yv1", "ye0", "ye1", "yp"):
+    SEMAPHORES.append("l_" + _n)
+for _t in range(1, VIS):
+    for _h in range(2):
+        for _k in "yv":
+            SEMAPHORES += ["a%s%d%d" % (_k, _t, _h), "o%s%d%d" % (_k, _t, _h)]
+
+PACK = {}
+SCRATCH = {}
+_ROOM = {}
+_KEEP = ("claimw", "parw", "whoi", "pari", "parb", "ypf", "wti", "limi", "hl", "zl", "vl", "h2l", "yl", "ol", "dd", "adat")
+for _n, (_w, _sh, _d) in BUF.items():
+    if _w == "sbuf" and _n not in _KEEP and _n[:2] not in ("yb", "vb", "yn", "vn") and _sh[0] == 128 and _sh[1] <= 512:
+        PACK[_n] = ("pack_" + _d, _ROOM.get(_d, 0))
+        _ROOM[_d] = _ROOM.get(_d, 0) + (_sh[1] + 15) // 16 * 16
+    else:
+        SCRATCH[_n] = BUF[_n]
+for _d in _ROOM:
+    SCRATCH["pack_" + _d] = ("sbuf", [128, _ROOM[_d]], _d)
+
+_CACHE = {}
+CY, PCY, GATH, SCAT = 0.00083 * 1.1, 0.00042 * 1.1, 1.5, 3.5
+VOV, SOV, POV, LAT = 0.04, 0.04, 0.02, 0.12
+SEED, EPS = 0, 0.0
+ONV = ()
+LEAD = {"x0": 2.7, "t1": 1.3, "t0": -0.4, "x1": 0.0, "n1": 1.3, "z0": -0.2, "m1": -0.6, "p0": 2.9, "w1": -1.1, "p1": -0.1, "w0": -3.1, "e1": -0.6, "n0": 0.6, "m0": 1.2, "z1": 0.4, "e0": -0.3}
+BONUS = {}
+ERRB = (("pf0", "pf1"), ("pf0", "pf1"))
+XL = 64
+
+
+def S(name, a, b, step=1, p=128):
+    return (name, a, b, step, p)
+
+
+def IND(name, a, b, off, c, d):
+    return (name, a, b, off, c, d, "ind")
+
+
+def ap(T, s):
+    if s[0] in PACK:
+        r, o = PACK[s[0]]
+        return T[r][0:s[4], o + s[1]:o + s[2]] if s[3] == 1 else T[r][0:s[4], o + s[1]:o + s[2]:s[3]]
+    if len(s) == 7:
+        return T[s[0]][:, s[1]:s[2]].indirect(T[s[3]][:, s[4]:s[5]])
+    t = T[s[0]]
+    if s[3] == 1:
+        return t[0:s[4], s[1]:s[2]]
+    return t[0:s[4], s[1]:s[2]:s[3]]
+
+
+def regs(s):
+    if len(s) == 7:
+        return [(s[0], s[1], s[2]), (s[3], s[4], s[5])]
+    return [(s[0], s[1], s[2])]
+
+
+def width(s):
+    if len(s) == 7:
+        return 16 * (s[5] - s[4])
+    return (s[2] - s[1] + s[3] - 1) // s[3]
+
+
+def half(*ss):
+    return all(BUF[s[0]][2] in (BF, U16) for s in ss)
+
+
+def build(nE):
+    ops = []
+    since = [100000]
+    part = [""]
+
+    def add(q, fns, R, W, cost, sem=None, val=0, send=None):
+        rr = [r for s in R for r in regs(s)]
+        ww = [(s[0], s[1], s[2]) for s in W]
+        offs = [(s[3], s[4], s[5]) for s in W if len(s) == 7]
+        ops.append({"q": q, "f": fns, "R": rr + offs, "W": ww, "c": cost, "sem": sem, "val": val, "send": send, "at": len(ops) - since[0], "part": part[0]})
+        return len(ops) - 1
+
+    def vcost(n, f=1.0):
+        return max(64, n * f) * CY + VOV
+
+    def tt(out, a, b, op):
+        n = width(b)
+        if len(a) == 7:
+            f = GATH
+        else:
+            f = 1.0 if "psum" in (BUF[a[0]][0], BUF[b[0]][0]) else 2.0
+        add("V", [lambda g, T: g.vector.tensor_tensor(out=ap(T, out), in0=ap(T, a), in1=ap(T, b), op=op)], [a, b], [out], vcost(n, f))
+
+    def cp(out, a):
+        f = SCAT if len(out) == 7 else GATH if len(a) == 7 else 0.5 if half(out, a) else 1.0
+        add("V", [lambda g, T: g.vector.tensor_copy(out=ap(T, out), in_=ap(T, a))], [a], [out], vcost(width(a), f))
+
+    def ts(out, a, s1, op0, s2=None, op1=None):
+        R = [a] + [s for s in (s1, s2) if isinstance(s, tuple)]
+
+        def f(g, T):
+            x1 = ap(T, s1) if isinstance(s1, tuple) else s1
+            x2 = ap(T, s2) if isinstance(s2, tuple) else s2
+            if op1 is None:
+                return g.vector.tensor_scalar(out=ap(T, out), in0=ap(T, a), scalar1=x1, scalar2=None, op0=op0)
+            return g.vector.tensor_scalar(out=ap(T, out), in0=ap(T, a), scalar1=x1, scalar2=x2, op0=op0, op1=op1)
+        add("V", [f], R, [out], vcost(width(a), 0.5 if half(out, a) else 1.0))
+
+    def scan(out, d0, d1, init, op0, op1):
+        add("V", [lambda g, T: g.vector.tensor_tensor_scan(out=ap(T, out), data0=ap(T, d0), data1=ap(T, d1), initial=init, op0=op0, op1=op1)],
+            [d0, d1], [out], vcost(width(d1), 0.5 if half(out, d0, d1) else 1.0))
+
+    def red(out, a, op, absv=False):
+        if absv:
+            fn = lambda g, T: g.vector.tensor_reduce(out=ap(T, out), in_=ap(T, a), axis=AxisListType.X, op=op, apply_absolute_value=True)
+        else:
+            fn = lambda g, T: g.vector.tensor_reduce(out=ap(T, out), in_=ap(T, a), axis=AxisListType.X, op=op)
+        add("V", [fn], [a], [out], vcost(width(a)))
+
+    def fill(out, c):
+        add("V", [lambda g, T: g.vector.memset(ap(T, out), c)], [], [out], vcost(width(out)))
+
+    def act(out, a, func, bias=None, scale=None):
+        R = [a] + ([bias] if isinstance(bias, tuple) else [])
+
+        def f(g, T):
+            kw = {}
+            if bias is not None:
+                kw["bias"] = ap(T, bias) if isinstance(bias, tuple) else bias
+            if scale is not None:
+                kw["scale"] = scale
+            return g.scalar.activation(out=ap(T, out), in_=ap(T, a), func=func, **kw)
+        add("S", [f], R, [out], max(64, width(a) * (GATH if len(a) == 7 else 1.0)) * CY + SOV)
+
+    def gather(tag, out, a):
+        if tag in ONV:
+            cp(out, a)
+        else:
+            act(out, a, AF.Copy)
+
+    def mm(groups):
+        fns = []
+        c = POV
+        for (o, l, r, st, sp) in groups:
+            fns.append(lambda g, T, o=o, l=l, r=r, st=st, sp=sp: g.tensor.matmul(out=ap(T, o), lhsT=ap(T, l), rhs=ap(T, r), start=st, stop=sp))
+            c += max(64, width(r)) * PCY * (4 if BUF[r[0]][2] == F32 else 1)
+        add("P", fns, [r for (o, l, r2, st, sp) in groups for r in (l, r2)], [x[0] for x in groups], c)
+
+    def one(out, l, r):
+        mm([(out, l, r, True, True)])
+
+    def dma(q, sem, pairs, R, W, cost):
+        add(q, [lambda g, T, o=o, i=i: (g.sync if q == "Y" else g.scalar).dma_start(o(T), i(T)) for (o, i) in pairs], R, W, cost, sem=sem, val=16 * len(pairs))
+
+    def iota(out, pattern, base, cm):
+        kw = {"allow_small_or_imprecise_dtypes": True} if BUF[out[0]][2] in (BF, F32) else {}
+        add("G", [lambda g, T: g.iota(ap(T, out), pattern, base, cm, **kw)], [], [out], 0.13 + 2 * width(out) * CY)
+
+    def asel(out, a, pattern, op, base, cm):
+        add("G", [lambda g, T: g.affine_select(ap(T, out), ap(T, a), pattern, op, 0.0, base, cm)], [a], [out], 0.17 + 2 * width(out) * CY)
+
+    def full(name):
+        sh = BUF[name][1]
+        return S(name, 0, sh[1], 1, sh[0])
+
+    dma("Y", "l_who", [(lambda T: T.whoi[:], lambda T: T.who[:])], [], [full("whoi")], 2.0)
+    dma("Y", "l_est", [(lambda T: T.yb0[:], lambda T: T.est[:])], [], [full("yb0")], 2.0)
+    dma("Y", "l_wt", [(lambda T: T.wti[:], lambda T: T.wt[:])], [], [full("wti")], 2.0)
+    dma("S", "l_claim0", [(lambda T: T.claimw[:, 0:2048], lambda T: T.claim[:, 0:2048])], [], [S("claimw", 0, 2048)], 3.0)
+    dma("S", "l_claim1", [(lambda T: T.claimw[:, 2048:4096], lambda T: T.claim[:, 2048:4096])], [], [S("claimw", 2048, 4096)], 4.0)
+    dma("Y", "l_par", [(lambda T: T.pari[:], lambda T: T.par[:])], [], [full("pari")], 2.0)
+    dma("Y", "l_lim", [(lambda T: T.limi[:], lambda T: T.lim[:])], [], [full("limi")], 2.0)
+    fill(full("ones"), 1.0)
+    asel(full("blk1"), full("ones"), [[-16, 8], [0, 16]], A.is_ge, 0, 1)
+    asel(full("blk"), full("blk1"), [[16, 8], [0, 16]], A.is_ge, 15, -1)
+    asel(full("eye"), full("ones"), [[-1, 128]], A.is_equal, 0, 1)
+    iota(S("pcol", 0, 1), [[0, 1]], 0, 1)
+    cp(full("vb0"), full("whoi"))
+    cp(full("vl"), full("vb0"))
+    ts(S("parlh", 0, 256), full("pari"), 255, A.bitwise_and)
+    ts(S("parlh", 256, 512), full("pari"), 8, A.logical_shift_right)
+    cp(full("parb"), full("parlh"))
+    dma("Y", "l_plo", [(lambda T: T.dlo[:], lambda T: T.parb[:, 0:256])], [S("parb", 0, 256)], [S("dlo", 0, 4096, 1, 8)], 2.0)
+    dma("Y", "l_phi", [(lambda T: T.dhi[:], lambda T: T.parb[:, 256:512])], [S("parb", 256, 512)], [S("dhi", 0, 4096, 1, 8)], 2.0)
+    dma("Y", "l_pwin", [(lambda T, i=i: T.parw[i::16, 16:4112], lambda T, i=i: (T.dhi if i % 2 else T.dlo)[:]) for i in range(16)],
+        [S("dlo", 0, 4096, 1, 8), S("dhi", 0, 4096, 1, 8)], [S("parw", 16, 4112)], 8.0)
+    cp(full("wtf"), full("wti"))
+    ts(full("wmat"), full("blk"), S("wtf", 0, 1), A.mult)
+    ts(S("pcol", 1, 2), S("pcol", 0, 1), 15, A.bitwise_and)
+    ts(S("pcol", 2, 3), S("pcol", 0, 1), 1, A.bitwise_and)
+    K16 = S("cols", 0, 1)
+    CODE = S("cols", 1, 2)
+    COLW = S("cols", 2, 3)
+    COLA = S("cols", 3, 4)
+    ACS = S("cols", 7, 8)
+    ACB = S("cols", 8, 9)
+    cp(K16, S("pcol", 1, 2))
+    ts(CODE, K16, -1.0, A.mult, 16.0, A.add)
+    ts(S("cols", 4, 5), K16, 1.0, A.is_equal, 256.0, A.mult)
+    ts(S("cols", 5, 6), K16, 0.0, A.is_equal)
+    tt(COLW, S("cols", 4, 5), S("cols", 5, 6), A.add)
+    ts(COLA, K16, 16.0, A.mult)
+    cp(S("cols", 6, 7), S("pcol", 2, 3))
+    ts(ACS, S("cols", 6, 7), -255.0 / 256.0, A.mult, 1.0, A.add)
+    ts(ACB, S("cols", 6, 7), -0.498, A.mult)
+    fill(full("sx"), 0.0)
+    for k in range(16):
+        cp(S("sx", 129 * k, 128 * k + 128, 16), S("blk", 0, 128, 16))
+    ts(full("px"), full("sx"), COLW, A.mult)
+    ts(full("neye"), full("eye"), -1.0, A.mult)
+    asel(full("tri"), full("blk"), [[1, 128]], A.is_gt, 0, -1)
+    ts(full("trim"), full("eye"), -32.0, A.mult)
+    tt(full("trim"), full("trim"), full("tri"), A.add)
+    ts(full("dm32"), full("eye"), 32.0, A.mult)
+    tt(full("dm32"), full("dm32"), full("blk"), A.subtract)
+    asel(S("exs", 0, 128, 1, 16), S("ones", 0, 128, 1, 16), [[1, 128]], A.is_ge, 0, -16)
+    asel(S("exs", 128, 256, 1, 16), S("exs", 0, 128, 1, 16), [[-1, 128]], A.is_ge, 15, 16)
+    asel(S("exs", 256, 384, 1, 16), S("ones", 0, 128, 1, 16), [[1, 128]], A.is_ge, 128, -16)
+    asel(S("exs", 384, 512, 1, 16), S("exs", 256, 384, 1, 16), [[-1, 128]], A.is_ge, -113, 16)
+    cp(full("exf"), S("exs", 128, 256, 1, 16))
+    cp(full("limf"), full("limi"))
+    cp(full("onesf"), full("ones"))
+    cp(full("eyef"), S("eye", 0, 16, 1, 16))
+    ts(full("limd"), S("eyef", 0, 8, 1, 8), S("limf", 1, 2, 1, 8), A.mult, 32.0, A.mult)
+    mm([(S("pk1", 0, 2), S("exf", 0, 128, 1, 8), full("limf"), True, True),
+        (S("pk1", 8, 16), S("onesf", 0, 128, 1, 8), full("limd"), True, True)])
+    cp(full("thb"), S("pk1", 0, 2))
+    cp(S("thc0", 0, 1), S("pk1", 0, 1))
+    fill(S("tht", 0, 8), -1.0)
+    cp(S("tht", 8, 16), S("pk1", 8, 16))
+    cp(full("blkf"), full("blk"))
+    fill(full("r1"), 1.0)
+    ts(S("r1", 0, 2048, 16), S("r1", 0, 2048, 16), 0.0, A.mult)
+    fill(full("rm"), 0.0)
+    ts(S("rm", 0, 2048, 16), S("rm", 0, 2048, 16), 256.0, A.add)
+    QB = (BLOCKS[0][1] - BLOCKS[0][0]) // 16
+    iota(S("io1", 0, 16 * QB), [[0, 16], [256, QB]], 0, 0)
+    ts(S("j1", 0, 16 * QB), S("io1", 0, 16 * QB), COLA, A.add)
+    iota(S("j2", 0, 16 * QB), [[1, 16], [0, QB]], 0, 0)
+    iota(full("kt"), [[0, 8], [-1, 16]], 16, 0)
+    iota(full("oc"), [[1, 256]], 0, 0)
+    fill(full("r2"), 1.0)
+    ts(S("r2", 1, 128, 16), S("r2", 1, 128, 16), 0.0, A.mult)
+    iota(full("io2"), [[1, 128]], 128, -1)
+    ts(full("io2"), full("io2"), 15, A.bitwise_and)
+    ts(full("dmask"), full("io2"), 0.0, A.is_equal)
+    ts(full("blk512"), full("blk"), 512.0, A.mult)
+    ts(full("blk8k"), full("blk"), 8192.0, A.mult)
+    iota(full("iod"), [[16, 16]], 4112, 0)
+    ts(full("dcon"), full("iod"), K16, A.add)
+    ts(full("px32"), full("px"), 32.0, A.mult)
+    fill(full("cb"), -131072.0)
+    for t in range(VIS):
+        fill(full("ct%d" % t), float(2464 * t))
+    fill(full("dd"), 4194304.0)
+    for h in range(2):
+        n, w = 512 + 512 * h, 128 + 128 * h
+        fill(full("rs%d" % h), 0.0)
+        ts(S("rs%d" % h, 0, n, w), S("rs%d" % h, 0, n, w), 4194304.0, A.add)
+    turn = [0]
+
+    def bank(names):
+        turn[0] += 1
+        return names[turn[0] % 2]
+
+    def send(what, t, h):
+        c = (128 * h, 128 * h + 128)
+        key = "%s%d%d" % (what, t + 1, h)
+        i = add("G", None, [S("%sn%d" % (what, t), *c)], [], 1.0, sem="o" + key, val=nE, send=(what, t + 1, h))
+        add("N", None, [], [S("%sb%d" % (what, t + 1), *c)], 2.0, sem="a" + key, val=nE, send=i)
+
+    def st_names(t, h):
+        c = (128 * h, 128 * h + 128)
+        v = S("vb%d" % t, *c)
+        if t > 0:
+            cp(S("vl", *c), v)
+        act(S("q1", *c), v, AF.Identity, float(2464 * t - 131072), 32.0)
+
+    def st_hash(t, h):
+        c = (128 * h, 128 * h + 128)
+        um, hi = S("um%d" % (t % 2), *c), S("hi%d" % (t % 2), *c)
+        U, W = S("pz%d" % (2 * h), 256, 384), S("pz%d" % (2 * h), 384, 512)
+        one(U, full("wmat"), S("yb%d" % t, *c))
+        cp(S("t1", *c), U)
+        ts(um, S("t1", *c), 4095, A.bitwise_and)
+        tt(W, S("vb%d" % t, *c), um, A.mult)
+        tt(S("t2", *c), W, S("q1", *c), A.add)
+        ts(hi, S("t2", *c), 5, A.arith_shift_right, 4095, A.bitwise_and)
+        cp(S("hl", *c), hi)
+
+    def st_xgather(t, h):
+        c = (128 * h, 128 * h + 128)
+        for a in range(c[0], c[1], XL):
+            gather("x%d" % (a // XL), S("x%d" % (t % 2), 16 * a, 16 * (a + XL)), IND("claimw", 0, 4096, "hl", a, a + XL))
+
+    def st_pgather(t, n):
+        c = BLOCKS[n]
+        gather("p%d" % n, S("pr", 16 * c[0], 16 * c[1]), IND("parw", 16, 4112, "vl", *c))
+
+    def st_z(t, n):
+        c = BLOCKS[n]
+        L = c[1] - c[0]
+        X, X2 = 16 * c[0], 16 * c[1]
+        b = "pz%d" % n
+        p, w2, w3, q = [S(b, 64 * e, 64 * e + L) for e in range(4)]
+        w4 = q
+        um, hi, dep = S("um%d" % (t % 2), *c), S("hi%d" % (t % 2), *c), S("dep", *c)
+        mm([(p, S("px", 128 * k, 128 * k + 128), S("pr", X + k, X2, 16), k == 0, k == 15) for k in range(16)])
+        mm([(q, full("eye"), full("cb"), True, False), (q, full("eye"), full("ct%d" % t), False, False)] +
+           [(q, S("px32", 128 * k, 128 * k + 128), S("pr", X + k, X2, 16), False, k == 15) for k in range(16)])
+        tt(S("q2", *c), p, um, A.mult)
+        tt(S("t3", *c), q, S("q2", *c), A.add)
+        ts(S("t3", *c), S("t3", *c), 5, A.arith_shift_right, 4095, A.bitwise_and)
+        cp(S("zl", *c), S("t3", *c))
+        tt(S("dif", *c), p, S("vb%d" % t, *c), A.subtract)
+        tt(S("d", X, X2), IND("claimw", 0, 4096, "zl", *c), S("x%d" % (t % 2), X, X2), A.subtract)
+        act(S("ad", X, X2), S("d", X, X2), AF.Abs)
+        mm([(w2, S("sx", 128 * k, 128 * k + 128), S("ad", X + k, X2, 16), k == 0, k == 15) for k in range(16)])
+        ts(dep, w2, S("thc%d" % t, 0, 1), A.is_lt)
+        mm([(w2, full("trim"), dep, True, True), (w3, full("dm32"), dep, True, True)])
+        ts(w2, w2, K16, A.is_equal)
+        tt(S("fh", *c), w2, hi, A.mult)
+        ts(w3, w3, 17.0, A.is_ge)
+        one(w2, full("blkf"), S("fh", *c))
+        tt(S("dlt", *c), w2, hi, A.subtract)
+        tt(w4, w3, S("dlt", *c), A.mult)
+        tt(S("h2f", *c), w4, hi, A.add)
+        cp(S("h2l", *c), S("h2f", *c))
+        gather("s%d" % n, S("xs", X, X2), IND("claimw", 0, 4096, "h2l", *c))
+
+    def st_m(t, n):
+        c = BLOCKS[n]
+        X, X2 = 16 * c[0], 16 * c[1]
+        xs = S("xs", X, X2)
+        scan(S("mx", X, X2), S("r1", 0, X2 - X), xs, 0.0, A.mult, A.max)
+        scan(S("mn", X, X2), S("rm", 0, X2 - X), xs, 256.0, A.max, A.min)
+        w = S("pz%d" % n, 64, 64 + c[1] - c[0])
+        mm([(w, full("eye"), S("mx", X + 15, X2, 16), True, False), (w, full("eye"), S("mn", X + 15, X2, 16), False, True)])
+        ts(S("mhalf", *c), w, 0.5, A.mult, -0.25, A.add)
+        cp(S("mm_", *c), S("mhalf", *c))
+
+    def st_newnames(t, h):
+        c = (128 * h, 128 * h + 128)
+        tt(S("vm", *c), S("dif", *c), S("dep", *c), A.mult)
+        tt(S("vn%d" % t, *c), S("vm", *c), S("vb%d" % t, *c), A.add)
+        if t < VIS - 1:
+            send("v", t, h)
+            red(S("dsum", h, h + 1), S("dep", *c), A.add)
+
+    def st_count(t):
+        if t == VIS - 1:
+            return
+        mm([(S("pk0", 0, 1), full("onesf"), S("dsum", 0, 1), True, False), (S("pk0", 0, 1), full("onesf"), S("dsum", 1, 2), False, True)])
+        cp(S("cint", 0, 1), S("pk0", 0, 1))
+        ts(S("cint", 1, 2), S("cint", 0, 1), 31, A.bitwise_and)
+        tt(S("thc%d" % (t + 1), 0, 1), S("cint", 1, 2), S("thb", 0, 1), A.add)
+
+    def distances(src, X, mid, out, scale, banks):
+        L = width(mid)
+        K = 512 // L
+        for q in range(16 // K):
+            b = bank(banks)
+            gr = []
+            for e in range(K):
+                k = K * q + e
+                o = S(b, L * e, L * e + L)
+                gr += [(o, full("eye"), S(src, X + k, X + 16 * L, 16), True, False), (o, full("neye"), mid, False, True)]
+            mm(gr)
+            act(S(out, X + 512 * q, X + 512 * q + 512), S(b, 0, 512), AF.Abs, None, scale)
+
+    def st_truth(t, n):
+        c = BLOCKS[n]
+        L = c[1] - c[0]
+        X, X2, Q, h = 16 * c[0], 16 * c[1], L // 16, c[0] // 128
+        distances("xs", X, S("mm_", *c), "af", 4096.0, ("pf0", "pf1"))
+        bk, K = "pk%d" % h, c[0] % 128
+        key = S(bk, K, K + L)
+        mm([(key, full("eye"), S("j1", 0, L), True, False), (key, full("eye"), S("j2", 0, L), False, False)] +
+           [(key, S("sx", 128 * a, 128 * a + 128), S("af", X + a, X2, 16), False, a == 15) for a in range(16)])
+        B = 2 * c[0]
+        cp(S("tr", B, B + L // 2), S(bk, K + L // 2, K + L))
+        tt(S("tr", B + L // 2, B + L), S(bk, K, K + L // 2), S("tr", B, B + L // 2), A.min)
+        a, w = B + L // 2, L // 4
+        while w > Q:
+            tt(S("tr", a + 2 * w, a + 3 * w), S("tr", a, a + w), S("tr", a + w, a + 2 * w), A.min)
+            a, w = a + 2 * w, w // 2
+        I = c[0] // 4
+        tt(S("kint", I, I + Q), S("tr", a, a + w), S("tr", a + w, a + 2 * w), A.min)
+        ts(S("kint", I + Q, I + 2 * Q), S("kint", I, I + Q), 4095, A.bitwise_and)
+        cp(S("yl", c[0] // 16, c[1] // 16), S("kint", I + Q, I + 2 * Q))
+        cp(S("yy", *c), IND("xs", X, X2, "yl", c[0] // 16, c[1] // 16))
+
+    def st_est(t, h):
+        c = (128 * h, 128 * h + 128)
+        key = S("pk%d" % h, 384, 512)
+        mm([(key, full("eye"), S("yy", *c), True, False), (key, full("eye"), S("yb%d" % t, *c), False, True)])
+        ts(S("yhalf", *c), key, 0.5, A.mult, -0.25, A.add)
+        cp(S("yn%d" % t, *c), S("yhalf", *c))
+        if t < VIS - 1:
+            send("y", t, h)
+
+    def st_err(t, h):
+        c = (128 * h, 128 * h + 128)
+        X = 2048 * h
+        distances("x%d" % (t % 2), X, S("yy", *c), "ae", 32.0, ERRB[h])
+        bk, ba, E = "pk%d" % h, "pz%d" % (2 * h + 1), 256
+        ek = S(bk, E, E + 128)
+        mm([(ek, full("eye"), full("kt"), True, False)] +
+           [(S(bk, E + k, E + 128, 16), S("ae", X + 128 * k, X + 128 * k + 128), S("blk", 0, 128, 16), False, k == 15) for k in range(16)])
+        B = 256 * h
+        scan(S("pm", B, B + 128), S("r1", 0, 128), ek, 0.0, A.mult, A.max)
+        tt(S("tt_", 128 * h + 1, 128 * h + 128), S(bk, E + 1, E + 128), S("pm", B, B + 127), A.min)
+        scan(S("pm", B + 129, B + 256), S("r2", 1, 128), S("tt_", 128 * h + 1, 128 * h + 128), 0.0, A.mult, A.max)
+        m = S("pm", B + 15, B + 256, 16)
+        cp(S("code", 32 * h, 32 * h + 16), m)
+        tt(S("ask", 16 * h, 16 * h + 16), m, full("tht"), A.is_ge)
+        ts(S("code", 32 * h + 16, 32 * h + 32), S("code", 32 * h, 32 * h + 16), 31, A.bitwise_and)
+        tt(S("kk", 16 * h, 16 * h + 16), S("code", 32 * h + 16, 32 * h + 32), S("ask", 16 * h, 16 * h + 16), A.mult)
+        one(S(ba, 0, 128, 1, 16), S("kk", 16 * h, 16 * h + 16), full("eye"))
+        kt = S("ktb", 128 * h, 128 * h + 128, 1, 16)
+        act(kt, S(ba, 0, 128, 1, 16), AF.Copy)
+        RA, RB, C, N = S(ba, 128, 256), S(ba, 256, 384), S(ba, 384, 512), S(ba, 0, 128)
+        mm([(RB, S("exs", 384, 512, 1, 16), kt, True, True), (RA, S("exs", 128, 256, 1, 16), kt, True, True)])
+        v = S("vb%d" % t, *c)
+        ts(S("ohb", *c), RB, CODE, A.is_equal)
+        tt(S("sb", *c), S("ohb", *c), v, A.mult)
+        mm([(C, full("blk512"), S("sb", *c), True, False), (C, full("blk8k"), S("ohb", *c), False, False), (C, full("eye"), S("oc", *c), False, True)])
+        act(S("cr", *c), C, AF.Copy)
+        tt(S("dg", *c), C, full("dmask"), A.mult)
+        scan(S("cs", *c), S("r1", 0, 128), S("dg", *c), 0.0, A.mult, A.add)
+        lst = S("cs", 128 * h + 15, 128 * h + 128, 16)
+        ts(S("bia", 8 * h, 8 * h + 8), lst, -1.0, A.mult, 128.0, A.add)
+        D0, DW = 1024 * h, 128 + 128 * h
+        for b in range(8 * h, 8 * h + 8):
+            w = 16 * b + 16
+            at = D0 + DW * (b - 8 * h)
+            act(S("dd", at, at + w), S("cr", 0, w), AF.Abs, S("bia", b, b + 1), 1.0)
+            if b % 4 == 3:
+                at += DW - 4 * DW
+                scan(S("dso", at, at + 4 * DW), full("rs%d" % h), S("dd", at, at + 4 * DW), 0.0, A.max, A.min)
+        ts(RA, RA, CODE, A.is_equal)
+        tt(S("sa", *c), RA, v, A.mult)
+        one(N, full("blkf"), S("sa", *c))
+        ts(S("aint", *c), N, ACS, A.mult, ACB, A.add)
+        ts(S("aint", *c), S("aint", *c), 255, A.bitwise_and)
+        cp(S("adat", *c), S("aint", *c))
+        cp(S("sint", 16 * h, 16 * h + 8), lst)
+        ts(S("sint", 16 * h + 8, 16 * h + 16), S("sint", 16 * h, 16 * h + 8), 9, A.logical_shift_right)
+        ts(S("dfl", 32 * h, 32 * h + 8), S("dso", D0 + DW - 1, D0 + 8 * DW, DW), 128.0, A.is_lt)
+        tt(S("dfl", 32 * h + 8, 32 * h + 16), S("dfl", 32 * h, 32 * h + 8), S("dcon", 8 * h, 8 * h + 8), A.mult)
+        tt(S("dfl", 32 * h + 16, 32 * h + 24), S("sint", 16 * h + 8, 16 * h + 16), S("dfl", 32 * h + 8, 32 * h + 16), A.max)
+        cp(S("ol", 8 * h, 8 * h + 8), S("dfl", 32 * h + 16, 32 * h + 24))
+
+    def st_scatter(t, h):
+        c = (128 * h, 128 * h + 128)
+        cp(IND("parw", 0, 4368, "ol", 8 * h, 8 * h + 8), S("adat", *c))
+
+    nb = len(BLOCKS)
+    for t in range(VIS):
+        since[0] = len(ops)
+        for h in range(2):
+            part[0] = "x%d" % h
+            st_names(t, h)
+        for h in range(2):
+            part[0] = "x%d" % h
+            st_hash(t, h)
+            st_xgather(t, h)
+        for n in range(nb):
+            part[0] = "p%d" % (2 * n // nb)
+            st_pgather(t, n)
+        for h in range(2):
+            for n in range(h * nb // 2, (h + 1) * nb // 2):
+                part[0] = "z%d" % h
+                st_z(t, n)
+                part[0] = "m%d" % h
+                st_m(t, n)
+            part[0] = "n%d" % h
+            st_newnames(t, h)
+        st_count(t)
+        for h in range(2):
+            part[0] = "t%d" % h
+            for n in range(h * nb // 2, (h + 1) * nb // 2):
+                st_truth(t, n)
+            st_est(t, h)
+        for h in range(2):
+            part[0] = "e%d" % h
+            st_err(t, h)
+        for h in range(2):
+            part[0] = "w%d" % h
+            st_scatter(t, h)
+    for h in range(2):
+        c = (128 * h, 128 * h + 128)
+        dma("Y", "l_yv%d" % h, [(lambda T, c=c: T.yv[:, c[0]:c[1]], lambda T, c=c: T.vn4[:, c[0]:c[1]])], [S("vn4", *c)], [], 2.0)
+        dma("Y", "l_ye%d" % h, [(lambda T, c=c: T.ye[:, c[0]:c[1]], lambda T, c=c: T.yn4[:, c[0]:c[1]])], [S("yn4", *c)], [], 2.0)
+    mm([(S("pf0", 0, 256), S("px", 128 * k, 128 * k + 128), S("parw", 16 + 256 * k, 272 + 256 * k), k == 0, k == 15) for k in range(16)])
+    cp(full("ypf"), S("pf0", 0, 256))
+    dma("Y", "l_yp", [(lambda T: T.yp[:], lambda T: T.ypf[:])], [full("ypf")], [], 2.0)
+
+    hist = {}
+    for i, o in enumerate(ops):
+        dep = set()
+        for (n, a, b) in o["R"]:
+            ps = BUF[n][0] == "psum"
+            for (j, a2, b2, w) in hist.get(n, ()):
+                if (w and a < b2 and a2 < b) or (ps and ops[j]["q"] != o["q"]):
+                    dep.add(j)
+        for (n, a, b) in o["W"]:
+            ps = BUF[n][0] == "psum"
+            for (j, a2, b2, w) in hist.get(n, ()):
+                if (a < b2 and a2 < b) or (ps and ops[j]["q"] != o["q"]):
+                    dep.add(j)
+        for (n, a, b) in o["R"]:
+            hist.setdefault(n, []).append((i, a, b, False))
+        for (n, a, b) in o["W"]:
+            l = hist.setdefault(n, [])
+            l[:] = [e for e in l if not (a <= e[1] and e[2] <= b) or BUF[n][0] == "psum"]
+            l.append((i, a, b, True))
+        if o["q"] == "N":
+            dep = {o["send"]}
+        dep.discard(i)
+        o["D"] = dep
+    return ops
+
+
+def schedule(ops, seed=0, eps=0.0):
+    n = len(ops)
+    succ = [[] for _ in range(n)]
+    for i, o in enumerate(ops):
+        for j in o["D"]:
+            succ[j].append(i)
+    prio = [0.0] * n
+    rnd = np.random.default_rng(seed).random(n)
+    for i in range(n - 1, -1, -1):
+        prio[i] = ops[i]["c"] + max([prio[j] + LAT for j in succ[i]], default=0.0)
+    key = [(-(prio[i] + BONUS.get(ops[i]["at"], 0.0) + LEAD.get(ops[i]["part"], 0.0) + eps * float(rnd[i])), i) for i in range(n)]
+    left = [len(o["D"]) for o in ops]
+    heap = sorted(key[i] for i in range(n) if left[i] == 0)
+    busy = {}
+    est, fin = [0.0] * n, [0.0] * n
+    order = []
+    while heap:
+        i = heap.pop(0)[1]
+        o = ops[i]
+        t = est[i]
+        if o["q"] != "N":
+            occ = 0.15 if o["sem"] and o["q"] in "YS" else o["c"]
+            b = busy.setdefault(o["q"], [])
+            at = len(b)
+            while at > 0 and b[at - 1][1] > t:
+                at -= 1
+            while at < len(b) and max(t, b[at - 1][1] if at else 0.0) + occ > b[at][0]:
+                at += 1
+            t = max(t, b[at - 1][1] if at else 0.0)
+            b.insert(at, (t, t + occ))
+        o["start"] = t
+        fin[i] = t + o["c"]
+        order.append((t, len(order), i))
+        for j in succ[i]:
+            est[j] = max(est[j], fin[i] + LAT)
+            left[j] -= 1
+            if left[j] == 0:
+                lo, hi = 0, len(heap)
+                while lo < hi:
+                    mid = (lo + hi) // 2
+                    if heap[mid] < key[j]:
+                        lo = mid + 1
+                    else:
+                        hi = mid
+                heap.insert(lo, key[j])
+    order.sort()
+    return [i for _, _, i in order], max(fin)
+
+
+SEMQ = {"V": "vv", "S": "ss", "P": "pp", "G": "gg"}
+
+
+def plan(nE):
+    if nE in _CACHE:
+        return _CACHE[nE]
+    ops = build(nE)
+    order, total = schedule(ops, SEED, EPS)
+    count = {s: 0 for s in SEMQ.values()}
+    know, kq, out = {}, {}, []
+    for i in order:
+        o = ops[i]
+        q = o["q"]
+        mine = kq.setdefault(q, {})
+        waits = {}
+        if q != "N":
+            for j in sorted(o["D"], key=lambda j: -ops[j]["start"]):
+                s, v = ops[j]["ev"]
+                if mine.get(s, 0) >= v:
+                    continue
+                waits[s] = max(waits.get(s, 0), v)
+                for s2, v2 in know[j].items():
+                    mine[s2] = max(mine.get(s2, 0), v2)
+                mine[s] = max(mine.get(s, 0), v)
+        know[i] = dict(mine) if q != "N" else {}
+        if o["sem"]:
+            o["ev"] = (o["sem"], o["val"])
+        else:
+            s = SEMQ[q]
+            count[s] += len(o["f"])
+            o["ev"] = (s, count[s])
+        out.append((o, sorted(waits.items())))
+    ends = {}
+    for o in ops:
+        s, v = o["ev"]
+        ends[s] = max(ends.get(s, 0), v)
+    _CACHE[nE] = (out, ends, total)
+    return _CACHE[nE]
+
+
+def rank_program(g, core, T, topo):
+    rank = T.rank_of(core)
+    if rank is None:
+        return
+    nxt = T.cores[(rank + 1) % len(T.cores)]
+    eng = topo.engines(core, nxt)[::2]
+    mask = 0
+    for e in eng:
+        mask |= 1 << e
+    rid, pid, _ = topo.addr(nxt)
+    steps, ends, _ = plan(len(eng))
+    queue = {"V": g.vector, "S": g.scalar, "P": g.tensor, "G": g, "Y": g.sync}
+    for o, waits in steps:
+        q = o["q"]
+        if q == "N":
+            continue
+        for s, v in waits:
+            queue[q].wait_ge(T.sem[s], v)
+        if o["send"]:
+            k, t, h = o["send"]
+            c = slice(128 * h, 128 * h + 128)
+            g.remote_dma(out_ap=T["%sb%d" % (k, t)][:, c], in_ap=T["%sn%d" % (k, t - 1)][:, c], remote_sem=T.sem["a%s%d%d" % (k, t, h)],
+                         local_sem=T.sem["o%s%d%d" % (k, t, h)], pid=pid, routing_id=rid, dma_engine_mask=mask)
+        elif o["sem"]:
+            for f in o["f"]:
+                f(g, T).then_inc(T.sem[o["sem"]], 16)
+        else:
+            for f in o["f"]:
+                f(g, T).then_inc(T.sem[SEMQ[q]], 1)
+    for s, v in sorted(ends.items()):
+        g.wait_ge(T.sem[s], v)

@@ -1,104 +1,110 @@
+import math
 import numpy as np
 from concourse.mybir import AluOpType, AxisListType, ActivationFunctionType
 
 A = AluOpType
 AF = ActivationFunctionType
 VIS = 5
-BLOCKS = [(0, 64), (64, 128), (128, 192), (192, 256)]
 BUF = {}
 SEMAPHORES = ["vv", "ss", "pp", "gg"]
+ZB = [(192, 256, "pz0", 0), (128, 192, "pz1", 0), (64, 128, "pz0", 128), (0, 64, "pz1", 128)]
+TB = [(128, 256, "pz0", 256), (0, 128, "pz1", 256)]
 
 
 def _b(name, shape, dtype="float32", where="sbuf"):
     BUF[name] = (where, shape, dtype)
 
 
-BF, F32, I32, U16 = "bfloat16", "float32", "int32", "uint16"
-_b("claimw", [128, 4096], BF)
-_b("parw", [128, 4368], BF)
+BF, F16, F32, I32, U16 = "bfloat16", "float16", "float32", "int32", "uint16"
+CW = 8512
+PW = 4128
+_b("claimw", [128, CW], BF)
+_b("parw", [128, PW], BF)
+_b("yb0", [128, 256], BF)
 for _t in range(VIS):
-    _b("yb%d" % _t, [128, 256], BF)
-    _b("vb%d" % _t, [128, 256], F32)
-    _b("yn%d" % _t, [128, 256], BF)
-    _b("vn%d" % _t, [128, 256], F32)
-    _b("thc%d" % _t, [128, 8], F32)
-for _n in ("x0", "x1", "xs", "pr", "d", "ad", "af", "ae", "mx", "mn"):
+    if _t:
+        _b("yb%d" % _t, [128, 256], F16)
+    for _n in ("vb", "yn", "vn"):
+        _b("%s%d" % (_n, _t), [128, 256], F16)
+    _b("thc%d" % _t, [128, 1], F32)
+for _n in ("x0", "x1", "pr", "d", "ad", "la", "af", "ae"):
     _b(_n, [128, 4096], BF)
-for _n in ("um0", "um1", "hi0", "hi1", "t1", "t2", "t3", "msum", "mhalf", "yhalf", "aint"):
+for _n in ("mx", "mn"):
+    _b(_n, [128, 4096], F16)
+for _n in ("um0", "um1", "t1", "t2", "t3", "t4", "t5"):
     _b(_n, [128, 256], I32)
-for _n in ("hl", "zl", "vl", "h2l"):
+for _n in ("hl", "zl", "vl"):
     _b(_n, [128, 256], U16)
-for _n in ("q1", "q2", "dif", "vm", "fh", "dlt", "h2f", "sa", "sb", "cr", "dg", "cs", "tt_"):
+for _n in ("c1", "c2", "vm", "yvf", "prd", "ypf"):
     _b(_n, [128, 256], F32)
-for _n in ("dep", "mm_", "yy", "ohb", "adat", "oc"):
+for _n in ("dep", "sg", "yy", "yeb", "tcon", "adat"):
     _b(_n, [128, 256], BF)
-_b("tr", [128, 512], F32)
-_b("kint", [128, 64], I32)
+for _n in ("mm_", "par16", "vh"):
+    _b(_n, [128, 256], F16)
+for _j in range(4):
+    _b("km%d" % _j, [128, 128], F32)
+    _b("pm%d" % _j, [128, 512], F32)
+    _b("tt%d" % _j, [128, 256], F32)
+    _b("rr%d" % _j, [128, 48], F32)
+    _b("cc%d" % _j, [128, 48], BF)
+_b("own", [128, 16], F16)
+_b("ini", [128, 16], BF)
+_b("kt8", [8, 256], BF)
+_b("kt32", [32, 256], BF)
 _b("yl", [128, 16], U16)
-_b("pm", [128, 512], F32)
-_b("code", [128, 64], I32)
-_b("ask", [128, 32], F32)
-_b("kk", [128, 32], BF)
-_b("ktb", [16, 256], BF)
-_b("bia", [128, 16], F32)
-_b("sint", [128, 32], I32)
-_b("dd", [128, 3072], BF)
-_b("dso", [128, 3072], BF)
-_b("rs0", [128, 512], BF)
-_b("rs1", [128, 1024], BF)
-_b("px32", [128, 2048], BF)
-_b("cb", [128, 64], BF)
-for _t in range(VIS):
-    _b("ct%d" % _t, [128, 64], BF)
-_b("dfl", [128, 64], F32)
-_b("ol", [128, 16], U16)
-_b("dsum", [128, 2], F32)
+_b("ol", [128, 32], U16)
+_b("fl", [128, 32], F32)
+_b("cs", [128, 1], BF)
 _b("cint", [128, 2], I32)
-for _n in ("ones", "eye", "neye", "blk", "blk1", "blk8k", "tri", "trim", "dm32", "wmat", "j1", "j2", "kt", "r2"):
+for _n in ("ones", "eye", "neye", "blk", "blk1", "dm32", "p0", "n0", "c2048", "cm256", "ktile", "ptile", "wmat",
+           "s64k", "neye7", "rm", "m2k", "m64", "dcon", "ncon", "e15"):
     _b(_n, [128, 128], BF)
-for _n in ("sx", "px", "r1", "rm"):
+for _n in ("zx", "zx2", "zxn"):
+    _b(_n, [128, 144], BF)
+_b("z8", [8, 144], BF)
+_b("zb", [32, 144], BF)
+for _n in ("ea", "eb", "eb7", "neb7"):
+    _b(_n, [32, 128], BF)
+_b("ex", [32, 512], BF)
+_b("kcon", [8, 256], BF)
+_b("kval", [128, 16], BF)
+_b("b64", [128, 8], BF)
+_b("b4k", [128, 16], BF)
+for _n in ("r2", "rmn"):
+    _b(_n, [128, 256], BF)
+for _n in ("sr", "lf"):
     _b(_n, [128, 2048], BF)
-for _n in ("blkf", "blk512", "onesf", "dmask"):
-    _b(_n, [128, 128], F32)
-_b("exs", [16, 512], BF)
-_b("exf", [16, 128], F32)
-_b("eyef", [16, 16], F32)
+_b("exf", [8, 128], F32)
 _b("io1", [128, 128], I32)
-_b("io2", [128, 128], I32)
-_b("pcol", [128, 4], I32)
+_b("io2", [128, 256], I32)
+_b("e16", [128, 16], F32)
+_b("coll", [128, 16], F32)
 _b("cols", [128, 16], F32)
 _b("wti", [128, 1], I32)
 _b("wtf", [128, 1], F32)
 _b("limi", [8, 2], I32)
 _b("limf", [8, 2], F32)
-_b("limd", [8, 8], F32)
-_b("tht", [128, 16], F32)
 _b("thb", [128, 2], F32)
-_b("dcon", [128, 16], F32)
-_b("iod", [128, 16], I32)
+_b("thi", [128, 4], I32)
 _b("whoi", [128, 256], I32)
 _b("pari", [128, 256], I32)
-_b("parlh", [128, 512], I32)
-_b("parb", [128, 512], BF)
-_b("ypf", [128, 256], F32)
-_b("dlo", [8, 4096], BF, "dram")
-_b("dhi", [8, 4096], BF, "dram")
-for _n in ("pz0", "pz1", "pz2", "pz3", "pk0", "pk1", "pf0", "pf1"):
+BIGB = ("pa0", "pa1", "pa2", "pa3")
+for _n in BIGB + ("pz0", "pz1", "pt0", "pt1"):
     _b(_n, [128, 512], F32, "psum")
 
-for _n in ("who", "est", "wt", "lim", "par", "claim0", "claim1", "plo", "phi", "pwin", "yv0", "yv1", "ye0", "ye1", "yp"):
+for _n in ("lim", "who", "est", "wt", "par", "claim0", "claim1", "again", "yv", "ye0", "ye1", "ye2", "yp"):
     SEMAPHORES.append("l_" + _n)
 for _t in range(1, VIS):
-    for _h in range(2):
+    for _h in range(len(TB)):
         for _k in "yv":
             SEMAPHORES += ["a%s%d%d" % (_k, _t, _h), "o%s%d%d" % (_k, _t, _h)]
 
 PACK = {}
 SCRATCH = {}
 _ROOM = {}
-_KEEP = ("claimw", "parw", "whoi", "pari", "parb", "ypf", "wti", "limi", "hl", "zl", "vl", "h2l", "yl", "ol", "dd", "adat")
+_KEEP = ("whoi", "pari", "ypf", "yvf", "yeb", "wti", "limi", "hl", "zl", "vl", "yl", "ol", "adat", "yy")
 for _n, (_w, _sh, _d) in BUF.items():
-    if _w == "sbuf" and _n not in _KEEP and _n[:2] not in ("yb", "vb", "yn", "vn") and _sh[0] == 128 and _sh[1] <= 512:
+    if _w == "sbuf" and _n not in _KEEP and _n[:2] not in ("yb", "vb", "yn", "vn") and _sh[1] <= 512:
         PACK[_n] = ("pack_" + _d, _ROOM.get(_d, 0))
         _ROOM[_d] = _ROOM.get(_d, 0) + (_sh[1] + 15) // 16 * 16
     else:
@@ -109,12 +115,18 @@ for _d in _ROOM:
 _CACHE = {}
 CY, PCY, GATH, SCAT = 0.00083 * 1.1, 0.00042 * 1.1, 1.5, 3.5
 VOV, SOV, POV, LAT = 0.04, 0.04, 0.02, 0.12
-SEED, EPS = 0, 0.0
-ONV = ()
-LEAD = {"x0": 2.7, "t1": 1.3, "t0": -0.4, "x1": 0.0, "n1": 1.3, "z0": -0.2, "m1": -0.6, "p0": 2.9, "w1": -1.1, "p1": -0.1, "w0": -3.1, "e1": -0.6, "n0": 0.6, "m0": 1.2, "z1": 0.4, "e0": -0.3}
-BONUS = {}
-ERRB = (("pf0", "pf1"), ("pf0", "pf1"))
-XL = 64
+OPT = {
+    "onv": ("y0", "y1", "p4", "p5"),
+    "relu": (),
+    "gl": 32,
+    "tries": 2500, "period": 34.0, "seed": 0, "heat": 0.4,
+}
+LEAD = {"n0": -15, "n1": -15, "x0": -12, "x1": 2, "p0": 0, "p1": 0, "p2": 1.5, "p3": 3, "z0": 1.6, "z1": 2.1, "z2": 3.1, "z3": 4.6,
+        "g0": 3.4, "g1": 5, "g2": 7, "g3": 8.5, "d0": 4.9, "d1": 6.5, "d2": 8.5, "d3": 10, "m0": 7, "m1": 8.5, "m2": 10.5, "m3": 12,
+        "s0": 10, "s1": 11, "s2": 13, "s3": 14, "v0": 16, "v1": 17, "c0": 20, "f0": 12, "t0": 14, "e0": 18, "a0": 21, "w0": 26,
+        "f1": 15, "t1": 17.5, "e1": 21, "a1": 23, "w1": 29, "b0": -5, "o0": 33}
+REAL = {}
+R64, R256 = 1.5 * 2 ** 29, 1.5 * 2 ** 31
 
 
 def S(name, a, b, step=1, p=128):
@@ -126,15 +138,12 @@ def IND(name, a, b, off, c, d):
 
 
 def ap(T, s):
-    if s[0] in PACK:
-        r, o = PACK[s[0]]
-        return T[r][0:s[4], o + s[1]:o + s[2]] if s[3] == 1 else T[r][0:s[4], o + s[1]:o + s[2]:s[3]]
     if len(s) == 7:
         return T[s[0]][:, s[1]:s[2]].indirect(T[s[3]][:, s[4]:s[5]])
-    t = T[s[0]]
+    r, o = PACK.get(s[0], (REAL.get(s[0], s[0]), 0))
     if s[3] == 1:
-        return t[0:s[4], s[1]:s[2]]
-    return t[0:s[4], s[1]:s[2]:s[3]]
+        return T[r][0:s[4], o + s[1]:o + s[2]]
+    return T[r][0:s[4], o + s[1]:o + s[2]:s[3]]
 
 
 def regs(s):
@@ -150,19 +159,19 @@ def width(s):
 
 
 def half(*ss):
-    return all(BUF[s[0]][2] in (BF, U16) for s in ss)
+    return all(BUF[s[0]][2] in (BF, F16, U16) for s in ss)
 
 
 def build(nE):
     ops = []
-    since = [100000]
-    part = [""]
+    GL = OPT["gl"]
+    part = ["", 0]
 
     def add(q, fns, R, W, cost, sem=None, val=0, send=None):
         rr = [r for s in R for r in regs(s)]
         ww = [(s[0], s[1], s[2]) for s in W]
         offs = [(s[3], s[4], s[5]) for s in W if len(s) == 7]
-        ops.append({"q": q, "f": fns, "R": rr + offs, "W": ww, "c": cost, "sem": sem, "val": val, "send": send, "at": len(ops) - since[0], "part": part[0]})
+        ops.append({"q": q, "f": fns, "R": rr + offs, "W": ww, "c": cost, "sem": sem, "val": val, "send": send, "part": part[0], "t": part[1]})
         return len(ops) - 1
 
     def vcost(n, f=1.0):
@@ -192,33 +201,28 @@ def build(nE):
         add("V", [f], R, [out], vcost(width(a), 0.5 if half(out, a) else 1.0))
 
     def scan(out, d0, d1, init, op0, op1):
-        add("V", [lambda g, T: g.vector.tensor_tensor_scan(out=ap(T, out), data0=ap(T, d0), data1=ap(T, d1), initial=init, op0=op0, op1=op1)],
-            [d0, d1], [out], vcost(width(d1), 0.5 if half(out, d0, d1) else 1.0))
-
-    def red(out, a, op, absv=False):
-        if absv:
-            fn = lambda g, T: g.vector.tensor_reduce(out=ap(T, out), in_=ap(T, a), axis=AxisListType.X, op=op, apply_absolute_value=True)
-        else:
-            fn = lambda g, T: g.vector.tensor_reduce(out=ap(T, out), in_=ap(T, a), axis=AxisListType.X, op=op)
-        add("V", [fn], [a], [out], vcost(width(a)))
+        R = [d0, d1] + ([init] if isinstance(init, tuple) else [])
+        add("V", [lambda g, T: g.vector.tensor_tensor_scan(out=ap(T, out), data0=ap(T, d0), data1=ap(T, d1),
+                                                           initial=ap(T, init) if isinstance(init, tuple) else init, op0=op0, op1=op1)],
+            R, [out], vcost(width(d1), 0.5 if half(out, d0, d1) else 1.0))
 
     def fill(out, c):
-        add("V", [lambda g, T: g.vector.memset(ap(T, out), c)], [], [out], vcost(width(out)))
+        add("V", [lambda g, T: g.vector.memset(ap(T, out), c)], [], [out], vcost(width(out), 0.5 if half(out) else 1.0))
 
     def act(out, a, func, bias=None, scale=None):
-        R = [a] + ([bias] if isinstance(bias, tuple) else [])
+        R = [a] + [s for s in (bias, scale) if isinstance(s, tuple)]
 
         def f(g, T):
             kw = {}
             if bias is not None:
                 kw["bias"] = ap(T, bias) if isinstance(bias, tuple) else bias
             if scale is not None:
-                kw["scale"] = scale
+                kw["scale"] = ap(T, scale) if isinstance(scale, tuple) else scale
             return g.scalar.activation(out=ap(T, out), in_=ap(T, a), func=func, **kw)
         add("S", [f], R, [out], max(64, width(a) * (GATH if len(a) == 7 else 1.0)) * CY + SOV)
 
-    def gather(tag, out, a):
-        if tag in ONV:
+    def move(tag, out, a):
+        if tag in OPT["onv"]:
             cp(out, a)
         else:
             act(out, a, AF.Copy)
@@ -228,11 +232,14 @@ def build(nE):
         c = POV
         for (o, l, r, st, sp) in groups:
             fns.append(lambda g, T, o=o, l=l, r=r, st=st, sp=sp: g.tensor.matmul(out=ap(T, o), lhsT=ap(T, l), rhs=ap(T, r), start=st, stop=sp))
-            c += max(64, width(r)) * PCY * (4 if BUF[r[0]][2] == F32 else 1)
+            c += max(min(64, width(l)), width(r)) * PCY * (4 if BUF[r[0]][2] == F32 else 1)
         add("P", fns, [r for (o, l, r2, st, sp) in groups for r in (l, r2)], [x[0] for x in groups], c)
 
-    def one(out, l, r):
-        mm([(out, l, r, True, True)])
+    def acc(out, terms):
+        mm([(out, l, r, i == 0, i == len(terms) - 1) for i, (l, r) in enumerate(terms)])
+
+    def pile(terms):
+        mm([(o, l, r, i == 0, i == len(terms) - 1) for i, (o, l, r) in enumerate(terms)])
 
     def dma(q, sem, pairs, R, W, cost):
         add(q, [lambda g, T, o=o, i=i: (g.sync if q == "Y" else g.scalar).dma_start(o(T), i(T)) for (o, i) in pairs], R, W, cost, sem=sem, val=16 * len(pairs))
@@ -248,412 +255,555 @@ def build(nE):
         sh = BUF[name][1]
         return S(name, 0, sh[1], 1, sh[0])
 
-    dma("Y", "l_who", [(lambda T: T.whoi[:], lambda T: T.who[:])], [], [full("whoi")], 2.0)
-    dma("Y", "l_est", [(lambda T: T.yb0[:], lambda T: T.est[:])], [], [full("yb0")], 2.0)
-    dma("Y", "l_wt", [(lambda T: T.wti[:], lambda T: T.wt[:])], [], [full("wti")], 2.0)
-    dma("S", "l_claim0", [(lambda T: T.claimw[:, 0:2048], lambda T: T.claim[:, 0:2048])], [], [S("claimw", 0, 2048)], 3.0)
-    dma("S", "l_claim1", [(lambda T: T.claimw[:, 2048:4096], lambda T: T.claim[:, 2048:4096])], [], [S("claimw", 2048, 4096)], 4.0)
-    dma("Y", "l_par", [(lambda T: T.pari[:], lambda T: T.par[:])], [], [full("pari")], 2.0)
-    dma("Y", "l_lim", [(lambda T: T.limi[:], lambda T: T.lim[:])], [], [full("limi")], 2.0)
-    fill(full("ones"), 1.0)
-    asel(full("blk1"), full("ones"), [[-16, 8], [0, 16]], A.is_ge, 0, 1)
-    asel(full("blk"), full("blk1"), [[16, 8], [0, 16]], A.is_ge, 15, -1)
-    asel(full("eye"), full("ones"), [[-1, 128]], A.is_equal, 0, 1)
-    iota(S("pcol", 0, 1), [[0, 1]], 0, 1)
-    cp(full("vb0"), full("whoi"))
-    cp(full("vl"), full("vb0"))
-    ts(S("parlh", 0, 256), full("pari"), 255, A.bitwise_and)
-    ts(S("parlh", 256, 512), full("pari"), 8, A.logical_shift_right)
-    cp(full("parb"), full("parlh"))
-    dma("Y", "l_plo", [(lambda T: T.dlo[:], lambda T: T.parb[:, 0:256])], [S("parb", 0, 256)], [S("dlo", 0, 4096, 1, 8)], 2.0)
-    dma("Y", "l_phi", [(lambda T: T.dhi[:], lambda T: T.parb[:, 256:512])], [S("parb", 256, 512)], [S("dhi", 0, 4096, 1, 8)], 2.0)
-    dma("Y", "l_pwin", [(lambda T, i=i: T.parw[i::16, 16:4112], lambda T, i=i: (T.dhi if i % 2 else T.dlo)[:]) for i in range(16)],
-        [S("dlo", 0, 4096, 1, 8), S("dhi", 0, 4096, 1, 8)], [S("parw", 16, 4112)], 8.0)
-    cp(full("wtf"), full("wti"))
-    ts(full("wmat"), full("blk"), S("wtf", 0, 1), A.mult)
-    ts(S("pcol", 1, 2), S("pcol", 0, 1), 15, A.bitwise_and)
-    ts(S("pcol", 2, 3), S("pcol", 0, 1), 1, A.bitwise_and)
-    K16 = S("cols", 0, 1)
-    CODE = S("cols", 1, 2)
-    COLW = S("cols", 2, 3)
-    COLA = S("cols", 3, 4)
-    ACS = S("cols", 7, 8)
-    ACB = S("cols", 8, 9)
-    cp(K16, S("pcol", 1, 2))
-    ts(CODE, K16, -1.0, A.mult, 16.0, A.add)
-    ts(S("cols", 4, 5), K16, 1.0, A.is_equal, 256.0, A.mult)
-    ts(S("cols", 5, 6), K16, 0.0, A.is_equal)
-    tt(COLW, S("cols", 4, 5), S("cols", 5, 6), A.add)
-    ts(COLA, K16, 16.0, A.mult)
-    cp(S("cols", 6, 7), S("pcol", 2, 3))
-    ts(ACS, S("cols", 6, 7), -255.0 / 256.0, A.mult, 1.0, A.add)
-    ts(ACB, S("cols", 6, 7), -0.498, A.mult)
-    fill(full("sx"), 0.0)
-    for k in range(16):
-        cp(S("sx", 129 * k, 128 * k + 128, 16), S("blk", 0, 128, 16))
-    ts(full("px"), full("sx"), COLW, A.mult)
-    ts(full("neye"), full("eye"), -1.0, A.mult)
-    asel(full("tri"), full("blk"), [[1, 128]], A.is_gt, 0, -1)
-    ts(full("trim"), full("eye"), -32.0, A.mult)
-    tt(full("trim"), full("trim"), full("tri"), A.add)
-    ts(full("dm32"), full("eye"), 32.0, A.mult)
-    tt(full("dm32"), full("dm32"), full("blk"), A.subtract)
-    asel(S("exs", 0, 128, 1, 16), S("ones", 0, 128, 1, 16), [[1, 128]], A.is_ge, 0, -16)
-    asel(S("exs", 128, 256, 1, 16), S("exs", 0, 128, 1, 16), [[-1, 128]], A.is_ge, 15, 16)
-    asel(S("exs", 256, 384, 1, 16), S("ones", 0, 128, 1, 16), [[1, 128]], A.is_ge, 128, -16)
-    asel(S("exs", 384, 512, 1, 16), S("exs", 256, 384, 1, 16), [[-1, 128]], A.is_ge, -113, 16)
-    cp(full("exf"), S("exs", 128, 256, 1, 16))
-    cp(full("limf"), full("limi"))
-    cp(full("onesf"), full("ones"))
-    cp(full("eyef"), S("eye", 0, 16, 1, 16))
-    ts(full("limd"), S("eyef", 0, 8, 1, 8), S("limf", 1, 2, 1, 8), A.mult, 32.0, A.mult)
-    mm([(S("pk1", 0, 2), S("exf", 0, 128, 1, 8), full("limf"), True, True),
-        (S("pk1", 8, 16), S("onesf", 0, 128, 1, 8), full("limd"), True, True)])
-    cp(full("thb"), S("pk1", 0, 2))
-    cp(S("thc0", 0, 1), S("pk1", 0, 1))
-    fill(S("tht", 0, 8), -1.0)
-    cp(S("tht", 8, 16), S("pk1", 8, 16))
-    cp(full("blkf"), full("blk"))
-    fill(full("r1"), 1.0)
-    ts(S("r1", 0, 2048, 16), S("r1", 0, 2048, 16), 0.0, A.mult)
-    fill(full("rm"), 0.0)
-    ts(S("rm", 0, 2048, 16), S("rm", 0, 2048, 16), 256.0, A.add)
-    QB = (BLOCKS[0][1] - BLOCKS[0][0]) // 16
-    iota(S("io1", 0, 16 * QB), [[0, 16], [256, QB]], 0, 0)
-    ts(S("j1", 0, 16 * QB), S("io1", 0, 16 * QB), COLA, A.add)
-    iota(S("j2", 0, 16 * QB), [[1, 16], [0, QB]], 0, 0)
-    iota(full("kt"), [[0, 8], [-1, 16]], 16, 0)
-    iota(full("oc"), [[1, 256]], 0, 0)
-    fill(full("r2"), 1.0)
-    ts(S("r2", 1, 128, 16), S("r2", 1, 128, 16), 0.0, A.mult)
-    iota(full("io2"), [[1, 128]], 128, -1)
-    ts(full("io2"), full("io2"), 15, A.bitwise_and)
-    ts(full("dmask"), full("io2"), 0.0, A.is_equal)
-    ts(full("blk512"), full("blk"), 512.0, A.mult)
-    ts(full("blk8k"), full("blk"), 8192.0, A.mult)
-    iota(full("iod"), [[16, 16]], 4112, 0)
-    ts(full("dcon"), full("iod"), K16, A.add)
-    ts(full("px32"), full("px"), 32.0, A.mult)
-    fill(full("cb"), -131072.0)
-    for t in range(VIS):
-        fill(full("ct%d" % t), float(2464 * t))
-    fill(full("dd"), 4194304.0)
-    for h in range(2):
-        n, w = 512 + 512 * h, 128 + 128 * h
-        fill(full("rs%d" % h), 0.0)
-        ts(S("rs%d" % h, 0, n, w), S("rs%d" % h, 0, n, w), 4194304.0, A.add)
+    EYE, NEYE, BLK = full("eye"), full("neye"), full("blk")
+
+    def sx(k, z="zx", p=128):
+        return S(z, 15 - k, 143 - k, 1, p)
+
     turn = [0]
 
-    def bank(names):
+    def bank():
         turn[0] += 1
-        return names[turn[0] % 2]
+        _b("bank%d" % turn[0], [128, 512], F32, "psum")
+        return "bank%d" % turn[0]
+
+    dma("Y", "l_est", [(lambda T: T.yb0[:], lambda T: T.est[:])], [], [full("yb0")], 2.0)
+    dma("Y", "l_wt", [(lambda T: T.wti[:], lambda T: T.wt[:])], [], [full("wti")], 2.0)
+    dma("Y", "l_who", [(lambda T: T.whoi[:], lambda T: T.who[:])], [], [full("whoi")], 2.0)
+    dma("S", "l_par", [(lambda T: T.pari[:], lambda T: T.par[:])], [], [full("pari")], 2.0)
+    dma("S", "l_claim0", [(lambda T: T.claimw[:, 0:2048], lambda T: T.claim[:, 0:2048])], [], [S("claimw", 0, 2048)], 3.0)
+    dma("S", "l_claim1", [(lambda T: T.claimw[:, 2048:4096], lambda T: T.claim[:, 2048:4096])], [], [S("claimw", 2048, 4096)], 4.0)
+    dma("Y", "l_lim", [(lambda T: T.limi[:], lambda T: T.lim[:])], [], [full("limi")], 2.0)
+    dma("Y", "l_again", [(lambda T: T.claimw[:, 4096:8192], lambda T: T.claim[:]), (lambda T: T.claimw[:, 8192:CW], lambda T: T.claim[:, 0:CW - 8192])],
+        [S("claimw", 0, 4096)], [S("claimw", 4096, CW)], 5.0)
+    fill(full("ones"), 1.0)
+    asel(full("blk1"), full("ones"), [[-16, 8], [0, 16]], A.is_ge, 0, 1)
+    asel(BLK, full("blk1"), [[16, 8], [0, 16]], A.is_ge, 15, -1)
+    asel(EYE, full("ones"), [[-1, 128]], A.is_equal, 0, 1)
+    iota(S("io1", 0, 16), [[-1, 16]], 16, 1)
+    ts(S("io1", 16, 32), S("io1", 0, 16), 15, A.bitwise_and)
+    ts(full("e16"), S("io1", 16, 32), 0.0, A.is_equal)
+    K16 = S("cols", 0, 1)
+    DCOL = S("cols", 2, 3)
+    UCOL = S("cols", 3, 4)
+    cp(K16, S("io1", 16, 17))
+    ts(full("vb0"), full("whoi"), -2048.0, A.add)
+    ts(full("par16"), full("pari"), -2048.0, A.add)
+    cp(full("wtf"), full("wti"))
+    ts(full("wmat"), BLK, full("wtf"), A.mult)
+    fill(full("c2048"), 2048.0)
+    for k in range(16):
+        act(S("sr", 128 * k, 128 * k + 128), BLK, AF.Identity, None, S("e16", k, k + 1))
+    iota(full("io2"), [[0, 16], [1, 16]], 0, 0)
+    ts(S("cols", 5, 6), K16, -256.0, A.mult, 2048.0, A.add)
+    ts(full("tcon"), full("io2"), 0.0, A.mult, S("cols", 5, 6), A.add)
+    part[0] = "b0"
+    for j in range(8):
+        b = bank()
+        mm([x for e in range(2) for x in ((S(b, 256 * e, 256 * e + 256), S("sr", 128 * (2 * j + e), 128 * (2 * j + e + 1)), full("par16"), True, False),
+                                           (S(b, 256 * e, 256 * e + 256), EYE, full("tcon"), False, True))])
+        ts(S("parw", 16 + 512 * j, 528 + 512 * j), S(b, 0, 512), 0.0, A.max, 256.0, A.min)
+    part[0] = ""
+    fill(full("zx"), 0.0)
+    cp(S("zx", 15, 143, 16), S("blk", 0, 128, 16))
+    ts(full("zx2"), full("zx"), 2.0, A.mult)
+    ts(full("zxn"), full("zx"), -1.0, A.mult)
+    ts(NEYE, EYE, -1.0, A.mult)
+    ts(full("m2k"), EYE, -2048.0, A.mult)
+    ts(full("dm32"), EYE, 32.0, A.mult)
+    tt(full("dm32"), full("dm32"), BLK, A.subtract)
+    asel(S("ex", 0, 128, 1, 32), S("ones", 0, 128, 1, 32), [[1, 128]], A.is_ge, 0, -16)
+    asel(S("ex", 128, 256, 1, 32), S("ex", 0, 128, 1, 32), [[-1, 128]], A.is_ge, 15, 16)
+    cp(full("exf"), S("ex", 128, 256, 1, 8))
+    cp(full("limf"), full("limi"))
+    mm([(S("pt0", 0, 2), full("exf"), full("limf"), True, True), (S("pt0", 2, 3), full("wmat"), S("c2048", 0, 1), True, True)])
+    cp(full("thb"), S("pt0", 0, 2))
+    cp(full("thc0"), S("pt0", 0, 1))
+    ts(UCOL, S("pt0", 2, 3), -0.5, A.mult)
+    tt(S("coll", 0, 15), S("e16", 1, 16), S("e16", 0, 15), A.subtract)
+    ts(S("coll", 15, 16), S("e16", 15, 16), -1.0, A.mult)
+    for k in range(16):
+        ts(S("lf", 128 * k, 128 * k + 128), BLK, S("coll", k, k + 1), A.mult, 256.0, A.mult)
+    ts(full("p0"), S("sr", 0, 128), 256.0, A.mult)
+    ts(full("n0"), S("sr", 0, 128), -256.0, A.mult)
+    fill(full("cm256"), -256.0)
+    ts(full("b64"), S("blk", 0, 128, 16), 64.0, A.mult)
+    ts(full("s64k"), EYE, 65536.0, A.mult)
+    cp(full("ktile"), S("io2", 0, 128))
+    ts(full("rm"), full("ktile"), 0.5, A.subtract, -1e9, A.mult)
+    ts(full("rmn"), full("io2"), 0.5, A.subtract, 1e9, A.mult)
+    ts(full("r2"), full("io2"), 1.0, A.not_equal)
+    fill(full("z8"), 0.0)
+    cp(S("z8", 15, 143, 16, 8), S("eye", 0, 8, 1, 8))
+    iota(S("io1", 32, 40), [[16, 8]], 0, 0)
+    ts(S("ptile", 0, 8), S("io1", 32, 40), K16, A.add, 16.0, A.mult)
+    for e in range(2):
+        ts(S("b4k", 8 * e, 8 * e + 8), S("blk", 0, 128, 16), 4096.0, A.mult)
+    ts(full("m64"), EYE, -64.0, A.mult)
+    ts(DCOL, K16, 4112.0, A.add)
+    cp(S("thi", 0, 1), S("thb", 1, 2))
+    ts(S("thi", 1, 2), S("thi", 0, 1), 4, A.arith_shift_right)
+    ts(S("thi", 2, 3), S("thi", 0, 1), 15, A.bitwise_and)
+    fill(full("kval"), 0.0)
+    ts(S("cols", 6, 7), K16, -256.0, A.mult, 3840.0, A.add)
+    for e in range(2):
+        ts(S("kval", 8 * e, 8 * e + 1), S("thi", 1, 2), -65536.0, A.mult)
+        ts(S("kval", 8 * e + 1, 8 * e + 2), S("thi", 2, 3), -4096.0, A.mult, S("cols", 6, 7), A.add)
+        fill(S("kval", 8 * e + 2, 8 * e + 3), 69632.0 if e else -1088.0)
+        fill(S("kval", 8 * e + 3, 8 * e + 4), 2048.0 if e else 1.0)
+    mm([(S("pt1", 128 * e, 128 * e + 128, 1, 8), S("kval", 8 * e, 8 * e + 8), EYE, True, True) for e in range(2)])
+    cp(full("kcon"), S("pt1", 0, 256, 1, 8))
+    for name, o in (("ea", 0), ("eb", 16)):
+        asel(S("ex", 0, 128, 1, 32), S("ones", 0, 128, 1, 32), [[1, 128]], A.is_ge, 16 * o, -16)
+        asel(S("ex", 256, 384, 1, 32), S("ex", 0, 128, 1, 32), [[-1, 128]], A.is_ge, 15 - 16 * o, 16)
+        asel(S("ex", 0, 128, 1, 32), S("ones", 0, 128, 1, 32), [[1, 128]], A.is_ge, 16 * (o + 8), -16)
+        asel(S("ex", 384, 512, 1, 32), S("ex", 0, 128, 1, 32), [[-1, 128]], A.is_ge, 15 - 16 * (o + 8), 16)
+        ts(S("ex", 256, 384, 1, 32), S("ex", 256, 384, 1, 32), 64.0, A.mult)
+        tt(full(name), S("ex", 256, 384, 1, 32), S("ex", 384, 512, 1, 32), A.add)
+    fill(full("zb"), 0.0)
+    cp(S("zb", 15, 143, 16, 32), S("eb", 0, 128, 16, 32))
+    ts(full("eb7"), full("eb"), 2.0 ** -7, A.mult)
+    ts(full("neb7"), full("eb"), -2.0 ** -7, A.mult)
+    ts(full("neye7"), EYE, -2.0 ** -7, A.mult)
+    ts(full("dcon"), full("ktile"), K16, A.is_ge, 128.0, A.mult)
+    ts(full("dcon"), full("dcon"), -16.5, A.add)
+    fill(S("dcon", 15, 128, 16), 0.0)
+    ts(full("ncon"), S("tcon", 0, 128), -2112.0, A.add)
+    ts(full("e15"), full("ktile"), 15.0, A.is_equal)
 
     def send(what, t, h):
-        c = (128 * h, 128 * h + 128)
+        c = TB[h][:2]
         key = "%s%d%d" % (what, t + 1, h)
         i = add("G", None, [S("%sn%d" % (what, t), *c)], [], 1.0, sem="o" + key, val=nE, send=(what, t + 1, h))
         add("N", None, [], [S("%sb%d" % (what, t + 1), *c)], 2.0, sem="a" + key, val=nE, send=i)
 
+    def place(t, s, um, a, b, c, out):
+        tt(a, s, um, A.mult)
+        ts(b, a, 5, A.arith_shift_right, 4095, A.bitwise_and)
+        if t == 0:
+            tt(a, s, b, A.add)
+            ts(b, a, 4095, A.bitwise_and)
+            cp(out, b)
+        else:
+            tt(c, s, b, A.add)
+            ts(out, c, 77.0 * t, A.add)
+
+    def window(t):
+        return 4096 if t == 0 else CW
+
     def st_names(t, h):
-        c = (128 * h, 128 * h + 128)
-        v = S("vb%d" % t, *c)
-        if t > 0:
-            cp(S("vl", *c), v)
-        act(S("q1", *c), v, AF.Identity, float(2464 * t - 131072), 32.0)
+        c = TB[h][:2]
+        ts(S("vl", *c), S("vb%d" % t, *c), 2048.0, A.add)
 
     def st_hash(t, h):
-        c = (128 * h, 128 * h + 128)
-        um, hi = S("um%d" % (t % 2), *c), S("hi%d" % (t % 2), *c)
-        U, W = S("pz%d" % (2 * h), 256, 384), S("pz%d" % (2 * h), 384, 512)
-        one(U, full("wmat"), S("yb%d" % t, *c))
-        cp(S("t1", *c), U)
+        c0, c1, b, o = TB[h]
+        c, L = (c0, c1), c1 - c0
+        um = S("um%d" % (t % 2), *c)
+        U, s = S(b, o, o + L), S(b, o + L, o + 2 * L)
+        mm([(s, EYE, S("vb%d" % t, *c), True, False), (s, EYE, S("c2048", 0, L), False, True), (U, full("wmat"), S("yb%d" % t, *c), True, True)])
+        if t == 0:
+            cp(S("t1", *c), U)
+        else:
+            ts(S("t1", *c), U, UCOL, A.add)
         ts(um, S("t1", *c), 4095, A.bitwise_and)
-        tt(W, S("vb%d" % t, *c), um, A.mult)
-        tt(S("t2", *c), W, S("q1", *c), A.add)
-        ts(hi, S("t2", *c), 5, A.arith_shift_right, 4095, A.bitwise_and)
-        cp(S("hl", *c), hi)
-
-    def st_xgather(t, h):
-        c = (128 * h, 128 * h + 128)
-        for a in range(c[0], c[1], XL):
-            gather("x%d" % (a // XL), S("x%d" % (t % 2), 16 * a, 16 * (a + XL)), IND("claimw", 0, 4096, "hl", a, a + XL))
+        place(t, s, um, S("t2", *c), S("t3", *c), S("c1", *c), S("hl", *c))
+        for a in range(c1 - GL, c0 - 1, -GL):
+            move("x%d" % (a // 32), S("x%d" % (t % 2), 16 * a, 16 * (a + GL)), IND("claimw", 0, window(t), "hl", a, a + GL))
 
     def st_pgather(t, n):
-        c = BLOCKS[n]
-        gather("p%d" % n, S("pr", 16 * c[0], 16 * c[1]), IND("parw", 16, 4112, "vl", *c))
+        for a in range(ZB[n][0], ZB[n][1], GL):
+            move("p%d" % (a // 32), S("pr", 16 * a, 16 * (a + GL)), IND("parw", 16, 4112, "vl", a, a + GL))
 
     def st_z(t, n):
-        c = BLOCKS[n]
-        L = c[1] - c[0]
-        X, X2 = 16 * c[0], 16 * c[1]
-        b = "pz%d" % n
-        p, w2, w3, q = [S(b, 64 * e, 64 * e + L) for e in range(4)]
-        w4 = q
-        um, hi, dep = S("um%d" % (t % 2), *c), S("hi%d" % (t % 2), *c), S("dep", *c)
-        mm([(p, S("px", 128 * k, 128 * k + 128), S("pr", X + k, X2, 16), k == 0, k == 15) for k in range(16)])
-        mm([(q, full("eye"), full("cb"), True, False), (q, full("eye"), full("ct%d" % t), False, False)] +
-           [(q, S("px32", 128 * k, 128 * k + 128), S("pr", X + k, X2, 16), False, k == 15) for k in range(16)])
-        tt(S("q2", *c), p, um, A.mult)
-        tt(S("t3", *c), q, S("q2", *c), A.add)
-        ts(S("t3", *c), S("t3", *c), 5, A.arith_shift_right, 4095, A.bitwise_and)
-        cp(S("zl", *c), S("t3", *c))
-        tt(S("dif", *c), p, S("vb%d" % t, *c), A.subtract)
-        tt(S("d", X, X2), IND("claimw", 0, 4096, "zl", *c), S("x%d" % (t % 2), X, X2), A.subtract)
-        act(S("ad", X, X2), S("d", X, X2), AF.Abs)
-        mm([(w2, S("sx", 128 * k, 128 * k + 128), S("ad", X + k, X2, 16), k == 0, k == 15) for k in range(16)])
-        ts(dep, w2, S("thc%d" % t, 0, 1), A.is_lt)
-        mm([(w2, full("trim"), dep, True, True), (w3, full("dm32"), dep, True, True)])
-        ts(w2, w2, K16, A.is_equal)
-        tt(S("fh", *c), w2, hi, A.mult)
-        ts(w3, w3, 17.0, A.is_ge)
-        one(w2, full("blkf"), S("fh", *c))
-        tt(S("dlt", *c), w2, hi, A.subtract)
-        tt(w4, w3, S("dlt", *c), A.mult)
-        tt(S("h2f", *c), w4, hi, A.add)
-        cp(S("h2l", *c), S("h2f", *c))
-        gather("s%d" % n, S("xs", X, X2), IND("claimw", 0, 4096, "h2l", *c))
+        c0, c1, b, o = ZB[n]
+        c, L, X, X2 = (c0, c1), c1 - c0, 16 * c0, 16 * c1
+        p, D = S(b, o, o + L), S(b, o + L, o + 2 * L)
+        v, dep = S("vb%d" % t, *c), S("dep", *c)
+        acc(p, [(sx(k), S("pr", X + k, X2, 16)) for k in range(16)])
+        place(t, p, S("um%d" % (t % 2), *c), S("t4", *c), S("t5", *c), S("c2", *c), S("zl", *c))
+        part[0] = "g%d" % n
+        for a in range(c0, c1, GL):
+            tt(S("d", 16 * a, 16 * (a + GL)), IND("claimw", 0, window(t), "zl", a, a + GL), S("x%d" % (t % 2), 16 * a, 16 * (a + GL)), A.subtract)
+        part[0] = "d%d" % n
+        if n in OPT["relu"]:
+            ts(S("ad", X, X2), S("d", X, X2), 0.0, A.max)
+            acc(D, [(sx(k, "zxn"), S("d", X + k, X2, 16)) for k in range(16)] + [(sx(k, "zx2"), S("ad", X + k, X2, 16)) for k in range(16)])
+        else:
+            act(S("ad", X, X2), S("d", X, X2), AF.Abs)
+            acc(D, [(sx(k), S("ad", X + k, X2, 16)) for k in range(16)])
+        ts(dep, D, full("thc%d" % t), A.is_lt)
+        acc(D, [(full("dm32"), dep)])
+        act(S("sg", *c), D, AF.Sign, -16.5)
+        part[0] = "v%d" % min(h for h in range(len(TB)) if TB[h][0] <= c0)
+        tt(p, p, v, A.subtract)
+        tt(S("vm", *c), p, dep, A.mult)
+        acc(p, [(EYE, v), (full("m2k"), dep)])
+        tt(S("vn%d" % t, *c), p, S("vm", *c), A.add)
 
     def st_m(t, n):
-        c = BLOCKS[n]
-        X, X2 = 16 * c[0], 16 * c[1]
-        xs = S("xs", X, X2)
-        scan(S("mx", X, X2), S("r1", 0, X2 - X), xs, 0.0, A.mult, A.max)
-        scan(S("mn", X, X2), S("rm", 0, X2 - X), xs, 256.0, A.max, A.min)
-        w = S("pz%d" % n, 64, 64 + c[1] - c[0])
-        mm([(w, full("eye"), S("mx", X + 15, X2, 16), True, False), (w, full("eye"), S("mn", X + 15, X2, 16), False, True)])
-        ts(S("mhalf", *c), w, 0.5, A.mult, -0.25, A.add)
-        cp(S("mm_", *c), S("mhalf", *c))
+        c0, c1, b, o = ZB[n]
+        c, L, X, X2 = (c0, c1), c1 - c0, 16 * c0, 16 * c1
+        x = "x%d" % (t % 2)
+        o += L
+        mm([(S(b, o, o + 1), full("p0"), S("sg", c0, c0 + 1), True, True), (S(b, o + 1, o + 2), full("n0"), S("sg", c0, c0 + 1), True, True)])
+        act(S("ini", 2 * n, 2 * n + 2), S(b, o, o + 2), AF.Copy)
+        for l in range(c0, c1, 32):
+            a, e = bank(), int(l + 32 == c1)
+            gr = [(S(a, k, 512, 16), S("lf", 128 * k, 128 * k + 128), S("sg", l, l + 32), True, True) for k in range(15)]
+            gr += [(S(a, 15, 512, 16), S("lf", 1920, 2048), S("sg", l, l + 32), True, False),
+                   (S(a, 15, 512 - 16 * e, 16), full("p0"), S("sg", l + 1, l + 33 - e), False, False),
+                   (S(a, 15, 512, 16), EYE, S("cm256", 0, 32), False, True)]
+            mm(gr)
+            act(S("la", 16 * l, 16 * l + 512), S(a, 0, 512), AF.Copy)
+        part[0] = "s%d" % n
+        scan(S("mx", X, X2), S(x, X, X2), S("la", X, X2), S("ini", 2 * n, 2 * n + 1), A.max, A.add)
+        scan(S("mn", X, X2), S(x, X, X2), S("la", X, X2), S("ini", 2 * n + 1, 2 * n + 2), A.min, A.subtract)
+        w = S(b, o, o + L)
+        acc(w, [(EYE, S("mx", X + 15, X2, 16)), (EYE, S("mn", X + 15, X2, 16))])
+        ts(S("mm_", *c), w, 0.5, A.mult, 1023.75, A.add)
 
-    def st_newnames(t, h):
-        c = (128 * h, 128 * h + 128)
-        tt(S("vm", *c), S("dif", *c), S("dep", *c), A.mult)
-        tt(S("vn%d" % t, *c), S("vm", *c), S("vb%d" % t, *c), A.add)
-        if t < VIS - 1:
-            send("v", t, h)
-            red(S("dsum", h, h + 1), S("dep", *c), A.add)
-
-    def st_count(t):
+    def st_count(t, h):
         if t == VIS - 1:
             return
-        mm([(S("pk0", 0, 1), full("onesf"), S("dsum", 0, 1), True, False), (S("pk0", 0, 1), full("onesf"), S("dsum", 1, 2), False, True)])
-        cp(S("cint", 0, 1), S("pk0", 0, 1))
+        b = "pt%d" % (len(TB) - 1)
+        acc(S(b, 500, 501), [(S("dep", 128, 256), S("ones", 0, 1)), (S("dep", 0, 128), S("ones", 0, 1))])
+        move("c", full("cs"), S(b, 500, 501))
+        acc(S(b, 501, 502), [(full("ones"), full("cs"))])
+        cp(S("cint", 0, 1), S(b, 501, 502))
         ts(S("cint", 1, 2), S("cint", 0, 1), 31, A.bitwise_and)
-        tt(S("thc%d" % (t + 1), 0, 1), S("cint", 1, 2), S("thb", 0, 1), A.add)
+        tt(full("thc%d" % (t + 1)), S("cint", 1, 2), S("thb", 0, 1), A.add)
 
-    def distances(src, X, mid, out, scale, banks):
-        L = width(mid)
+    def distances(t, h, mid, out, bias):
+        c0, c1 = TB[h][:2]
+        L, X = c1 - c0, 16 * c0
         K = 512 // L
-        for q in range(16 // K):
-            b = bank(banks)
+        for q in range(0, 16, K):
+            b = bank()
             gr = []
-            for e in range(K):
-                k = K * q + e
+            n = min(K, 16 - q)
+            for e in range(n):
                 o = S(b, L * e, L * e + L)
-                gr += [(o, full("eye"), S(src, X + k, X + 16 * L, 16), True, False), (o, full("neye"), mid, False, True)]
+                gr += [(o, EYE, S("x%d" % (t % 2), X + q + e, X + 16 * L, 16), True, False), (o, NEYE, mid, False, True)]
             mm(gr)
-            act(S(out, X + 512 * q, X + 512 * q + 512), S(b, 0, 512), AF.Abs, None, scale)
+            act(S(out, X + L * q, X + L * (q + n)), S(b, 0, L * n), AF.Abs, bias)
 
-    def st_truth(t, n):
-        c = BLOCKS[n]
-        L = c[1] - c[0]
-        X, X2, Q, h = 16 * c[0], 16 * c[1], L // 16, c[0] // 128
-        distances("xs", X, S("mm_", *c), "af", 4096.0, ("pf0", "pf1"))
-        bk, K = "pk%d" % h, c[0] % 128
-        key = S(bk, K, K + L)
-        mm([(key, full("eye"), S("j1", 0, L), True, False), (key, full("eye"), S("j2", 0, L), False, False)] +
-           [(key, S("sx", 128 * a, 128 * a + 128), S("af", X + a, X2, 16), False, a == 15) for a in range(16)])
-        B = 2 * c[0]
-        cp(S("tr", B, B + L // 2), S(bk, K + L // 2, K + L))
-        tt(S("tr", B + L // 2, B + L), S(bk, K, K + L // 2), S("tr", B, B + L // 2), A.min)
-        a, w = B + L // 2, L // 4
-        while w > Q:
-            tt(S("tr", a + 2 * w, a + 3 * w), S("tr", a, a + w), S("tr", a + w, a + 2 * w), A.min)
-            a, w = a + 2 * w, w // 2
-        I = c[0] // 4
-        tt(S("kint", I, I + Q), S("tr", a, a + w), S("tr", a + w, a + 2 * w), A.min)
-        ts(S("kint", I + Q, I + 2 * Q), S("kint", I, I + Q), 4095, A.bitwise_and)
-        cp(S("yl", c[0] // 16, c[1] // 16), S("kint", I + Q, I + 2 * Q))
-        cp(S("yy", *c), IND("xs", X, X2, "yl", c[0] // 16, c[1] // 16))
+    def sums(h, b, w, src, first, weight):
+        c0, c1 = TB[h][:2]
+        L, X = c1 - c0, 16 * c0
+        pile(first + [(S(b, k, w, 16, L), S(src, X + L * k, X + L * k + L), weight) for k in range(16)])
 
-    def st_est(t, h):
-        c = (128 * h, 128 * h + 128)
-        key = S("pk%d" % h, 384, 512)
-        mm([(key, full("eye"), S("yy", *c), True, False), (key, full("eye"), S("yb%d" % t, *c), False, True)])
-        ts(S("yhalf", *c), key, 0.5, A.mult, -0.25, A.add)
-        cp(S("yn%d" % t, *c), S("yhalf", *c))
+    def st_far(t, h):
+        distances(t, h, S("mm_", *TB[h][:2]), "af", 1024.0)
+
+    def st_truth(t, h):
+        c = TB[h][:2]
+        L, b = c[1] - c[0], "pt%d" % h
+        Q, q = L // 16, c[0] // 16
+        key = S(b, 0, 128, 1, L)
+        sums(h, b, 128, "af", [(key, S("eye", 0, L), full("ktile")), (key, S("sg", *c), full("s64k"))], full("b64"))
+        scan(S("km%d" % h, 0, 128, 1, L), S("rm", 0, 128, 1, L), key, 0.0, A.max, A.min)
+        m, r, k = S("km%d" % h, 15, 128, 16, L), S("rr%d" % h, 0, 8, 1, L), S("cc%d" % h, 0, 8, 1, L)
+        ts(r, m, R64, A.add, -R64, A.add)
+        tt(k, m, r, A.subtract)
+        acc(S(b, 128, 128 + L, 1, 8), [(k, S("eye", 0, L, 1, L))])
+        move("k%d" % h, S("kt8", c[0], c[1], 1, 8), S(b, 128, 128 + L, 1, 8))
+        acc(S(b, 256, 256 + Q), [(EYE, S("ptile", 0, Q))] + [(sx(a, "z8", 8), S("kt8", c[0] + a, c[1], 16, 8)) for a in range(16)])
+        cp(S("yl", q, q + Q), S(b, 256, 256 + Q))
+        move("y%d" % h, S("yy", *c), IND("x%d" % (t % 2), 16 * c[0], 16 * c[1], "yl", q, q + Q))
+        e = S(b, 384, 384 + L)
+        acc(e, [(EYE, S("yb%d" % t, *c)), (EYE, S("yy", *c))])
+        ts(S("yn%d" % t, *c), e, 0.5, A.mult, 511.75 if t else 1023.75, A.add)
         if t < VIS - 1:
             send("y", t, h)
 
     def st_err(t, h):
-        c = (128 * h, 128 * h + 128)
-        X = 2048 * h
-        distances("x%d" % (t % 2), X, S("yy", *c), "ae", 32.0, ERRB[h])
-        bk, ba, E = "pk%d" % h, "pz%d" % (2 * h + 1), 256
-        ek = S(bk, E, E + 128)
-        mm([(ek, full("eye"), full("kt"), True, False)] +
-           [(S(bk, E + k, E + 128, 16), S("ae", X + 128 * k, X + 128 * k + 128), S("blk", 0, 128, 16), False, k == 15) for k in range(16)])
-        B = 256 * h
-        scan(S("pm", B, B + 128), S("r1", 0, 128), ek, 0.0, A.mult, A.max)
-        tt(S("tt_", 128 * h + 1, 128 * h + 128), S(bk, E + 1, E + 128), S("pm", B, B + 127), A.min)
-        scan(S("pm", B + 129, B + 256), S("r2", 1, 128), S("tt_", 128 * h + 1, 128 * h + 128), 0.0, A.mult, A.max)
-        m = S("pm", B + 15, B + 256, 16)
-        cp(S("code", 32 * h, 32 * h + 16), m)
-        tt(S("ask", 16 * h, 16 * h + 16), m, full("tht"), A.is_ge)
-        ts(S("code", 32 * h + 16, 32 * h + 32), S("code", 32 * h, 32 * h + 16), 31, A.bitwise_and)
-        tt(S("kk", 16 * h, 16 * h + 16), S("code", 32 * h + 16, 32 * h + 32), S("ask", 16 * h, 16 * h + 16), A.mult)
-        one(S(ba, 0, 128, 1, 16), S("kk", 16 * h, 16 * h + 16), full("eye"))
-        kt = S("ktb", 128 * h, 128 * h + 128, 1, 16)
-        act(kt, S(ba, 0, 128, 1, 16), AF.Copy)
-        RA, RB, C, N = S(ba, 128, 256), S(ba, 256, 384), S(ba, 384, 512), S(ba, 0, 128)
-        mm([(RB, S("exs", 384, 512, 1, 16), kt, True, True), (RA, S("exs", 128, 256, 1, 16), kt, True, True)])
-        v = S("vb%d" % t, *c)
-        ts(S("ohb", *c), RB, CODE, A.is_equal)
-        tt(S("sb", *c), S("ohb", *c), v, A.mult)
-        mm([(C, full("blk512"), S("sb", *c), True, False), (C, full("blk8k"), S("ohb", *c), False, False), (C, full("eye"), S("oc", *c), False, True)])
-        act(S("cr", *c), C, AF.Copy)
-        tt(S("dg", *c), C, full("dmask"), A.mult)
-        scan(S("cs", *c), S("r1", 0, 128), S("dg", *c), 0.0, A.mult, A.add)
-        lst = S("cs", 128 * h + 15, 128 * h + 128, 16)
-        ts(S("bia", 8 * h, 8 * h + 8), lst, -1.0, A.mult, 128.0, A.add)
-        D0, DW = 1024 * h, 128 + 128 * h
-        for b in range(8 * h, 8 * h + 8):
-            w = 16 * b + 16
-            at = D0 + DW * (b - 8 * h)
-            act(S("dd", at, at + w), S("cr", 0, w), AF.Abs, S("bia", b, b + 1), 1.0)
-            if b % 4 == 3:
-                at += DW - 4 * DW
-                scan(S("dso", at, at + 4 * DW), full("rs%d" % h), S("dd", at, at + 4 * DW), 0.0, A.max, A.min)
-        ts(RA, RA, CODE, A.is_equal)
-        tt(S("sa", *c), RA, v, A.mult)
-        one(N, full("blkf"), S("sa", *c))
-        ts(S("aint", *c), N, ACS, A.mult, ACB, A.add)
-        ts(S("aint", *c), S("aint", *c), 255, A.bitwise_and)
-        cp(S("adat", *c), S("aint", *c))
-        cp(S("sint", 16 * h, 16 * h + 8), lst)
-        ts(S("sint", 16 * h + 8, 16 * h + 16), S("sint", 16 * h, 16 * h + 8), 9, A.logical_shift_right)
-        ts(S("dfl", 32 * h, 32 * h + 8), S("dso", D0 + DW - 1, D0 + 8 * DW, DW), 128.0, A.is_lt)
-        tt(S("dfl", 32 * h + 8, 32 * h + 16), S("dfl", 32 * h, 32 * h + 8), S("dcon", 8 * h, 8 * h + 8), A.mult)
-        tt(S("dfl", 32 * h + 16, 32 * h + 24), S("sint", 16 * h + 8, 16 * h + 16), S("dfl", 32 * h + 8, 32 * h + 16), A.max)
-        cp(S("ol", 8 * h, 8 * h + 8), S("dfl", 32 * h + 16, 32 * h + 24))
+        c = TB[h][:2]
+        ts(S("vh", *c), S("vb%d" % t, *c), 1.0 / 64, A.mult, 1119.5078125, A.add)
+        distances(t, h, S("yy", *c), "ae", None)
 
-    def st_scatter(t, h):
-        c = (128 * h, 128 * h + 128)
-        cp(IND("parw", 0, 4368, "ol", 8 * h, 8 * h + 8), S("adat", *c))
+    def st_ask(t, h):
+        c = TB[h][:2]
+        L, b = c[1] - c[0], "pt%d" % h
+        Q, q = L // 16, c[0] // 16
+        hi, lo = S(b, 0, 128, 1, L), S(b, 128, 256, 1, L)
+        sums(h, b, 256, "ae", [(S(b, 0, 256, 1, L), S("ones", 0, L, 1, 8), full("kcon")), (lo, S("vh", *c), full("m64")),
+                               (lo, S("vb%d" % t, *c), EYE), (hi, S("vh", *c), EYE)], full("b4k"))
+        pm, t2 = "pm%d" % h, S("tt%d" % h, 1, 256, 1, L)
+        scan(S(pm, 0, 256, 1, L), S("rmn", 0, 256, 1, L), S(b, 0, 256, 1, L), 0.0, A.min, A.max)
+        tt(t2, S(b, 1, 256, 1, L), S(pm, 0, 255, 1, L), A.min)
+        scan(S(pm, 257, 512, 1, L), S("r2", 1, 256, 1, L), t2, 0.0, A.mult, A.max)
+        m, r, k = S(pm, 15, 512, 16, L), S("rr%d" % h, 16, 48, 1, L), S("cc%d" % h, 16, 48, 1, L)
+        ts(r, m, R256, A.add, -R256, A.add)
+        tt(k, m, r, A.subtract)
+        acc(S(b, 256, 256 + L, 1, 32), [(k, S("eye", 0, L, 1, L))])
+        kt = S("kt32", c[0], c[1], 1, 32)
+        move("l%d" % h, kt, S(b, 256, 256 + L, 1, 32))
+        own, o16 = S(b, 0, Q), S("own", q, q + Q)
+        acc(own, [(sx(a, "zb", 32), S("kt32", c[0] + a, c[1], 16, 32)) for a in range(16)])
+        ts(o16, own, -2112.0, A.add)
+        N, D = S(b, 384, 384 + L), S(b, 128, 128 + L)
+        acc(N, [(EYE, S("ncon", 0, L)), (full("ea"), kt)])
+        pile([(D, EYE, S("dcon", 0, L)), (D, full("eb7"), kt), (S(b, 128 + 15, 128 + L, 16), full("neb7"), S("kt32", c[0] + 15, c[1], 16, 32))] +
+             [(S(b, 128 + a, 128 + L, 16), full("neye7"), o16) for a in range(15)])
+        ts(S("adat", *c), N, 0.0, A.max, 256.0, A.min)
+        scan(S("prd", *c), D, S("e15", 0, L), 1.0, A.mult, A.add)
+        f, f2 = S("fl", q, q + Q), S("fl", 16 + q, 16 + q + Q)
+        ts(f, S("prd", c[0] + 14, c[1], 16), 0.0, A.is_equal, 8192.0, A.mult)
+        tt(f2, f, o16, A.add)
+        ts(S("ol", 2 * q, 2 * (q + Q), 2), f2, 2064.0, A.add, DCOL, A.min)
+        part[0] = "w%d" % h
+        for a in range(q + Q - 1, q - 1, -1):
+            cp(IND("parw", 0, PW, "ol", 2 * a, 2 * a + 1), S("adat", 16 * a, 16 * a + 16))
 
-    nb = len(BLOCKS)
+    def st_send(t, h):
+        if t < VIS - 1:
+            send("v", t, h)
+
     for t in range(VIS):
-        since[0] = len(ops)
-        for h in range(2):
-            part[0] = "x%d" % h
-            st_names(t, h)
-        for h in range(2):
-            part[0] = "x%d" % h
-            st_hash(t, h)
-            st_xgather(t, h)
-        for n in range(nb):
-            part[0] = "p%d" % (2 * n // nb)
-            st_pgather(t, n)
-        for h in range(2):
-            for n in range(h * nb // 2, (h + 1) * nb // 2):
-                part[0] = "z%d" % h
-                st_z(t, n)
-                part[0] = "m%d" % h
-                st_m(t, n)
-            part[0] = "n%d" % h
-            st_newnames(t, h)
-        st_count(t)
-        for h in range(2):
-            part[0] = "t%d" % h
-            for n in range(h * nb // 2, (h + 1) * nb // 2):
-                st_truth(t, n)
-            st_est(t, h)
-        for h in range(2):
-            part[0] = "e%d" % h
-            st_err(t, h)
-        for h in range(2):
-            part[0] = "w%d" % h
-            st_scatter(t, h)
-    for h in range(2):
-        c = (128 * h, 128 * h + 128)
-        dma("Y", "l_yv%d" % h, [(lambda T, c=c: T.yv[:, c[0]:c[1]], lambda T, c=c: T.vn4[:, c[0]:c[1]])], [S("vn4", *c)], [], 2.0)
-        dma("Y", "l_ye%d" % h, [(lambda T, c=c: T.ye[:, c[0]:c[1]], lambda T, c=c: T.yn4[:, c[0]:c[1]])], [S("yn4", *c)], [], 2.0)
-    mm([(S("pf0", 0, 256), S("px", 128 * k, 128 * k + 128), S("parw", 16 + 256 * k, 272 + 256 * k), k == 0, k == 15) for k in range(16)])
-    cp(full("ypf"), S("pf0", 0, 256))
+        for k, f, n in (("n", st_names, TB), ("x", st_hash, TB), ("p", st_pgather, ZB), ("z", st_z, ZB), ("v", st_send, TB), ("c", st_count, [0]),
+                        ("m", st_m, ZB), ("f", st_far, TB), ("t", st_truth, TB), ("e", st_err, TB), ("a", st_ask, TB)):
+            for h in range(len(n)):
+                part[:] = ["%s%d" % (k, h), t]
+                f(t, h)
+    part[0] = "o0"
+    ts(full("yvf"), full("vn4"), 2048.0, A.add)
+    dma("Y", "l_yv", [(lambda T: T.yv[:], lambda T: T.yvf[:])], [full("yvf")], [], 2.0)
+    for h in range(len(TB)):
+        c = TB[h][:2]
+        ts(S("yeb", *c), S("yn4", *c), -1024.0, A.add)
+        dma("Y", "l_ye%d" % h, [(lambda T, c=c: T.ye[:, c[0]:c[1]], lambda T, c=c: T.yeb[:, c[0]:c[1]])], [S("yeb", *c)], [], 2.0)
+    b = bank()
+    acc(S(b, 0, 256), [(sx(k), S("parw", 16 + 256 * k, 272 + 256 * k)) for k in range(16)])
+    cp(full("ypf"), S(b, 0, 256))
     dma("Y", "l_yp", [(lambda T: T.yp[:], lambda T: T.ypf[:])], [full("ypf")], [], 2.0)
 
     hist = {}
     for i, o in enumerate(ops):
         dep = set()
         for (n, a, b) in o["R"]:
-            ps = BUF[n][0] == "psum"
             for (j, a2, b2, w) in hist.get(n, ()):
-                if (w and a < b2 and a2 < b) or (ps and ops[j]["q"] != o["q"]):
+                if w and a < b2 and a2 < b:
                     dep.add(j)
         for (n, a, b) in o["W"]:
-            ps = BUF[n][0] == "psum"
             for (j, a2, b2, w) in hist.get(n, ()):
-                if (a < b2 and a2 < b) or (ps and ops[j]["q"] != o["q"]):
+                if a < b2 and a2 < b:
                     dep.add(j)
         for (n, a, b) in o["R"]:
             hist.setdefault(n, []).append((i, a, b, False))
         for (n, a, b) in o["W"]:
             l = hist.setdefault(n, [])
-            l[:] = [e for e in l if not (a <= e[1] and e[2] <= b) or BUF[n][0] == "psum"]
+            l[:] = [e for e in l if not (a <= e[1] and e[2] <= b)]
             l.append((i, a, b, True))
         if o["q"] == "N":
             dep = {o["send"]}
         dep.discard(i)
         o["D"] = dep
+        o["B"] = sorted(set(r[0] for r in o["R"] + o["W"] if BUF[r[0]][0] == "psum"))
     return ops
 
 
-def schedule(ops, seed=0, eps=0.0):
+def _slot(line, t, c, q):
+    lo, hi = 0, len(line)
+    while lo < hi:
+        mid = (lo + hi) // 2
+        if line[mid][1] + LAT <= t:
+            lo = mid + 1
+        else:
+            hi = mid
+    while lo < len(line):
+        a, b, r = line[lo]
+        pad = 0.0 if r == q else LAT
+        if t + c + pad <= a + 1e-9:
+            break
+        t = max(t, b + pad)
+        lo += 1
+    return t
+
+
+def _put(line, e):
+    lo, hi = 0, len(line)
+    while lo < hi:
+        mid = (lo + hi) // 2
+        if line[mid] < e:
+            lo = mid + 1
+        else:
+            hi = mid
+    line.insert(lo, e)
+
+
+def _pass(ops, pred, succ, mate, key, back):
     n = len(ops)
-    succ = [[] for _ in range(n)]
-    for i, o in enumerate(ops):
-        for j in o["D"]:
-            succ[j].append(i)
-    prio = [0.0] * n
-    rnd = np.random.default_rng(seed).random(n)
-    for i in range(n - 1, -1, -1):
-        prio[i] = ops[i]["c"] + max([prio[j] + LAT for j in succ[i]], default=0.0)
-    key = [(-(prio[i] + BONUS.get(ops[i]["at"], 0.0) + LEAD.get(ops[i]["part"], 0.0) + eps * float(rnd[i])), i) for i in range(n)]
-    left = [len(o["D"]) for o in ops]
-    heap = sorted(key[i] for i in range(n) if left[i] == 0)
-    busy = {}
-    est, fin = [0.0] * n, [0.0] * n
-    order = []
+    first = {j: i for i, j in mate.items()}
+    left = [len(pred[i]) for i in range(n)]
+    for i, j in mate.items():
+        left[i] += len([k for k in pred[j] if k != i])
+    heap = sorted((key[i], i) for i in range(n) if left[i] == 0 and i not in first)
+    lines, start, real = {}, [0.0] * n, {}
+
+    def room(i, t):
+        o = ops[i]
+        if o["q"] == "N":
+            return t
+        off = o["c"] - o["occ"] if back else 0.0
+        while True:
+            u = _slot(lines.setdefault(o["q"], []), t + off, o["occ"], o["q"]) - off
+            for b in o["fix"]:
+                u = _slot(lines.setdefault(b, []), u, o["c"], o["q"])
+            if u <= t + 1e-9:
+                return t
+            t = u
+
+    def take(i, t):
+        o = ops[i]
+        start[i] = t
+        if o["q"] != "N":
+            off = o["c"] - o["occ"] if back else 0.0
+            _put(lines[o["q"]], (t + off, t + off + o["occ"], o["q"]))
+            for b in o["fix"]:
+                _put(lines[b], (t, t + o["c"], o["q"]))
+
+    def ready(i, skip=None):
+        return max([start[k] + ops[k]["c"] + LAT for k in pred[i] if k != skip], default=0.0)
+
     while heap:
         i = heap.pop(0)[1]
-        o = ops[i]
-        t = est[i]
-        if o["q"] != "N":
-            occ = 0.15 if o["sem"] and o["q"] in "YS" else o["c"]
-            b = busy.setdefault(o["q"], [])
-            at = len(b)
-            while at > 0 and b[at - 1][1] > t:
-                at -= 1
-            while at < len(b) and max(t, b[at - 1][1] if at else 0.0) + occ > b[at][0]:
-                at += 1
-            t = max(t, b[at - 1][1] if at else 0.0)
-            b.insert(at, (t, t + occ))
-        o["start"] = t
-        fin[i] = t + o["c"]
-        order.append((t, len(order), i))
-        for j in succ[i]:
-            est[j] = max(est[j], fin[i] + LAT)
-            left[j] -= 1
-            if left[j] == 0:
-                lo, hi = 0, len(heap)
-                while lo < hi:
-                    mid = (lo + hi) // 2
-                    if heap[mid] < key[j]:
-                        lo = mid + 1
+        t = room(i, ready(i))
+        done = [i]
+        if i in mate:
+            j = mate[i]
+            e, c = ready(j, i), ops[i]["c"]
+            while True:
+                u = room(j, max(e, t + c + LAT))
+                while True:
+                    v = room(i, max(t + 1e-6, u - LAT - c - 0.3))
+                    if v + c + LAT <= u + 1e-9 and v > t + 1e-3:
+                        t = v
                     else:
-                        hi = mid
-                heap.insert(lo, key[j])
-    order.sort()
-    return [i for _, _, i in order], max(fin)
+                        break
+                w, b = min((_slot(lines.setdefault(b, []), t, u + ops[j]["c"] - t, ""), b) for b in BIGB)
+                if w <= t + 1e-9:
+                    break
+                t = room(i, w)
+            _put(lines[b], (t, u + ops[j]["c"], "*"))
+            real[ops[i]["any"]] = b
+            take(j, u)
+            done.append(j)
+        take(i, t)
+        for d in done:
+            for k in succ[d]:
+                k2 = first.get(k, k)
+                if k2 in done:
+                    continue
+                left[k2] -= 1
+                if left[k2] == 0:
+                    _put(heap, (key[k2], k2))
+    return start, real, max(start[i] + ops[i]["c"] for i in range(n))
+
+
+def schedule(ops):
+    n = len(ops)
+    pred = [sorted(o["D"]) for o in ops]
+    succ = [[] for _ in range(n)]
+    pair, seen = {}, {}
+    for i, o in enumerate(ops):
+        for j in pred[i]:
+            succ[j].append(i)
+        o["occ"] = 0.15 * len(o["f"]) if o["sem"] and o["q"] in "YS" else o["c"]
+        o["fix"] = [b for b in o["B"] if b in SCRATCH]
+        for b in o["B"]:
+            if b not in SCRATCH:
+                o["any"] = b
+                pair.setdefault(b, []).append(i)
+        w = (o["t"], o["part"])
+        o["cls"] = (o["part"], seen.get(w, 0))
+        seen[w] = seen.get(w, 0) + 1
+    mate = {p[0]: p[1] for p in pair.values()}
+    key = [0.0] * n
+    for i in range(n - 1, -1, -1):
+        key[i] = min([key[j] - LAT for j in succ[i]], default=0.0) - ops[i]["c"]
+    head = {}
+    for i, o in enumerate(ops):
+        w = (o["t"], o["part"])
+        head[w] = min(head.get(w, 0.0), key[i])
+    turns = {}
+    for i, o in enumerate(ops):
+        if o["part"] in LEAD and (o["t"] == 2 or o["cls"] not in turns):
+            turns[o["cls"]] = LEAD[o["part"]] + key[i] - head[(o["t"], o["part"])]
+
+    def run(turns):
+        key = [0.0] * n
+        for i in range(n - 1, -1, -1):
+            o = ops[i]
+            if o["cls"] in turns:
+                key[i] = OPT["period"] * o["t"] + turns[o["cls"]]
+            else:
+                key[i] = min([key[j] - LAT for j in succ[i]], default=0.0) - o["c"]
+        return _pass(ops, pred, succ, mate, key, False), key
+
+    def held(start, real):
+        by, prev, out = {}, {}, []
+        for i in sorted(range(n), key=lambda i: start[i]):
+            for r in ([ops[i]["q"]] if ops[i]["q"] != "N" else []) + [real.get(b, b) for b in ops[i]["B"]]:
+                if r in by:
+                    prev.setdefault(i, []).append((by[r], r))
+                by[r] = i
+        i = max(range(n), key=lambda i: start[i] + ops[i]["c"])
+        while True:
+            c = [(start[j] + ops[j]["c"] + LAT, 1, j) for j in pred[i]]
+            for j, r in prev.get(i, ()):
+                if j not in pred[i]:
+                    c.append((start[j] + (ops[j]["occ"] if r == ops[i]["q"] else ops[j]["c"] + (LAT if ops[j]["q"] != ops[i]["q"] else 0.0)), 0, j))
+            if not c:
+                return out
+            t, d, j = max(c)
+            if not d:
+                out.append((j, i))
+            i = j
+
+    rnd = np.random.default_rng(OPT["seed"])
+    best, key = run(turns)
+    now, pairs = best[2], held(best[0], best[1])
+    for it in range(OPT["tries"]):
+        r = [float(x) for x in rnd.random(5)]
+        j, i = pairs[int(r[0] * len(pairs))]
+        new = dict(turns)
+        if r[1] < 0.5 and ops[i]["cls"] in turns:
+            d = key[i] - key[j] + 0.01 + 0.3 * r[2]
+            d = d if d > 0 else r[2]
+            new[ops[i]["cls"]] -= d
+            todo, moved, lim = [i], set(), key[i] - d
+            while todo:
+                for p in pred[todo.pop()]:
+                    if p not in moved and key[p] > lim and ops[p]["cls"] in turns and len(moved) < 12:
+                        moved.add(p)
+                        new[ops[p]["cls"]] -= key[p] - lim + 0.01
+                        todo.append(p)
+        elif ops[j]["cls"] in turns:
+            d = key[i] - key[j] + 0.01 + r[2] * (0.3 if r[3] < 0.7 else 3.0)
+            new[ops[j]["cls"]] += d if d > 0 else r[2]
+        else:
+            continue
+        got, key2 = run(new)
+        if got[2] <= now + OPT["heat"] * max(0.02, 1.0 - it / OPT["tries"]) * -math.log(1.0 - r[4]):
+            turns, now, key, pairs = new, got[2], key2, held(got[0], got[1])
+            if now < best[2]:
+                best = got
+    start, real, total = best
+    REAL.clear()
+    REAL.update(real)
+    order = sorted(range(n), key=lambda i: (start[i], i))
+    last, other = {}, {}
+    for i in order:
+        o = ops[i]
+        o["start"] = start[i]
+        for b in o["B"]:
+            r = REAL.get(b, b)
+            if r in last and ops[last[r]]["q"] != o["q"]:
+                other[r] = last[r]
+            if r in other:
+                o["D"].add(other[r])
+            last[r] = i
+    return order, total
 
 
 SEMQ = {"V": "vv", "S": "ss", "P": "pp", "G": "gg"}
@@ -663,7 +813,7 @@ def plan(nE):
     if nE in _CACHE:
         return _CACHE[nE]
     ops = build(nE)
-    order, total = schedule(ops, SEED, EPS)
+    order, total = schedule(ops)
     count = {s: 0 for s in SEMQ.values()}
     know, kq, out = {}, {}, []
     for i in order:
@@ -716,7 +866,7 @@ def rank_program(g, core, T, topo):
             queue[q].wait_ge(T.sem[s], v)
         if o["send"]:
             k, t, h = o["send"]
-            c = slice(128 * h, 128 * h + 128)
+            c = slice(TB[h][0], TB[h][1])
             g.remote_dma(out_ap=T["%sb%d" % (k, t)][:, c], in_ap=T["%sn%d" % (k, t - 1)][:, c], remote_sem=T.sem["a%s%d%d" % (k, t, h)],
                          local_sem=T.sem["o%s%d%d" % (k, t, h)], pid=pid, routing_id=rid, dma_engine_mask=mask)
         elif o["sem"]:

@@ -9,6 +9,8 @@ BUF = {}
 SEMAPHORES = ["vv", "ss", "pp", "gg"]
 ZB = [(192, 256, "pz0", 0), (128, 192, "pz1", 0), (64, 128, "pz0", 128), (0, 64, "pz1", 128)]
 TB = [(128, 256, "pz0", 256), (0, 128, "pz1", 256)]
+BIGB = ["pa0", "pa1", "pa2", "pa3"]
+TBANK = ["pt0", "pt1"]
 
 
 def _b(name, shape, dtype="float32", where="sbuf"):
@@ -41,7 +43,7 @@ for _n in ("dep", "sg", "yy", "yeb", "tcon", "adat"):
     _b(_n, [128, 256], BF)
 for _n in ("mm_", "par16", "vh"):
     _b(_n, [128, 256], F16)
-for _j in range(4):
+for _j in range(3):
     _b("km%d" % _j, [128, 128], F32)
     _b("pm%d" % _j, [128, 512], F32)
     _b("tt%d" % _j, [128, 256], F32)
@@ -56,20 +58,24 @@ _b("ol", [128, 32], U16)
 _b("fl", [128, 32], F32)
 _b("cs", [128, 1], BF)
 _b("cint", [128, 2], I32)
-for _n in ("ones", "eye", "neye", "blk", "blk1", "dm32", "p0", "n0", "c2048", "cm256", "ktile", "ptile", "wmat",
-           "s64k", "neye7", "rm", "m2k", "m64", "dcon", "ncon", "e15"):
+for _n in ("ones", "eye", "neye", "blk", "blk1", "dm32", "p0", "n0", "c2048", "cm256", "cm1k", "ktile", "ptile", "wmat",
+           "s64k", "neye7", "rm", "m2k", "m64", "dcon", "ncon", "e15", "vrow"):
     _b(_n, [128, 128], BF)
+for _j in (4, 8, 12, 16):
+    _b("cmf%d" % _j, [128, 128], BF)
+    _b("ckf%d" % _j, [128, 128], BF)
+    _b("cme%d" % _j, [128, 256], BF)
 for _n in ("zx", "zx2", "zxn"):
     _b(_n, [128, 144], BF)
 _b("z8", [8, 144], BF)
 _b("zb", [32, 144], BF)
 for _n in ("ea", "eb", "eb7", "neb7"):
     _b(_n, [32, 128], BF)
-_b("ex", [32, 512], BF)
+_b("ex", [32, 256], BF)
 _b("kcon", [8, 256], BF)
 _b("kval", [128, 16], BF)
-_b("b64", [128, 8], BF)
-_b("b4k", [128, 16], BF)
+_b("b64", [128, 24], BF)
+_b("b4k", [128, 48], BF)
 for _n in ("r2", "rmn"):
     _b(_n, [128, 256], BF)
 for _n in ("sr", "lf"):
@@ -88,11 +94,10 @@ _b("thb", [128, 2], F32)
 _b("thi", [128, 4], I32)
 _b("whoi", [128, 256], I32)
 _b("pari", [128, 256], I32)
-BIGB = ("pa0", "pa1", "pa2", "pa3")
-for _n in BIGB + ("pz0", "pz1", "pt0", "pt1"):
+for _n in BIGB + TBANK + ["pz0", "pz1"]:
     _b(_n, [128, 512], F32, "psum")
 
-for _n in ("lim", "who", "est", "wt", "par", "claim0", "claim1", "again", "yv", "ye0", "ye1", "ye2", "yp"):
+for _n in ("lim", "who", "est", "wt", "par", "claim0", "claim1", "again", "yv", "ye0", "ye1", "ye2", "yp0", "yp1"):
     SEMAPHORES.append("l_" + _n)
 for _t in range(1, VIS):
     for _h in range(len(TB)):
@@ -116,15 +121,19 @@ _CACHE = {}
 CY, PCY, GATH, SCAT = 0.00083 * 1.1, 0.00042 * 1.1, 1.5, 3.5
 VOV, SOV, POV, LAT = 0.04, 0.04, 0.02, 0.12
 OPT = {
-    "onv": ("y0", "y1", "p4", "p5"),
+    "onv": ("y0", "y1", "p7", "p5"),
     "relu": (),
+    "rows": {"f1": 8, "e1": 8},
     "gl": 32,
-    "tries": 2500, "period": 34.0, "seed": 0, "heat": 0.4,
+    "srv": 6,
+    "al": 32,
+    "tabs": 4,
+    "tries": 20000, "period": 35.0, "seed": 0, "heat": 0.5, "visits": 3,
 }
-LEAD = {"n0": -15, "n1": -15, "x0": -12, "x1": 2, "p0": 0, "p1": 0, "p2": 1.5, "p3": 3, "z0": 1.6, "z1": 2.1, "z2": 3.1, "z3": 4.6,
-        "g0": 3.4, "g1": 5, "g2": 7, "g3": 8.5, "d0": 4.9, "d1": 6.5, "d2": 8.5, "d3": 10, "m0": 7, "m1": 8.5, "m2": 10.5, "m3": 12,
-        "s0": 10, "s1": 11, "s2": 13, "s3": 14, "v0": 16, "v1": 17, "c0": 20, "f0": 12, "t0": 14, "e0": 18, "a0": 21, "w0": 26,
-        "f1": 15, "t1": 17.5, "e1": 21, "a1": 23, "w1": 29, "b0": -5, "o0": 33}
+LEAD = {"b0": -6, "n0": -16, "n1": -9, "x0": -9, "x1": -5.4, "y0": -6.6, "y1": -3.2, "p0": 0, "p1": 0.7, "p2": 1.5, "p3": 3,
+        "z0": 0.9, "z1": 1.6, "z2": 3.1, "z3": 4.6, "g0": 2.5, "g1": 4.5, "g2": 6.4, "g3": 8.8, "d0": 4.4, "d1": 6.2, "d2": 8, "d3": 10.4,
+        "m0": 7, "m1": 9, "m2": 11, "m3": 13, "s0": 10.5, "s1": 11.7, "s2": 14, "s3": 15.5, "v0": 11.4, "v1": 19.5, "c0": 20,
+        "f0": 14, "t0": 15, "u0": 21, "e0": 21, "a0": 22, "w0": 30.3, "f1": 17.5, "t1": 18.6, "u1": 25, "e1": 24.5, "a1": 26, "w1": 33, "o0": 35}
 REAL = {}
 R64, R256 = 1.5 * 2 ** 29, 1.5 * 2 ** 31
 
@@ -162,7 +171,7 @@ def half(*ss):
     return all(BUF[s[0]][2] in (BF, F16, U16) for s in ss)
 
 
-def build(nE):
+def build(nE, vis):
     ops = []
     GL = OPT["gl"]
     part = ["", 0]
@@ -238,8 +247,9 @@ def build(nE):
     def acc(out, terms):
         mm([(out, l, r, i == 0, i == len(terms) - 1) for i, (l, r) in enumerate(terms)])
 
-    def pile(terms):
-        mm([(o, l, r, i == 0, i == len(terms) - 1) for i, (o, l, r) in enumerate(terms)])
+    def pile(*lots):
+        for n, terms in enumerate(lots):
+            mm([(o, l, r, n == 0 and i == 0, n == len(lots) - 1 and i == len(terms) - 1) for i, (o, l, r) in enumerate(terms)])
 
     def dma(q, sem, pairs, R, W, cost):
         add(q, [lambda g, T, o=o, i=i: (g.sync if q == "Y" else g.scalar).dma_start(o(T), i(T)) for (o, i) in pairs], R, W, cost, sem=sem, val=16 * len(pairs))
@@ -248,8 +258,8 @@ def build(nE):
         kw = {"allow_small_or_imprecise_dtypes": True} if BUF[out[0]][2] in (BF, F32) else {}
         add("G", [lambda g, T: g.iota(ap(T, out), pattern, base, cm, **kw)], [], [out], 0.13 + 2 * width(out) * CY)
 
-    def asel(out, a, pattern, op, base, cm):
-        add("G", [lambda g, T: g.affine_select(ap(T, out), ap(T, a), pattern, op, 0.0, base, cm)], [a], [out], 0.17 + 2 * width(out) * CY)
+    def asel(out, a, pattern, op, base, cm, fill=0.0):
+        add("G", [lambda g, T: g.affine_select(ap(T, out), ap(T, a), pattern, op, fill, base, cm)], [a], [out], 0.17 + 2 * width(out) * CY)
 
     def full(name):
         sh = BUF[name][1]
@@ -267,20 +277,20 @@ def build(nE):
         _b("bank%d" % turn[0], [128, 512], F32, "psum")
         return "bank%d" % turn[0]
 
+    dma("Y", "l_par", [(lambda T: T.pari[:], lambda T: T.par[:])], [], [full("pari")], 2.0)
     dma("Y", "l_est", [(lambda T: T.yb0[:], lambda T: T.est[:])], [], [full("yb0")], 2.0)
     dma("Y", "l_wt", [(lambda T: T.wti[:], lambda T: T.wt[:])], [], [full("wti")], 2.0)
     dma("Y", "l_who", [(lambda T: T.whoi[:], lambda T: T.who[:])], [], [full("whoi")], 2.0)
-    dma("S", "l_par", [(lambda T: T.pari[:], lambda T: T.par[:])], [], [full("pari")], 2.0)
     dma("S", "l_claim0", [(lambda T: T.claimw[:, 0:2048], lambda T: T.claim[:, 0:2048])], [], [S("claimw", 0, 2048)], 3.0)
     dma("S", "l_claim1", [(lambda T: T.claimw[:, 2048:4096], lambda T: T.claim[:, 2048:4096])], [], [S("claimw", 2048, 4096)], 4.0)
     dma("Y", "l_lim", [(lambda T: T.limi[:], lambda T: T.lim[:])], [], [full("limi")], 2.0)
     dma("Y", "l_again", [(lambda T: T.claimw[:, 4096:8192], lambda T: T.claim[:]), (lambda T: T.claimw[:, 8192:CW], lambda T: T.claim[:, 0:CW - 8192])],
         [S("claimw", 0, 4096)], [S("claimw", 4096, CW)], 5.0)
     fill(full("ones"), 1.0)
+    iota(S("io1", 0, 16), [[-1, 16]], 16, 1)
     asel(full("blk1"), full("ones"), [[-16, 8], [0, 16]], A.is_ge, 0, 1)
     asel(BLK, full("blk1"), [[16, 8], [0, 16]], A.is_ge, 15, -1)
     asel(EYE, full("ones"), [[-1, 128]], A.is_equal, 0, 1)
-    iota(S("io1", 0, 16), [[-1, 16]], 16, 1)
     ts(S("io1", 16, 32), S("io1", 0, 16), 15, A.bitwise_and)
     ts(full("e16"), S("io1", 16, 32), 0.0, A.is_equal)
     K16 = S("cols", 0, 1)
@@ -293,41 +303,57 @@ def build(nE):
     ts(full("wmat"), BLK, full("wtf"), A.mult)
     fill(full("c2048"), 2048.0)
     for k in range(16):
-        act(S("sr", 128 * k, 128 * k + 128), BLK, AF.Identity, None, S("e16", k, k + 1))
-    iota(full("io2"), [[0, 16], [1, 16]], 0, 0)
+        if k < OPT["srv"]:
+            ts(S("sr", 128 * k, 128 * k + 128), BLK, S("e16", k, k + 1), A.mult)
+        else:
+            act(S("sr", 128 * k, 128 * k + 128), BLK, AF.Identity, None, S("e16", k, k + 1))
     ts(S("cols", 5, 6), K16, -256.0, A.mult, 2048.0, A.add)
-    ts(full("tcon"), full("io2"), 0.0, A.mult, S("cols", 5, 6), A.add)
+    for e in range(2):
+        act(S("tcon", 128 * e, 128 * e + 128), full("ones"), AF.Identity, None, S("cols", 5, 6))
     part[0] = "b0"
     for j in range(8):
         b = bank()
         mm([x for e in range(2) for x in ((S(b, 256 * e, 256 * e + 256), S("sr", 128 * (2 * j + e), 128 * (2 * j + e + 1)), full("par16"), True, False),
                                            (S(b, 256 * e, 256 * e + 256), EYE, full("tcon"), False, True))])
-        ts(S("parw", 16 + 512 * j, 528 + 512 * j), S(b, 0, 512), 0.0, A.max, 256.0, A.min)
+        if j % 2 and j < 2 * OPT["tabs"]:
+            act(S("la", 512 * j, 512 * j + 512), S(b, 0, 512), AF.Relu)
+            ts(S("parw", 16 + 512 * j, 528 + 512 * j), S("la", 512 * j, 512 * j + 512), 256.0, A.min)
+        else:
+            ts(S("parw", 16 + 512 * j, 528 + 512 * j), S(b, 0, 512), 0.0, A.max, 256.0, A.min)
     part[0] = ""
+    iota(full("io2"), [[0, 16], [1, 16]], 0, 0)
     fill(full("zx"), 0.0)
     cp(S("zx", 15, 143, 16), S("blk", 0, 128, 16))
-    ts(full("zx2"), full("zx"), 2.0, A.mult)
-    ts(full("zxn"), full("zx"), -1.0, A.mult)
+    if OPT["relu"]:
+        ts(full("zx2"), full("zx"), 2.0, A.mult)
+        ts(full("zxn"), full("zx"), -1.0, A.mult)
     ts(NEYE, EYE, -1.0, A.mult)
     ts(full("m2k"), EYE, -2048.0, A.mult)
     ts(full("dm32"), EYE, 32.0, A.mult)
     tt(full("dm32"), full("dm32"), BLK, A.subtract)
-    asel(S("ex", 0, 128, 1, 32), S("ones", 0, 128, 1, 32), [[1, 128]], A.is_ge, 0, -16)
-    asel(S("ex", 128, 256, 1, 32), S("ex", 0, 128, 1, 32), [[-1, 128]], A.is_ge, 15, 16)
-    cp(full("exf"), S("ex", 128, 256, 1, 8))
+
+    def own8(out, o):
+        asel(out, S("ones", 0, 128, 1, out[4]), [[-1, 8], [0, 16]], A.is_equal, -o, 1)
+
+    own8(S("ex", 0, 128, 1, 8), 0)
+    cp(full("exf"), S("ex", 0, 128, 1, 8))
     cp(full("limf"), full("limi"))
     mm([(S("pt0", 0, 2), full("exf"), full("limf"), True, True), (S("pt0", 2, 3), full("wmat"), S("c2048", 0, 1), True, True)])
     cp(full("thb"), S("pt0", 0, 2))
     cp(full("thc0"), S("pt0", 0, 1))
     ts(UCOL, S("pt0", 2, 3), -0.5, A.mult)
-    tt(S("coll", 0, 15), S("e16", 1, 16), S("e16", 0, 15), A.subtract)
-    ts(S("coll", 15, 16), S("e16", 15, 16), -1.0, A.mult)
-    for k in range(16):
-        ts(S("lf", 128 * k, 128 * k + 128), BLK, S("coll", k, k + 1), A.mult, 256.0, A.mult)
+    for e in range(2):
+        iota(S("ae", 1024 * e, 1024 * e + 1024), [[0, 1024]], 0, 0)
+        asel(S("af", 1024 * e, 1024 * e + 1024), S("ae", 1024 * e, 1024 * e + 1024), [[-1, 8], [-16, 8], [0, 16]], A.not_equal, -8 * e, 1, -256.0)
+        asel(S("lf", 1024 * e, 1024 + 896 * e), S("af", 1024 * e, 1024 + 896 * e), [[-1, 8 - e], [-16, 8], [0, 16]], A.not_equal, -8 * e - 1, 1, 256.0)
+    cp(S("lf", 1920, 2048), S("af", 1920, 2048))
     ts(full("p0"), S("sr", 0, 128), 256.0, A.mult)
     ts(full("n0"), S("sr", 0, 128), -256.0, A.mult)
     fill(full("cm256"), -256.0)
-    ts(full("b64"), S("blk", 0, 128, 16), 64.0, A.mult)
+    for e, w in enumerate((1.0, 2.0, -1.0)):
+        ts(S("b64", 8 * e, 8 * e + 8), S("blk", 0, 128, 16), 64.0 * w, A.mult)
+        for j in range(2):
+            ts(S("b4k", 16 * e + 8 * j, 16 * e + 8 * j + 8), S("blk", 0, 128, 16), 4096.0 * w, A.mult)
     ts(full("s64k"), EYE, 65536.0, A.mult)
     cp(full("ktile"), S("io2", 0, 128))
     ts(full("rm"), full("ktile"), 0.5, A.subtract, -1e9, A.mult)
@@ -337,8 +363,14 @@ def build(nE):
     cp(S("z8", 15, 143, 16, 8), S("eye", 0, 8, 1, 8))
     iota(S("io1", 32, 40), [[16, 8]], 0, 0)
     ts(S("ptile", 0, 8), S("io1", 32, 40), K16, A.add, 16.0, A.mult)
-    for e in range(2):
-        ts(S("b4k", 8 * e, 8 * e + 8), S("blk", 0, 128, 16), 4096.0, A.mult)
+    fill(full("cm1k"), -1024.0)
+    for n in sorted(set(OPT["rows"].values())):
+        ts(full("vrow"), full("ktile"), 16.0 - n, A.is_ge)
+        ts(full("ckf%d" % n), full("vrow"), 2.0 ** 20, A.mult)
+        tt(full("vrow"), full("vrow"), BLK, A.mult)
+        ts(full("cmf%d" % n), full("vrow"), -64.0, A.mult)
+        for j in range(2):
+            ts(S("cme%d" % n, 128 * j, 128 * j + 128), full("vrow"), -4096.0, A.mult)
     ts(full("m64"), EYE, -64.0, A.mult)
     ts(DCOL, K16, 4112.0, A.add)
     cp(S("thi", 0, 1), S("thb", 1, 2))
@@ -346,20 +378,20 @@ def build(nE):
     ts(S("thi", 2, 3), S("thi", 0, 1), 15, A.bitwise_and)
     fill(full("kval"), 0.0)
     ts(S("cols", 6, 7), K16, -256.0, A.mult, 3840.0, A.add)
-    for e in range(2):
-        ts(S("kval", 8 * e, 8 * e + 1), S("thi", 1, 2), -65536.0, A.mult)
-        ts(S("kval", 8 * e + 1, 8 * e + 2), S("thi", 2, 3), -4096.0, A.mult, S("cols", 6, 7), A.add)
-        fill(S("kval", 8 * e + 2, 8 * e + 3), 69632.0 if e else -1088.0)
-        fill(S("kval", 8 * e + 3, 8 * e + 4), 2048.0 if e else 1.0)
+    ts(S("kval", 0, 16, 8), S("ones", 0, 2), S("cols", 6, 7), A.mult)
+    cp(S("cols", 8, 10), S("thi", 1, 3))
+    ts(S("kval", 1, 16, 8), S("ones", 0, 2), S("cols", 8, 9), A.mult, -65536.0, A.mult)
+    ts(S("kval", 2, 16, 8), S("ones", 0, 2), S("cols", 9, 10), A.mult, -4096.0, A.mult)
+    fill(S("kval", 3, 4), -1088.0)
+    fill(S("kval", 11, 12), 69632.0)
+    fill(S("kval", 12, 13), 2112.0)
     mm([(S("pt1", 128 * e, 128 * e + 128, 1, 8), S("kval", 8 * e, 8 * e + 8), EYE, True, True) for e in range(2)])
     cp(full("kcon"), S("pt1", 0, 256, 1, 8))
     for name, o in (("ea", 0), ("eb", 16)):
-        asel(S("ex", 0, 128, 1, 32), S("ones", 0, 128, 1, 32), [[1, 128]], A.is_ge, 16 * o, -16)
-        asel(S("ex", 256, 384, 1, 32), S("ex", 0, 128, 1, 32), [[-1, 128]], A.is_ge, 15 - 16 * o, 16)
-        asel(S("ex", 0, 128, 1, 32), S("ones", 0, 128, 1, 32), [[1, 128]], A.is_ge, 16 * (o + 8), -16)
-        asel(S("ex", 384, 512, 1, 32), S("ex", 0, 128, 1, 32), [[-1, 128]], A.is_ge, 15 - 16 * (o + 8), 16)
-        ts(S("ex", 256, 384, 1, 32), S("ex", 256, 384, 1, 32), 64.0, A.mult)
-        tt(full(name), S("ex", 256, 384, 1, 32), S("ex", 384, 512, 1, 32), A.add)
+        own8(S("ex", 0, 128, 1, 32), o)
+        own8(S("ex", 128, 256, 1, 32), o + 8)
+        ts(S("ex", 0, 128, 1, 32), S("ex", 0, 128, 1, 32), 64.0, A.mult)
+        tt(full(name), S("ex", 0, 128, 1, 32), S("ex", 128, 256, 1, 32), A.add)
     fill(full("zb"), 0.0)
     cp(S("zb", 15, 143, 16, 32), S("eb", 0, 128, 16, 32))
     ts(full("eb7"), full("eb"), 2.0 ** -7, A.mult)
@@ -407,6 +439,7 @@ def build(nE):
             ts(S("t1", *c), U, UCOL, A.add)
         ts(um, S("t1", *c), 4095, A.bitwise_and)
         place(t, s, um, S("t2", *c), S("t3", *c), S("c1", *c), S("hl", *c))
+        part[0] = "y%d" % h
         for a in range(c1 - GL, c0 - 1, -GL):
             move("x%d" % (a // 32), S("x%d" % (t % 2), 16 * a, 16 * (a + GL)), IND("claimw", 0, window(t), "hl", a, a + GL))
 
@@ -429,7 +462,9 @@ def build(nE):
             ts(S("ad", X, X2), S("d", X, X2), 0.0, A.max)
             acc(D, [(sx(k, "zxn"), S("d", X + k, X2, 16)) for k in range(16)] + [(sx(k, "zx2"), S("ad", X + k, X2, 16)) for k in range(16)])
         else:
-            act(S("ad", X, X2), S("d", X, X2), AF.Abs)
+            for a in range(c0, c1, OPT.get("al", 64)):
+                e = min(c1, a + OPT.get("al", 64))
+                act(S("ad", 16 * a, 16 * e), S("d", 16 * a, 16 * e), AF.Abs)
             acc(D, [(sx(k), S("ad", X + k, X2, 16)) for k in range(16)])
         ts(dep, D, full("thc%d" % t), A.is_lt)
         acc(D, [(full("dm32"), dep)])
@@ -446,7 +481,7 @@ def build(nE):
         x = "x%d" % (t % 2)
         o += L
         mm([(S(b, o, o + 1), full("p0"), S("sg", c0, c0 + 1), True, True), (S(b, o + 1, o + 2), full("n0"), S("sg", c0, c0 + 1), True, True)])
-        act(S("ini", 2 * n, 2 * n + 2), S(b, o, o + 2), AF.Copy)
+        move("i%d" % n, S("ini", 2 * n, 2 * n + 2), S(b, o, o + 2))
         for l in range(c0, c1, 32):
             a, e = bank(), int(l + 32 == c1)
             gr = [(S(a, k, 512, 16), S("lf", 128 * k, 128 * k + 128), S("sg", l, l + 32), True, True) for k in range(15)]
@@ -454,7 +489,7 @@ def build(nE):
                    (S(a, 15, 512 - 16 * e, 16), full("p0"), S("sg", l + 1, l + 33 - e), False, False),
                    (S(a, 15, 512, 16), EYE, S("cm256", 0, 32), False, True)]
             mm(gr)
-            act(S("la", 16 * l, 16 * l + 512), S(a, 0, 512), AF.Copy)
+            move("l%d" % (l // 32), S("la", 16 * l, 16 * l + 512), S(a, 0, 512))
         part[0] = "s%d" % n
         scan(S("mx", X, X2), S(x, X, X2), S("la", X, X2), S("ini", 2 * n, 2 * n + 1), A.max, A.add)
         scan(S("mn", X, X2), S(x, X, X2), S("la", X, X2), S("ini", 2 * n + 1, 2 * n + 2), A.min, A.subtract)
@@ -463,9 +498,9 @@ def build(nE):
         ts(S("mm_", *c), w, 0.5, A.mult, 1023.75, A.add)
 
     def st_count(t, h):
-        if t == VIS - 1:
+        if t == vis - 1:
             return
-        b = "pt%d" % (len(TB) - 1)
+        b = TBANK[-1]
         acc(S(b, 500, 501), [(S("dep", 128, 256), S("ones", 0, 1)), (S("dep", 0, 128), S("ones", 0, 1))])
         move("c", full("cs"), S(b, 500, 501))
         acc(S(b, 501, 502), [(full("ones"), full("cs"))])
@@ -473,34 +508,40 @@ def build(nE):
         ts(S("cint", 1, 2), S("cint", 0, 1), 31, A.bitwise_and)
         tt(full("thc%d" % (t + 1)), S("cint", 1, 2), S("thb", 0, 1), A.add)
 
-    def distances(t, h, mid, out, bias):
-        c0, c1 = TB[h][:2]
-        L, X = c1 - c0, 16 * c0
-        K = 512 // L
-        for q in range(0, 16, K):
-            b = bank()
-            gr = []
-            n = min(K, 16 - q)
-            for e in range(n):
-                o = S(b, L * e, L * e + L)
-                gr += [(o, EYE, S("x%d" % (t % 2), X + q + e, X + 16 * L, 16), True, False), (o, NEYE, mid, False, True)]
+    def distances(t, h, mid, out, bias, w, weights):
+        c0, c1, zb, zo = TB[h]
+        L, X, x, b = c1 - c0, 16 * c0, "x%d" % (t % 2), TBANK[h]
+        K, nv, n = 512 // L, OPT["rows"].get(part[0], 0), width(full(weights)) // 3
+        own = [(S(b, k, w, 16, L), S(x, X + k, X + 16 * L, 16), S(weights, 2 * n, 3 * n)) for k in range(16 - nv, 16)]
+        lots = []
+        if nv:
+            m = S(zb, zo, zo + L)
+            acc(m, [(EYE, mid)] + ([(EYE, S("cm1k", 0, L))] if bias else []))
+        for q in range(0, 16 - nv, K):
+            a, gr, e1 = bank(), [], min(K, 16 - nv - q)
+            for e in range(e1):
+                o = S(a, L * e, L * e + L)
+                gr += [(o, EYE, S(x, X + q + e, X + 16 * L, 16), True, False), (o, NEYE, mid, False, True)]
             mm(gr)
-            act(S(out, X + L * q, X + L * (q + n)), S(b, 0, L * n), AF.Abs, bias)
-
-    def sums(h, b, w, src, first, weight):
-        c0, c1 = TB[h][:2]
-        L, X = c1 - c0, 16 * c0
-        pile(first + [(S(b, k, w, 16, L), S(src, X + L * k, X + L * k + L), weight) for k in range(16)])
-
-    def st_far(t, h):
-        distances(t, h, S("mm_", *TB[h][:2]), "af", 1024.0)
+            act(S(out, X + L * q, X + L * (q + e1)), S(a, 0, L * e1), AF.Abs, bias)
+            lots.append([(S(b, k, w, 16, L), S(out, X + L * k, X + L * k + L), S(weights, 0, n)) for k in range(q, q + e1)])
+        for k in range(16 - nv, 16):
+            tt(S(out, X + L * k, X + L * k + L), S(x, X + k, X + 16 * L, 16), m, A.max)
+        for j, q in enumerate(range(16 - nv, 16, 4)):
+            lots.insert(min(2 * j, len(lots)), [(S(b, k, w, 16, L), S(out, X + L * k, X + L * k + L), S(weights, n, 2 * n)) for k in range(q, q + 4)])
+        return nv, own, lots
 
     def st_truth(t, h):
         c = TB[h][:2]
-        L, b = c[1] - c[0], "pt%d" % h
+        L, b = c[1] - c[0], TBANK[h]
         Q, q = L // 16, c[0] // 16
-        key = S(b, 0, 128, 1, L)
-        sums(h, b, 128, "af", [(key, S("eye", 0, L), full("ktile")), (key, S("sg", *c), full("s64k"))], full("b64"))
+        key, mid = S(b, 0, 128, 1, L), S("mm_", *c)
+        nv, own, lots = distances(t, h, mid, "af", 1024.0, 128, "b64")
+        part[0] = "t%d" % h
+        first = [(key, S("eye", 0, L), full("ktile")), (key, S("sg", *c), full("s64k"))] + own
+        if nv:
+            first += [(key, S("eye", 0, L), full("ckf%d" % nv)), (key, mid, full("cmf%d" % nv))]
+        pile(first, *lots)
         scan(S("km%d" % h, 0, 128, 1, L), S("rm", 0, 128, 1, L), key, 0.0, A.max, A.min)
         m, r, k = S("km%d" % h, 15, 128, 16, L), S("rr%d" % h, 0, 8, 1, L), S("cc%d" % h, 0, 8, 1, L)
         ts(r, m, R64, A.add, -R64, A.add)
@@ -510,26 +551,31 @@ def build(nE):
         acc(S(b, 256, 256 + Q), [(EYE, S("ptile", 0, Q))] + [(sx(a, "z8", 8), S("kt8", c[0] + a, c[1], 16, 8)) for a in range(16)])
         cp(S("yl", q, q + Q), S(b, 256, 256 + Q))
         move("y%d" % h, S("yy", *c), IND("x%d" % (t % 2), 16 * c[0], 16 * c[1], "yl", q, q + Q))
+        part[0] = "u%d" % h
         e = S(b, 384, 384 + L)
         acc(e, [(EYE, S("yb%d" % t, *c)), (EYE, S("yy", *c))])
         ts(S("yn%d" % t, *c), e, 0.5, A.mult, 511.75 if t else 1023.75, A.add)
-        if t < VIS - 1:
+        if t < vis - 1:
             send("y", t, h)
-
-    def st_err(t, h):
-        c = TB[h][:2]
-        ts(S("vh", *c), S("vb%d" % t, *c), 1.0 / 64, A.mult, 1119.5078125, A.add)
-        distances(t, h, S("yy", *c), "ae", None)
 
     def st_ask(t, h):
         c = TB[h][:2]
-        L, b = c[1] - c[0], "pt%d" % h
+        L, b = c[1] - c[0], TBANK[h]
         Q, q = L // 16, c[0] // 16
-        hi, lo = S(b, 0, 128, 1, L), S(b, 128, 256, 1, L)
-        sums(h, b, 256, "ae", [(S(b, 0, 256, 1, L), S("ones", 0, L, 1, 8), full("kcon")), (lo, S("vh", *c), full("m64")),
-                               (lo, S("vb%d" % t, *c), EYE), (hi, S("vh", *c), EYE)], full("b4k"))
+        ts(S("vh", *c), S("vb%d" % t, *c), 1.0 / 64, A.mult, 1120.5078125, A.add)
+        nv, own, lots = distances(t, h, S("yy", *c), "ae", None, 256, "b4k")
+        part[0] = "a%d" % h
+        key, hi, lo = S(b, 0, 256, 1, L), S(b, 0, 128, 1, L), S(b, 128, 256, 1, L)
+        first = [(key, S("ones", 0, L, 1, 8), full("kcon"))] + own
+        names = [(lo, S("vh", *c), full("m64")), (lo, S("vb%d" % t, *c), EYE), (hi, S("vh", *c), EYE)]
+        if nv:
+            first.append((key, S("yy", *c), full("cme%d" % nv)))
+            lots[-1] = lots[-1] + names
+        else:
+            first += names
+        pile(first, *lots)
         pm, t2 = "pm%d" % h, S("tt%d" % h, 1, 256, 1, L)
-        scan(S(pm, 0, 256, 1, L), S("rmn", 0, 256, 1, L), S(b, 0, 256, 1, L), 0.0, A.min, A.max)
+        scan(S(pm, 0, 256, 1, L), S("rmn", 0, 256, 1, L), key, 0.0, A.min, A.max)
         tt(t2, S(b, 1, 256, 1, L), S(pm, 0, 255, 1, L), A.min)
         scan(S(pm, 257, 512, 1, L), S("r2", 1, 256, 1, L), t2, 0.0, A.mult, A.max)
         m, r, k = S(pm, 15, 512, 16, L), S("rr%d" % h, 16, 48, 1, L), S("cc%d" % h, 16, 48, 1, L)
@@ -537,11 +583,11 @@ def build(nE):
         tt(k, m, r, A.subtract)
         acc(S(b, 256, 256 + L, 1, 32), [(k, S("eye", 0, L, 1, L))])
         kt = S("kt32", c[0], c[1], 1, 32)
-        move("l%d" % h, kt, S(b, 256, 256 + L, 1, 32))
+        move("j%d" % h, kt, S(b, 256, 256 + L, 1, 32))
         own, o16 = S(b, 0, Q), S("own", q, q + Q)
         acc(own, [(sx(a, "zb", 32), S("kt32", c[0] + a, c[1], 16, 32)) for a in range(16)])
         ts(o16, own, -2112.0, A.add)
-        N, D = S(b, 384, 384 + L), S(b, 128, 128 + L)
+        N, D = S(bank(), 0, L), S(b, 128, 128 + L)
         acc(N, [(EYE, S("ncon", 0, L)), (full("ea"), kt)])
         pile([(D, EYE, S("dcon", 0, L)), (D, full("eb7"), kt), (S(b, 128 + 15, 128 + L, 16), full("neb7"), S("kt32", c[0] + 15, c[1], 16, 32))] +
              [(S(b, 128 + a, 128 + L, 16), full("neye7"), o16) for a in range(15)])
@@ -556,28 +602,30 @@ def build(nE):
             cp(IND("parw", 0, PW, "ol", 2 * a, 2 * a + 1), S("adat", 16 * a, 16 * a + 16))
 
     def st_send(t, h):
-        if t < VIS - 1:
+        if t < vis - 1:
             send("v", t, h)
 
-    for t in range(VIS):
+    for t in range(vis):
         for k, f, n in (("n", st_names, TB), ("x", st_hash, TB), ("p", st_pgather, ZB), ("z", st_z, ZB), ("v", st_send, TB), ("c", st_count, [0]),
-                        ("m", st_m, ZB), ("f", st_far, TB), ("t", st_truth, TB), ("e", st_err, TB), ("a", st_ask, TB)):
+                        ("m", st_m, ZB), ("f", st_truth, TB), ("e", st_ask, TB)):
             for h in range(len(n)):
                 part[:] = ["%s%d" % (k, h), t]
                 f(t, h)
     part[0] = "o0"
-    ts(full("yvf"), full("vn4"), 2048.0, A.add)
+    ts(full("yvf"), full("vn%d" % (vis - 1)), 2048.0, A.add)
     dma("Y", "l_yv", [(lambda T: T.yv[:], lambda T: T.yvf[:])], [full("yvf")], [], 2.0)
     for h in range(len(TB)):
         c = TB[h][:2]
-        ts(S("yeb", *c), S("yn4", *c), -1024.0, A.add)
+        ts(S("yeb", *c), S("yn%d" % (vis - 1), *c), -1024.0, A.add)
         dma("Y", "l_ye%d" % h, [(lambda T, c=c: T.ye[:, c[0]:c[1]], lambda T, c=c: T.yeb[:, c[0]:c[1]])], [S("yeb", *c)], [], 2.0)
-    b = bank()
-    acc(S(b, 0, 256), [(sx(k), S("parw", 16 + 256 * k, 272 + 256 * k)) for k in range(16)])
-    cp(full("ypf"), S(b, 0, 256))
-    dma("Y", "l_yp", [(lambda T: T.yp[:], lambda T: T.ypf[:])], [full("ypf")], [], 2.0)
+    for e in range(2):
+        b = bank()
+        acc(S(b, 0, 128), [(sx(k), S("parw", 16 + 2048 * e + 128 * k, 144 + 2048 * e + 128 * k)) for k in range(16)])
+        move("o%d" % e, S("ypf", 128 * e, 128 * e + 128), S(b, 0, 128))
+        dma("YS"[e], "l_yp%d" % e, [(lambda T, e=e: T.yp[:, 2048 * e:2048 * e + 2048], lambda T, e=e: T.ypf[:, 128 * e:128 * e + 128])],
+            [S("ypf", 128 * e, 128 * e + 128)], [], 2.0)
 
-    hist = {}
+    hist, sums = {}, {}
     for i, o in enumerate(ops):
         dep = set()
         for (n, a, b) in o["R"]:
@@ -596,9 +644,15 @@ def build(nE):
             l.append((i, a, b, True))
         if o["q"] == "N":
             dep = {o["send"]}
-        dep.discard(i)
-        o["D"] = dep
         o["B"] = sorted(set(r[0] for r in o["R"] + o["W"] if BUF[r[0]][0] == "psum"))
+        for b in o["B"]:
+            if o["q"] == "P" and b in TBANK:
+                if b in sums:
+                    dep.add(sums[b])
+                sums[b] = i
+        dep.discard(i)
+        o["O"] = set(j for j in dep if o["q"] == "P" and ops[j]["q"] == "P")
+        o["D"], o["i"] = dep, i
     return ops
 
 
@@ -615,7 +669,8 @@ def _slot(line, t, c, q):
         pad = 0.0 if r == q else LAT
         if t + c + pad <= a + 1e-9:
             break
-        t = max(t, b + pad)
+        if b + pad > t:
+            t = b + pad
         lo += 1
     return t
 
@@ -631,47 +686,44 @@ def _put(line, e):
     line.insert(lo, e)
 
 
-def _pass(ops, pred, succ, mate, key, back):
+def _pass(ops, pred, succ, mate, key):
     n = len(ops)
     first = {j: i for i, j in mate.items()}
-    left = [len(pred[i]) for i in range(n)]
+    left = [len(p) for p in pred]
     for i, j in mate.items():
         left[i] += len([k for k in pred[j] if k != i])
     heap = sorted((key[i], i) for i in range(n) if left[i] == 0 and i not in first)
-    lines, start, real = {}, [0.0] * n, {}
+    lines = {r: [] for r in list("VSPGY") + BIGB + TBANK + ["pz0", "pz1"]}
+    start, end, real = [0.0] * n, [0.0] * n, {}
 
     def room(i, t):
         o = ops[i]
-        if o["q"] == "N":
+        q = o["q"]
+        if q == "N":
             return t
-        off = o["c"] - o["occ"] if back else 0.0
         while True:
-            u = _slot(lines.setdefault(o["q"], []), t + off, o["occ"], o["q"]) - off
+            u = _slot(lines[q], t, o["occ"], q)
             for b in o["fix"]:
-                u = _slot(lines.setdefault(b, []), u, o["c"], o["q"])
+                u = _slot(lines[b], u, o["c"], q)
             if u <= t + 1e-9:
                 return t
             t = u
 
     def take(i, t):
         o = ops[i]
-        start[i] = t
+        start[i], end[i] = t, t + o["c"] + LAT
         if o["q"] != "N":
-            off = o["c"] - o["occ"] if back else 0.0
-            _put(lines[o["q"]], (t + off, t + off + o["occ"], o["q"]))
+            _put(lines[o["q"]], (t, t + o["occ"], o["q"]))
             for b in o["fix"]:
                 _put(lines[b], (t, t + o["c"], o["q"]))
 
-    def ready(i, skip=None):
-        return max([start[k] + ops[k]["c"] + LAT for k in pred[i] if k != skip], default=0.0)
-
     while heap:
         i = heap.pop(0)[1]
-        t = room(i, ready(i))
-        done = [i]
+        t = room(i, max([end[k] - (LAT if k in ops[i]["O"] else 0.0) for k in pred[i]], default=0.0))
+        done = (i,)
         if i in mate:
             j = mate[i]
-            e, c = ready(j, i), ops[i]["c"]
+            e, c = max([end[k] for k in pred[j] if k != i], default=0.0), ops[i]["c"]
             while True:
                 u = room(j, max(e, t + c + LAT))
                 while True:
@@ -680,27 +732,26 @@ def _pass(ops, pred, succ, mate, key, back):
                         t = v
                     else:
                         break
-                w, b = min((_slot(lines.setdefault(b, []), t, u + ops[j]["c"] - t, ""), b) for b in BIGB)
+                w, b = min((_slot(lines[b], t, u + ops[j]["c"] - t, ""), b) for b in BIGB)
                 if w <= t + 1e-9:
                     break
                 t = room(i, w)
             _put(lines[b], (t, u + ops[j]["c"], "*"))
             real[ops[i]["any"]] = b
             take(j, u)
-            done.append(j)
+            done = (i, j)
         take(i, t)
         for d in done:
             for k in succ[d]:
                 k2 = first.get(k, k)
-                if k2 in done:
-                    continue
-                left[k2] -= 1
-                if left[k2] == 0:
-                    _put(heap, (key[k2], k2))
-    return start, real, max(start[i] + ops[i]["c"] for i in range(n))
+                if k2 not in done:
+                    left[k2] -= 1
+                    if left[k2] == 0:
+                        _put(heap, (key[k2], k2))
+    return start, real, max(end) - LAT
 
 
-def schedule(ops):
+def _graph(ops):
     n = len(ops)
     pred = [sorted(o["D"]) for o in ops]
     succ = [[] for _ in range(n)]
@@ -717,7 +768,23 @@ def schedule(ops):
         w = (o["t"], o["part"])
         o["cls"] = (o["part"], seen.get(w, 0))
         seen[w] = seen.get(w, 0) + 1
-    mate = {p[0]: p[1] for p in pair.values()}
+    return pred, succ, {p[0]: p[1] for p in pair.values()}
+
+
+def _run(ops, pred, succ, mate, turns):
+    key = [0.0] * len(ops)
+    for i in range(len(ops) - 1, -1, -1):
+        o = ops[i]
+        if o["cls"] in turns:
+            key[i] = OPT["period"] * o["t"] + turns[o["cls"]]
+        else:
+            key[i] = min([key[j] - LAT for j in succ[i]], default=0.0) - o["c"]
+    return _pass(ops, pred, succ, mate, key), key
+
+
+def find_turns(ops):
+    n = len(ops)
+    pred, succ, mate = _graph(ops)
     key = [0.0] * n
     for i in range(n - 1, -1, -1):
         key[i] = min([key[j] - LAT for j in succ[i]], default=0.0) - ops[i]["c"]
@@ -727,18 +794,9 @@ def schedule(ops):
         head[w] = min(head.get(w, 0.0), key[i])
     turns = {}
     for i, o in enumerate(ops):
-        if o["part"] in LEAD and (o["t"] == 2 or o["cls"] not in turns):
-            turns[o["cls"]] = LEAD[o["part"]] + key[i] - head[(o["t"], o["part"])]
-
-    def run(turns):
-        key = [0.0] * n
-        for i in range(n - 1, -1, -1):
-            o = ops[i]
-            if o["cls"] in turns:
-                key[i] = OPT["period"] * o["t"] + turns[o["cls"]]
-            else:
-                key[i] = min([key[j] - LAT for j in succ[i]], default=0.0) - o["c"]
-        return _pass(ops, pred, succ, mate, key, False), key
+        lead = {"y": LEAD.get("x" + o["part"][1:], 0) + 2, "u": LEAD.get("t" + o["part"][1:], 0) + 3}.get(o["part"][:1], LEAD.get(o["part"]))
+        if lead is not None and (o["t"] == 1 or o["cls"] not in turns):
+            turns[o["cls"]] = lead + key[i] - head[(o["t"], o["part"])]
 
     def held(start, real):
         by, prev, out = {}, {}, []
@@ -749,7 +807,7 @@ def schedule(ops):
                 by[r] = i
         i = max(range(n), key=lambda i: start[i] + ops[i]["c"])
         while True:
-            c = [(start[j] + ops[j]["c"] + LAT, 1, j) for j in pred[i]]
+            c = [(start[j] + ops[j]["c"] + (0.0 if j in ops[i]["O"] else LAT), 1, j) for j in pred[i]]
             for j, r in prev.get(i, ()):
                 if j not in pred[i]:
                     c.append((start[j] + (ops[j]["occ"] if r == ops[i]["q"] else ops[j]["c"] + (LAT if ops[j]["q"] != ops[i]["q"] else 0.0)), 0, j))
@@ -761,8 +819,9 @@ def schedule(ops):
             i = j
 
     rnd = np.random.default_rng(OPT["seed"])
-    best, key = run(turns)
-    now, pairs = best[2], held(best[0], best[1])
+    got, key = _run(ops, pred, succ, mate, turns)
+    now, pairs = got[2], held(got[0], got[1])
+    best = (now, turns)
     for it in range(OPT["tries"]):
         r = [float(x) for x in rnd.random(5)]
         j, i = pairs[int(r[0] * len(pairs))]
@@ -783,15 +842,145 @@ def schedule(ops):
             new[ops[j]["cls"]] += d if d > 0 else r[2]
         else:
             continue
-        got, key2 = run(new)
+        got, key2 = _run(ops, pred, succ, mate, new)
         if got[2] <= now + OPT["heat"] * max(0.02, 1.0 - it / OPT["tries"]) * -math.log(1.0 - r[4]):
             turns, now, key, pairs = new, got[2], key2, held(got[0], got[1])
-            if now < best[2]:
-                best = got
-    start, real, total = best
+            if now < best[0]:
+                best = (now, turns)
+    return best[1]
+
+
+def schedule(ops, turns):
+    pred, succ, mate = _graph(ops)
+    start, real, total = _run(ops, pred, succ, mate, turns)[0]
     REAL.clear()
     REAL.update(real)
-    order = sorted(range(n), key=lambda i: (start[i], i))
+    order = sorted(range(len(ops)), key=lambda i: (start[i], i))
+    last, other = {}, {}
+    for i in order:
+        o = ops[i]
+        o["start"] = start[i]
+        for b in o["B"]:
+            r = REAL.get(b, b)
+            if r in last and ops[last[r]]["q"] != o["q"]:
+                other[r] = last[r]
+            if r in other:
+                o["D"].add(other[r])
+            last[r] = i
+    return order, total
+
+
+def timer(ops, period):
+    n = len(ops)
+    pred, succ, mate = _graph(ops)
+    second = {j: i for i, j in mate.items()}
+    c, occ, q, fix = [[o[k] for o in ops] for k in ("c", "occ", "q", "fix")]
+    cls, base = [o["cls"] + (min(o["t"], 1),) for o in ops], [period * o["t"] for o in ops]
+    pl = [[(j, 0.0 if j in ops[i]["O"] else LAT) for j in pred[i]] for i in range(n)]
+
+    def run(turns):
+        key = [turns[cls[i]] + base[i] for i in range(n)]
+        for i in range(n):
+            for j in pred[i]:
+                if key[j] >= key[i]:
+                    key[i] = key[j] + 1e-5
+        order = sorted(range(n), key=lambda i: key[i])
+        end, why, start = [0.0] * n, [None] * n, [0.0] * n
+        free, last, big, hold, idle = {}, {}, [(0.0, -1)] * len(BIGB), {}, list(range(len(BIGB)))
+        for i in order:
+            t, w, qi = 0.0, None, q[i]
+            for j, l in pl[i]:
+                if end[j] + l > t:
+                    t, w = end[j] + l, (j, 1)
+            if qi != "N":
+                e = free.get(qi)
+                if e is not None and e[0] >= t:
+                    t, w = e[0], (e[1], 0)
+                for b in fix[i]:
+                    e = last.get(b)
+                    if e is not None:
+                        u = end[e] + (LAT if q[e] != qi else 0.0)
+                        if u > t:
+                            t, w = u, (e, 0)
+                    last[b] = i
+                if i in mate:
+                    if not idle:
+                        return None
+                    b = min(idle, key=lambda b: big[b][0])
+                    idle.remove(b)
+                    hold[i] = b
+                    if big[b][0] > t:
+                        t, w = big[b][0], (big[b][1], 0)
+                free[qi] = (t + occ[i], i)
+            start[i], end[i], why[i] = t, t + c[i], w
+            if i in second:
+                big[hold[second[i]]] = (end[i] + LAT, i)
+                idle.append(hold[second[i]])
+        i = max(range(n), key=lambda i: end[i])
+        total, pairs = end[i], []
+        while why[i] is not None:
+            if not why[i][1]:
+                pairs.append((why[i][0], i))
+            i = why[i][0]
+        return total, pairs, start, hold, order, key
+    return run, pred, succ, mate, cls, base
+
+
+def find_turns(ops):
+    n = len(ops)
+    run, pred, succ, mate, cls, base = timer(ops, OPT["period"])
+    off, turns, parts = [0.0] * n, {}, {}
+    for i, o in enumerate(ops):
+        off[i] = max([off[j] + ops[j]["c"] + LAT for j in pred[i] if (ops[j]["part"], ops[j]["t"]) == (o["part"], o["t"])], default=0.0)
+        if cls[i] not in turns:
+            parts.setdefault((o["part"], cls[i][2]), []).append(cls[i])
+            turns[cls[i]] = LEAD.get(o["part"], 0.0) + off[i] + 1e-3 * o["cls"][1]
+    for i in range(n - 1, -1, -1):
+        if not ops[i]["part"]:
+            turns[cls[i]] = min([turns[cls[j]] + base[j] - LAT for j in succ[i]], default=0.0) - ops[i]["c"]
+    seen = {}
+    for i in sorted(mate):
+        w = (ops[i]["part"], ops[i]["t"])
+        if ops[i]["t"] <= 1 or w[0][0] == "o":
+            turns[cls[i]] += 0.55 * seen.get(w, 0)
+            turns[cls[mate[i]]] = turns[cls[i]] + 0.6
+        seen[w] = seen.get(w, 0) + 1
+    rnd = np.random.default_rng(OPT["seed"])
+    got = run(turns)
+    best = (got[0], turns)
+    for it in range(OPT["tries"]):
+        r = [float(x) for x in rnd.random(6)]
+        j, i = got[1][int(r[0] * len(got[1]))]
+        key, new = got[5], dict(turns)
+        more = 0.5 * r[2] if r[2] > 0.5 else 0.0
+        if r[4] < 0.2:
+            a, sign = (i, -1) if r[1] < 0.5 else (j, 1)
+            for w in parts[(ops[a]["part"], cls[a][2])]:
+                if r[5] >= 0.5 or sign * (w[1] - cls[a][1]) >= 0:
+                    new[w] += sign * (key[i] - key[j] + 1e-3 + 2 * r[2] ** 2)
+        elif r[1] < 0.5:
+            todo, count = [(i, key[j] - 1e-4 - more)], 0
+            while todo and count < 40:
+                a, l = todo.pop()
+                count += 1
+                if key[a] > l:
+                    new[cls[a]] = min(new[cls[a]], l - base[a])
+                    todo += [(p, l - 1e-4) for p in pred[a]]
+        else:
+            new[cls[j]] = key[i] + 1e-4 + more - base[j]
+        g2 = run(new)
+        if g2 is not None and g2[0] <= got[0] - OPT["heat"] * max(0.03, 1.0 - it / OPT["tries"]) * math.log(1.0 - r[3]):
+            turns, got = new, g2
+            if got[0] < best[0]:
+                best = (got[0], turns)
+    return best[1]
+
+
+def schedule(ops, turns):
+    total, pairs, start, hold, order, key = timer(ops, OPT["period"])[0](turns)
+    REAL.clear()
+    for i, b in hold.items():
+        REAL[ops[i]["any"]] = BIGB[b]
     last, other = {}, {}
     for i in order:
         o = ops[i]
@@ -812,8 +1001,9 @@ SEMQ = {"V": "vv", "S": "ss", "P": "pp", "G": "gg"}
 def plan(nE):
     if nE in _CACHE:
         return _CACHE[nE]
-    ops = build(nE)
-    order, total = schedule(ops)
+    turns = find_turns(build(nE, OPT["visits"]))
+    ops = build(nE, VIS)
+    order, total = schedule(ops, turns)
     count = {s: 0 for s in SEMQ.values()}
     know, kq, out = {}, {}, []
     for i in order:
@@ -822,7 +1012,7 @@ def plan(nE):
         mine = kq.setdefault(q, {})
         waits = {}
         if q != "N":
-            for j in sorted(o["D"], key=lambda j: -ops[j]["start"]):
+            for j in sorted(o["D"] - o["O"], key=lambda j: -ops[j]["start"]):
                 s, v = ops[j]["ev"]
                 if mine.get(s, 0) >= v:
                     continue

@@ -59,7 +59,7 @@ _b("fl", [128, 32], F32)
 _b("cs", [128, 1], BF)
 _b("cint", [128, 2], I32)
 for _n in ("ones", "eye", "neye", "blk", "blk1", "dm32", "p0", "n0", "c2048", "cm256", "cm1k", "ktile", "ptile", "wmat",
-           "s64k", "neye7", "rm", "m2k", "m64", "dcon", "ncon", "e15", "vrow"):
+           "s64k", "neye7", "m2k", "m64", "dcon", "ncon", "e15", "vrow"):
     _b(_n, [128, 128], BF)
 for _j in (4, 8, 12, 16):
     _b("cmf%d" % _j, [128, 128], BF)
@@ -76,7 +76,7 @@ _b("kcon", [8, 256], BF)
 _b("kval", [128, 16], BF)
 _b("b64", [128, 24], BF)
 _b("b4k", [128, 48], BF)
-for _n in ("r2", "rmn"):
+for _n in ("r2", "rm", "rmn", "zero"):
     _b(_n, [128, 256], BF)
 for _n in ("sr", "lf"):
     _b(_n, [128, 2048], BF)
@@ -121,19 +121,19 @@ _CACHE = {}
 CY, PCY, GATH, SCAT = 0.00083 * 1.1, 0.00042 * 1.1, 1.5, 3.5
 VOV, SOV, POV, LAT = 0.04, 0.04, 0.02, 0.12
 OPT = {
-    "onv": ("y0", "y1", "p7", "p5"),
+    "onv": ("p7", "p5"),
     "relu": (),
     "rows": {"f1": 8, "e1": 8},
     "gl": 32,
     "srv": 6,
     "al": 32,
     "tabs": 4,
-    "tries": 20000, "period": 35.0, "seed": 0, "heat": 0.5, "visits": 3,
+    "tries": (6000, 12000), "starts": 3, "period": 33.0, "seed": 0, "heat": 0.3, "visits": 3,
 }
-LEAD = {"b0": -6, "n0": -16, "n1": -9, "x0": -9, "x1": -5.4, "y0": -6.6, "y1": -3.2, "p0": 0, "p1": 0.7, "p2": 1.5, "p3": 3,
-        "z0": 0.9, "z1": 1.6, "z2": 3.1, "z3": 4.6, "g0": 2.5, "g1": 4.5, "g2": 6.4, "g3": 8.8, "d0": 4.4, "d1": 6.2, "d2": 8, "d3": 10.4,
-        "m0": 7, "m1": 9, "m2": 11, "m3": 13, "s0": 10.5, "s1": 11.7, "s2": 14, "s3": 15.5, "v0": 11.4, "v1": 19.5, "c0": 20,
-        "f0": 14, "t0": 15, "u0": 21, "e0": 21, "a0": 22, "w0": 30.3, "f1": 17.5, "t1": 18.6, "u1": 25, "e1": 24.5, "a1": 26, "w1": 33, "o0": 35}
+LEAD = {"b0": -6, "n0": -9, "n1": -6, "x0": -8.6, "x1": -6, "y0": -5.2, "y1": -2.6, "p0": 0, "p1": 0.4, "p2": 1.4, "p3": 3,
+        "z0": 0.8, "z1": 1.6, "z2": 3, "z3": 5, "g0": 2.3, "g1": 4.4, "g2": 6.5, "g3": 8.5, "d0": 3.7, "d1": 6, "d2": 7.6, "d3": 9.7,
+        "m0": 6.8, "m1": 9, "m2": 10.5, "m3": 12.6, "s0": 10.4, "s1": 12, "s2": 13.7, "s3": 14.9, "v0": 11, "v1": 15.5, "c0": 17,
+        "f0": 14.2, "t0": 15, "u0": 20, "e0": 20.2, "a0": 21, "w0": 28.6, "f1": 17, "t1": 17.8, "u1": 22.5, "e1": 22.6, "a1": 23.4, "w1": 31.2, "o0": 33}
 REAL = {}
 R64, R256 = 1.5 * 2 ** 29, 1.5 * 2 ** 31
 
@@ -321,87 +321,84 @@ def build(nE, vis):
         else:
             ts(S("parw", 16 + 512 * j, 528 + 512 * j), S(b, 0, 512), 0.0, A.max, 256.0, A.min)
     part[0] = ""
-    iota(full("io2"), [[0, 16], [1, 16]], 0, 0)
-    fill(full("zx"), 0.0)
-    cp(S("zx", 15, 143, 16), S("blk", 0, 128, 16))
+
+    def flat(out, c):
+        iota(out, [[0, width(out)]], c, 0)
+
+    def mark(out, a, pattern, base, cm, c):
+        asel(out, S(a, 0, width(out), 1, out[4]), pattern, A.not_equal, base, cm, float(c))
+
+    def times(out, a, c):
+        act(out, a, AF.Identity, None, float(c))
+
+    flat(full("zero"), 0)
+    flat(full("zx"), 0)
+    times(S("zx", 15, 143, 16), S("blk", 0, 128, 16), 1)
     if OPT["relu"]:
-        ts(full("zx2"), full("zx"), 2.0, A.mult)
-        ts(full("zxn"), full("zx"), -1.0, A.mult)
-    ts(NEYE, EYE, -1.0, A.mult)
-    ts(full("m2k"), EYE, -2048.0, A.mult)
-    ts(full("dm32"), EYE, 32.0, A.mult)
-    tt(full("dm32"), full("dm32"), BLK, A.subtract)
-
-    def own8(out, o):
-        asel(out, S("ones", 0, 128, 1, out[4]), [[-1, 8], [0, 16]], A.is_equal, -o, 1)
-
-    own8(S("ex", 0, 128, 1, 8), 0)
-    cp(full("exf"), S("ex", 0, 128, 1, 8))
+        times(full("zx2"), full("zx"), 2)
+        times(full("zxn"), full("zx"), -1)
+    for name, c in (("m2k", -2048), ("neye", -1), ("s64k", 65536), ("m64", -64), ("neye7", -2.0 ** -7)):
+        mark(full(name), "zero", [[-1, 128]], 0, 1, c)
+    times(full("blk1"), BLK, -1)
+    mark(full("dm32"), "blk1", [[-1, 128]], 0, 1, 31)
+    GRP = [[-1, 8], [0, 16]]
+    mark(full("exf"), "zero", GRP, 0, 1, 1)
     cp(full("limf"), full("limi"))
     mm([(S("pt0", 0, 2), full("exf"), full("limf"), True, True), (S("pt0", 2, 3), full("wmat"), S("c2048", 0, 1), True, True)])
-    cp(full("thb"), S("pt0", 0, 2))
-    cp(full("thc0"), S("pt0", 0, 1))
-    ts(UCOL, S("pt0", 2, 3), -0.5, A.mult)
+    times(full("thb"), S("pt0", 0, 2), 1)
+    times(UCOL, S("pt0", 2, 3), -0.5)
     for e in range(2):
         iota(S("ae", 1024 * e, 1024 * e + 1024), [[0, 1024]], 0, 0)
         asel(S("af", 1024 * e, 1024 * e + 1024), S("ae", 1024 * e, 1024 * e + 1024), [[-1, 8], [-16, 8], [0, 16]], A.not_equal, -8 * e, 1, -256.0)
         asel(S("lf", 1024 * e, 1024 + 896 * e), S("af", 1024 * e, 1024 + 896 * e), [[-1, 8 - e], [-16, 8], [0, 16]], A.not_equal, -8 * e - 1, 1, 256.0)
-    cp(S("lf", 1920, 2048), S("af", 1920, 2048))
-    ts(full("p0"), S("sr", 0, 128), 256.0, A.mult)
-    ts(full("n0"), S("sr", 0, 128), -256.0, A.mult)
-    fill(full("cm256"), -256.0)
-    for e, w in enumerate((1.0, 2.0, -1.0)):
-        ts(S("b64", 8 * e, 8 * e + 8), S("blk", 0, 128, 16), 64.0 * w, A.mult)
+    times(S("lf", 1920, 2048), S("af", 1920, 2048), 1)
+    times(full("p0"), S("sr", 0, 128), 256)
+    times(full("n0"), S("sr", 0, 128), -256)
+    flat(full("cm256"), -256)
+    ROW = [[0, 16], [1, 16]]
+    for e, w in enumerate((1, 2, -1)):
+        times(S("b64", 8 * e, 8 * e + 8), S("blk", 0, 128, 16), 64 * w)
         for j in range(2):
-            ts(S("b4k", 16 * e + 8 * j, 16 * e + 8 * j + 8), S("blk", 0, 128, 16), 4096.0 * w, A.mult)
-    ts(full("s64k"), EYE, 65536.0, A.mult)
-    cp(full("ktile"), S("io2", 0, 128))
-    ts(full("rm"), full("ktile"), 0.5, A.subtract, -1e9, A.mult)
-    ts(full("rmn"), full("io2"), 0.5, A.subtract, 1e9, A.mult)
-    ts(full("r2"), full("io2"), 1.0, A.not_equal)
-    fill(full("z8"), 0.0)
-    cp(S("z8", 15, 143, 16, 8), S("eye", 0, 8, 1, 8))
+            times(S("b4k", 16 * e + 8 * j, 16 * e + 8 * j + 8), S("blk", 0, 128, 16), 4096 * w)
+    iota(full("ktile"), [[0, 8], [1, 16]], 0, 0)
+    flat(full("rm"), 1 - 2 ** 24)
+    mark(full("rm"), "rm", ROW, 0, 0, 1e9)
+    flat(full("rmn"), 2 ** 24 - 1)
+    mark(full("rmn"), "rmn", ROW, 0, 0, -1e9)
+    asel(full("r2"), full("zero"), ROW, A.is_equal, -1, 0, 1.0)
+    mark(full("z8"), "zero", [[1, 144]], -15, -16, 1)
     iota(S("io1", 32, 40), [[16, 8]], 0, 0)
     ts(S("ptile", 0, 8), S("io1", 32, 40), K16, A.add, 16.0, A.mult)
-    fill(full("cm1k"), -1024.0)
+    flat(full("cm1k"), -1024)
     for n in sorted(set(OPT["rows"].values())):
-        ts(full("vrow"), full("ktile"), 16.0 - n, A.is_ge)
-        ts(full("ckf%d" % n), full("vrow"), 2.0 ** 20, A.mult)
-        tt(full("vrow"), full("vrow"), BLK, A.mult)
-        ts(full("cmf%d" % n), full("vrow"), -64.0, A.mult)
+        asel(full("ckf%d" % n), S("zero", 0, 128), [[0, 8], [-1, 16]], A.is_ge, 15 - n, 0, 2.0 ** 20)
+        asel(full("vrow"), BLK, [[0, 8], [1, 16]], A.is_ge, n - 16, 0)
+        times(full("cmf%d" % n), full("vrow"), -64)
         for j in range(2):
-            ts(S("cme%d" % n, 128 * j, 128 * j + 128), full("vrow"), -4096.0, A.mult)
-    ts(full("m64"), EYE, -64.0, A.mult)
-    ts(DCOL, K16, 4112.0, A.add)
+            times(S("cme%d" % n, 128 * j, 128 * j + 128), full("vrow"), -4096)
+    act(DCOL, K16, AF.Identity, 4112.0)
     cp(S("thi", 0, 1), S("thb", 1, 2))
     ts(S("thi", 1, 2), S("thi", 0, 1), 4, A.arith_shift_right)
     ts(S("thi", 2, 3), S("thi", 0, 1), 15, A.bitwise_and)
-    fill(full("kval"), 0.0)
-    ts(S("cols", 6, 7), K16, -256.0, A.mult, 3840.0, A.add)
-    ts(S("kval", 0, 16, 8), S("ones", 0, 2), S("cols", 6, 7), A.mult)
-    cp(S("cols", 8, 10), S("thi", 1, 3))
-    ts(S("kval", 1, 16, 8), S("ones", 0, 2), S("cols", 8, 9), A.mult, -65536.0, A.mult)
-    ts(S("kval", 2, 16, 8), S("ones", 0, 2), S("cols", 9, 10), A.mult, -4096.0, A.mult)
-    fill(S("kval", 3, 4), -1088.0)
-    fill(S("kval", 11, 12), 69632.0)
-    fill(S("kval", 12, 13), 2112.0)
+    mark(full("kval"), "zero", [[1, 16]], -3, 0, -1088)
+    mark(full("kval"), "kval", [[1, 16]], -11, 0, 69632)
+    mark(full("kval"), "kval", [[1, 16]], -12, 0, 2112)
+    for e in range(2):
+        act(S("kval", 8 * e, 8 * e + 1), K16, AF.Identity, 3840.0, -256.0)
+        ts(S("kval", 8 * e + 1, 8 * e + 2), S("thi", 1, 2), -65536.0, A.mult)
+        ts(S("kval", 8 * e + 2, 8 * e + 3), S("thi", 2, 3), -4096.0, A.mult)
     mm([(S("pt1", 128 * e, 128 * e + 128, 1, 8), S("kval", 8 * e, 8 * e + 8), EYE, True, True) for e in range(2)])
-    cp(full("kcon"), S("pt1", 0, 256, 1, 8))
-    for name, o in (("ea", 0), ("eb", 16)):
-        own8(S("ex", 0, 128, 1, 32), o)
-        own8(S("ex", 128, 256, 1, 32), o + 8)
-        ts(S("ex", 0, 128, 1, 32), S("ex", 0, 128, 1, 32), 64.0, A.mult)
-        tt(full(name), S("ex", 0, 128, 1, 32), S("ex", 128, 256, 1, 32), A.add)
-    fill(full("zb"), 0.0)
-    cp(S("zb", 15, 143, 16, 32), S("eb", 0, 128, 16, 32))
-    ts(full("eb7"), full("eb"), 2.0 ** -7, A.mult)
-    ts(full("neb7"), full("eb"), -2.0 ** -7, A.mult)
-    ts(full("neye7"), EYE, -2.0 ** -7, A.mult)
-    ts(full("dcon"), full("ktile"), K16, A.is_ge, 128.0, A.mult)
-    ts(full("dcon"), full("dcon"), -16.5, A.add)
-    fill(S("dcon", 15, 128, 16), 0.0)
-    ts(full("ncon"), S("tcon", 0, 128), -2112.0, A.add)
-    ts(full("e15"), full("ktile"), 15.0, A.is_equal)
+    times(full("kcon"), S("pt1", 0, 256, 1, 8), 1)
+    for name, o, c in (("ea", 0, 1), ("eb7", 16, 2.0 ** -7), ("neb7", 16, -2.0 ** -7)):
+        mark(full(name), "zero", GRP, -o, 1, 64 * c)
+        mark(full(name), name, GRP, -o - 8, 1, c)
+    mark(full("zb"), "zero", [[1, 144]], 256 - 15, -16, 64)
+    mark(full("zb"), "zb", [[1, 144]], 384 - 15, -16, 1)
+    ts(full("vrow"), full("ktile"), K16, A.is_ge, 128.0, A.mult)
+    act(full("vrow"), full("vrow"), AF.Identity, -16.5)
+    mark(full("dcon"), "vrow", [[0, 8], [1, 16]], -15, 0, 0)
+    act(full("ncon"), S("tcon", 0, 128), AF.Identity, -2112.0)
+    mark(full("e15"), "zero", [[0, 8], [1, 16]], -15, 0, 1)
 
     def send(what, t, h):
         c = TB[h][:2]
@@ -441,7 +438,7 @@ def build(nE, vis):
         place(t, s, um, S("t2", *c), S("t3", *c), S("c1", *c), S("hl", *c))
         part[0] = "y%d" % h
         for a in range(c1 - GL, c0 - 1, -GL):
-            move("x%d" % (a // 32), S("x%d" % (t % 2), 16 * a, 16 * (a + GL)), IND("claimw", 0, window(t), "hl", a, a + GL))
+            move("%s%d" % ("x" if t else "first", a // 32), S("x%d" % (t % 2), 16 * a, 16 * (a + GL)), IND("claimw", 0, window(t), "hl", a, a + GL))
 
     def st_pgather(t, n):
         for a in range(ZB[n][0], ZB[n][1], GL):
@@ -466,7 +463,7 @@ def build(nE, vis):
                 e = min(c1, a + OPT.get("al", 64))
                 act(S("ad", 16 * a, 16 * e), S("d", 16 * a, 16 * e), AF.Abs)
             acc(D, [(sx(k), S("ad", X + k, X2, 16)) for k in range(16)])
-        ts(dep, D, full("thc%d" % t), A.is_lt)
+        ts(dep, D, full("thc%d" % t) if t else S("thb", 0, 1), A.is_lt)
         acc(D, [(full("dm32"), dep)])
         act(S("sg", *c), D, AF.Sign, -16.5)
         part[0] = "v%d" % min(h for h in range(len(TB)) if TB[h][0] <= c0)
@@ -538,10 +535,11 @@ def build(nE, vis):
         key, mid = S(b, 0, 128, 1, L), S("mm_", *c)
         nv, own, lots = distances(t, h, mid, "af", 1024.0, 128, "b64")
         part[0] = "t%d" % h
-        first = [(key, S("eye", 0, L), full("ktile")), (key, S("sg", *c), full("s64k"))] + own
+        first, then = [(key, S("eye", 0, L), full("ktile"))] + own, [(key, S("sg", *c), full("s64k"))]
         if nv:
-            first += [(key, S("eye", 0, L), full("ckf%d" % nv)), (key, mid, full("cmf%d" % nv))]
-        pile(first, *lots)
+            first.append((key, S("eye", 0, L), full("ckf%d" % nv)))
+            lots[0] = [(key, mid, full("cmf%d" % nv))] + lots[0]
+        pile(first, then, *lots)
         scan(S("km%d" % h, 0, 128, 1, L), S("rm", 0, 128, 1, L), key, 0.0, A.max, A.min)
         m, r, k = S("km%d" % h, 15, 128, 16, L), S("rr%d" % h, 0, 8, 1, L), S("cc%d" % h, 0, 8, 1, L)
         ts(r, m, R64, A.add, -R64, A.add)
@@ -876,15 +874,25 @@ def timer(ops, period):
     second = {j: i for i, j in mate.items()}
     c, occ, q, fix = [[o[k] for o in ops] for k in ("c", "occ", "q", "fix")]
     cls, base = [o["cls"] + (min(o["t"], 1),) for o in ops], [period * o["t"] for o in ops]
+    above = [0] * n
+    for i in range(n):
+        far = 0
+        for j in pred[i]:
+            far |= above[j]
+        above[i] = far
+        for j in pred[i]:
+            above[i] |= 1 << j
+        pred[i] = [j for j in pred[i] if not far >> j & 1]
     pl = [[(j, 0.0 if j in ops[i]["O"] else LAT) for j in pred[i]] for i in range(n)]
+    arcs = [(j, i) for i in range(n) for j in pred[i]]
+    both = list(zip(cls, base))
 
     def run(turns):
-        key = [turns[cls[i]] + base[i] for i in range(n)]
-        for i in range(n):
-            for j in pred[i]:
-                if key[j] >= key[i]:
-                    key[i] = key[j] + 1e-5
-        order = sorted(range(n), key=lambda i: key[i])
+        key = [turns[w] + b for w, b in both]
+        for j, i in arcs:
+            if key[j] >= key[i]:
+                key[i] = key[j] + 1e-5
+        order = np.argsort(key, kind="stable").tolist()
         end, why, start = [0.0] * n, [None] * n, [0.0] * n
         free, last, big, hold, idle = {}, {}, [(0.0, -1)] * len(BIGB), {}, list(range(len(BIGB)))
         for i in order:
@@ -917,12 +925,14 @@ def timer(ops, period):
                 big[hold[second[i]]] = (end[i] + LAT, i)
                 idle.append(hold[second[i]])
         i = max(range(n), key=lambda i: end[i])
-        total, pairs = end[i], []
+        total, pairs = end[i] + more * (end[marks[1]] - end[marks[0]]), []
         while why[i] is not None:
             if not why[i][1]:
                 pairs.append((why[i][0], i))
             i = why[i][0]
         return total, pairs, start, hold, order, key
+    marks = [max(i for i in range(n) if ops[i]["t"] == t) for t in range(2)]
+    more = VIS - 1 - ops[-1]["t"]
     return run, pred, succ, mate, cls, base
 
 
@@ -946,11 +956,20 @@ def find_turns(ops):
             turns[cls[mate[i]]] = turns[cls[i]] + 0.6
         seen[w] = seen.get(w, 0) + 1
     rnd = np.random.default_rng(OPT["seed"])
+    found = [_anneal(ops, run, pred, parts, cls, base, turns, rnd, OPT["tries"][0], OPT["heat"]) for k in range(OPT["starts"])]
+    turns = min(found, key=lambda f: f[0])[1]
+    return _anneal(ops, run, pred, parts, cls, base, turns, rnd, OPT["tries"][1], OPT["heat"] / 2)[1]
+
+
+def _anneal(ops, run, pred, parts, cls, base, turns, rnd, tries, heat):
     got = run(turns)
     best = (got[0], turns)
-    for it in range(OPT["tries"]):
-        r = [float(x) for x in rnd.random(6)]
-        j, i = got[1][int(r[0] * len(got[1]))]
+    for it in range(tries):
+        r = rnd.random(6).tolist()
+        pairs = got[1]
+        if it % 3 == 0:
+            pairs = [p for p in pairs if ops[p[1]]["t"] == 0] or pairs
+        j, i = pairs[int(r[0] * len(pairs))]
         key, new = got[5], dict(turns)
         more = 0.5 * r[2] if r[2] > 0.5 else 0.0
         if r[4] < 0.2:
@@ -969,11 +988,11 @@ def find_turns(ops):
         else:
             new[cls[j]] = key[i] + 1e-4 + more - base[j]
         g2 = run(new)
-        if g2 is not None and g2[0] <= got[0] - OPT["heat"] * max(0.03, 1.0 - it / OPT["tries"]) * math.log(1.0 - r[3]):
+        if g2 is not None and g2[0] <= got[0] - heat * max(0.03, 1.0 - it / tries) * math.log(1.0 - r[3]):
             turns, got = new, g2
             if got[0] < best[0]:
                 best = (got[0], turns)
-    return best[1]
+    return best
 
 
 def schedule(ops, turns):

@@ -7,10 +7,7 @@ AF = ActivationFunctionType
 VIS = 5
 BUF = {}
 SEMAPHORES = ["vv", "ss", "pp", "gg"]
-ZB = [(192, 256, "pz0", 0), (128, 192, "pz1", 0), (64, 128, "pz0", 128), (0, 64, "pz1", 128)]
-TB = [(128, 256, "pz0", 256), (0, 128, "pz1", 256)]
 BIGB = ["pa0", "pa1", "pa2", "pa3"]
-TBANK = ["pt0", "pt1"]
 
 
 def _b(name, shape, dtype="float32", where="sbuf"):
@@ -19,95 +16,97 @@ def _b(name, shape, dtype="float32", where="sbuf"):
 
 BF, F16, F32, I32, U16 = "bfloat16", "float16", "float32", "int32", "uint16"
 CW = 8512
-PW = 4128
-_b("claimw", [128, CW], BF)
-_b("parw", [128, PW], BF)
+PW = (4160, 6240)
+WIDE = {"y": 128, "v": 384}
+_b("dq", [128, 768], BF)
+for _z in range(2):
+    _b("claimw%d" % _z, [128, CW], BF)
+    _b("parw%d" % _z, [128, PW[_z]], BF)
+    _b("km%d" % _z, [128, 256], F32)
+    _b("pm%d" % _z, [128, 512], F32)
+    _b("tt%d" % _z, [128, 256], F32)
+    _b("rr%d" % _z, [128, 48], F32)
+    _b("ct%d" % _z, [128, 16], BF)
+    _b("ca%d" % _z, [128, 32], BF)
+    for _n in ("wmat", "en"):
+        _b("%s%d" % (_n, _z), [128, 128], BF)
+    _b("dup%d" % _z, [128, 128], F32)
+    _b("exf%d" % _z, [8, 128], F32)
 _b("yb0", [128, 256], BF)
 for _t in range(VIS):
     if _t:
         _b("yb%d" % _t, [128, 256], F16)
     for _n in ("vb", "yn", "vn"):
-        _b("%s%d" % (_n, _t), [128, 256], F16)
-    _b("thc%d" % _t, [128, 1], F32)
+        _b("%s%d" % (_n, _t), [128, 2 * WIDE[_n[0]]], F16)
+    _b("thc%d" % _t, [128, 2], F32)
 for _n in ("x0", "x1", "pr", "d", "ad", "la", "af", "ae"):
     _b(_n, [128, 4096], BF)
 for _n in ("mx", "mn"):
     _b(_n, [128, 4096], F16)
-for _n in ("um0", "um1", "t1", "t2", "t3", "t4", "t5"):
+for _n in ("um0", "um1", "t1", "t2", "t3", "t4", "t5", "whoi"):
     _b(_n, [128, 256], I32)
+for _n in ("pari", "parj"):
+    _b(_n, [128, 512], I32)
 for _n in ("hl", "zl", "vl"):
     _b(_n, [128, 256], U16)
-for _n in ("c1", "c2", "vm", "yvf", "prd", "ypf"):
+for _n in ("c1", "c2", "vm", "yvf"):
     _b(_n, [128, 256], F32)
-for _n in ("dep", "sg", "yy", "yeb", "tcon", "adat"):
+for _n in ("prd", "ypf"):
+    _b(_n, [128, 512], F32)
+for _n in ("dep", "yy", "yeb", "zy", "mk", "b2", "dcon", "wcon", "r2", "rm", "rmn", "zero", "jt"):
     _b(_n, [128, 256], BF)
-for _n in ("mm_", "par16", "vh"):
+for _n in ("adat", "zz", "ee", "parb", "zr", "b3"):
+    _b(_n, [128, 512], BF)
+for _n in ("mm_", "vh"):
     _b(_n, [128, 256], F16)
-for _j in range(3):
-    _b("km%d" % _j, [128, 128], F32)
-    _b("pm%d" % _j, [128, 512], F32)
-    _b("tt%d" % _j, [128, 256], F32)
-    _b("rr%d" % _j, [128, 48], F32)
-    _b("cc%d" % _j, [128, 48], BF)
-_b("own", [128, 16], F16)
-_b("ini", [128, 16], BF)
-_b("kt8", [8, 256], BF)
 _b("kt32", [32, 256], BF)
 _b("yl", [128, 16], U16)
 _b("ol", [128, 32], U16)
-_b("fl", [128, 32], F32)
-_b("cs", [128, 1], BF)
-_b("cint", [128, 2], I32)
-for _n in ("ones", "eye", "neye", "blk", "blk1", "dm32", "p0", "n0", "c2048", "cm256", "cm1k", "ktile", "ptile", "wmat",
-           "s64k", "neye7", "m2k", "m64", "dcon", "ncon", "e15", "vrow"):
+_b("zo", [128, 16], U16)
+_b("cs", [128, 2], BF)
+_b("cint", [128, 4], I32)
+for _n in ("ones", "eye", "neye", "blk", "blk1", "c2048", "cm256", "cm1k", "ptile", "e18", "m64", "vrow"):
     _b(_n, [128, 128], BF)
-for _j in (4, 8, 12, 16):
-    _b("cmf%d" % _j, [128, 128], BF)
-    _b("ckf%d" % _j, [128, 128], BF)
+for _j in (4, 8):
+    _b("cmf%d" % _j, [128, 256], BF)
+    _b("ckf%d" % _j, [128, 256], BF)
     _b("cme%d" % _j, [128, 256], BF)
 for _n in ("zx", "zx2", "zxn"):
     _b(_n, [128, 144], BF)
-_b("z8", [8, 144], BF)
-_b("zb", [32, 144], BF)
-for _n in ("ea", "eb", "eb7", "neb7"):
-    _b(_n, [32, 128], BF)
-_b("ex", [32, 256], BF)
-_b("kcon", [8, 256], BF)
-_b("kval", [128, 16], BF)
-_b("b64", [128, 24], BF)
+_b("eb", [32, 128], BF)
+_b("kcon", [8, 512], BF)
+_b("kval", [128, 32], BF)
+_b("b64", [128, 48], BF)
+_b("ktile", [128, 256], BF)
 _b("b4k", [128, 48], BF)
-for _n in ("r2", "rm", "rmn", "zero"):
-    _b(_n, [128, 256], BF)
-for _n in ("sr", "lf"):
+for _n in ("tb", "lf"):
     _b(_n, [128, 2048], BF)
-_b("exf", [8, 128], F32)
 _b("io1", [128, 128], I32)
-_b("io2", [128, 256], I32)
 _b("e16", [128, 16], F32)
-_b("coll", [128, 16], F32)
 _b("cols", [128, 16], F32)
 _b("wti", [128, 1], I32)
 _b("wtf", [128, 1], F32)
 _b("limi", [8, 2], I32)
 _b("limf", [8, 2], F32)
-_b("thb", [128, 2], F32)
-_b("thi", [128, 4], I32)
-_b("whoi", [128, 256], I32)
-_b("pari", [128, 256], I32)
-for _n in BIGB + TBANK + ["pz0", "pz1"]:
+_b("thb", [128, 4], F32)
+_b("thi", [128, 8], I32)
+for _n in BIGB + ["pz0", "pz1", "pt0", "pt1"]:
     _b(_n, [128, 512], F32, "psum")
 
-for _n in ("lim", "who", "est", "wt", "par", "claim0", "claim1", "again", "yv", "ye0", "ye1", "ye2", "yp0", "yp1"):
+for _n in ("lim", "wt"):
     SEMAPHORES.append("l_" + _n)
+for _z in range(2):
+    for _n in ("who", "est", "par", "tab", "claim", "again", "yv", "ye", "yp0", "yp1"):
+        SEMAPHORES.append("l_%s%d" % (_n, _z))
 for _t in range(1, VIS):
-    for _h in range(len(TB)):
+    for _h in range(2):
         for _k in "yv":
             SEMAPHORES += ["a%s%d%d" % (_k, _t, _h), "o%s%d%d" % (_k, _t, _h)]
 
 PACK = {}
 SCRATCH = {}
 _ROOM = {}
-_KEEP = ("whoi", "pari", "ypf", "yvf", "yeb", "wti", "limi", "hl", "zl", "vl", "yl", "ol", "adat", "yy")
+_KEEP = ("whoi", "pari", "parb", "ypf", "yvf", "yeb", "wti", "limi", "hl", "zl", "vl", "yl", "ol", "zo", "adat", "yy", "zz", "zr", "zy", "mk", "ct0", "ct1", "ca0", "ca1")
 for _n, (_w, _sh, _d) in BUF.items():
     if _w == "sbuf" and _n not in _KEEP and _n[:2] not in ("yb", "vb", "yn", "vn") and _sh[1] <= 512:
         PACK[_n] = ("pack_" + _d, _ROOM.get(_d, 0))
@@ -117,29 +116,37 @@ for _n, (_w, _sh, _d) in BUF.items():
 for _d in _ROOM:
     SCRATCH["pack_" + _d] = ("sbuf", [128, _ROOM[_d]], _d)
 
+HALVES = {"ol": ["ol", "ol0", "ol1"]}
+for _n in HALVES["ol"][1:]:
+    BUF[_n], PACK[_n] = BUF["ol"], ("ol", 0)
 _CACHE = {}
-CY, PCY, GATH, SCAT = 0.00083 * 1.1, 0.00042 * 1.1, 1.5, 3.5
-VOV, SOV, POV, LAT = 0.04, 0.04, 0.02, 0.12
+CY, PCY, GATH, SCAT = 0.00083 * 1.08, 0.00042 * 1.08, 1.56, 3.8
+VOV, SOV, POV, LAT = 0.04, 0.04, 0.02, 0.2
 OPT = {
-    "onv": ("p7", "p5"),
+    "onv": ("p1",),
     "relu": (),
-    "rows": {"f1": 8, "e1": 8},
-    "gl": 32,
-    "srv": 6,
+    "rows": {"f": 4, "e": 4},
+    "gl": {"x": 32, "p": 32, "g": 32},
     "al": 32,
-    "tabs": 4,
-    "tries": (6000, 12000), "starts": 3, "period": 33.0, "seed": 0, "heat": 0.3, "visits": 3,
+    "zv": "VVSSSSSSSS",
+    "job": {0: {"onv": ("p1", "p3", "x1", "x3")}, 9: {"rows": {"f": 8, "e": 8}, "onv": ("p1", "p3")}},
+    "cross": True, "rep": True, "norm": 200, "tol": 1, "at": 5,
+    "apart": (),
+    "direct": (),
+    "sl": (64, 64),
+    "send": (1, 3, 4),
+    "tries": (55000, 40000, 30000), "seed": (2, 0, 0), "heat": (0.35, 0.15, 0.15), "own": (2, 7),
 }
-LEAD = {"b0": -6, "n0": -9, "n1": -6, "x0": -8.6, "x1": -6, "y0": -5.2, "y1": -2.6, "p0": 0, "p1": 0.4, "p2": 1.4, "p3": 3,
-        "z0": 0.8, "z1": 1.6, "z2": 3, "z3": 5, "g0": 2.3, "g1": 4.4, "g2": 6.5, "g3": 8.5, "d0": 3.7, "d1": 6, "d2": 7.6, "d3": 9.7,
-        "m0": 6.8, "m1": 9, "m2": 10.5, "m3": 12.6, "s0": 10.4, "s1": 12, "s2": 13.7, "s3": 14.9, "v0": 11, "v1": 15.5, "c0": 17,
-        "f0": 14.2, "t0": 15, "u0": 20, "e0": 20.2, "a0": 21, "w0": 28.6, "f1": 17, "t1": 17.8, "u1": 22.5, "e1": 22.6, "a1": 23.4, "w1": 31.2, "o0": 33}
+AHEAD = ("n", "x", "y")
+HALF = 16.0
+LEAD = {"n": -12.4, "x": -7.9, "y": -2.5, "p0": 0.0, "q0": 0.3, "z0": 2.0, "g0": 4.5, "d0": 5.5, "p1": 0.7, "q1": 0.4, "z1": 3.4, "g1": 6.5, "d1": 7.8,
+        "m0": 8.5, "s0": 11.3, "m1": 10.3, "s1": 12.5, "v0": 10.0, "v1": 11.0, "c": 11.9, "f": 14.5, "t": 14.5, "u": 20.0, "e": 19.5, "a": 21.0, "h": 26.1, "w": 29.6}
 REAL = {}
 R64, R256 = 1.5 * 2 ** 29, 1.5 * 2 ** 31
 
 
-def S(name, a, b, step=1, p=128):
-    return (name, a, b, step, p)
+def S(name, a, b, step=1, p=128, p0=0):
+    return (name, a, b, step, p, p0)
 
 
 def IND(name, a, b, off, c, d):
@@ -151,13 +158,13 @@ def ap(T, s):
         return T[s[0]][:, s[1]:s[2]].indirect(T[s[3]][:, s[4]:s[5]])
     r, o = PACK.get(s[0], (REAL.get(s[0], s[0]), 0))
     if s[3] == 1:
-        return T[r][0:s[4], o + s[1]:o + s[2]]
-    return T[r][0:s[4], o + s[1]:o + s[2]:s[3]]
+        return T[r][s[5]:s[5] + s[4], o + s[1]:o + s[2]]
+    return T[r][s[5]:s[5] + s[4], o + s[1]:o + s[2]:s[3]]
 
 
 def regs(s):
     if len(s) == 7:
-        return [(s[0], s[1], s[2]), (s[3], s[4], s[5])]
+        return [(s[0], s[1], s[2])] + [(n, s[4], s[5]) for n in HALVES.get(s[3], [s[3]])]
     return [(s[0], s[1], s[2])]
 
 
@@ -171,16 +178,25 @@ def half(*ss):
     return all(BUF[s[0]][2] in (BF, F16, U16) for s in ss)
 
 
+def send_sides(Tto, Tfrom, what):
+    k, t, z = what
+    c = slice(WIDE[k] * z, WIDE[k] * (z + 1))
+    return Tto["%sb%d" % (k, t)][:, c], Tfrom["%sn%d" % (k, t - 1)][:, c]
+
+
+def third(name, a, b):
+    return S(name, 3 * a + 2, 3 * b, 3)
+
+
 def build(nE, vis):
     ops = []
-    GL = OPT["gl"]
     part = ["", 0]
 
-    def add(q, fns, R, W, cost, sem=None, val=0, send=None):
+    def add(q, fns, R, W, cost, sem=None, val=0, send=None, lot=None):
         rr = [r for s in R for r in regs(s)]
         ww = [(s[0], s[1], s[2]) for s in W]
-        offs = [(s[3], s[4], s[5]) for s in W if len(s) == 7]
-        ops.append({"q": q, "f": fns, "R": rr + offs, "W": ww, "c": cost, "sem": sem, "val": val, "send": send, "part": part[0], "t": part[1]})
+        offs = [r for s in W if len(s) == 7 for r in regs(s)[1:]]
+        ops.append({"q": q, "f": fns, "R": rr + offs, "W": ww, "c": cost, "sem": sem, "val": val, "send": send, "part": part[0], "t": part[1], "lot": lot})
         return len(ops) - 1
 
     def vcost(n, f=1.0):
@@ -210,10 +226,8 @@ def build(nE, vis):
         add("V", [f], R, [out], vcost(width(a), 0.5 if half(out, a) else 1.0))
 
     def scan(out, d0, d1, init, op0, op1):
-        R = [d0, d1] + ([init] if isinstance(init, tuple) else [])
-        add("V", [lambda g, T: g.vector.tensor_tensor_scan(out=ap(T, out), data0=ap(T, d0), data1=ap(T, d1),
-                                                           initial=ap(T, init) if isinstance(init, tuple) else init, op0=op0, op1=op1)],
-            R, [out], vcost(width(d1), 0.5 if half(out, d0, d1) else 1.0))
+        add("V", [lambda g, T: g.vector.tensor_tensor_scan(out=ap(T, out), data0=ap(T, d0), data1=ap(T, d1), initial=init, op0=op0, op1=op1)],
+            [d0, d1], [out], vcost(width(d1), 0.5 if half(out, d0, d1) else 1.0))
 
     def fill(out, c):
         add("V", [lambda g, T: g.vector.memset(ap(T, out), c)], [], [out], vcost(width(out), 0.5 if half(out) else 1.0))
@@ -230,26 +244,30 @@ def build(nE, vis):
             return g.scalar.activation(out=ap(T, out), in_=ap(T, a), func=func, **kw)
         add("S", [f], R, [out], max(64, width(a) * (GATH if len(a) == 7 else 1.0)) * CY + SOV)
 
+    def opt(name):
+        return OPT["job"].get(2 * part[1] + (part[0][1:2] == "1"), {}).get(name, OPT[name])
+
     def move(tag, out, a):
-        if tag in OPT["onv"]:
+        if tag in opt("onv"):
             cp(out, a)
         else:
             act(out, a, AF.Copy)
 
-    def mm(groups):
+    def mm(groups, lot=None):
         fns = []
         c = POV
         for (o, l, r, st, sp) in groups:
             fns.append(lambda g, T, o=o, l=l, r=r, st=st, sp=sp: g.tensor.matmul(out=ap(T, o), lhsT=ap(T, l), rhs=ap(T, r), start=st, stop=sp))
             c += max(min(64, width(l)), width(r)) * PCY * (4 if BUF[r[0]][2] == F32 else 1)
-        add("P", fns, [r for (o, l, r2, st, sp) in groups for r in (l, r2)], [x[0] for x in groups], c)
+        add("P", fns, [r for (o, l, r2, st, sp) in groups for r in (l, r2)], [x[0] for x in groups], c, lot=lot)
 
     def acc(out, terms):
         mm([(out, l, r, i == 0, i == len(terms) - 1) for i, (l, r) in enumerate(terms)])
 
     def pile(*lots):
         for n, terms in enumerate(lots):
-            mm([(o, l, r, n == 0 and i == 0, n == len(lots) - 1 and i == len(terms) - 1) for i, (o, l, r) in enumerate(terms)])
+            mm([(o, l, r, n == 0 and i == 0, n == len(lots) - 1 and i == len(terms) - 1) for i, (o, l, r) in enumerate(terms)],
+               None if len(lots) == 1 else "first" if n == 0 else "last" if n == len(lots) - 1 else "more")
 
     def dma(q, sem, pairs, R, W, cost):
         add(q, [lambda g, T, o=o, i=i: (g.sync if q == "Y" else g.scalar).dma_start(o(T), i(T)) for (o, i) in pairs], R, W, cost, sem=sem, val=16 * len(pairs))
@@ -266,9 +284,10 @@ def build(nE, vis):
         return S(name, 0, sh[1], 1, sh[0])
 
     EYE, NEYE, BLK = full("eye"), full("neye"), full("blk")
+    SET = S("blk", 0, 128, 16)
 
-    def sx(k, z="zx", p=128):
-        return S(z, 15 - k, 143 - k, 1, p)
+    def sx(k, z="zx"):
+        return S(z, 15 - k, 143 - k)
 
     turn = [0]
 
@@ -276,51 +295,6 @@ def build(nE, vis):
         turn[0] += 1
         _b("bank%d" % turn[0], [128, 512], F32, "psum")
         return "bank%d" % turn[0]
-
-    dma("Y", "l_par", [(lambda T: T.pari[:], lambda T: T.par[:])], [], [full("pari")], 2.0)
-    dma("Y", "l_est", [(lambda T: T.yb0[:], lambda T: T.est[:])], [], [full("yb0")], 2.0)
-    dma("Y", "l_wt", [(lambda T: T.wti[:], lambda T: T.wt[:])], [], [full("wti")], 2.0)
-    dma("Y", "l_who", [(lambda T: T.whoi[:], lambda T: T.who[:])], [], [full("whoi")], 2.0)
-    dma("S", "l_claim0", [(lambda T: T.claimw[:, 0:2048], lambda T: T.claim[:, 0:2048])], [], [S("claimw", 0, 2048)], 3.0)
-    dma("S", "l_claim1", [(lambda T: T.claimw[:, 2048:4096], lambda T: T.claim[:, 2048:4096])], [], [S("claimw", 2048, 4096)], 4.0)
-    dma("Y", "l_lim", [(lambda T: T.limi[:], lambda T: T.lim[:])], [], [full("limi")], 2.0)
-    dma("Y", "l_again", [(lambda T: T.claimw[:, 4096:8192], lambda T: T.claim[:]), (lambda T: T.claimw[:, 8192:CW], lambda T: T.claim[:, 0:CW - 8192])],
-        [S("claimw", 0, 4096)], [S("claimw", 4096, CW)], 5.0)
-    fill(full("ones"), 1.0)
-    iota(S("io1", 0, 16), [[-1, 16]], 16, 1)
-    asel(full("blk1"), full("ones"), [[-16, 8], [0, 16]], A.is_ge, 0, 1)
-    asel(BLK, full("blk1"), [[16, 8], [0, 16]], A.is_ge, 15, -1)
-    asel(EYE, full("ones"), [[-1, 128]], A.is_equal, 0, 1)
-    ts(S("io1", 16, 32), S("io1", 0, 16), 15, A.bitwise_and)
-    ts(full("e16"), S("io1", 16, 32), 0.0, A.is_equal)
-    K16 = S("cols", 0, 1)
-    DCOL = S("cols", 2, 3)
-    UCOL = S("cols", 3, 4)
-    cp(K16, S("io1", 16, 17))
-    ts(full("vb0"), full("whoi"), -2048.0, A.add)
-    ts(full("par16"), full("pari"), -2048.0, A.add)
-    cp(full("wtf"), full("wti"))
-    ts(full("wmat"), BLK, full("wtf"), A.mult)
-    fill(full("c2048"), 2048.0)
-    for k in range(16):
-        if k < OPT["srv"]:
-            ts(S("sr", 128 * k, 128 * k + 128), BLK, S("e16", k, k + 1), A.mult)
-        else:
-            act(S("sr", 128 * k, 128 * k + 128), BLK, AF.Identity, None, S("e16", k, k + 1))
-    ts(S("cols", 5, 6), K16, -256.0, A.mult, 2048.0, A.add)
-    for e in range(2):
-        act(S("tcon", 128 * e, 128 * e + 128), full("ones"), AF.Identity, None, S("cols", 5, 6))
-    part[0] = "b0"
-    for j in range(8):
-        b = bank()
-        mm([x for e in range(2) for x in ((S(b, 256 * e, 256 * e + 256), S("sr", 128 * (2 * j + e), 128 * (2 * j + e + 1)), full("par16"), True, False),
-                                           (S(b, 256 * e, 256 * e + 256), EYE, full("tcon"), False, True))])
-        if j % 2 and j < 2 * OPT["tabs"]:
-            act(S("la", 512 * j, 512 * j + 512), S(b, 0, 512), AF.Relu)
-            ts(S("parw", 16 + 512 * j, 528 + 512 * j), S("la", 512 * j, 512 * j + 512), 256.0, A.min)
-        else:
-            ts(S("parw", 16 + 512 * j, 528 + 512 * j), S(b, 0, 512), 0.0, A.max, 256.0, A.min)
-    part[0] = ""
 
     def flat(out, c):
         iota(out, [[0, width(out)]], c, 0)
@@ -331,80 +305,154 @@ def build(nE, vis):
     def times(out, a, c):
         act(out, a, AF.Identity, None, float(c))
 
-    flat(full("zero"), 0)
-    flat(full("zx"), 0)
-    times(S("zx", 15, 143, 16), S("blk", 0, 128, 16), 1)
+    def both(q, sem, out, in_, W, cost, R=()):
+        dma(q, sem, [(lambda T, e=e: out(T, e), lambda T, e=e: in_(T, e)) for e in range(2)], list(R), [W], cost)
+
+    for z in range(2):
+        part[0] = "l%d" % z
+        r, c = slice(64 * z, 64 * z + 64), slice(128 * z, 128 * z + 128)
+        cw = "claimw%d" % z
+        both("Y", "l_par%d" % z, lambda T, e, z=z: T.pari[64 * e:64 * e + 64, 256 * z:256 * z + 256], lambda T, e, z=z: T.par[4 * z:4 * z + 4, :],
+             S("pari", 256 * z, 256 * z + 256), 2.0)
+        both("Y", "l_est%d" % z, lambda T, e, c=c: T.yb0[64 * e:64 * e + 64, c], lambda T, e, r=r: T.est[r, 128 * e:128 * e + 128], S("yb0", 128 * z, 128 * z + 128), 2.0)
+        if not z:
+            dma("Y", "l_wt", [(lambda T: T.wti[:], lambda T: T.wt[:])], [], [full("wti")], 2.0)
+        both("Y", "l_who%d" % z, lambda T, e, c=c: T.whoi[64 * e:64 * e + 64, c], lambda T, e, r=r: T.who[r, 128 * e:128 * e + 128], S("whoi", 128 * z, 128 * z + 128), 2.0)
+        if not z:
+            dma("Y", "l_lim", [(lambda T: T.limi[:], lambda T: T.lim[:])], [], [full("limi")], 2.0)
+        both("SY"[z], "l_claim%d" % z, lambda T, e, cw=cw: T[cw][64 * e:64 * e + 64, 0:4096], lambda T, e, r=r: T.claim[r, :], S(cw, 0, 4096), 6.0 - z,
+             [S("claimw0", 0, 4096)] if z else [])
+    part[0] = ""
+    fill(full("ones"), 1.0)
+    iota(S("io1", 0, 16), [[-1, 16]], 16, 1)
+    asel(full("blk1"), full("ones"), [[-16, 8], [0, 16]], A.is_ge, 0, 1)
+    asel(BLK, full("blk1"), [[16, 8], [0, 16]], A.is_ge, 15, -1)
+    asel(EYE, full("ones"), [[-1, 128]], A.is_equal, 0, 1)
+    ts(S("io1", 16, 32), S("io1", 0, 16), 15, A.bitwise_and)
+    ts(full("e16"), S("io1", 16, 32), 0.0, A.is_equal)
+    K16 = S("cols", 0, 1)
+    NCOL = S("cols", 1, 2)
+    cp(K16, S("io1", 16, 17))
+    fill(full("zero"), 0.0)
+    fill(full("c2048"), 2048.0)
+    fill(S("tb", 0, 1040), 0.0)
+    for e in range(10):
+        o = S("parw0", 1040 * e, 1040 * e + 1040) if e < 4 else S("parw1", 1040 * (e - 4), 1040 * (e - 3))
+        if OPT["zv"][e] == "V":
+            fill(o, 0.0)
+        elif OPT["zv"][e] == "G":
+            flat(o, 0)
+        else:
+            act(o, S("tb", 0, 1040), AF.Copy)
+    for e in range(2):
+        fill(S("cols", 4, 5, 1, 64, 64 * e), 4096.0 - 2048 * e)
+        fill(S("cols", 5, 6, 1, 64, 64 * e), 6192.0 - 2048 * e)
+    cp(full("wtf"), full("wti"))
+    cp(full("limf"), full("limi"))
+    for z in range(2):
+        part[0] = "b%d" % z
+        c = (256 * z, 256 * z + 256)
+        ts(third("vb0", 128 * z, 128 * z + 128), S("whoi", 128 * z, 128 * z + 128), -2048.0, A.add)
+        for e in range(2):
+            ts(S("parj", *c, 1, 64, 64 * e), S("pari", *c, 1, 64, 64 * e), (4032, 63)[e], A.bitwise_and)
+        cp(S("parb", *c), S("parj", *c))
+        dma("Y", "l_tab%d" % z, [(lambda T, e=e, h=h, z=z: T["parw%d" % z][64 * h + e:64 * h + 64:16, 16 + 2048 * (z > h):4112 + 2048 * (z > h)],
+                                  lambda T, e=e, c=c: T.parb[64 * e:64 * e + 64, c[0]:c[1]]) for e in range(2) for h in range(2)],
+            [S("parb", *c)], [S("parw%d" % z, 16, 4112 + 2048 * z)], 3.2)
+        part[0] = ""
+        mark(full("dup%d" % z), "zero", [[0, 2], [-1, 64]], -64 * z, 1, 1)
+        mark(full("exf%d" % z), "zero", [[0, 2], [-1, 4], [0, 16]], -4 * z, 1, 1)
+        b = "pt%d" % z
+        mm([(S(b, 0, 1), full("dup%d" % z), full("wtf"), True, True), (S(b, 2, 4), full("exf%d" % z), full("limf"), True, True)])
+        ts(full("wmat%d" % z), BLK, S(b, 0, 1), A.mult)
+        times(S("thb", z, 4, 2), S(b, 2, 4), 1)
+        acc(S(b, 4, 5), [(full("wmat%d" % z), S("c2048", 0, 1))])
+        times(S("cols", 2 + z, 3 + z), S(b, 4, 5), -0.5)
+    for z in range(2):
+        part[0] = "r%d" % z
+        r, cw = slice(64 * z, 64 * z + 64), "claimw%d" % z
+        dma("Y", "l_again%d" % z, [(lambda T, e=e, a=a, b=b, cw=cw, r=r: T[cw][64 * e:64 * e + 64, a:b], lambda T, a=a, b=b, r=r: T.claim[r, 0:b - a])
+                                   for e in range(2) for a, b in ((4096, 8192), (8192, CW))],
+            [S("claimw0", 4096, CW)] if z else [S("claimw1", 0, 4096), S("parw1", 16, 17)], [S(cw, 4096, CW)], 5.5)
+    part[0] = ""
+    fill(full("zx"), 0.0)
+    times(S("zx", 15, 143, 16), SET, 1)
     if OPT["relu"]:
         times(full("zx2"), full("zx"), 2)
         times(full("zxn"), full("zx"), -1)
-    for name, c in (("m2k", -2048), ("neye", -1), ("s64k", 65536), ("m64", -64), ("neye7", -2.0 ** -7)):
+    for name, c in (("neye", -1), ("e18", 2 ** 18), ("m64", -64)):
         mark(full(name), "zero", [[-1, 128]], 0, 1, c)
-    times(full("blk1"), BLK, -1)
-    mark(full("dm32"), "blk1", [[-1, 128]], 0, 1, 31)
-    GRP = [[-1, 8], [0, 16]]
-    mark(full("exf"), "zero", GRP, 0, 1, 1)
-    cp(full("limf"), full("limi"))
-    mm([(S("pt0", 0, 2), full("exf"), full("limf"), True, True), (S("pt0", 2, 3), full("wmat"), S("c2048", 0, 1), True, True)])
-    times(full("thb"), S("pt0", 0, 2), 1)
-    times(UCOL, S("pt0", 2, 3), -0.5)
     for e in range(2):
-        iota(S("ae", 1024 * e, 1024 * e + 1024), [[0, 1024]], 0, 0)
-        asel(S("af", 1024 * e, 1024 * e + 1024), S("ae", 1024 * e, 1024 * e + 1024), [[-1, 8], [-16, 8], [0, 16]], A.not_equal, -8 * e, 1, -256.0)
-        asel(S("lf", 1024 * e, 1024 + 896 * e), S("af", 1024 * e, 1024 + 896 * e), [[-1, 8 - e], [-16, 8], [0, 16]], A.not_equal, -8 * e - 1, 1, 256.0)
-    times(S("lf", 1920, 2048), S("af", 1920, 2048), 1)
-    times(full("p0"), S("sr", 0, 128), 256)
-    times(full("n0"), S("sr", 0, 128), -256)
-    flat(full("cm256"), -256)
+        asel(S("lf", 1024 * e, 1024 * e + 1024), S("tb", 0, 1024), [[-1, 8], [-16, 8], [0, 16]], A.not_equal, -8 * e, 1, -256.0)
+        asel(S("lf", 1024 * e, 1024 + 896 * e), S("lf", 1024 * e, 1024 + 896 * e), [[-1, 8 - e], [-16, 8], [0, 16]], A.not_equal, -8 * e - 1, 1, 256.0)
+    fill(full("cm256"), -256.0)
     ROW = [[0, 16], [1, 16]]
     for e, w in enumerate((1, 2, -1)):
-        times(S("b64", 8 * e, 8 * e + 8), S("blk", 0, 128, 16), 64 * w)
         for j in range(2):
-            times(S("b4k", 16 * e + 8 * j, 16 * e + 8 * j + 8), S("blk", 0, 128, 16), 4096 * w)
-    iota(full("ktile"), [[0, 8], [1, 16]], 0, 0)
-    flat(full("rm"), 1 - 2 ** 24)
-    mark(full("rm"), "rm", ROW, 0, 0, 1e9)
+            times(S("b4k", 16 * e + 8 * j, 16 * e + 8 * j + 8), SET, 4096 * w)
+    times(full("b64"), full("b4k"), 1.0 / 64)
+    iota(S("ktile", 0, 128), [[0, 8], [1, 16]], 0, 0)
+    fill(S("ktile", 128, 256), 0.0)
+    mark(full("rm"), "zero", ROW, 0, 0, 1e9)
     flat(full("rmn"), 2 ** 24 - 1)
-    mark(full("rmn"), "rmn", ROW, 0, 0, -1e9)
+    fill(S("rmn", 0, 256, 16), -1e9)
     asel(full("r2"), full("zero"), ROW, A.is_equal, -1, 0, 1.0)
-    mark(full("z8"), "zero", [[1, 144]], -15, -16, 1)
     iota(S("io1", 32, 40), [[16, 8]], 0, 0)
     ts(S("ptile", 0, 8), S("io1", 32, 40), K16, A.add, 16.0, A.mult)
-    flat(full("cm1k"), -1024)
-    for n in sorted(set(OPT["rows"].values())):
-        asel(full("ckf%d" % n), S("zero", 0, 128), [[0, 8], [-1, 16]], A.is_ge, 15 - n, 0, 2.0 ** 20)
+    iota(S("io1", 48, 64), [[1, 16]], 0, 0)
+    cp(full("zo"), S("io1", 48, 64))
+    ts(S("mk", 0, 128), S("ktile", 0, 128), K16, A.is_equal, 64.0, A.mult)
+    times(S("mk", 128, 256), S("mk", 0, 128), 1.0 / 64)
+    rows = sorted(set(n for o in [OPT] + list(OPT["job"].values()) for n in o.get("rows", {}).values()) - {0})
+    if rows:
+        flat(full("cm1k"), -1024)
+    for n in rows:
+        asel(full("ckf%d" % n), full("zero"), [[0, 16], [-1, 16]], A.is_ge, 15 - n, 0, 2.0 ** 20)
         asel(full("vrow"), BLK, [[0, 8], [1, 16]], A.is_ge, n - 16, 0)
-        times(full("cmf%d" % n), full("vrow"), -64)
         for j in range(2):
             times(S("cme%d" % n, 128 * j, 128 * j + 128), full("vrow"), -4096)
-    act(DCOL, K16, AF.Identity, 4112.0)
-    cp(S("thi", 0, 1), S("thb", 1, 2))
-    ts(S("thi", 1, 2), S("thi", 0, 1), 4, A.arith_shift_right)
-    ts(S("thi", 2, 3), S("thi", 0, 1), 15, A.bitwise_and)
-    mark(full("kval"), "zero", [[1, 16]], -3, 0, -1088)
-    mark(full("kval"), "kval", [[1, 16]], -11, 0, 69632)
-    mark(full("kval"), "kval", [[1, 16]], -12, 0, 2112)
-    for e in range(2):
+        ts(full("cmf%d" % n), full("cme%d" % n), 1.0 / 64, A.mult)
+    cp(S("thi", 0, 2), S("thb", 2, 4))
+    ts(S("thi", 2, 4), S("thi", 0, 2), 4, A.arith_shift_right)
+    ts(S("thi", 4, 6), S("thi", 0, 2), 15, A.bitwise_and)
+    mark(full("kval"), "zero", [[0, 2], [1, 16]], -3, 0, -1088)
+    mark(full("kval"), "kval", [[0, 2], [1, 16]], -11, 0, 69632)
+    mark(full("kval"), "kval", [[0, 2], [1, 16]], -12, 0, 2112)
+    for e in range(4):
         act(S("kval", 8 * e, 8 * e + 1), K16, AF.Identity, 3840.0, -256.0)
-        ts(S("kval", 8 * e + 1, 8 * e + 2), S("thi", 1, 2), -65536.0, A.mult)
-        ts(S("kval", 8 * e + 2, 8 * e + 3), S("thi", 2, 3), -4096.0, A.mult)
-    mm([(S("pt1", 128 * e, 128 * e + 128, 1, 8), S("kval", 8 * e, 8 * e + 8), EYE, True, True) for e in range(2)])
-    times(full("kcon"), S("pt1", 0, 256, 1, 8), 1)
-    for name, o, c in (("ea", 0, 1), ("eb7", 16, 2.0 ** -7), ("neb7", 16, -2.0 ** -7)):
-        mark(full(name), "zero", GRP, -o, 1, 64 * c)
-        mark(full(name), name, GRP, -o - 8, 1, c)
-    mark(full("zb"), "zero", [[1, 144]], 256 - 15, -16, 64)
-    mark(full("zb"), "zb", [[1, 144]], 384 - 15, -16, 1)
-    ts(full("vrow"), full("ktile"), K16, A.is_ge, 128.0, A.mult)
-    act(full("vrow"), full("vrow"), AF.Identity, -16.5)
-    mark(full("dcon"), "vrow", [[0, 8], [1, 16]], -15, 0, 0)
-    act(full("ncon"), S("tcon", 0, 128), AF.Identity, -2112.0)
-    mark(full("e15"), "zero", [[0, 8], [1, 16]], -15, 0, 1)
+        ts(S("kval", 8 * e + 1, 8 * e + 2), S("thi", 2 + e // 2, 3 + e // 2), -65536.0, A.mult)
+        ts(S("kval", 8 * e + 2, 8 * e + 3), S("thi", 4 + e // 2, 5 + e // 2), -4096.0, A.mult)
+    b = bank()
+    mm([(S(b, 128 * e, 128 * e + 128, 1, 8), S("kval", 8 * e, 8 * e + 8), EYE, True, True) for e in range(4)])
+    times(full("kcon"), S(b, 0, 512, 1, 8), 1)
+    mark(full("eb"), "zero", [[-1, 8], [0, 16]], -16, 1, 64)
+    mark(full("eb"), "eb", [[-1, 8], [0, 16]], -24, 1, 1)
+    for e in range(2):
+        o = S("en%d" % e, 0, 128, 1, 32)
+        mark(o, "zero", [[0, 2], [-1, 4], [-1000, 16]], -4 * e, 1, 64)
+        mark(o, o[0], [[0, 2], [-1, 4], [-1000, 16]], 992 - 4 * e, 1, 1)
+    times(NCOL, S("e16", 0, 1), -64)
+    iota(full("jt"), [[0, 4], [-16, 2], [1, 32]], 0, 0)
+    ts(full("dcon"), full("jt"), K16, A.is_ge, 8192.0, A.mult)
+    fill(S("dcon", 31, 256, 32), 0.0)
+    iota(full("wcon"), [[0, 4], [-16, 2], [0, 32]], 31, 0)
+    ts(full("wcon"), full("wcon"), K16, A.subtract)
+    fill(S("wcon", 0, 256, 32), 4192.0)
+    for e in range(2):
+        fill(S("dq", e, 768, 3), float(e))
+    asel(full("b2"), full("zero"), [[16, 8], [0, 32]], A.is_gt, 0, -1, -1.0)
+    asel(full("b2"), full("b2"), [[16, 8], [0, 32]], A.is_ge, 15, -1)
+    fill(S("b2", 31, 256, 32), 0.0)
+    if OPT["rep"]:
+        for e in range(2):
+            mark(S("b3", 256 * e, 256 * e + 256), "zero", [[-32, 4], [0, 2], [-1, 32]], 0, 1, 64 ** (1 - e))
+        fill(S("b3", 31, 512, 32), 0.0)
 
-    def send(what, t, h):
-        c = TB[h][:2]
-        key = "%s%d%d" % (what, t + 1, h)
-        i = add("G", None, [S("%sn%d" % (what, t), *c)], [], 1.0, sem="o" + key, val=nE, send=(what, t + 1, h))
-        add("N", None, [], [S("%sb%d" % (what, t + 1), *c)], 2.0, sem="a" + key, val=nE, send=i)
+    def send(what, t, z):
+        c = (WIDE[what] * z, WIDE[what] * (z + 1))
+        key = "%s%d%d" % (what, t + 1, z)
+        i = add("G", None, [S("%sn%d" % (what, t), *c)], [], OPT["send"][0] + OPT["send"][2] * (key == "v10"), sem="o" + key, val=nE, send=(what, t + 1, z))
+        add("N", None, [], [S("%sb%d" % (what, t + 1), *c)], OPT["send"][1], sem="a" + key, val=nE, send=i)
 
     def place(t, s, um, a, b, c, out):
         tt(a, s, um, A.mult)
@@ -417,211 +465,247 @@ def build(nE, vis):
             tt(c, s, b, A.add)
             ts(out, c, 77.0 * t, A.add)
 
-    def window(t):
-        return 4096 if t == 0 else CW
+    def claims(t, z, off, a, n):
+        return IND("claimw%d" % z, 0, 4096 if t == 0 else CW, off, a, a + n)
 
-    def st_names(t, h):
-        c = TB[h][:2]
-        ts(S("vl", *c), S("vb%d" % t, *c), 2048.0, A.add)
+    def block(z, n):
+        return 128 * z + 64 * n, 128 * z + 64 * n + 64, ("pz%d", "pt%d")[n] % z, 256 * n
 
-    def st_hash(t, h):
-        c0, c1, b, o = TB[h]
-        c, L = (c0, c1), c1 - c0
+    def st_hash(t, z):
+        c0, c1, b = 128 * z, 128 * z + 128, "pz%d" % z
+        c = (c0, c1)
+        part[0] = "n%d" % z
+        ts(S("vl", *c), third("vb%d" % t, *c), S("cols", 4, 5) if z else 2048.0, A.add)
+        part[0] = "x%d" % z
         um = S("um%d" % (t % 2), *c)
-        U, s = S(b, o, o + L), S(b, o + L, o + 2 * L)
-        mm([(s, EYE, S("vb%d" % t, *c), True, False), (s, EYE, S("c2048", 0, L), False, True), (U, full("wmat"), S("yb%d" % t, *c), True, True)])
+        U, s = S(b, 256, 384), S(b, 384, 512)
+        acc(s, [(EYE, third("vb%d" % t, *c)), (EYE, full("c2048"))])
+        acc(U, [(full("wmat%d" % z), S("yb%d" % t, *c))])
         if t == 0:
             cp(S("t1", *c), U)
         else:
-            ts(S("t1", *c), U, UCOL, A.add)
+            ts(S("t1", *c), U, S("cols", 2 + z, 3 + z), A.add)
         ts(um, S("t1", *c), 4095, A.bitwise_and)
         place(t, s, um, S("t2", *c), S("t3", *c), S("c1", *c), S("hl", *c))
-        part[0] = "y%d" % h
-        for a in range(c1 - GL, c0 - 1, -GL):
-            move("%s%d" % ("x" if t else "first", a // 32), S("x%d" % (t % 2), 16 * a, 16 * (a + GL)), IND("claimw", 0, window(t), "hl", a, a + GL))
+        part[0] = "y%d" % z
+        n = OPT["gl"]["x"]
+        for a in range(c0, c1, n):
+            move("x%d" % ((a - c0) // 32), S("x%d" % (t % 2), 16 * a, 16 * (a + n)), claims(t, z, "hl", a, n))
 
-    def st_pgather(t, n):
-        for a in range(ZB[n][0], ZB[n][1], GL):
-            move("p%d" % (a // 32), S("pr", 16 * a, 16 * (a + GL)), IND("parw", 16, 4112, "vl", a, a + GL))
-
-    def st_z(t, n):
-        c0, c1, b, o = ZB[n]
+    def st_z(t, z, n):
+        c0, c1, b, o = block(z, n)
         c, L, X, X2 = (c0, c1), c1 - c0, 16 * c0, 16 * c1
-        p, D = S(b, o, o + L), S(b, o + L, o + 2 * L)
-        v, dep = S("vb%d" % t, *c), S("dep", *c)
+        p, D, v = S(b, o, o + 192, 3), S(b, o + 192, o + 256), third("vb%d" % t, *c)
+        part[0] = "p%d%d" % (z, n)
+        n1, n2 = OPT["gl"]["p"], OPT["gl"]["g"]
+        for a in range(c0, c1, n1):
+            move("p%d" % (a % 128 // 32), S("pr", 16 * a, 16 * (a + n1)), IND("parw%d" % z, 16, 4112 + 2048 * z, "vl", a, a + n1))
+        part[0] = "q%d%d" % (z, n)
+        mm([(S(b, o + 1, o + 192, 3), NEYE, v, True, False), (S(b, o + 1, o + 192, 3), NEYE, S("c2048", 0, L), False, True), (S(b, o + 2, o + 192, 3), EYE, v, True, True)])
+        part[0] = "z%d%d" % (z, n)
         acc(p, [(sx(k), S("pr", X + k, X2, 16)) for k in range(16)])
         place(t, p, S("um%d" % (t % 2), *c), S("t4", *c), S("t5", *c), S("c2", *c), S("zl", *c))
-        part[0] = "g%d" % n
-        for a in range(c0, c1, GL):
-            tt(S("d", 16 * a, 16 * (a + GL)), IND("claimw", 0, window(t), "zl", a, a + GL), S("x%d" % (t % 2), 16 * a, 16 * (a + GL)), A.subtract)
-        part[0] = "d%d" % n
-        if n in OPT["relu"]:
-            ts(S("ad", X, X2), S("d", X, X2), 0.0, A.max)
-            acc(D, [(sx(k, "zxn"), S("d", X + k, X2, 16)) for k in range(16)] + [(sx(k, "zx2"), S("ad", X + k, X2, 16)) for k in range(16)])
-        else:
-            for a in range(c0, c1, OPT.get("al", 64)):
-                e = min(c1, a + OPT.get("al", 64))
-                act(S("ad", 16 * a, 16 * e), S("d", 16 * a, 16 * e), AF.Abs)
+        part[0] = "g%d%d" % (z, n)
+        for a in range(c0, c1, n2):
+            if a % 128 // 32 in opt("apart"):
+                act(S("d", 16 * a, 16 * (a + n2)), claims(t, z, "zl", a, n2), AF.Copy)
+            else:
+                tt(S("d", 16 * a, 16 * (a + n2)), claims(t, z, "zl", a, n2), S("x%d" % (t % 2), 16 * a, 16 * (a + n2)), A.subtract)
+        part[0] = "d%d%d" % (z, n)
+        if opt("apart"):
+            for a in range(16 * c0, 16 * c1, 512):
+                e = S("d", a, a + 512)
+                if a % 2048 // 512 in opt("apart"):
+                    e = S(bank(), 0, 512)
+                    acc(e, [(NEYE, S("x%d" % (t % 2), a, a + 512)), (EYE, S("d", a, a + 512))])
+                act(S("ad", a, a + 512), e, AF.Abs)
             acc(D, [(sx(k), S("ad", X + k, X2, 16)) for k in range(16)])
-        ts(dep, D, full("thc%d" % t) if t else S("thb", 0, 1), A.is_lt)
-        acc(D, [(full("dm32"), dep)])
-        act(S("sg", *c), D, AF.Sign, -16.5)
-        part[0] = "v%d" % min(h for h in range(len(TB)) if TB[h][0] <= c0)
-        tt(p, p, v, A.subtract)
-        tt(S("vm", *c), p, dep, A.mult)
-        acc(p, [(EYE, v), (full("m2k"), dep)])
-        tt(S("vn%d" % t, *c), p, S("vm", *c), A.add)
+        elif n in opt("relu"):
+            ts(S("ad", X, X2), S("d", X, X2), 0.0, A.max)
+            pile([(D, sx(k, "zxn"), S("d", X + k, X2, 16)) for k in range(16)], [(D, sx(k, "zx2"), S("ad", X + k, X2, 16)) for k in range(16)])
+        else:
+            for a in range(c0, c1, OPT["al"]):
+                act(S("ad", 16 * a, 16 * (a + OPT["al"])), S("d", 16 * a, 16 * (a + OPT["al"])), AF.Abs)
+            acc(D, [(sx(k), S("ad", X + k, X2, 16)) for k in range(16)])
+        ts(third("dq", *c), D, S("thc%d" % t if t else "thb", z, z + 1), A.is_lt)
 
-    def st_m(t, n):
-        c0, c1, b, o = ZB[n]
+    def st_names(t, z, n):
+        c0, c1, b, o = block(z, n)
+        part[0] = "v%d%d" % (z, n)
+        scan(S("vn%d" % t, 3 * c0, 3 * c1), S("dq", 3 * c0, 3 * c1), S(b, o, o + 192), 0.0, A.mult, A.add)
+
+    def st_m(t, z, n):
+        c0, c1, b, o = block(z, n)
         c, L, X, X2 = (c0, c1), c1 - c0, 16 * c0, 16 * c1
         x = "x%d" % (t % 2)
-        o += L
-        mm([(S(b, o, o + 1), full("p0"), S("sg", c0, c0 + 1), True, True), (S(b, o + 1, o + 2), full("n0"), S("sg", c0, c0 + 1), True, True)])
-        move("i%d" % n, S("ini", 2 * n, 2 * n + 2), S(b, o, o + 2))
+        part[0] = "m%d%d" % (z, n)
         for l in range(c0, c1, 32):
-            a, e = bank(), int(l + 32 == c1)
-            gr = [(S(a, k, 512, 16), S("lf", 128 * k, 128 * k + 128), S("sg", l, l + 32), True, True) for k in range(15)]
-            gr += [(S(a, 15, 512, 16), S("lf", 1920, 2048), S("sg", l, l + 32), True, False),
-                   (S(a, 15, 512 - 16 * e, 16), full("p0"), S("sg", l + 1, l + 33 - e), False, False),
-                   (S(a, 15, 512, 16), EYE, S("cm256", 0, 32), False, True)]
-            mm(gr)
-            move("l%d" % (l // 32), S("la", 16 * l, 16 * l + 512), S(a, 0, 512))
-        part[0] = "s%d" % n
-        scan(S("mx", X, X2), S(x, X, X2), S("la", X, X2), S("ini", 2 * n, 2 * n + 1), A.max, A.add)
-        scan(S("mn", X, X2), S(x, X, X2), S("la", X, X2), S("ini", 2 * n + 1, 2 * n + 2), A.min, A.subtract)
-        w = S(b, o, o + L)
+            a = bank()
+            mm([(S(a, k, 512, 16), S("lf", 128 * k, 128 * k + 128), third("dq", l, l + 32), True, k < 15) for k in range(16)] +
+               [(S(a, 15, 512, 16), EYE, S("cm256", 0, 32), False, True)])
+            if l % 128 // 32 in opt("direct"):
+                e = (16 * l, 16 * l + 512)
+                scan(S("mx", *e), S(x, *e), S(a, 0, 512), -1.0, A.max, A.add)
+                scan(S("mn", *e), S(x, *e), S(a, 0, 512), 256.0, A.min, A.subtract)
+            else:
+                move("l%d" % (l % 128 // 32), S("la", 16 * l, 16 * l + 512), S(a, 0, 512))
+        part[0] = "s%d%d" % (z, n)
+        for a in range(X, X2, 16 * OPT["sl"][n]):
+            if a % 2048 // 512 in opt("direct"):
+                continue
+            e = a + 16 * OPT["sl"][n]
+            scan(S("mx", a, e), S(x, a, e), S("la", a, e), -1.0, A.max, A.add)
+            scan(S("mn", a, e), S(x, a, e), S("la", a, e), 256.0, A.min, A.subtract)
+        w = S(b, o + 192, o + 256)
         acc(w, [(EYE, S("mx", X + 15, X2, 16)), (EYE, S("mn", X + 15, X2, 16))])
         ts(S("mm_", *c), w, 0.5, A.mult, 1023.75, A.add)
 
-    def st_count(t, h):
-        if t == vis - 1:
-            return
-        b = TBANK[-1]
-        acc(S(b, 500, 501), [(S("dep", 128, 256), S("ones", 0, 1)), (S("dep", 0, 128), S("ones", 0, 1))])
-        move("c", full("cs"), S(b, 500, 501))
-        acc(S(b, 501, 502), [(full("ones"), full("cs"))])
-        cp(S("cint", 0, 1), S(b, 501, 502))
-        ts(S("cint", 1, 2), S("cint", 0, 1), 31, A.bitwise_and)
-        tt(full("thc%d" % (t + 1)), S("cint", 1, 2), S("thb", 0, 1), A.add)
+    def st_count(t):
+        part[0] = "c1"
+        a, b = S(bank(), 0, 2), S(bank(), 0, 2)
+        acc(a, [(third("dq", 128, 256), S("ones", 0, 2)), (third("dq", 0, 128), S("ones", 0, 2))])
+        move("c", full("cs"), a)
+        acc(b, [(full("ones"), full("cs"))])
+        cp(S("cint", 0, 2), b)
+        ts(S("cint", 2, 4), S("cint", 0, 2), 31, A.bitwise_and)
+        tt(full("thc%d" % (t + 1)), S("cint", 2, 4), S("thb", 0, 2), A.add)
 
-    def distances(t, h, mid, out, bias, w, weights):
-        c0, c1, zb, zo = TB[h]
-        L, X, x, b = c1 - c0, 16 * c0, "x%d" % (t % 2), TBANK[h]
-        K, nv, n = 512 // L, OPT["rows"].get(part[0], 0), width(full(weights)) // 3
-        own = [(S(b, k, w, 16, L), S(x, X + k, X + 16 * L, 16), S(weights, 2 * n, 3 * n)) for k in range(16 - nv, 16)]
+    def distances(t, z, mid, out, bias, w, weights):
+        L, X, x, b = 128, 2048 * z, "x%d" % (t % 2), "pt%d" % z
+        K, nv, n = 512 // L, opt("rows")[part[0][0]], width(full(weights)) // 3
+        own = [(S(b, k, w, 16), S(x, X + k, X + 16 * L, 16), S(weights, 2 * n, 3 * n)) for k in range(16 - nv, 16)]
         lots = []
         if nv:
-            m = S(zb, zo, zo + L)
-            acc(m, [(EYE, mid)] + ([(EYE, S("cm1k", 0, L))] if bias else []))
+            m = S("pz%d" % z, 0, L)
+            acc(m, [(EYE, mid)] + ([(EYE, full("cm1k"))] if bias else []))
         for q in range(0, 16 - nv, K):
-            a, gr, e1 = bank(), [], min(K, 16 - nv - q)
-            for e in range(e1):
+            a, gr = bank(), []
+            for e in range(K):
                 o = S(a, L * e, L * e + L)
                 gr += [(o, EYE, S(x, X + q + e, X + 16 * L, 16), True, False), (o, NEYE, mid, False, True)]
             mm(gr)
-            act(S(out, X + L * q, X + L * (q + e1)), S(a, 0, L * e1), AF.Abs, bias)
-            lots.append([(S(b, k, w, 16, L), S(out, X + L * k, X + L * k + L), S(weights, 0, n)) for k in range(q, q + e1)])
+            act(S(out, X + L * q, X + L * (q + K)), S(a, 0, L * K), AF.Abs, bias)
+            lots.append([(S(b, k, w, 16), S(out, X + L * k, X + L * k + L), S(weights, 0, n)) for k in range(q, q + K)])
         for k in range(16 - nv, 16):
             tt(S(out, X + L * k, X + L * k + L), S(x, X + k, X + 16 * L, 16), m, A.max)
         for j, q in enumerate(range(16 - nv, 16, 4)):
-            lots.insert(min(2 * j, len(lots)), [(S(b, k, w, 16, L), S(out, X + L * k, X + L * k + L), S(weights, n, 2 * n)) for k in range(q, q + 4)])
+            lots.insert(min(2 * j, len(lots)), [(S(b, k, w, 16), S(out, X + L * k, X + L * k + L), S(weights, n, 2 * n)) for k in range(q, q + 4)])
         return nv, own, lots
 
-    def st_truth(t, h):
-        c = TB[h][:2]
-        L, b = c[1] - c[0], TBANK[h]
-        Q, q = L // 16, c[0] // 16
-        key, mid = S(b, 0, 128, 1, L), S("mm_", *c)
-        nv, own, lots = distances(t, h, mid, "af", 1024.0, 128, "b64")
-        part[0] = "t%d" % h
-        first, then = [(key, S("eye", 0, L), full("ktile"))] + own, [(key, S("sg", *c), full("s64k"))]
+    def st_truth(t, z):
+        c, b, q = (128 * z, 128 * z + 128), "pt%d" % z, 8 * z
+        key, mid = S(b, 0, 256), S("mm_", *c)
+        part[0] = "f%d" % z
+        nv, own, lots = distances(t, z, mid, "af", 1024.0, 256, "b64")
+        part[0] = "t%d" % z
+        first = [(key, EYE, full("ktile"))] + own + [(S(b, e, e + 128), third("dq", *c), full("e18")) for e in (0, 128)]
         if nv:
-            first.append((key, S("eye", 0, L), full("ckf%d" % nv)))
+            first.append((key, EYE, full("ckf%d" % nv)))
             lots[0] = [(key, mid, full("cmf%d" % nv))] + lots[0]
-        pile(first, then, *lots)
-        scan(S("km%d" % h, 0, 128, 1, L), S("rm", 0, 128, 1, L), key, 0.0, A.max, A.min)
-        m, r, k = S("km%d" % h, 15, 128, 16, L), S("rr%d" % h, 0, 8, 1, L), S("cc%d" % h, 0, 8, 1, L)
-        ts(r, m, R64, A.add, -R64, A.add)
-        tt(k, m, r, A.subtract)
-        acc(S(b, 128, 128 + L, 1, 8), [(k, S("eye", 0, L, 1, L))])
-        move("k%d" % h, S("kt8", c[0], c[1], 1, 8), S(b, 128, 128 + L, 1, 8))
-        acc(S(b, 256, 256 + Q), [(EYE, S("ptile", 0, Q))] + [(sx(a, "z8", 8), S("kt8", c[0] + a, c[1], 16, 8)) for a in range(16)])
-        cp(S("yl", q, q + Q), S(b, 256, 256 + Q))
-        move("y%d" % h, S("yy", *c), IND("x%d" % (t % 2), 16 * c[0], 16 * c[1], "yl", q, q + Q))
-        part[0] = "u%d" % h
-        e = S(b, 384, 384 + L)
+        pile(first, *lots)
+        scan(full("km%d" % z), full("rm"), key, 0.0, A.max, A.min)
+        tt(S("ct%d" % z, 0, 8), S("km%d" % z, 15, 128, 16), S("km%d" % z, 143, 256, 16), A.subtract)
+        tt(S("zy", *c), IND("ct%d" % z, 0, 8, "zo", 0, 8), S("mk", 128, 256), A.mult)
+        acc(S(b, 448, 456), [(EYE, S("ptile", 0, 8)), (S("zy", *c), SET)])
+        cp(S("yl", q, q + 8), S(b, 448, 456))
+        move("y", S("yy", *c), IND("x%d" % (t % 2), 16 * c[0], 16 * c[1], "yl", q, q + 8))
+        part[0] = "u%d" % z
+        e = S("pz%d" % z, 128, 256)
         acc(e, [(EYE, S("yb%d" % t, *c)), (EYE, S("yy", *c))])
         ts(S("yn%d" % t, *c), e, 0.5, A.mult, 511.75 if t else 1023.75, A.add)
         if t < vis - 1:
-            send("y", t, h)
+            send("y", t, z)
 
-    def st_ask(t, h):
-        c = TB[h][:2]
-        L, b = c[1] - c[0], TBANK[h]
-        Q, q = L // 16, c[0] // 16
-        ts(S("vh", *c), S("vb%d" % t, *c), 1.0 / 64, A.mult, 1120.5078125, A.add)
-        nv, own, lots = distances(t, h, S("yy", *c), "ae", None, 256, "b4k")
-        part[0] = "a%d" % h
-        key, hi, lo = S(b, 0, 256, 1, L), S(b, 0, 128, 1, L), S(b, 128, 256, 1, L)
-        first = [(key, S("ones", 0, L, 1, 8), full("kcon"))] + own
-        names = [(lo, S("vh", *c), full("m64")), (lo, S("vb%d" % t, *c), EYE), (hi, S("vh", *c), EYE)]
+    def st_ask(t, z):
+        c, b, c2 = (128 * z, 128 * z + 128), "pt%d" % z, 256 * z
+        part[0] = "e%d" % z
+        v = third("vb%d" % t, *c)
+        ts(S("vh", *c), v, 1.0 / 64, A.mult, 1120.5078125, A.add)
+        nv, own, lots = distances(t, z, S("yy", *c), "ae", None, 256, "b4k")
+        part[0] = "a%d" % z
+        key, hi, lo = S(b, 0, 256), S(b, 0, 128), S(b, 128, 256)
+        first = [(key, S("ones", 0, 128, 1, 8), S("kcon", c2, c2 + 256, 1, 8))] + own
+        names = [(lo, S("vh", *c), full("m64")), (lo, v, EYE), (hi, S("vh", *c), EYE)]
         if nv:
             first.append((key, S("yy", *c), full("cme%d" % nv)))
             lots[-1] = lots[-1] + names
         else:
             first += names
         pile(first, *lots)
-        pm, t2 = "pm%d" % h, S("tt%d" % h, 1, 256, 1, L)
-        scan(S(pm, 0, 256, 1, L), S("rmn", 0, 256, 1, L), key, 0.0, A.min, A.max)
-        tt(t2, S(b, 1, 256, 1, L), S(pm, 0, 255, 1, L), A.min)
-        scan(S(pm, 257, 512, 1, L), S("r2", 1, 256, 1, L), t2, 0.0, A.mult, A.max)
-        m, r, k = S(pm, 15, 512, 16, L), S("rr%d" % h, 16, 48, 1, L), S("cc%d" % h, 16, 48, 1, L)
+        pm, t2, k = "pm%d" % z, S("tt%d" % z, 1, 256), full("ca%d" % z)
+        scan(S(pm, 0, 256), full("rmn"), key, 0.0, A.min, A.max)
+        tt(t2, S(b, 1, 256), S(pm, 0, 255), A.min)
+        scan(S(pm, 257, 512), S("r2", 1, 256), t2, 0.0, A.mult, A.max)
+        m, r = S(pm, 15, 512, 16), S("rr%d" % z, 16, 48)
         ts(r, m, R256, A.add, -R256, A.add)
         tt(k, m, r, A.subtract)
-        acc(S(b, 256, 256 + L, 1, 32), [(k, S("eye", 0, L, 1, L))])
-        kt = S("kt32", c[0], c[1], 1, 32)
-        move("j%d" % h, kt, S(b, 256, 256 + L, 1, 32))
-        own, o16 = S(b, 0, Q), S("own", q, q + Q)
-        acc(own, [(sx(a, "zb", 32), S("kt32", c[0] + a, c[1], 16, 32)) for a in range(16)])
-        ts(o16, own, -2112.0, A.add)
-        N, D = S(bank(), 0, L), S(b, 128, 128 + L)
-        acc(N, [(EYE, S("ncon", 0, L)), (full("ea"), kt)])
-        pile([(D, EYE, S("dcon", 0, L)), (D, full("eb7"), kt), (S(b, 128 + 15, 128 + L, 16), full("neb7"), S("kt32", c[0] + 15, c[1], 16, 32))] +
-             [(S(b, 128 + a, 128 + L, 16), full("neye7"), o16) for a in range(15)])
-        ts(S("adat", *c), N, 0.0, A.max, 256.0, A.min)
-        scan(S("prd", *c), D, S("e15", 0, L), 1.0, A.mult, A.add)
-        f, f2 = S("fl", q, q + Q), S("fl", 16 + q, 16 + q + Q)
-        ts(f, S("prd", c[0] + 14, c[1], 16), 0.0, A.is_equal, 8192.0, A.mult)
-        tt(f2, f, o16, A.add)
-        ts(S("ol", 2 * q, 2 * (q + Q), 2), f2, 2064.0, A.add, DCOL, A.min)
-        part[0] = "w%d" % h
-        for a in range(q + Q - 1, q - 1, -1):
-            cp(IND("parw", 0, PW, "ol", 2 * a, 2 * a + 1), S("adat", 16 * a, 16 * a + 16))
+        part[0] = "h%d" % z
+        tt(S("zz", c2, c2 + 256), IND(k[0], 16, 32, "zo", 0, 16), full("mk"), A.mult)
+        Z = [S("zz", c2 + 128 * e, c2 + 128 * e + 128) for e in range(2)]
+        kt = S(bank(), 0, 128, 1, 32)
+        acc(kt, [(k, EYE)])
+        move("j", S("kt32", *c, 1, 32), kt)
+        N, D, W = bank(), S(b, 0, 256), S("pz%d" % z, 0, 256)
+        mm([(S(N, 128 * e, 128 * e + 128), S("en%d" % e, 0, 128, 1, 32), S("kt32", *c, 1, 32), True, True) for e in range(2)])
+        act(S("adat", c2, c2 + 256), S(N, 0, 256), AF.Identity, NCOL)
+        mm([(W, EYE, full("wcon"), True, False)] + [(S(W[0], 0, 256, 32), Z[e], S("b2", 0, 256, 32), False, e == 1) for e in range(2)])
+        if OPT["rep"]:
+            move("r", S("zr", c2, c2 + 256), IND(k[0], 16, 32, "zo", 0, 16))
+            pile([(D, EYE, full("dcon"))], [(D, S("zr", c2 + 128 * e, c2 + 128 * e + 128), S("b3", 256 * e, 256 * e + 256)) for e in range(2)], [(D, Z[e], full("b2")) for e in range(2)])
+        else:
+            pile([(D, EYE, full("dcon"))], [(D, Z[e], full("b2")) for e in range(2)],
+                 [(S(b, 32 * j, 32 * j + 31), full("eb"), S("kt32", c[0] + 32 * (j // 2), c[0] + 32 * (j // 2) + 31, 1, 32)) for j in range(8)])
+        if "e" in opt("onv"):
+            ts(S("ee", c2, c2 + 256), D, 0.0, A.not_equal, 8192.0, A.mult)
+        else:
+            act(S("ee", c2, c2 + 256), D, AF.Abs, None, 8192.0)
+        scan(S("prd", c2, c2 + 256), W, S("ee", c2, c2 + 256), 0.0, A.max, A.min)
+        if OPT["cross"]:
+            for e in (1, 0):
+                for h in range(2):
+                    ts(S("ol%d" % h, 16 * z + 8 * e, 16 * z + 8 * e + 8, 1, 64, 64 * h), S("prd", c2 + 30, c2 + 256, 32, 64, 64 * e), -1.0, A.mult, 4144.0 + 2048 * (z > h), A.add)
+        else:
+            mm([(S(b, 8 * e, 8 * e + 8), full("dup%d" % e), S("prd", c2 + 30, c2 + 256, 32), True, True) for e in range(2)])
+            ts(S("ol", 16 * z, 16 * z + 16), S(b, 0, 16), -1.0, A.mult, S("cols", 5, 6) if z else 4144.0, A.add)
+        part[0] = "w%d" % z
+        for a in range(7, -1, -1):
+            cp(IND("parw%d" % z, 0, PW[z], "ol", 16 * z + 2 * a, 16 * z + 2 * a + 2), S("adat", c2 + 32 * a, c2 + 32 * a + 32))
 
-    def st_send(t, h):
-        if t < vis - 1:
-            send("v", t, h)
+    def st_store(z):
+        c, t = (128 * z, 128 * z + 128), vis - 1
+        r = slice(64 * z, 64 * z + 64)
+        part[0] = "o%d" % z
+        ts(S("yvf", *c), third("vn%d" % t, *c), 2048.0, A.add)
+        ts(S("yeb", *c), S("yn%d" % t, *c), -1024.0, A.add)
+        for n, b in (("yv", "yvf"), ("ye", "yeb")):
+            dma("Y", "l_%s%d" % (n, z), [(lambda T, e=e, n=n: T[n][r, 128 * e:128 * e + 128], lambda T, e=e, b=b: T[b][64 * e:64 * e + 64, c[0]:c[1]]) for e in range(2)],
+                [S(b, *c)], [], 2.0)
+        b = S(bank(), 0, 128)
+        if z:
+            acc(b, [(sx(k), S("parw1", 2064 + 128 * k, 2192 + 128 * k)) for k in range(16)])
+        else:
+            mm([(S(b[0], 0, 128, 1, 64, 64 * e), S("zx", 15 - k, 79 - k), S("parw0", 16 + 2048 * e + 128 * k, 144 + 2048 * e + 128 * k), k == 0, k == 15)
+                for e in range(2) for k in range(16)])
+        move("o", S("ypf", *c), b)
+        for e in range(2):
+            dma("YS"[e], "l_yp%d%d" % (e, z), [(lambda T, e=e: T.yp[4 * z:4 * z + 4, 2048 * e:2048 * e + 2048], lambda T, e=e: T.ypf[64 * e:64 * e + 64, c[0]:c[1]])],
+                [S("ypf", *c)], [], 2.0)
 
     for t in range(vis):
-        for k, f, n in (("n", st_names, TB), ("x", st_hash, TB), ("p", st_pgather, ZB), ("z", st_z, ZB), ("v", st_send, TB), ("c", st_count, [0]),
-                        ("m", st_m, ZB), ("f", st_truth, TB), ("e", st_ask, TB)):
-            for h in range(len(n)):
-                part[:] = ["%s%d" % (k, h), t]
-                f(t, h)
-    part[0] = "o0"
-    ts(full("yvf"), full("vn%d" % (vis - 1)), 2048.0, A.add)
-    dma("Y", "l_yv", [(lambda T: T.yv[:], lambda T: T.yvf[:])], [full("yvf")], [], 2.0)
-    for h in range(len(TB)):
-        c = TB[h][:2]
-        ts(S("yeb", *c), S("yn%d" % (vis - 1), *c), -1024.0, A.add)
-        dma("Y", "l_ye%d" % h, [(lambda T, c=c: T.ye[:, c[0]:c[1]], lambda T, c=c: T.yeb[:, c[0]:c[1]])], [S("yeb", *c)], [], 2.0)
-    for e in range(2):
-        b = bank()
-        acc(S(b, 0, 128), [(sx(k), S("parw", 16 + 2048 * e + 128 * k, 144 + 2048 * e + 128 * k)) for k in range(16)])
-        move("o%d" % e, S("ypf", 128 * e, 128 * e + 128), S(b, 0, 128))
-        dma("YS"[e], "l_yp%d" % e, [(lambda T, e=e: T.yp[:, 2048 * e:2048 * e + 2048], lambda T, e=e: T.ypf[:, 128 * e:128 * e + 128])],
-            [S("ypf", 128 * e, 128 * e + 128)], [], 2.0)
+        part[1] = t
+        for z in range(2):
+            st_hash(t, z)
+            for f in (st_z, st_m, st_names):
+                for n in range(2):
+                    f(t, z, n)
+            if t < vis - 1:
+                send("v", t, z)
+            st_truth(t, z)
+            st_ask(t, z)
+            if t == vis - 1:
+                st_store(z)
+        if t < vis - 1:
+            st_count(t)
 
     hist, sums = {}, {}
     for i, o in enumerate(ops):
@@ -642,121 +726,31 @@ def build(nE, vis):
             l.append((i, a, b, True))
         if o["q"] == "N":
             dep = {o["send"]}
+        if o["q"] == "V" and o["R"][-1:] and o["R"][-1][0][:4] == "bank" and ops[i - 1]["R"][-1:] == o["R"][-1:]:
+            o["after"] = i - 1
         o["B"] = sorted(set(r[0] for r in o["R"] + o["W"] if BUF[r[0]][0] == "psum"))
         for b in o["B"]:
-            if o["q"] == "P" and b in TBANK:
-                if b in sums:
-                    dep.add(sums[b])
-                sums[b] = i
+            if o["q"] == "P":
+                l = sums.setdefault(b, [])
+                if o["lot"]:
+                    dep.update(l)
+                    l[:] = [i]
+                else:
+                    dep.update(l[:1])
+                    l.append(i)
         dep.discard(i)
         o["O"] = set(j for j in dep if o["q"] == "P" and ops[j]["q"] == "P")
+        if "after" in o:
+            dep.add(o["after"])
+            o["O"].add(o["after"])
         o["D"], o["i"] = dep, i
     return ops
 
 
-def _slot(line, t, c, q):
-    lo, hi = 0, len(line)
-    while lo < hi:
-        mid = (lo + hi) // 2
-        if line[mid][1] + LAT <= t:
-            lo = mid + 1
-        else:
-            hi = mid
-    while lo < len(line):
-        a, b, r = line[lo]
-        pad = 0.0 if r == q else LAT
-        if t + c + pad <= a + 1e-9:
-            break
-        if b + pad > t:
-            t = b + pad
-        lo += 1
-    return t
-
-
-def _put(line, e):
-    lo, hi = 0, len(line)
-    while lo < hi:
-        mid = (lo + hi) // 2
-        if line[mid] < e:
-            lo = mid + 1
-        else:
-            hi = mid
-    line.insert(lo, e)
-
-
-def _pass(ops, pred, succ, mate, key):
+def graph(ops):
     n = len(ops)
-    first = {j: i for i, j in mate.items()}
-    left = [len(p) for p in pred]
-    for i, j in mate.items():
-        left[i] += len([k for k in pred[j] if k != i])
-    heap = sorted((key[i], i) for i in range(n) if left[i] == 0 and i not in first)
-    lines = {r: [] for r in list("VSPGY") + BIGB + TBANK + ["pz0", "pz1"]}
-    start, end, real = [0.0] * n, [0.0] * n, {}
-
-    def room(i, t):
-        o = ops[i]
-        q = o["q"]
-        if q == "N":
-            return t
-        while True:
-            u = _slot(lines[q], t, o["occ"], q)
-            for b in o["fix"]:
-                u = _slot(lines[b], u, o["c"], q)
-            if u <= t + 1e-9:
-                return t
-            t = u
-
-    def take(i, t):
-        o = ops[i]
-        start[i], end[i] = t, t + o["c"] + LAT
-        if o["q"] != "N":
-            _put(lines[o["q"]], (t, t + o["occ"], o["q"]))
-            for b in o["fix"]:
-                _put(lines[b], (t, t + o["c"], o["q"]))
-
-    while heap:
-        i = heap.pop(0)[1]
-        t = room(i, max([end[k] - (LAT if k in ops[i]["O"] else 0.0) for k in pred[i]], default=0.0))
-        done = (i,)
-        if i in mate:
-            j = mate[i]
-            e, c = max([end[k] for k in pred[j] if k != i], default=0.0), ops[i]["c"]
-            while True:
-                u = room(j, max(e, t + c + LAT))
-                while True:
-                    v = room(i, max(t + 1e-6, u - LAT - c - 0.3))
-                    if v + c + LAT <= u + 1e-9 and v > t + 1e-3:
-                        t = v
-                    else:
-                        break
-                w, b = min((_slot(lines[b], t, u + ops[j]["c"] - t, ""), b) for b in BIGB)
-                if w <= t + 1e-9:
-                    break
-                t = room(i, w)
-            _put(lines[b], (t, u + ops[j]["c"], "*"))
-            real[ops[i]["any"]] = b
-            take(j, u)
-            done = (i, j)
-        take(i, t)
-        for d in done:
-            for k in succ[d]:
-                k2 = first.get(k, k)
-                if k2 not in done:
-                    left[k2] -= 1
-                    if left[k2] == 0:
-                        _put(heap, (key[k2], k2))
-    return start, real, max(end) - LAT
-
-
-def _graph(ops):
-    n = len(ops)
-    pred = [sorted(o["D"]) for o in ops]
-    succ = [[] for _ in range(n)]
-    pair, seen = {}, {}
+    pred, pair, seen, above = [sorted(o["D"]) for o in ops], {}, {}, [0] * n
     for i, o in enumerate(ops):
-        for j in pred[i]:
-            succ[j].append(i)
         o["occ"] = 0.15 * len(o["f"]) if o["sem"] and o["q"] in "YS" else o["c"]
         o["fix"] = [b for b in o["B"] if b in SCRATCH]
         for b in o["B"]:
@@ -764,128 +758,79 @@ def _graph(ops):
                 o["any"] = b
                 pair.setdefault(b, []).append(i)
         w = (o["t"], o["part"])
-        o["cls"] = (o["part"], seen.get(w, 0))
+        o["cls"] = (o["part"], seen.get(w, 0), OPT.get("phase", (0, 1, 1, 1, 2))[o["t"]])
         seen[w] = seen.get(w, 0) + 1
-    return pred, succ, {p[0]: p[1] for p in pair.values()}
-
-
-def _run(ops, pred, succ, mate, turns):
-    key = [0.0] * len(ops)
-    for i in range(len(ops) - 1, -1, -1):
-        o = ops[i]
-        if o["cls"] in turns:
-            key[i] = OPT["period"] * o["t"] + turns[o["cls"]]
-        else:
-            key[i] = min([key[j] - LAT for j in succ[i]], default=0.0) - o["c"]
-    return _pass(ops, pred, succ, mate, key), key
-
-
-def find_turns(ops):
-    n = len(ops)
-    pred, succ, mate = _graph(ops)
-    key = [0.0] * n
-    for i in range(n - 1, -1, -1):
-        key[i] = min([key[j] - LAT for j in succ[i]], default=0.0) - ops[i]["c"]
-    head = {}
-    for i, o in enumerate(ops):
-        w = (o["t"], o["part"])
-        head[w] = min(head.get(w, 0.0), key[i])
-    turns = {}
-    for i, o in enumerate(ops):
-        lead = {"y": LEAD.get("x" + o["part"][1:], 0) + 2, "u": LEAD.get("t" + o["part"][1:], 0) + 3}.get(o["part"][:1], LEAD.get(o["part"]))
-        if lead is not None and (o["t"] == 1 or o["cls"] not in turns):
-            turns[o["cls"]] = lead + key[i] - head[(o["t"], o["part"])]
-
-    def held(start, real):
-        by, prev, out = {}, {}, []
-        for i in sorted(range(n), key=lambda i: start[i]):
-            for r in ([ops[i]["q"]] if ops[i]["q"] != "N" else []) + [real.get(b, b) for b in ops[i]["B"]]:
-                if r in by:
-                    prev.setdefault(i, []).append((by[r], r))
-                by[r] = i
-        i = max(range(n), key=lambda i: start[i] + ops[i]["c"])
-        while True:
-            c = [(start[j] + ops[j]["c"] + (0.0 if j in ops[i]["O"] else LAT), 1, j) for j in pred[i]]
-            for j, r in prev.get(i, ()):
-                if j not in pred[i]:
-                    c.append((start[j] + (ops[j]["occ"] if r == ops[i]["q"] else ops[j]["c"] + (LAT if ops[j]["q"] != ops[i]["q"] else 0.0)), 0, j))
-            if not c:
-                return out
-            t, d, j = max(c)
-            if not d:
-                out.append((j, i))
-            i = j
-
-    rnd = np.random.default_rng(OPT["seed"])
-    got, key = _run(ops, pred, succ, mate, turns)
-    now, pairs = got[2], held(got[0], got[1])
-    best = (now, turns)
-    for it in range(OPT["tries"]):
-        r = [float(x) for x in rnd.random(5)]
-        j, i = pairs[int(r[0] * len(pairs))]
-        new = dict(turns)
-        if r[1] < 0.5 and ops[i]["cls"] in turns:
-            d = key[i] - key[j] + 0.01 + 0.3 * r[2]
-            d = d if d > 0 else r[2]
-            new[ops[i]["cls"]] -= d
-            todo, moved, lim = [i], set(), key[i] - d
-            while todo:
-                for p in pred[todo.pop()]:
-                    if p not in moved and key[p] > lim and ops[p]["cls"] in turns and len(moved) < 12:
-                        moved.add(p)
-                        new[ops[p]["cls"]] -= key[p] - lim + 0.01
-                        todo.append(p)
-        elif ops[j]["cls"] in turns:
-            d = key[i] - key[j] + 0.01 + r[2] * (0.3 if r[3] < 0.7 else 3.0)
-            new[ops[j]["cls"]] += d if d > 0 else r[2]
-        else:
-            continue
-        got, key2 = _run(ops, pred, succ, mate, new)
-        if got[2] <= now + OPT["heat"] * max(0.02, 1.0 - it / OPT["tries"]) * -math.log(1.0 - r[4]):
-            turns, now, key, pairs = new, got[2], key2, held(got[0], got[1])
-            if now < best[0]:
-                best = (now, turns)
-    return best[1]
-
-
-def schedule(ops, turns):
-    pred, succ, mate = _graph(ops)
-    start, real, total = _run(ops, pred, succ, mate, turns)[0]
-    REAL.clear()
-    REAL.update(real)
-    order = sorted(range(len(ops)), key=lambda i: (start[i], i))
-    last, other = {}, {}
-    for i in order:
-        o = ops[i]
-        o["start"] = start[i]
-        for b in o["B"]:
-            r = REAL.get(b, b)
-            if r in last and ops[last[r]]["q"] != o["q"]:
-                other[r] = last[r]
-            if r in other:
-                o["D"].add(other[r])
-            last[r] = i
-    return order, total
-
-
-def timer(ops, period):
-    n = len(ops)
-    pred, succ, mate = _graph(ops)
-    second = {j: i for i, j in mate.items()}
-    c, occ, q, fix = [[o[k] for o in ops] for k in ("c", "occ", "q", "fix")]
-    cls, base = [o["cls"] + (min(o["t"], 1),) for o in ops], [period * o["t"] for o in ops]
-    above = [0] * n
-    for i in range(n):
         far = 0
         for j in pred[i]:
             far |= above[j]
         above[i] = far
         for j in pred[i]:
             above[i] |= 1 << j
-        pred[i] = [j for j in pred[i] if not far >> j & 1]
-    pl = [[(j, 0.0 if j in ops[i]["O"] else LAT) for j in pred[i]] for i in range(n)]
-    arcs = [(j, i) for i in range(n) for j in pred[i]]
-    both = list(zip(cls, base))
+        pred[i] = [(j, 0.0 if j in o["O"] else LAT) for j in pred[i] if not far >> j & 1]
+    return pred, {p[0]: p[-1] for p in pair.values()}
+
+
+def greedy(ops, pred, mate):
+    n = len(ops)
+    succ = [[] for _ in range(n)]
+    for i in range(n):
+        for j, l in pred[i]:
+            succ[j].append((i, l))
+    way = [0.0] * n
+    for i in range(n - 1, -1, -1):
+        way[i] = ops[i]["c"] + max([way[j] + l for j, l in succ[i]], default=OPT["ahead"] * (ops[i]["part"][1:2] == "0"))
+    second = {j: i for i, j in mate.items()}
+    left, ready, at = [len(p) for p in pred], {q: [] for q in "VSPGYN"}, [0.0] * n
+    for i in range(n):
+        if not left[i]:
+            ready[ops[i]["q"]].append(i)
+    free, last, big, hold, start = {}, {}, {b: 0.0 for b in range(len(BIGB))}, {}, [0.0] * n
+    for _ in range(n):
+        best = None
+        for q, l in ready.items():
+            can = []
+            for i in l:
+                t = max(at[i], free.get(q, 0.0))
+                for b in ops[i]["fix"]:
+                    if b in last:
+                        t = max(t, last[b][0] + (LAT if last[b][1] != q else 0.0))
+                if i in mate:
+                    if not big:
+                        continue
+                    t = max(t, min(big.values()))
+                can.append((t, i))
+            if can:
+                t0 = min(can)[0] + OPT["slack"]
+                w, t, i = max((way[i] + (50.0 if i in second else 0.0), t, i) for t, i in can if t <= t0)
+                if best is None or t < best[0]:
+                    best = (t, i)
+        t, i = best
+        o = ops[i]
+        ready[o["q"]].remove(i)
+        start[i] = t
+        if o["q"] != "N":
+            free[o["q"]] = t + o["occ"]
+        for b in o["fix"]:
+            last[b] = (t + o["c"], o["q"])
+        if i in mate:
+            hold[i] = min(big, key=big.get)
+            del big[hold[i]]
+        if i in second:
+            big[hold[second[i]]] = t + o["c"] + LAT
+        for j, l in succ[i]:
+            at[j] = max(at[j], t + o["c"] + l)
+            left[j] -= 1
+            if not left[j]:
+                ready[ops[j]["q"]].append(j)
+    return start
+
+
+def timer(ops, pred, mate, base):
+    n = len(ops)
+    second = {j: i for i, j in mate.items()}
+    c, occ, q, fix = [[o[k] for o in ops] for k in ("c", "occ", "q", "fix")]
+    arcs = [(j, i) for i in range(n) for j, l in pred[i]]
+    both = [(o["cls"], b) for o, b in zip(ops, base)]
 
     def run(turns):
         key = [turns[w] + b for w, b in both]
@@ -897,7 +842,7 @@ def timer(ops, period):
         free, last, big, hold, idle = {}, {}, [(0.0, -1)] * len(BIGB), {}, list(range(len(BIGB)))
         for i in order:
             t, w, qi = 0.0, None, q[i]
-            for j, l in pl[i]:
+            for j, l in pred[i]:
                 if end[j] + l > t:
                     t, w = end[j] + l, (j, 1)
             if qi != "N":
@@ -925,56 +870,31 @@ def timer(ops, period):
                 big[hold[second[i]]] = (end[i] + LAT, i)
                 idle.append(hold[second[i]])
         i = max(range(n), key=lambda i: end[i])
-        total, pairs = end[i] + more * (end[marks[1]] - end[marks[0]]), []
+        total, pairs = end[i], []
         while why[i] is not None:
             if not why[i][1]:
                 pairs.append((why[i][0], i))
             i = why[i][0]
         return total, pairs, start, hold, order, key
-    marks = [max(i for i in range(n) if ops[i]["t"] == t) for t in range(2)]
-    more = VIS - 1 - ops[-1]["t"]
-    return run, pred, succ, mate, cls, base
+    return run
 
 
-def find_turns(ops):
-    n = len(ops)
-    run, pred, succ, mate, cls, base = timer(ops, OPT["period"])
-    off, turns, parts = [0.0] * n, {}, {}
-    for i, o in enumerate(ops):
-        off[i] = max([off[j] + ops[j]["c"] + LAT for j in pred[i] if (ops[j]["part"], ops[j]["t"]) == (o["part"], o["t"])], default=0.0)
-        if cls[i] not in turns:
-            parts.setdefault((o["part"], cls[i][2]), []).append(cls[i])
-            turns[cls[i]] = LEAD.get(o["part"], 0.0) + off[i] + 1e-3 * o["cls"][1]
-    for i in range(n - 1, -1, -1):
-        if not ops[i]["part"]:
-            turns[cls[i]] = min([turns[cls[j]] + base[j] - LAT for j in succ[i]], default=0.0) - ops[i]["c"]
-    seen = {}
-    for i in sorted(mate):
-        w = (ops[i]["part"], ops[i]["t"])
-        if ops[i]["t"] <= 1 or w[0][0] == "o":
-            turns[cls[i]] += 0.55 * seen.get(w, 0)
-            turns[cls[mate[i]]] = turns[cls[i]] + 0.6
-        seen[w] = seen.get(w, 0) + 1
-    rnd = np.random.default_rng(OPT["seed"])
-    found = [_anneal(ops, run, pred, parts, cls, base, turns, rnd, OPT["tries"][0], OPT["heat"]) for k in range(OPT["starts"])]
-    turns = min(found, key=lambda f: f[0])[1]
-    return _anneal(ops, run, pred, parts, cls, base, turns, rnd, OPT["tries"][1], OPT["heat"] / 2)[1]
-
-
-def _anneal(ops, run, pred, parts, cls, base, turns, rnd, tries, heat):
+def anneal(ops, pred, run, base):
+    cls = [o["cls"] for o in ops]
+    turns, parts = {w: 0.0 for w in cls}, {}
+    for w in turns:
+        parts.setdefault((w[0], w[2]), []).append(w)
+    rnd, tries, heat = np.random.default_rng(OPT["seed"]), OPT["tries"], OPT["heat"]
     got = run(turns)
-    best = (got[0], turns)
+    best = got
     for it in range(tries):
         r = rnd.random(6).tolist()
-        pairs = got[1]
-        if it % 3 == 0:
-            pairs = [p for p in pairs if ops[p[1]]["t"] == 0] or pairs
-        j, i = pairs[int(r[0] * len(pairs))]
+        j, i = got[1][int(r[0] * len(got[1]))]
         key, new = got[5], dict(turns)
         more = 0.5 * r[2] if r[2] > 0.5 else 0.0
         if r[4] < 0.2:
             a, sign = (i, -1) if r[1] < 0.5 else (j, 1)
-            for w in parts[(ops[a]["part"], cls[a][2])]:
+            for w in parts[(cls[a][0], cls[a][2])]:
                 if r[5] >= 0.5 or sign * (w[1] - cls[a][1]) >= 0:
                     new[w] += sign * (key[i] - key[j] + 1e-3 + 2 * r[2] ** 2)
         elif r[1] < 0.5:
@@ -984,19 +904,21 @@ def _anneal(ops, run, pred, parts, cls, base, turns, rnd, tries, heat):
                 count += 1
                 if key[a] > l:
                     new[cls[a]] = min(new[cls[a]], l - base[a])
-                    todo += [(p, l - 1e-4) for p in pred[a]]
+                    todo += [(p, l - 1e-4) for p, _ in pred[a]]
         else:
             new[cls[j]] = key[i] + 1e-4 + more - base[j]
         g2 = run(new)
         if g2 is not None and g2[0] <= got[0] - heat * max(0.03, 1.0 - it / tries) * math.log(1.0 - r[3]):
             turns, got = new, g2
             if got[0] < best[0]:
-                best = (got[0], turns)
+                best = got
     return best
 
 
-def schedule(ops, turns):
-    total, pairs, start, hold, order, key = timer(ops, OPT["period"])[0](turns)
+def schedule(ops):
+    pred, mate = graph(ops)
+    base = greedy(ops, pred, mate)
+    total, pairs, start, hold, order, key = anneal(ops, pred, timer(ops, pred, mate, base), base)
     REAL.clear()
     for i, b in hold.items():
         REAL[ops[i]["any"]] = BIGB[b]
@@ -1014,15 +936,257 @@ def schedule(ops, turns):
     return order, total
 
 
+def clock(ops, pred, mate, goal=None):
+    n, NB = len(ops), len(BIGB)
+    res = {r: k for k, r in enumerate(list("VSPGYN") + ["pz0", "pz1", "pt0", "pt1"])}
+    second = {j: i for i, j in mate.items()}
+    J, I = np.array([[j, i] for i in range(n) for j, l in pred[i]]).T
+    kinds = sorted(set(o["kind"] for o in ops))
+    num = {w: k for k, w in enumerate(kinds)}
+    ci, base = np.array([num[o["kind"]] for o in ops]), np.array([HALF * o["j"] for o in ops])
+    row = [(pred[i], res[o["q"]], o["c"], o["occ"] if o["q"] != "N" else -1e9, [res[b] for b in o["fix"]], i in mate, second.get(i, -1)) for i, o in enumerate(ops)]
+
+    def run(turns, soon):
+        key = turns[ci] + base
+        while True:
+            bad = np.nonzero(key[J] >= key[I])[0]
+            if not len(bad):
+                break
+            np.maximum.at(key, I[bad], key[J[bad]] + 1e-5)
+        order = np.argsort(key, kind="stable").tolist()
+        end, why, dep = [0.0] * (n + 1), [-1] * n, [True] * n
+        free, who, lq, big, hold, idle = [-1.0] * 10, [n] * 10, [-1] * 10, [(0.0, -1)] * NB, {}, list(range(NB))
+        for i in order:
+            pr, qi, c, occ, fix, first, sec = row[i]
+            t, w, d = free[qi], who[qi], False
+            for j, l in pr:
+                u = end[j] + l
+                if u > t:
+                    t, w, d = u, j, True
+            for b in fix:
+                u = free[b] if lq[b] == qi else free[b] + LAT
+                if u > t:
+                    t, w, d = u, who[b], False
+            if first:
+                if not idle:
+                    return None
+                b = min(idle, key=lambda b: big[b])
+                idle.remove(b)
+                hold[i] = b
+                if big[b][0] > t:
+                    t, w = big[b]
+                    d = False
+            if t < soon[i]:
+                t, w = soon[i], -1
+            free[qi], who[qi] = t + occ, i
+            t += c
+            for b in fix:
+                free[b], who[b], lq[b] = t, i, qi
+            end[i], why[i], dep[i] = t, w, d
+            if sec >= 0:
+                big[hold[sec]] = (t + LAT, i)
+                idle.append(hold[sec])
+        i = goal if goal is not None else end.index(max(end))
+        total, pairs = end[i], []
+        while i < n and why[i] >= 0:
+            if not dep[i] and why[i] < n:
+                pairs.append((why[i], i))
+            i = why[i]
+        return total, pairs, end, hold, order, key
+    return run, kinds, ci.tolist(), base
+
+
+def improve(ops, pred, mate, given, keep, free, n, half=None):
+    ix = [i for i, o in enumerate(ops) if keep(o)]
+    m = {i: k for k, i in enumerate(ix)}
+    ops, pred, mate = [ops[i] for i in ix], [[(m[j], l) for j, l in pred[i] if j in m] for i in ix], {m[i]: m[j] for i, j in mate.items() if i in m}
+    marks = [i for i, o in enumerate(ops) if o["kind"][:2] == ("w", 7)]
+    goal = marks[-2] if ops[-1]["part"][0] != "o" else None
+    run, kinds, cls, base = clock(ops, pred, mate, goal)
+    parts, tries, heat = {}, OPT["tries"][n], OPT["heat"][n]
+    for k, w in enumerate(kinds):
+        parts.setdefault((w[0], w[2]), []).append(k)
+    rep = [i for i, o in enumerate(ops) if free(o)]
+    at, cost, held = np.array(cls)[rep], np.array([o["c"] for o in ops]), np.ones(len(kinds), bool)
+    held[at] = False
+    rest = np.nonzero(held[cls])[0]
+
+
+    def score(g):
+        return g[0] if half else 1.3 * g[0] - g[2][marks[-4]]
+    rnd = np.random.default_rng(OPT["seed"][n])
+    turns, soon = np.array([given[w] for w in kinds]), [0.0] * len(ops)
+    got = run(turns, soon)
+    now = score(got)
+    best = (now, got, turns)
+    for it in range(tries + 1):
+        if it == tries:
+            now, got, turns = best
+        h = half or (got[0] - got[2][marks[-4]]) / 2
+        if it == tries:
+            OPT.get("log", []).append(round(now if half else 2 * h, 2))
+            turns[at] = (got[5] - base)[rep]
+            return given | dict(zip(kinds, turns.tolist())), h
+        if it % OPT["norm"] == 0:
+            key = (np.array(got[2][:-1]) - cost) * (HALF / h)
+            new = turns.copy()
+            new[at] = (key + (np.median((got[5] - key)[rest]) if len(rest) else 0.0) - base)[rep]
+            g2 = run(new, soon)
+            if g2 is not None and score(g2) <= now + OPT["tol"]:
+                turns, got, now = new, g2, score(g2)
+        r = rnd.random(6).tolist()
+        pairs = [p for p in got[1] if not (held[cls[p[0]]] and held[cls[p[1]]])] if half else got[1]
+        j, i = pairs[int(r[0] * len(pairs))]
+        key, new = got[5], turns.copy()
+        more = 0.5 * r[2] if r[2] > 0.5 else 0.0
+        if r[4] < 0.1:
+            a, sign = (i, -1) if r[1] < 0.5 else (j, 1)
+            w = kinds[cls[a]]
+            for k in parts[(w[0], w[2])]:
+                if r[5] >= 0.5 or sign * (kinds[k][1] - w[1]) >= 0:
+                    new[k] += sign * (key[i] - key[j] + 1e-3 + 2 * r[2] ** 2)
+        elif r[1] < 0.5:
+            todo, count = [(i, key[j] - 1e-4 - more)], 0
+            while todo and count < 40:
+                a, l = todo.pop()
+                count += 1
+                if key[a] > l:
+                    new[cls[a]] = min(new[cls[a]], l - base[a])
+                    todo += [(p, l - 1e-4) for p, _ in pred[a]]
+        else:
+            new[cls[j]] = key[i] + 1e-4 + more - base[j]
+        new[held] = turns[held]
+        g2 = run(new, soon)
+        if g2 is not None:
+            s2 = score(g2)
+            if s2 <= now - heat * max(0.03, 1.0 - it / tries) * math.log(1.0 - r[3]):
+                turns, got, now = new, g2, s2
+                if now < best[0]:
+                    best = (now, got, turns)
+
+
+def fit(ops, pred, mate, key):
+    n, first = len(ops), {j: i for i, j in mate.items()}
+    lines, start, end = {}, [0.0] * n, [None] * n
+
+    def slot(r, t, c, q):
+        for a, b, w in lines.setdefault(r, []):
+            pad = 0.0 if w == q else LAT
+            if t + c + pad <= a + 1e-9:
+                break
+            t = max(t, b + pad)
+        return t
+
+    def room(i, t):
+        o = ops[i]
+        while o["q"] != "N":
+            u = slot(o["q"], t, o["occ"], o["q"])
+            for b in o["fix"]:
+                u = slot(b, u, o["c"], o["q"])
+            if u <= t + 1e-9:
+                break
+            t = u
+        return t
+
+    def take(i, t):
+        o = ops[i]
+        start[i], end[i] = t, t + o["c"]
+        for r, c in [(o["q"], o["occ"])] * (o["q"] != "N") + [(b, o["c"]) for b in o["fix"]]:
+            lines[r] = sorted(lines.get(r, []) + [(t, t + c, o["q"])])
+
+    def needs(i):
+        return [(j, l) for j, l in pred[i] + pred[mate.get(i, i)] if j != i]
+    todo = sorted((i for i in range(n) if i not in first), key=lambda i: key[i])
+    while todo:
+        i = next(i for i in todo if all(end[j] is not None for j, l in needs(i)))
+        todo.remove(i)
+        t = room(i, max([end[j] + l for j, l in pred[i]], default=0.0))
+        while i in mate:
+            j, c = mate[i], ops[i]["c"]
+            u = room(j, max([t + c + LAT] + [end[k] + l for k, l in pred[j] if k != i]))
+            v = room(i, max(t, u - LAT - c - 0.3))
+            t = v if v + c + LAT <= u + 1e-9 else t
+            w, b = min((slot(b, t, u + ops[j]["c"] - t, ""), b) for b in BIGB)
+            if w <= t + 1e-9:
+                lines[b] = sorted(lines[b] + [(t, u + ops[j]["c"], "*")])
+                take(j, u)
+                break
+            t = room(i, w)
+        take(i, t)
+    return start
+
+
+def steady_turns(ops, pred, mate):
+    off, turns, seen = [0.0] * len(ops), {}, {}
+    for i, o in enumerate(ops):
+        off[i] = max([off[j] + ops[j]["c"] + l for j, l in pred[i] if (ops[j]["part"], ops[j]["t"]) == (o["part"], o["t"])], default=0.0)
+        if o["t"] == 2:
+            turns[o["kind"]] = LEAD[o["kind"][0]] + off[i] + 1e-3 * o["kind"][1]
+    for i in sorted(mate):
+        if ops[i]["j"] == 4 + (ops[i]["part"] == "c1"):
+            w = ops[i]["part"]
+            turns[ops[i]["kind"]] += 0.55 * seen.get(w, 0)
+            turns[ops[mate[i]]["kind"]] = turns[ops[i]["kind"]] + 0.6
+            seen[w] = seen.get(w, 0) + 1
+    return improve(ops, pred, mate, turns, lambda o: 2 <= o["j"] <= 6 + (o["part"][:1] in AHEAD), lambda o: o["j"] == (5 if o["part"] == "c1" else OPT["at"] + 2 * (o["part"][:1] in AHEAD)), 0)
+
+
+def schedule(ops):
+    pred, mate = graph(ops)
+    for o in ops:
+        p = o["part"]
+        o["j"] = 2 * o["t"] + (p[1:2] == "1")
+        o["kind"] = (p if p[:1] in "lrbo" else p[:1] + p[2:], o["cls"][1], 0)
+    steady, half = OPT.get("steady") or steady_turns(ops, pred, mate)
+    key = [steady[o["kind"]] + HALF * o["j"] if o["kind"] in steady else None for o in ops]
+    for i, o in enumerate(ops):
+        if o["j"] in OPT["job"] and (o["kind"][0], 0, 0) in steady:
+            key[i] = max([steady[(o["kind"][0], 0, 0)] + HALF * o["j"]] + [key[j] + ops[j]["c"] + l for j, l in pred[i] if ops[j]["part"] == o["part"] and key[j]])
+    late = [1e9] * len(ops)
+    for i in range(len(ops) - 1, -1, -1):
+        if key[i] is None:
+            key[i] = min(late[i] - ops[i]["c"] - 10.0 * (ops[i]["part"] == "r1"), 0.0 if late[i] == 1e9 or not ops[i]["part"] else 1e9)
+        for j, l in pred[i]:
+            late[j] = min(late[j], key[i] - l)
+    start = fit(ops, pred, mate, key)
+    for a, b, near in ((0, OPT["own"][0] - 1, OPT["own"][0]), (OPT["own"][1] + 1, 9, OPT["own"][1])):
+        shift = float(np.median([key[i] - start[i] * HALF / half for i, o in enumerate(ops) if o["j"] == near]))
+        key = [start[i] * HALF / half + shift if a <= o["j"] <= b else key[i] for i, o in enumerate(ops)]
+    turns = {}
+    for o, k in zip(ops, key):
+        o["kind"] = o["kind"][:2] + (0 if OPT["own"][0] <= o["j"] <= OPT["own"][1] else o["j"] + 1,)
+        turns[o["kind"]] = k - HALF * o["j"]
+    if "hook" in OPT:
+        return OPT["hook"](ops, pred, mate, turns, half)
+    turns = improve(ops, pred, mate, turns, lambda o: o["j"] <= 4 + 2 * (o["part"][:1] in AHEAD), lambda o: o["j"] < OPT["own"][0], 1, half)[0]
+    turns = improve(ops, pred, mate, turns, lambda o: o["j"] >= 5, lambda o: o["j"] > OPT["own"][1], 2, half)[0]
+    run, kinds = clock(ops, pred, mate)[:2]
+    total, pairs, end, hold, order, key = run(np.array([turns[w] for w in kinds]), [0.0] * len(ops))
+    REAL.clear()
+    for i, b in hold.items():
+        REAL[ops[i]["any"]] = BIGB[b]
+    last, other = {}, {}
+    for i in order:
+        o = ops[i]
+        o["start"] = end[i] - o["c"]
+        for b in o["B"]:
+            r = REAL.get(b, b)
+            if r in last and ops[last[r]]["q"] != o["q"]:
+                other[r] = last[r]
+            if r in other:
+                o["D"].add(other[r])
+            last[r] = i
+    return order, total
+
+
 SEMQ = {"V": "vv", "S": "ss", "P": "pp", "G": "gg"}
 
 
 def plan(nE):
     if nE in _CACHE:
         return _CACHE[nE]
-    turns = find_turns(build(nE, OPT["visits"]))
     ops = build(nE, VIS)
-    order, total = schedule(ops, turns)
+    order, total = schedule(ops)
     count = {s: 0 for s in SEMQ.values()}
     know, kq, out = {}, {}, []
     for i in order:
@@ -1060,7 +1224,7 @@ def rank_program(g, core, T, topo):
     if rank is None:
         return
     nxt = T.cores[(rank + 1) % len(T.cores)]
-    eng = topo.engines(core, nxt)[::2]
+    eng = topo.engines(core, nxt)
     mask = 0
     for e in eng:
         mask |= 1 << e
@@ -1075,8 +1239,8 @@ def rank_program(g, core, T, topo):
             queue[q].wait_ge(T.sem[s], v)
         if o["send"]:
             k, t, h = o["send"]
-            c = slice(TB[h][0], TB[h][1])
-            g.remote_dma(out_ap=T["%sb%d" % (k, t)][:, c], in_ap=T["%sn%d" % (k, t - 1)][:, c], remote_sem=T.sem["a%s%d%d" % (k, t, h)],
+            dst, src = send_sides(T, T, o["send"])
+            g.remote_dma(out_ap=dst, in_ap=src, remote_sem=T.sem["a%s%d%d" % (k, t, h)],
                          local_sem=T.sem["o%s%d%d" % (k, t, h)], pid=pid, routing_id=rid, dma_engine_mask=mask)
         elif o["sem"]:
             for f in o["f"]:

@@ -1,6 +1,5 @@
-import math
 import numpy as np
-from concourse.mybir import AluOpType, AxisListType, ActivationFunctionType
+from concourse.mybir import AluOpType, ActivationFunctionType
 
 A = AluOpType
 AF = ActivationFunctionType
@@ -8,6 +7,7 @@ VIS = 5
 BUF = {}
 SEMAPHORES = ["vv", "ss", "pp", "gg"]
 BIGB = ["pa0", "pa1", "pa2", "pa3"]
+FIXB = ["pz0", "pz1", "pt0", "pt1"]
 
 
 def _b(name, shape, dtype="float32", where="sbuf"):
@@ -16,19 +16,21 @@ def _b(name, shape, dtype="float32", where="sbuf"):
 
 BF, F16, F32, I32, U16 = "bfloat16", "float16", "float32", "int32", "uint16"
 CW = 8512
-PW = (4160, 6240)
+PW, P0 = 4160, 32
 WIDE = {"y": 128, "v": 384}
 _b("dq", [128, 768], BF)
 for _z in range(2):
     _b("claimw%d" % _z, [128, CW], BF)
-    _b("parw%d" % _z, [128, PW[_z]], BF)
+    _b("parw%d" % _z, [128, PW], BF)
+    _b("plain%d" % _z, [128, PW], F32)
+    _b("adf%d" % _z, [128, 256], F32)
     _b("km%d" % _z, [128, 256], F32)
     _b("pm%d" % _z, [128, 512], F32)
     _b("tt%d" % _z, [128, 256], F32)
     _b("rr%d" % _z, [128, 48], F32)
     _b("ct%d" % _z, [128, 16], BF)
-    _b("ca%d" % _z, [128, 32], BF)
-    for _n in ("wmat", "en"):
+    _b("ca%d" % _z, [128, 512], BF)
+    for _n in ("wmat", "en", "enf"):
         _b("%s%d" % (_n, _z), [128, 128], BF)
     _b("dup%d" % _z, [128, 128], F32)
     _b("exf%d" % _z, [8, 128], F32)
@@ -39,64 +41,58 @@ for _t in range(VIS):
     for _n in ("vb", "yn", "vn"):
         _b("%s%d" % (_n, _t), [128, 2 * WIDE[_n[0]]], F16)
     _b("thc%d" % _t, [128, 2], F32)
-for _n in ("x0", "x1", "pr", "d", "ad", "la", "af", "ae"):
+for _n in ("x0", "x1", "d", "ad", "la", "af"):
     _b(_n, [128, 4096], BF)
-for _n in ("mx", "mn"):
-    _b(_n, [128, 4096], F16)
-for _n in ("um0", "um1", "t1", "t2", "t3", "t4", "t5", "whoi"):
+MW = 3120
+_b("mx", [128, 4 * MW], F16)
+_b("sum3", [128, 192], F16)
+_b("mm_", [128, 768], F16)
+for _n in ("um0", "um1", "t1", "t2", "t3", "t4", "t5", "whoi", "pari"):
     _b(_n, [128, 256], I32)
-for _n in ("pari", "parj"):
-    _b(_n, [128, 512], I32)
 for _n in ("hl", "zl", "vl"):
     _b(_n, [128, 256], U16)
-for _n in ("c1", "c2", "vm", "yvf"):
+for _n in ("c1", "c2", "yvf", "ypf"):
     _b(_n, [128, 256], F32)
-for _n in ("prd", "ypf"):
-    _b(_n, [128, 512], F32)
-for _n in ("dep", "yy", "yeb", "zy", "mk", "b2", "dcon", "wcon", "r2", "rm", "rmn", "zero", "jt"):
+for _n in ("yy", "yeb", "zy", "mk", "mkn", "nsel", "dcon", "rm", "rmn", "zero", "ktile"):
     _b(_n, [128, 256], BF)
-for _n in ("adat", "zz", "ee", "parb", "zr", "b3"):
+_b("r2", [128, 272], BF)
+for _n in ("adat", "zz", "ee", "parb", "zr", "cm1k"):
     _b(_n, [128, 512], BF)
-for _n in ("mm_", "vh"):
-    _b(_n, [128, 256], F16)
+_b("vh", [128, 256], F16)
 _b("kt32", [32, 256], BF)
 _b("yl", [128, 16], U16)
 _b("ol", [128, 32], U16)
 _b("zo", [128, 16], U16)
 _b("cs", [128, 2], BF)
 _b("cint", [128, 4], I32)
-for _n in ("ones", "eye", "neye", "blk", "blk1", "c2048", "cm256", "cm1k", "ptile", "e18", "m64", "vrow"):
+for _n in ("ones", "eye", "neye", "blk", "blk1", "c2048", "cm256", "e18", "m64", "vrow"):
     _b(_n, [128, 128], BF)
 for _j in (4, 8):
-    _b("cmf%d" % _j, [128, 256], BF)
-    _b("ckf%d" % _j, [128, 256], BF)
-    _b("cme%d" % _j, [128, 256], BF)
-for _n in ("zx", "zx2", "zxn"):
-    _b(_n, [128, 144], BF)
-_b("eb", [32, 128], BF)
+    for _n in ("cmf", "ckf", "cme"):
+        _b("%s%d" % (_n, _j), [128, 256], BF)
+_b("zx", [128, 144], BF)
 _b("kcon", [8, 512], BF)
 _b("kval", [128, 32], BF)
-_b("b64", [128, 48], BF)
-_b("ktile", [128, 256], BF)
-_b("b4k", [128, 48], BF)
-for _n in ("tb", "lf"):
-    _b(_n, [128, 2048], BF)
+for _n in ("b64", "b4k"):
+    _b(_n, [128, 48], BF)
+for _n in ("ptile", "nset", "ns32"):
+    _b(_n, [128, 8], BF)
+_b("tb", [128, 1040], BF)
+_b("lf", [128, 2048], BF)
 _b("io1", [128, 128], I32)
-_b("e16", [128, 16], F32)
 _b("cols", [128, 16], F32)
 _b("wti", [128, 1], I32)
 _b("wtf", [128, 1], F32)
 _b("limi", [8, 2], I32)
 _b("limf", [8, 2], F32)
 _b("thb", [128, 4], F32)
-_b("thi", [128, 8], I32)
-for _n in BIGB + ["pz0", "pz1", "pt0", "pt1"]:
+for _n in BIGB + FIXB:
     _b(_n, [128, 512], F32, "psum")
 
-for _n in ("lim", "wt"):
+for _n in ("lim", "wt", "par", "first"):
     SEMAPHORES.append("l_" + _n)
 for _z in range(2):
-    for _n in ("who", "est", "par", "tab", "claim", "again", "yv", "ye", "yp0", "yp1"):
+    for _n in ("who", "est", "plain", "tab", "claim", "again", "yv", "ye", "yp0", "yp1"):
         SEMAPHORES.append("l_%s%d" % (_n, _z))
 for _t in range(1, VIS):
     for _h in range(2):
@@ -106,7 +102,7 @@ for _t in range(1, VIS):
 PACK = {}
 SCRATCH = {}
 _ROOM = {}
-_KEEP = ("whoi", "pari", "parb", "ypf", "yvf", "yeb", "wti", "limi", "hl", "zl", "vl", "yl", "ol", "zo", "adat", "yy", "zz", "zr", "zy", "mk", "ct0", "ct1", "ca0", "ca1")
+_KEEP = ("whoi", "pari", "parb", "ypf", "yvf", "yeb", "wti", "limi", "hl", "zl", "vl", "yl", "ol", "zo", "adat", "yy", "zy", "mk", "ct0", "ct1", "adf0", "adf1")
 for _n, (_w, _sh, _d) in BUF.items():
     if _w == "sbuf" and _n not in _KEEP and _n[:2] not in ("yb", "vb", "yn", "vn") and _sh[1] <= 512:
         PACK[_n] = ("pack_" + _d, _ROOM.get(_d, 0))
@@ -116,33 +112,29 @@ for _n, (_w, _sh, _d) in BUF.items():
 for _d in _ROOM:
     SCRATCH["pack_" + _d] = ("sbuf", [128, _ROOM[_d]], _d)
 
-HALVES = {"ol": ["ol", "ol0", "ol1"]}
-for _n in HALVES["ol"][1:]:
-    BUF[_n], PACK[_n] = BUF["ol"], ("ol", 0)
+HALVES = {"ol": ["ol", "ol0", "ol1"], "la": ["la", "la0", "la1"], "mx": ["mx", "mx0", "mx1"], "claimw0": ["claimw0", "claimw0_0", "claimw0_1"]}
+for _h in HALVES:
+    for _n in HALVES[_h][1:]:
+        BUF[_n], PACK[_n] = BUF[_h], (_h, 0)
 _CACHE = {}
 CY, PCY, GATH, SCAT = 0.00083 * 1.08, 0.00042 * 1.08, 1.56, 3.8
 VOV, SOV, POV, LAT = 0.04, 0.04, 0.02, 0.2
 OPT = {
     "onv": ("p1",),
-    "relu": (),
     "rows": {"f": 4, "e": 4},
     "gl": {"x": 32, "p": 32, "g": 32},
     "al": 32,
-    "zv": "VVSSSSSSSS",
-    "job": {0: {"onv": ("p1", "p3", "x1", "x3")}, 9: {"rows": {"f": 8, "e": 8}, "onv": ("p1", "p3")}},
-    "cross": True, "rep": True, "norm": 200, "tol": 1, "at": 5,
-    "apart": (),
-    "direct": (),
-    "sl": (64, 64),
+    "zv": "VVVVSSSS",
+    "job": {0: {"onv": ("p1", "p3", "x1")}, 9: {"rows": {"f": 8, "e": 8}, "onv": ("p1", "p3")}},
     "send": (1, 3, 4),
-    "tries": (55000, 40000, 30000), "seed": (2, 0, 0), "heat": (0.35, 0.15, 0.15), "own": (2, 7),
+    "seed": 0,
+    "sweeps": [(100, 1000, 0.12 * 0.983 ** k) for k in range(100)],
 }
-AHEAD = ("n", "x", "y")
-HALF = 16.0
+HALF, ALONE = 15.0, 0.85
 LEAD = {"n": -12.4, "x": -7.9, "y": -2.5, "p0": 0.0, "q0": 0.3, "z0": 2.0, "g0": 4.5, "d0": 5.5, "p1": 0.7, "q1": 0.4, "z1": 3.4, "g1": 6.5, "d1": 7.8,
-        "m0": 8.5, "s0": 11.3, "m1": 10.3, "s1": 12.5, "v0": 10.0, "v1": 11.0, "c": 11.9, "f": 14.5, "t": 14.5, "u": 20.0, "e": 19.5, "a": 21.0, "h": 26.1, "w": 29.6}
+        "m0": 8.5, "s0": 11.3, "m1": 10.3, "s1": 12.5, "v0": 10.0, "v1": 11.0, "c": 11.9, "f": 14.5, "t": 14.5, "u": 20.0, "e": 19.5, "a": 21.0, "h": 26.1, "w": 29.6, "o": 10.0}
 REAL = {}
-R64, R256 = 1.5 * 2 ** 29, 1.5 * 2 ** 31
+R256 = 1.5 * 2 ** 31
 
 
 def S(name, a, b, step=1, p=128, p0=0):
@@ -164,8 +156,8 @@ def ap(T, s):
 
 def regs(s):
     if len(s) == 7:
-        return [(s[0], s[1], s[2])] + [(n, s[4], s[5]) for n in HALVES.get(s[3], [s[3]])]
-    return [(s[0], s[1], s[2])]
+        return [(n, s[1], s[2]) for n in HALVES.get(s[0], [s[0]])] + [(n, s[4], s[5]) for n in HALVES.get(s[3], [s[3]])]
+    return [(n, s[1], s[2]) for n in HALVES.get(s[0], [s[0]])]
 
 
 def width(s):
@@ -266,7 +258,8 @@ def build(nE, vis):
 
     def pile(*lots):
         for n, terms in enumerate(lots):
-            mm([(o, l, r, n == 0 and i == 0, n == len(lots) - 1 and i == len(terms) - 1) for i, (o, l, r) in enumerate(terms)],
+            ends = set({o[5]: i for i, (o, l, r) in enumerate(terms)}.values())
+            mm([(o, l, r, n == 0 and i == 0, n == len(lots) - 1 and i in ends) for i, (o, l, r) in enumerate(terms)],
                None if len(lots) == 1 else "first" if n == 0 else "last" if n == len(lots) - 1 else "more")
 
     def dma(q, sem, pairs, R, W, cost):
@@ -286,8 +279,8 @@ def build(nE, vis):
     EYE, NEYE, BLK = full("eye"), full("neye"), full("blk")
     SET = S("blk", 0, 128, 16)
 
-    def sx(k, z="zx"):
-        return S(z, 15 - k, 143 - k)
+    def sx(k):
+        return S("zx", 15 - k, 143 - k)
 
     turn = [0]
 
@@ -302,63 +295,81 @@ def build(nE, vis):
     def mark(out, a, pattern, base, cm, c):
         asel(out, S(a, 0, width(out), 1, out[4]), pattern, A.not_equal, base, cm, float(c))
 
+    def band(out, pattern, n):
+        asel(out, S("zero", 0, width(out)), pattern, A.is_gt, 0, -1, -1.0)
+        asel(out, out, pattern, A.is_ge, n - 1, -1)
+
     def times(out, a, c):
         act(out, a, AF.Identity, None, float(c))
+
+    def level(out, c):
+        act(out, S("zero", 0, width(out)), AF.Identity, float(c) if c else None)
 
     def both(q, sem, out, in_, W, cost, R=()):
         dma(q, sem, [(lambda T, e=e: out(T, e), lambda T, e=e: in_(T, e)) for e in range(2)], list(R), [W], cost)
 
-    for z in range(2):
-        part[0] = "l%d" % z
+    issued = {}
+
+    def in_turn():
+        q = ops[-1]["q"]
+        if q in issued:
+            ops[-1]["after"] = issued[q]
+        issued[q] = len(ops) - 1
+
+    def objects(z, q):
         r, c = slice(64 * z, 64 * z + 64), slice(128 * z, 128 * z + 128)
+        for q, n, to in ((q, "est", "yb0"), ("Y", "who", "whoi")):
+            both(q, "l_%s%d" % (n, z), lambda T, e, to=to: T[to][64 * e:64 * e + 64, c], lambda T, e, n=n: T[n][r, 128 * e:128 * e + 128], S(to, 128 * z, 128 * z + 128), 2.0 + 2 * z)
+            in_turn()
+
+    def claims_in(q, sem, z, halves, spans, cost):
         cw = "claimw%d" % z
-        both("Y", "l_par%d" % z, lambda T, e, z=z: T.pari[64 * e:64 * e + 64, 256 * z:256 * z + 256], lambda T, e, z=z: T.par[4 * z:4 * z + 4, :],
-             S("pari", 256 * z, 256 * z + 256), 2.0)
-        both("Y", "l_est%d" % z, lambda T, e, c=c: T.yb0[64 * e:64 * e + 64, c], lambda T, e, r=r: T.est[r, 128 * e:128 * e + 128], S("yb0", 128 * z, 128 * z + 128), 2.0)
-        if not z:
-            dma("Y", "l_wt", [(lambda T: T.wti[:], lambda T: T.wt[:])], [], [full("wti")], 2.0)
-        both("Y", "l_who%d" % z, lambda T, e, c=c: T.whoi[64 * e:64 * e + 64, c], lambda T, e, r=r: T.who[r, 128 * e:128 * e + 128], S("whoi", 128 * z, 128 * z + 128), 2.0)
-        if not z:
-            dma("Y", "l_lim", [(lambda T: T.limi[:], lambda T: T.lim[:])], [], [full("limi")], 2.0)
-        both("SY"[z], "l_claim%d" % z, lambda T, e, cw=cw: T[cw][64 * e:64 * e + 64, 0:4096], lambda T, e, r=r: T.claim[r, :], S(cw, 0, 4096), 6.0 - z,
-             [S("claimw0", 0, 4096)] if z else [])
+        dma(q, sem, [(lambda T, e=e, a=a, b=b: T[cw][64 * e:64 * e + 64, a:b], lambda T, a=a, b=b: T.claim[64 * z:64 * z + 64, 0:b - a]) for e in halves for a, b in spans],
+            [], [S(cw + ("" if len(halves) > 1 else "_%d" % halves[0]), spans[0][0], spans[-1][1])], cost)
+        in_turn()
+
+    part[0] = "l0"
+    for n, to in (("par", "pari"), ("wt", "wti"), ("lim", "limi")):
+        dma("Y", "l_" + n, [(lambda T, to=to: T[to][:], lambda T, n=n: T[n][:])], [], [full(to)], 2.0)
+        in_turn()
+    objects(0, "S")
+    claims_in("S", "l_first", 0, [0], [(0, 4096)], 3.9)
     part[0] = ""
     fill(full("ones"), 1.0)
-    iota(S("io1", 0, 16), [[-1, 16]], 16, 1)
+    iota(S("io1", 0, 1), [[0, 1]], 0, 1)
     asel(full("blk1"), full("ones"), [[-16, 8], [0, 16]], A.is_ge, 0, 1)
     asel(BLK, full("blk1"), [[16, 8], [0, 16]], A.is_ge, 15, -1)
     asel(EYE, full("ones"), [[-1, 128]], A.is_equal, 0, 1)
-    ts(S("io1", 16, 32), S("io1", 0, 16), 15, A.bitwise_and)
-    ts(full("e16"), S("io1", 16, 32), 0.0, A.is_equal)
+    ts(S("io1", 16, 17), S("io1", 0, 1), 15, A.bitwise_and)
     K16 = S("cols", 0, 1)
     NCOL = S("cols", 1, 2)
     cp(K16, S("io1", 16, 17))
     fill(full("zero"), 0.0)
-    fill(full("c2048"), 2048.0)
-    fill(S("tb", 0, 1040), 0.0)
-    for e in range(10):
-        o = S("parw0", 1040 * e, 1040 * e + 1040) if e < 4 else S("parw1", 1040 * (e - 4), 1040 * (e - 3))
+    level(full("c2048"), 2048)
+    fill(full("tb"), 0.0)
+    for e in range(8):
+        o = S("parw%d" % (e // 4), 1040 * (e % 4), 1040 * (e % 4) + 1040)
         if OPT["zv"][e] == "V":
             fill(o, 0.0)
         elif OPT["zv"][e] == "G":
             flat(o, 0)
         else:
-            act(o, S("tb", 0, 1040), AF.Copy)
-    for e in range(2):
-        fill(S("cols", 4, 5, 1, 64, 64 * e), 4096.0 - 2048 * e)
-        fill(S("cols", 5, 6, 1, 64, 64 * e), 6192.0 - 2048 * e)
+            act(o, full("tb"), AF.Copy)
     cp(full("wtf"), full("wti"))
     cp(full("limf"), full("limi"))
+    part[0] = "b0"
+    cp(S("parb", 0, 256), full("pari"))
+    tt(S("parb", 256, 512), full("pari"), S("parb", 0, 256), A.subtract)
     for z in range(2):
         part[0] = "b%d" % z
-        c = (256 * z, 256 * z + 256)
+        if z:
+            objects(1, "Y")
         ts(third("vb0", 128 * z, 128 * z + 128), S("whoi", 128 * z, 128 * z + 128), -2048.0, A.add)
-        for e in range(2):
-            ts(S("parj", *c, 1, 64, 64 * e), S("pari", *c, 1, 64, 64 * e), (4032, 63)[e], A.bitwise_and)
-        cp(S("parb", *c), S("parj", *c))
-        dma("Y", "l_tab%d" % z, [(lambda T, e=e, h=h, z=z: T["parw%d" % z][64 * h + e:64 * h + 64:16, 16 + 2048 * (z > h):4112 + 2048 * (z > h)],
-                                  lambda T, e=e, c=c: T.parb[64 * e:64 * e + 64, c[0]:c[1]]) for e in range(2) for h in range(2)],
-            [S("parb", *c)], [S("parw%d" % z, 16, 4112 + 2048 * z)], 3.2)
+        dma("Y", "l_tab%d" % z, [(lambda T, e=e, h=h, z=z: T["parw%d" % z][64 * h + e:64 * h + 64:16, P0:P0 + 4096],
+                                  lambda T, e=e, z=z: T.parb[64 * z:64 * z + 64, 256 * e:256 * e + 256]) for e in range(2) for h in range(2)],
+            [full("parb")], [S("parw%d" % z, P0, P0 + 4096)], 1.7 + 1.5 * z)
+        in_turn()
+        claims_in("Y", "l_claim%d" % z, z, [0, 1] if z else [1], [(0, 4096)], 3.2 + 3.4 * z)
         part[0] = ""
         mark(full("dup%d" % z), "zero", [[0, 2], [-1, 64]], -64 * z, 1, 1)
         mark(full("exf%d" % z), "zero", [[0, 2], [-1, 4], [0, 16]], -4 * z, 1, 1)
@@ -370,83 +381,76 @@ def build(nE, vis):
         times(S("cols", 2 + z, 3 + z), S(b, 4, 5), -0.5)
     for z in range(2):
         part[0] = "r%d" % z
-        r, cw = slice(64 * z, 64 * z + 64), "claimw%d" % z
-        dma("Y", "l_again%d" % z, [(lambda T, e=e, a=a, b=b, cw=cw, r=r: T[cw][64 * e:64 * e + 64, a:b], lambda T, a=a, b=b, r=r: T.claim[r, 0:b - a])
-                                   for e in range(2) for a, b in ((4096, 8192), (8192, CW))],
-            [S("claimw0", 4096, CW)] if z else [S("claimw1", 0, 4096), S("parw1", 16, 17)], [S(cw, 4096, CW)], 5.5)
+        claims_in("Y", "l_again%d" % z, z, [0, 1], [(4096, 8192), (8192, CW)], 11.0 + 4.5 * z)
     part[0] = ""
-    fill(full("zx"), 0.0)
+    level(full("zx"), 0)
     times(S("zx", 15, 143, 16), SET, 1)
-    if OPT["relu"]:
-        times(full("zx2"), full("zx"), 2)
-        times(full("zxn"), full("zx"), -1)
     for name, c in (("neye", -1), ("e18", 2 ** 18), ("m64", -64)):
         mark(full(name), "zero", [[-1, 128]], 0, 1, c)
     for e in range(2):
         asel(S("lf", 1024 * e, 1024 * e + 1024), S("tb", 0, 1024), [[-1, 8], [-16, 8], [0, 16]], A.not_equal, -8 * e, 1, -256.0)
         asel(S("lf", 1024 * e, 1024 + 896 * e), S("lf", 1024 * e, 1024 + 896 * e), [[-1, 8 - e], [-16, 8], [0, 16]], A.not_equal, -8 * e - 1, 1, 256.0)
-    fill(full("cm256"), -256.0)
+    level(full("cm256"), -256)
+    for e, w in enumerate((0.0, 1.0, 0.5 - 2.0 ** -11)):
+        fill(S("sum3", e, 192, 3), w)
+    fill(S("mx", 77, 4 * MW, 48), 1024.0)
     ROW = [[0, 16], [1, 16]]
     for e, w in enumerate((1, 2, -1)):
         for j in range(2):
             times(S("b4k", 16 * e + 8 * j, 16 * e + 8 * j + 8), SET, 4096 * w)
     times(full("b64"), full("b4k"), 1.0 / 64)
     iota(S("ktile", 0, 128), [[0, 8], [1, 16]], 0, 0)
-    fill(S("ktile", 128, 256), 0.0)
+    level(S("ktile", 128, 256), 0)
     mark(full("rm"), "zero", ROW, 0, 0, 1e9)
     flat(full("rmn"), 2 ** 24 - 1)
-    fill(S("rmn", 0, 256, 16), -1e9)
-    asel(full("r2"), full("zero"), ROW, A.is_equal, -1, 0, 1.0)
+    mark(full("rmn"), "rmn", ROW, 0, 0, -1e9)
+    asel(full("r2"), S("tb", 0, 272), [[0, 17], [1, 16]], A.is_equal, -1, 0, 1.0)
     iota(S("io1", 32, 40), [[16, 8]], 0, 0)
-    ts(S("ptile", 0, 8), S("io1", 32, 40), K16, A.add, 16.0, A.mult)
+    ts(full("ptile"), S("io1", 32, 40), K16, A.add, 16.0, A.mult)
     iota(S("io1", 48, 64), [[1, 16]], 0, 0)
     cp(full("zo"), S("io1", 48, 64))
     ts(S("mk", 0, 128), S("ktile", 0, 128), K16, A.is_equal, 64.0, A.mult)
     times(S("mk", 128, 256), S("mk", 0, 128), 1.0 / 64)
+    times(full("mkn"), full("mk"), -1)
     rows = sorted(set(n for o in [OPT] + list(OPT["job"].values()) for n in o.get("rows", {}).values()) - {0})
     if rows:
         flat(full("cm1k"), -1024)
     for n in rows:
-        asel(full("ckf%d" % n), full("zero"), [[0, 16], [-1, 16]], A.is_ge, 15 - n, 0, 2.0 ** 20)
-        asel(full("vrow"), BLK, [[0, 8], [1, 16]], A.is_ge, n - 16, 0)
+        asel(full("ckf%d" % n), full("zero"), [[0, 64], [-1, 4]], A.is_ge, 3 - n // 4, 0, 2.0 ** 20)
+        asel(full("vrow"), BLK, [[0, 32], [1, 4]], A.is_ge, n // 4 - 4, 0)
         for j in range(2):
             times(S("cme%d" % n, 128 * j, 128 * j + 128), full("vrow"), -4096)
-        ts(full("cmf%d" % n), full("cme%d" % n), 1.0 / 64, A.mult)
-    cp(S("thi", 0, 2), S("thb", 2, 4))
-    ts(S("thi", 2, 4), S("thi", 0, 2), 4, A.arith_shift_right)
-    ts(S("thi", 4, 6), S("thi", 0, 2), 15, A.bitwise_and)
+        times(full("cmf%d" % n), full("cme%d" % n), 1.0 / 64)
     mark(full("kval"), "zero", [[0, 2], [1, 16]], -3, 0, -1088)
     mark(full("kval"), "kval", [[0, 2], [1, 16]], -11, 0, 69632)
     mark(full("kval"), "kval", [[0, 2], [1, 16]], -12, 0, 2112)
-    for e in range(4):
-        act(S("kval", 8 * e, 8 * e + 1), K16, AF.Identity, 3840.0, -256.0)
-        ts(S("kval", 8 * e + 1, 8 * e + 2), S("thi", 2 + e // 2, 3 + e // 2), -65536.0, A.mult)
-        ts(S("kval", 8 * e + 2, 8 * e + 3), S("thi", 4 + e // 2, 5 + e // 2), -4096.0, A.mult)
+    act(S("kval", 0, 32, 8), S("cm256", 0, 4), AF.Identity, 3840.0, K16)
+    times(S("cols", 6, 8), S("thb", 2, 4), -4096)
+    for e in (1, 9):
+        times(S("kval", e, 32, 16), S("cols", 6, 8), 1)
+        tt(S("kval", e + 1, 32, 16), S("cols", 6, 8), S("kval", e, 32, 16), A.subtract)
     b = bank()
     mm([(S(b, 128 * e, 128 * e + 128, 1, 8), S("kval", 8 * e, 8 * e + 8), EYE, True, True) for e in range(4)])
     times(full("kcon"), S(b, 0, 512, 1, 8), 1)
-    mark(full("eb"), "zero", [[-1, 8], [0, 16]], -16, 1, 64)
-    mark(full("eb"), "eb", [[-1, 8], [0, 16]], -24, 1, 1)
     for e in range(2):
-        o = S("en%d" % e, 0, 128, 1, 32)
-        mark(o, "zero", [[0, 2], [-1, 4], [-1000, 16]], -4 * e, 1, 64)
-        mark(o, o[0], [[0, 2], [-1, 4], [-1000, 16]], 992 - 4 * e, 1, 1)
-    times(NCOL, S("e16", 0, 1), -64)
-    iota(full("jt"), [[0, 4], [-16, 2], [1, 32]], 0, 0)
-    ts(full("dcon"), full("jt"), K16, A.is_ge, 8192.0, A.mult)
-    fill(S("dcon", 31, 256, 32), 0.0)
-    iota(full("wcon"), [[0, 4], [-16, 2], [0, 32]], 31, 0)
-    ts(full("wcon"), full("wcon"), K16, A.subtract)
-    fill(S("wcon", 0, 256, 32), 4192.0)
+        for name, base in (("en%d", 992), ("enf%d", -8)):
+            o = S(name % e, 0, 128, 1, 32)
+            mark(o, "zero", [[0, 2], [-1, 4], [-1000, 16]], -4 * e, 1, 64)
+            mark(o, o[0], [[0, 2], [-1, 4], [-1000, 16]], base - 4 * e, 1, 1)
+    ts(NCOL, K16, 0.0, A.is_equal, -64.0, A.mult)
+    ASIDE = [K16, S("cols", 4, 5)]
+    act(ASIDE[1], K16, AF.Identity, 16.0)
+    ts(S("io1", 65, 66), S("io1", 0, 1), 31, A.bitwise_and)
+    cp(S("cols", 5, 6), S("io1", 65, 66))
+    iota(full("dcon"), [[16, 2], [0, 8], [1, 16]], 0, 0)
+    ts(full("dcon"), full("dcon"), S("cols", 5, 6), A.is_le, 8192.0, A.mult)
+    band(full("nsel"), [[16, 2], [32, 4], [0, 32]], 16)
+    band(S("ns32", 0, 4), [[32, 4]], 32)
+    times(full("nset"), SET, -1)
     for e in range(2):
-        fill(S("dq", e, 768, 3), float(e))
-    asel(full("b2"), full("zero"), [[16, 8], [0, 32]], A.is_gt, 0, -1, -1.0)
-    asel(full("b2"), full("b2"), [[16, 8], [0, 32]], A.is_ge, 15, -1)
-    fill(S("b2", 31, 256, 32), 0.0)
-    if OPT["rep"]:
-        for e in range(2):
-            mark(S("b3", 256 * e, 256 * e + 256), "zero", [[-32, 4], [0, 2], [-1, 32]], 0, 1, 64 ** (1 - e))
-        fill(S("b3", 31, 512, 32), 0.0)
+        level(S("dq", e, 768, 3), e)
+    for z in range(2):
+        flat(full("ca%d" % z), 0)
 
     def send(what, t, z):
         c = (WIDE[what] * z, WIDE[what] * (z + 1))
@@ -475,7 +479,7 @@ def build(nE, vis):
         c0, c1, b = 128 * z, 128 * z + 128, "pz%d" % z
         c = (c0, c1)
         part[0] = "n%d" % z
-        ts(S("vl", *c), third("vb%d" % t, *c), S("cols", 4, 5) if z else 2048.0, A.add)
+        ts(S("vl", *c), third("vb%d" % t, *c), 2048.0, A.add)
         part[0] = "x%d" % z
         um = S("um%d" % (t % 2), *c)
         U, s = S(b, 256, 384), S(b, 384, 512)
@@ -488,7 +492,7 @@ def build(nE, vis):
         ts(um, S("t1", *c), 4095, A.bitwise_and)
         place(t, s, um, S("t2", *c), S("t3", *c), S("c1", *c), S("hl", *c))
         part[0] = "y%d" % z
-        n = OPT["gl"]["x"]
+        n = opt("gl")["x"]
         for a in range(c0, c1, n):
             move("x%d" % ((a - c0) // 32), S("x%d" % (t % 2), 16 * a, 16 * (a + n)), claims(t, z, "hl", a, n))
 
@@ -497,36 +501,21 @@ def build(nE, vis):
         c, L, X, X2 = (c0, c1), c1 - c0, 16 * c0, 16 * c1
         p, D, v = S(b, o, o + 192, 3), S(b, o + 192, o + 256), third("vb%d" % t, *c)
         part[0] = "p%d%d" % (z, n)
-        n1, n2 = OPT["gl"]["p"], OPT["gl"]["g"]
+        n1, n2, n3 = opt("gl")["p"], opt("gl")["g"], opt("al")
         for a in range(c0, c1, n1):
-            move("p%d" % (a % 128 // 32), S("pr", 16 * a, 16 * (a + n1)), IND("parw%d" % z, 16, 4112 + 2048 * z, "vl", a, a + n1))
+            move("p%d" % (a % 128 // 32), S("d", 16 * a, 16 * (a + n1)), IND("parw%d" % z, P0, P0 + 4096, "vl", a, a + n1))
         part[0] = "q%d%d" % (z, n)
         mm([(S(b, o + 1, o + 192, 3), NEYE, v, True, False), (S(b, o + 1, o + 192, 3), NEYE, S("c2048", 0, L), False, True), (S(b, o + 2, o + 192, 3), EYE, v, True, True)])
         part[0] = "z%d%d" % (z, n)
-        acc(p, [(sx(k), S("pr", X + k, X2, 16)) for k in range(16)])
+        acc(p, [(sx(k), S("d", X + k, X2, 16)) for k in range(16)])
         place(t, p, S("um%d" % (t % 2), *c), S("t4", *c), S("t5", *c), S("c2", *c), S("zl", *c))
         part[0] = "g%d%d" % (z, n)
         for a in range(c0, c1, n2):
-            if a % 128 // 32 in opt("apart"):
-                act(S("d", 16 * a, 16 * (a + n2)), claims(t, z, "zl", a, n2), AF.Copy)
-            else:
-                tt(S("d", 16 * a, 16 * (a + n2)), claims(t, z, "zl", a, n2), S("x%d" % (t % 2), 16 * a, 16 * (a + n2)), A.subtract)
+            tt(S("d", 16 * a, 16 * (a + n2)), claims(t, z, "zl", a, n2), S("x%d" % (t % 2), 16 * a, 16 * (a + n2)), A.subtract)
         part[0] = "d%d%d" % (z, n)
-        if opt("apart"):
-            for a in range(16 * c0, 16 * c1, 512):
-                e = S("d", a, a + 512)
-                if a % 2048 // 512 in opt("apart"):
-                    e = S(bank(), 0, 512)
-                    acc(e, [(NEYE, S("x%d" % (t % 2), a, a + 512)), (EYE, S("d", a, a + 512))])
-                act(S("ad", a, a + 512), e, AF.Abs)
-            acc(D, [(sx(k), S("ad", X + k, X2, 16)) for k in range(16)])
-        elif n in opt("relu"):
-            ts(S("ad", X, X2), S("d", X, X2), 0.0, A.max)
-            pile([(D, sx(k, "zxn"), S("d", X + k, X2, 16)) for k in range(16)], [(D, sx(k, "zx2"), S("ad", X + k, X2, 16)) for k in range(16)])
-        else:
-            for a in range(c0, c1, OPT["al"]):
-                act(S("ad", 16 * a, 16 * (a + OPT["al"])), S("d", 16 * a, 16 * (a + OPT["al"])), AF.Abs)
-            acc(D, [(sx(k), S("ad", X + k, X2, 16)) for k in range(16)])
+        for a in range(c0, c1, n3):
+            act(S("ad", 16 * a, 16 * (a + n3)), S("d", 16 * a, 16 * (a + n3)), AF.Abs)
+        acc(D, [(sx(k), S("ad", X + k, X2, 16)) for k in range(16)])
         ts(third("dq", *c), D, S("thc%d" % t if t else "thb", z, z + 1), A.is_lt)
 
     def st_names(t, z, n):
@@ -539,26 +528,16 @@ def build(nE, vis):
         c, L, X, X2 = (c0, c1), c1 - c0, 16 * c0, 16 * c1
         x = "x%d" % (t % 2)
         part[0] = "m%d%d" % (z, n)
-        for l in range(c0, c1, 32):
+        for e in range(2):
             a = bank()
-            mm([(S(a, k, 512, 16), S("lf", 128 * k, 128 * k + 128), third("dq", l, l + 32), True, k < 15) for k in range(16)] +
-               [(S(a, 15, 512, 16), EYE, S("cm256", 0, 32), False, True)])
-            if l % 128 // 32 in opt("direct"):
-                e = (16 * l, 16 * l + 512)
-                scan(S("mx", *e), S(x, *e), S(a, 0, 512), -1.0, A.max, A.add)
-                scan(S("mn", *e), S(x, *e), S(a, 0, 512), 256.0, A.min, A.subtract)
-            else:
-                move("l%d" % (l % 128 // 32), S("la", 16 * l, 16 * l + 512), S(a, 0, 512))
+            mm([(S(a, k // 2, 512, 8), S("lf", 128 * k, 128 * k + 128), third("dq", *c), True, k < 15) for k in range(e, 16, 2)] +
+               [(S(a, 7, 512, 8), EYE, S("cm256", 0, L), False, True)] * e)
+            move("l%d" % (2 * n + e), S("la%d" % e, X + e, X2, 2), S(a, 0, 512))
         part[0] = "s%d%d" % (z, n)
-        for a in range(X, X2, 16 * OPT["sl"][n]):
-            if a % 2048 // 512 in opt("direct"):
-                continue
-            e = a + 16 * OPT["sl"][n]
-            scan(S("mx", a, e), S(x, a, e), S("la", a, e), -1.0, A.max, A.add)
-            scan(S("mn", a, e), S(x, a, e), S("la", a, e), 256.0, A.min, A.subtract)
-        w = S(b, o + 192, o + 256)
-        acc(w, [(EYE, S("mx", X + 15, X2, 16)), (EYE, S("mn", X + 15, X2, 16))])
-        ts(S("mm_", *c), w, 0.5, A.mult, 1023.75, A.add)
+        a = MW * (c0 // 64)
+        scan(S("mx0", a, a + 3072, 3), S(x, X, X2), S("la", X, X2), -1.0, A.max, A.add)
+        scan(S("mx1", a + 16, a + 3088, 3), S(x, X, X2), S("la", X, X2), 256.0, A.min, A.subtract)
+        scan(S("mm_", 3 * c0, 3 * c1), full("sum3"), S("mx", a + 45, a + 3104, 16), 0.0, A.mult, A.add)
 
     def st_count(t):
         part[0] = "c1"
@@ -570,33 +549,32 @@ def build(nE, vis):
         ts(S("cint", 2, 4), S("cint", 0, 2), 31, A.bitwise_and)
         tt(full("thc%d" % (t + 1)), S("cint", 2, 4), S("thb", 0, 2), A.add)
 
-    def distances(t, z, mid, out, bias, w, weights):
-        L, X, x, b = 128, 2048 * z, "x%d" % (t % 2), "pt%d" % z
-        K, nv, n = 512 // L, opt("rows")[part[0][0]], width(full(weights)) // 3
-        own = [(S(b, k, w, 16), S(x, X + k, X + 16 * L, 16), S(weights, 2 * n, 3 * n)) for k in range(16 - nv, 16)]
+    def distances(t, z, mid, bias, weights):
+        X, x, b = 2048 * z, "x%d" % (t % 2), "pt%d" % z
+        nv, n = opt("rows")[part[0][0]], width(full(weights)) // 3
+        onv = range(4 - nv // 4, 4)
+        own = [(S(b, k, 256, 16), S(x, X + k, X + 2048, 16), S(weights, 2 * n, 3 * n)) for k in range(16) if k % 4 in onv]
         lots = []
-        if nv:
-            m = S("pz%d" % z, 0, L)
-            acc(m, [(EYE, mid)] + ([(EYE, full("cm1k"))] if bias else []))
-        for q in range(0, 16 - nv, K):
-            a, gr = bank(), []
-            for e in range(K):
-                o = S(a, L * e, L * e + L)
-                gr += [(o, EYE, S(x, X + q + e, X + 16 * L, 16), True, False), (o, NEYE, mid, False, True)]
-            mm(gr)
-            act(S(out, X + L * q, X + L * (q + K)), S(a, 0, L * K), AF.Abs, bias)
-            lots.append([(S(b, k, w, 16), S(out, X + L * k, X + L * k + L), S(weights, 0, n)) for k in range(q, q + K)])
-        for k in range(16 - nv, 16):
-            tt(S(out, X + L * k, X + L * k + L), S(x, X + k, X + 16 * L, 16), m, A.max)
-        for j, q in enumerate(range(16 - nv, 16, 4)):
-            lots.insert(min(2 * j, len(lots)), [(S(b, k, w, 16), S(out, X + L * k, X + L * k + L), S(weights, n, 2 * n)) for k in range(q, q + 4)])
+        for q in (3, 0, 2, 1) if nv else range(4):
+            a, rows, out = bank(), S(x, X + q, X + 2048, 4), S("af", X + 512 * q, X + 512 * q + 512)
+            if q not in onv:
+                pile([(S(a, 0, 512), EYE, rows)], [(S(a, r, 512, 4), NEYE, mid) for r in range(4)])
+                act(out, S(a, 0, 512), AF.Abs, bias)
+            else:
+                if bias:
+                    pile([(S(a, 0, 512), EYE, full("cm1k"))], [(S(a, r, 512, 4), EYE, mid) for r in range(4)])
+                else:
+                    mm([(S(a, r, 512, 4), EYE, mid, True, True) for r in range(4)])
+                tt(out, rows, S(a, 0, 512), A.max)
+            w = S(weights, n, 2 * n) if q in onv else S(weights, 0, n)
+            lots.append([(S(b, 4 * r + q, 256, 16), S("af", out[1] + r, out[2], 4), w) for r in range(4)])
         return nv, own, lots
 
     def st_truth(t, z):
         c, b, q = (128 * z, 128 * z + 128), "pt%d" % z, 8 * z
-        key, mid = S(b, 0, 256), S("mm_", *c)
+        key, mid = S(b, 0, 256), third("mm_", *c)
         part[0] = "f%d" % z
-        nv, own, lots = distances(t, z, mid, "af", 1024.0, 256, "b64")
+        nv, own, lots = distances(t, z, mid, 1024.0, "b64")
         part[0] = "t%d" % z
         first = [(key, EYE, full("ktile"))] + own + [(S(b, e, e + 128), third("dq", *c), full("e18")) for e in (0, 128)]
         if nv:
@@ -606,7 +584,7 @@ def build(nE, vis):
         scan(full("km%d" % z), full("rm"), key, 0.0, A.max, A.min)
         tt(S("ct%d" % z, 0, 8), S("km%d" % z, 15, 128, 16), S("km%d" % z, 143, 256, 16), A.subtract)
         tt(S("zy", *c), IND("ct%d" % z, 0, 8, "zo", 0, 8), S("mk", 128, 256), A.mult)
-        acc(S(b, 448, 456), [(EYE, S("ptile", 0, 8)), (S("zy", *c), SET)])
+        acc(S(b, 448, 456), [(EYE, full("ptile")), (S("zy", *c), SET)])
         cp(S("yl", q, q + 8), S(b, 448, 456))
         move("y", S("yy", *c), IND("x%d" % (t % 2), 16 * c[0], 16 * c[1], "yl", q, q + 8))
         part[0] = "u%d" % z
@@ -621,18 +599,19 @@ def build(nE, vis):
         part[0] = "e%d" % z
         v = third("vb%d" % t, *c)
         ts(S("vh", *c), v, 1.0 / 64, A.mult, 1120.5078125, A.add)
-        nv, own, lots = distances(t, z, S("yy", *c), "ae", None, 256, "b4k")
+        nv, own, lots = distances(t, z, S("yy", *c), None, "b4k")
         part[0] = "a%d" % z
         key, hi, lo = S(b, 0, 256), S(b, 0, 128), S(b, 128, 256)
         first = [(key, S("ones", 0, 128, 1, 8), S("kcon", c2, c2 + 256, 1, 8))] + own
         names = [(lo, S("vh", *c), full("m64")), (lo, v, EYE), (hi, S("vh", *c), EYE)]
         if nv:
             first.append((key, S("yy", *c), full("cme%d" % nv)))
-            lots[-1] = lots[-1] + names
+            late = 1 if nv == 4 else 3
+            lots[late] = names + lots[late]
         else:
             first += names
         pile(first, *lots)
-        pm, t2, k = "pm%d" % z, S("tt%d" % z, 1, 256), full("ca%d" % z)
+        pm, t2, k = "pm%d" % z, S("tt%d" % z, 1, 256), S("ca%d" % z, 0, 512, 16)
         scan(S(pm, 0, 256), full("rmn"), key, 0.0, A.min, A.max)
         tt(t2, S(b, 1, 256), S(pm, 0, 255), A.min)
         scan(S(pm, 257, 512), S("r2", 1, 256), t2, 0.0, A.mult, A.max)
@@ -640,36 +619,43 @@ def build(nE, vis):
         ts(r, m, R256, A.add, -R256, A.add)
         tt(k, m, r, A.subtract)
         part[0] = "h%d" % z
-        tt(S("zz", c2, c2 + 256), IND(k[0], 16, 32, "zo", 0, 16), full("mk"), A.mult)
-        Z = [S("zz", c2 + 128 * e, c2 + 128 * e + 128) for e in range(2)]
+        scan(S("zr", c2, c2 + 256), S("r2", 1, 257), S(k[0], 256, 512), 0.0, A.mult, A.add)
+        scan(S("zz", c2, c2 + 256), S("zr", c2, c2 + 256), full("mkn"), 0.0, A.max, A.mult)
         kt = S(bank(), 0, 128, 1, 32)
         acc(kt, [(k, EYE)])
         move("j", S("kt32", *c, 1, 32), kt)
-        N, D, W = bank(), S(b, 0, 256), S("pz%d" % z, 0, 256)
-        mm([(S(N, 128 * e, 128 * e + 128), S("en%d" % e, 0, 128, 1, 32), S("kt32", *c, 1, 32), True, True) for e in range(2)])
-        act(S("adat", c2, c2 + 256), S(N, 0, 256), AF.Identity, NCOL)
-        mm([(W, EYE, full("wcon"), True, False)] + [(S(W[0], 0, 256, 32), Z[e], S("b2", 0, 256, 32), False, e == 1) for e in range(2)])
-        if OPT["rep"]:
-            move("r", S("zr", c2, c2 + 256), IND(k[0], 16, 32, "zo", 0, 16))
-            pile([(D, EYE, full("dcon"))], [(D, S("zr", c2 + 128 * e, c2 + 128 * e + 128), S("b3", 256 * e, 256 * e + 256)) for e in range(2)], [(D, Z[e], full("b2")) for e in range(2)])
-        else:
-            pile([(D, EYE, full("dcon"))], [(D, Z[e], full("b2")) for e in range(2)],
-                 [(S(b, 32 * j, 32 * j + 31), full("eb"), S("kt32", c[0] + 32 * (j // 2), c[0] + 32 * (j // 2) + 31, 1, 32)) for j in range(8)])
-        if "e" in opt("onv"):
-            ts(S("ee", c2, c2 + 256), D, 0.0, A.not_equal, 8192.0, A.mult)
-        else:
-            act(S("ee", c2, c2 + 256), D, AF.Abs, None, 8192.0)
-        scan(S("prd", c2, c2 + 256), W, S("ee", c2, c2 + 256), 0.0, A.max, A.min)
-        if OPT["cross"]:
-            for e in (1, 0):
-                for h in range(2):
-                    ts(S("ol%d" % h, 16 * z + 8 * e, 16 * z + 8 * e + 8, 1, 64, 64 * h), S("prd", c2 + 30, c2 + 256, 32, 64, 64 * e), -1.0, A.mult, 4144.0 + 2048 * (z > h), A.add)
-        else:
-            mm([(S(b, 8 * e, 8 * e + 8), full("dup%d" % e), S("prd", c2 + 30, c2 + 256, 32), True, True) for e in range(2)])
-            ts(S("ol", 16 * z, 16 * z + 16), S(b, 0, 16), -1.0, A.mult, S("cols", 5, 6) if z else 4144.0, A.add)
+        N = bank()
+        last = t == vis - 1
+        ad, a0, table = ("adf%d" % z, 0, "plain%d" % z) if last else ("adat", c2, "parw%d" % z)
+        mm([(S(N, 128 * e, 128 * e + 128), S(("enf%d" if last else "en%d") % e, 0, 128, 1, 32), S("kt32", *c, 1, 32), True, True) for e in range(2)])
+        act(S(ad, a0, a0 + 256), S(N, 0, 256), AF.Identity, NCOL)
+        pile([(key, EYE, full("dcon"))],
+             [(S(b, 128 * j, 128 * j + 128), (full("m64"), NEYE)[e], S("zr", c2 + 128 * e, c2 + 128 * e + 128)) for j in range(2) for e in range(2)],
+             [(S(b, 128 * j, 128 * j + 128), S("nsel", 128 * j, 128 * j + 128), S("zz", c2 + 128 * e, c2 + 128 * e + 128)) for j in range(2) for e in range(2)])
+        ts(S("ee", c2, c2 + 256), key, 0.0, A.is_equal, 8192.0, A.mult)
+        O = bank()
+        both2 = [(e, h) for h in range(2) for e in range(2)]
+        pile([(S(O, 0, 16), EYE, S("zero", 0, 16))] +
+             [(S(O, 8 * e, 8 * e + 8, 1, 64, 64 * h), S("zz", c2 + 128 * j + 64 * e, c2 + 128 * j + 64 * e + 64), full("nset")) for e, h in both2 for j in range(2)],
+             [(S(O, 8 * e + j, 8 * e + 8, 2, 64, 64 * h), S("ee", c2 + 128 * j + 64 * e, c2 + 128 * j + 64 * e + 64), S("ns32", 0, 4)) for e, h in both2 for j in range(2)])
+        for j in range(2):
+            ts(S("ol%d" % j, 16 * z + j, 16 * z + 16, 2), S(O, j, 16, 2), P0 - 64.0, A.add, ASIDE[j], A.max)
+        ops[-1]["after"] = len(ops) - 2
         part[0] = "w%d" % z
         for a in range(7, -1, -1):
-            cp(IND("parw%d" % z, 0, PW[z], "ol", 16 * z + 2 * a, 16 * z + 2 * a + 2), S("adat", c2 + 32 * a, c2 + 32 * a + 32))
+            cp(IND(table, 0, PW, "ol", 16 * z + 2 * a, 16 * z + 2 * a + 2), S(ad, a0 + 32 * a, a0 + 32 * a + 32))
+
+    def halves(z, T, e):
+        return T["plain%d" % z][64 * e:64 * e + 64:16, P0 + 2048 * e:P0 + 2048 * e + 2048]
+
+    def st_plain(z):
+        c = (128 * z, 128 * z + 128)
+        part[0] = "o%d" % z
+        b = S(bank(), 0, 128)
+        mm([(S(b[0], 0, 128, 1, 64, 64 * e), S("zx", 15 - k, 79 - k), S("parw%d" % z, P0 + 2048 * e + 128 * k, P0 + 2048 * e + 128 * k + 128), k == 0, k == 15)
+            for e in range(2) for k in range(16)])
+        move("o", S("ypf", *c), b)
+        both("Y", "l_plain%d" % z, lambda T, e: halves(z, T, e), lambda T, e: T.ypf[64 * e:64 * e + 64, c[0]:c[1]], full("plain%d" % z), 2.5, [S("ypf", *c)])
 
     def st_store(z):
         c, t = (128 * z, 128 * z + 128), vis - 1
@@ -680,21 +666,16 @@ def build(nE, vis):
         for n, b in (("yv", "yvf"), ("ye", "yeb")):
             dma("Y", "l_%s%d" % (n, z), [(lambda T, e=e, n=n: T[n][r, 128 * e:128 * e + 128], lambda T, e=e, b=b: T[b][64 * e:64 * e + 64, c[0]:c[1]]) for e in range(2)],
                 [S(b, *c)], [], 2.0)
-        b = S(bank(), 0, 128)
-        if z:
-            acc(b, [(sx(k), S("parw1", 2064 + 128 * k, 2192 + 128 * k)) for k in range(16)])
-        else:
-            mm([(S(b[0], 0, 128, 1, 64, 64 * e), S("zx", 15 - k, 79 - k), S("parw0", 16 + 2048 * e + 128 * k, 144 + 2048 * e + 128 * k), k == 0, k == 15)
-                for e in range(2) for k in range(16)])
-        move("o", S("ypf", *c), b)
         for e in range(2):
-            dma("YS"[e], "l_yp%d%d" % (e, z), [(lambda T, e=e: T.yp[4 * z:4 * z + 4, 2048 * e:2048 * e + 2048], lambda T, e=e: T.ypf[64 * e:64 * e + 64, c[0]:c[1]])],
-                [S("ypf", *c)], [], 2.0)
+            dma("YS"[e], "l_yp%d%d" % (e, z), [(lambda T, e=e: T.yp[4 * z:4 * z + 4, 2048 * e:2048 * e + 2048], lambda T, e=e: halves(z, T, e))],
+                [full("plain%d" % z)], [], 2.0)
 
     for t in range(vis):
         part[1] = t
         for z in range(2):
             st_hash(t, z)
+            if t == vis - 1:
+                st_plain(z)
             for f in (st_z, st_m, st_names):
                 for n in range(2):
                     f(t, z, n)
@@ -726,8 +707,6 @@ def build(nE, vis):
             l.append((i, a, b, True))
         if o["q"] == "N":
             dep = {o["send"]}
-        if o["q"] == "V" and o["R"][-1:] and o["R"][-1][0][:4] == "bank" and ops[i - 1]["R"][-1:] == o["R"][-1:]:
-            o["after"] = i - 1
         o["B"] = sorted(set(r[0] for r in o["R"] + o["W"] if BUF[r[0]][0] == "psum"))
         for b in o["B"]:
             if o["q"] == "P":
@@ -743,428 +722,246 @@ def build(nE, vis):
         if "after" in o:
             dep.add(o["after"])
             o["O"].add(o["after"])
-        o["D"], o["i"] = dep, i
+        o["D"], o["i"], o["j"] = dep, i, 2 * o["t"] + (o["part"][1:2] == "1")
     return ops
 
 
 def graph(ops):
     n = len(ops)
-    pred, pair, seen, above = [sorted(o["D"]) for o in ops], {}, {}, [0] * n
+    pred, users, above = [sorted(o["D"]) for o in ops], {}, [0] * n
     for i, o in enumerate(ops):
         o["occ"] = 0.15 * len(o["f"]) if o["sem"] and o["q"] in "YS" else o["c"]
         o["fix"] = [b for b in o["B"] if b in SCRATCH]
         for b in o["B"]:
             if b not in SCRATCH:
                 o["any"] = b
-                pair.setdefault(b, []).append(i)
-        w = (o["t"], o["part"])
-        o["cls"] = (o["part"], seen.get(w, 0), OPT.get("phase", (0, 1, 1, 1, 2))[o["t"]])
-        seen[w] = seen.get(w, 0) + 1
+                users.setdefault(b, []).append(i)
         far = 0
         for j in pred[i]:
             far |= above[j]
         above[i] = far
         for j in pred[i]:
             above[i] |= 1 << j
-        pred[i] = [(j, 0.0 if j in o["O"] else LAT) for j in pred[i] if not far >> j & 1]
-    return pred, {p[0]: p[-1] for p in pair.values()}
+        pred[i] = [(j, ops[j]["occ"] - ops[j]["c"] if j in o["O"] else LAT) for j in pred[i] if not far >> j & 1]
+    return pred, {u[0]: u for u in users.values()}
 
 
-def greedy(ops, pred, mate):
+def first_turns(ops, pred):
     n = len(ops)
+    off, key, late = [0.0] * n, [None] * n, [1e9] * n
+    for i, o in enumerate(ops):
+        p = o["part"]
+        off[i] = max([off[j] + ops[j]["c"] + l for j, l in pred[i] if (ops[j]["part"], ops[j]["t"]) == (p, o["t"])], default=0.0)
+        if p[:1] + p[2:] in LEAD:
+            lead, j = LEAD[p[:1] + p[2:]] + off[i], o["j"]
+            key[i] = max([lead * (ALONE if j in (0, 2 * VIS - 1) and lead > 0 else 1.0) + HALF * j - (j > 0) * (1 - ALONE) * 2 * HALF] + [key[j] + 1e-3 for j, l in pred[i] if key[j] is not None])
+    for i in range(n - 1, -1, -1):
+        if key[i] is None:
+            key[i] = min(late[i] - ops[i]["c"], 0.0) - 20.0 * (ops[i]["part"][:1] == "l")
+        for j, l in pred[i]:
+            late[j] = min(late[j], key[i] - l)
+    return key
+
+
+def line_up(ops, pred, users, key, early=False):
+    n = len(ops)
+    need = [set(j for j, l in pred[i]) for i in range(n)]
+    safe = {i: set(j for k in u for j, l in pred[k]) - set(u) for i, u in users.items()}
+    last = set(u[-1] for u in users.values())
+    todo, done, seq, free = sorted(range(n), key=lambda i: key[i]), set(), [], len(BIGB)
+    while todo:
+        i = next(i for i in todo if need[i] <= done and (i not in users or free > (1 if early else len(BIGB)) or free and safe[i] <= done))
+        todo.remove(i)
+        done.add(i)
+        seq.append(i)
+        free += (i in last) - (i in users)
+    return seq
+
+
+def refine(ops, pred, users, seq):
+    n, NB, STEP = len(ops), len(BIGB), 20
+    res = {r: k for k, r in enumerate(list("VSPGYN") + FIXB)}
+    NR = len(res)
+    last = set(u[-1] for u in users.values())
+    Q = [res[o["q"]] for o in ops]
+    C = [o["c"] for o in ops]
+    OCC = [o["occ"] if o["q"] != "N" else -1e9 for o in ops]
+    FIX = [[res[b] for b in o["fix"]] for o in ops]
+    POOL = [1 if i in users else 2 if i in last else 0 for i in range(n)]
     succ = [[] for _ in range(n)]
     for i in range(n):
         for j, l in pred[i]:
             succ[j].append((i, l))
-    way = [0.0] * n
-    for i in range(n - 1, -1, -1):
-        way[i] = ops[i]["c"] + max([way[j] + l for j, l in succ[i]], default=OPT["ahead"] * (ops[i]["part"][1:2] == "0"))
-    second = {j: i for i, j in mate.items()}
-    left, ready, at = [len(p) for p in pred], {q: [] for q in "VSPGYN"}, [0.0] * n
-    for i in range(n):
-        if not left[i]:
-            ready[ops[i]["q"]].append(i)
-    free, last, big, hold, start = {}, {}, {b: 0.0 for b in range(len(BIGB))}, {}, [0.0] * n
-    for _ in range(n):
-        best = None
-        for q, l in ready.items():
-            can = []
-            for i in l:
-                t = max(at[i], free.get(q, 0.0))
-                for b in ops[i]["fix"]:
-                    if b in last:
-                        t = max(t, last[b][0] + (LAT if last[b][1] != q else 0.0))
-                if i in mate:
-                    if not big:
-                        continue
-                    t = max(t, min(big.values()))
-                can.append((t, i))
-            if can:
-                t0 = min(can)[0] + OPT["slack"]
-                w, t, i = max((way[i] + (50.0 if i in second else 0.0), t, i) for t, i in can if t <= t0)
-                if best is None or t < best[0]:
-                    best = (t, i)
-        t, i = best
-        o = ops[i]
-        ready[o["q"]].remove(i)
-        start[i] = t
-        if o["q"] != "N":
-            free[o["q"]] = t + o["occ"]
-        for b in o["fix"]:
-            last[b] = (t + o["c"], o["q"])
-        if i in mate:
-            hold[i] = min(big, key=big.get)
-            del big[hold[i]]
-        if i in second:
-            big[hold[second[i]]] = t + o["c"] + LAT
-        for j, l in succ[i]:
-            at[j] = max(at[j], t + o["c"] + l)
-            left[j] -= 1
-            if not left[j]:
-                ready[ops[j]["q"]].append(j)
-    return start
+    whole = [(pred[i], 0.0, Q[i], C[i], OCC[i], FIX[i], POOL[i], 0.0, 0.0) for i in range(n)]
+    rnd = np.random.default_rng(OPT["seed"])
 
+    def tails(seq, b):
+        tail = [0.0] * n
+        nq, acq = [None] * NR, [i for i in seq if POOL[i] == 1]
+        r = len(acq)
+        for i in reversed(seq[b:]):
+            t = max([l + tail[j] for j, l in succ[i]], default=0.0)
+            for k in FIX[i]:
+                j = nq[k]
+                if j is not None:
+                    t = max(t, tail[j] + (LAT if Q[j] != Q[i] else 0.0))
+                nq[k] = i
+            if POOL[i] == 2:
+                r -= 1
+                if r + NB < len(acq):
+                    t = max(t, LAT + tail[acq[r + NB]])
+            t += C[i]
+            j = nq[Q[i]]
+            if j is not None:
+                t = max(t, OCC[i] + tail[j])
+            nq[Q[i]] = i
+            tail[i] = t
+        return tail, nq
 
-def timer(ops, pred, mate, base):
-    n = len(ops)
-    second = {j: i for i, j in mate.items()}
-    c, occ, q, fix = [[o[k] for o in ops] for k in ("c", "occ", "q", "fix")]
-    arcs = [(j, i) for i in range(n) for j, l in pred[i]]
-    both = [(o["cls"], b) for o, b in zip(ops, base)]
-
-    def run(turns):
-        key = [turns[w] + b for w, b in both]
-        for j, i in arcs:
-            if key[j] >= key[i]:
-                key[i] = key[j] + 1e-5
-        order = np.argsort(key, kind="stable").tolist()
-        end, why, start = [0.0] * n, [None] * n, [0.0] * n
-        free, last, big, hold, idle = {}, {}, [(0.0, -1)] * len(BIGB), {}, list(range(len(BIGB)))
-        for i in order:
-            t, w, qi = 0.0, None, q[i]
-            for j, l in pred[i]:
-                if end[j] + l > t:
-                    t, w = end[j] + l, (j, 1)
-            if qi != "N":
-                e = free.get(qi)
-                if e is not None and e[0] >= t:
-                    t, w = e[0], (e[1], 0)
-                for b in fix[i]:
-                    e = last.get(b)
-                    if e is not None:
-                        u = end[e] + (LAT if q[e] != qi else 0.0)
+    def forward(part, st, row, snaps, end, why, thr):
+        free, who, lq, rel, na, best, arg = st[0][:], st[1][:], st[2][:], st[3][:], st[4], st[5], st[6]
+        for k in range(0, len(part), STEP):
+            snaps.append((free[:], who[:], lq[:], rel[:], na, best, arg))
+            for i in part[k:k + STEP]:
+                pr, soon, qi, c, occ, fix, pool, xt, lb = row[i]
+                t, w = free[qi], who[qi]
+                if soon > t:
+                    t, w = soon, -1
+                for j, l in pr:
+                    u = end[j] + l
+                    if u > t:
+                        t, w = u, -2 - j
+                if pool:
+                    if pool == 2:
+                        rel.append(i)
+                    else:
+                        if na >= len(rel):
+                            return None
+                        j = rel[na]
+                        na += 1
+                        if end[j] + LAT > t:
+                            t, w = end[j] + LAT, j
+                if fix:
+                    for b in fix:
+                        u = free[b] if lq[b] == qi else free[b] + LAT
                         if u > t:
-                            t, w = u, (e, 0)
-                    last[b] = i
-                if i in mate:
-                    if not idle:
+                            t, w = u, who[b]
+                    for b in fix:
+                        free[b], who[b], lq[b] = t + c, i, qi
+                free[qi], who[qi] = t + occ, i
+                t += c
+                end[i], why[i] = t, w
+                if t + lb > best:
+                    if t + lb > thr:
                         return None
-                    b = min(idle, key=lambda b: big[b][0])
-                    idle.remove(b)
-                    hold[i] = b
-                    if big[b][0] > t:
-                        t, w = big[b][0], (big[b][1], 0)
-                free[qi] = (t + occ[i], i)
-            start[i], end[i], why[i] = t, t + c[i], w
-            if i in second:
-                big[hold[second[i]]] = (end[i] + LAT, i)
-                idle.append(hold[second[i]])
-        i = max(range(n), key=lambda i: end[i])
-        total, pairs = end[i], []
-        while why[i] is not None:
-            if not why[i][1]:
-                pairs.append((why[i][0], i))
-            i = why[i][0]
-        return total, pairs, start, hold, order, key
-    return run
+                    if t + xt > best:
+                        best, arg = t + xt, i
+        return free, who, lq, rel, na, best, arg
 
+    def close(s, end, exits, after, tail):
+        free, who, lq, rel, na, best, arg = s
+        soft = 0.0
+        for q, t, e in exits:
+            u = free[q] + t + (LAT if q > 5 and lq[q] != e else 0.0)
+            if q < 3:
+                soft += u
+            if u > best:
+                best, arg = u, who[q]
+        for r, j in zip(rel[na:], after):
+            if end[r] + LAT + tail[j] > best:
+                best, arg = end[r] + LAT + tail[j], r
+        return arg, best + 0.02 * soft, best
 
-def anneal(ops, pred, run, base):
-    cls = [o["cls"] for o in ops]
-    turns, parts = {w: 0.0 for w in cls}, {}
-    for w in turns:
-        parts.setdefault((w[0], w[2]), []).append(w)
-    rnd, tries, heat = np.random.default_rng(OPT["seed"]), OPT["tries"], OPT["heat"]
-    got = run(turns)
-    best = got
-    for it in range(tries):
-        r = rnd.random(6).tolist()
-        j, i = got[1][int(r[0] * len(got[1]))]
-        key, new = got[5], dict(turns)
-        more = 0.5 * r[2] if r[2] > 0.5 else 0.0
-        if r[4] < 0.2:
-            a, sign = (i, -1) if r[1] < 0.5 else (j, 1)
-            for w in parts[(cls[a][0], cls[a][2])]:
-                if r[5] >= 0.5 or sign * (w[1] - cls[a][1]) >= 0:
-                    new[w] += sign * (key[i] - key[j] + 1e-3 + 2 * r[2] ** 2)
-        elif r[1] < 0.5:
-            todo, count = [(i, key[j] - 1e-4 - more)], 0
-            while todo and count < 40:
-                a, l = todo.pop()
-                count += 1
-                if key[a] > l:
-                    new[cls[a]] = min(new[cls[a]], l - base[a])
-                    todo += [(p, l - 1e-4) for p, _ in pred[a]]
-        else:
-            new[cls[j]] = key[i] + 1e-4 + more - base[j]
-        g2 = run(new)
-        if g2 is not None and g2[0] <= got[0] - heat * max(0.03, 1.0 - it / tries) * math.log(1.0 - r[3]):
-            turns, got = new, g2
-            if got[0] < best[0]:
-                best = got
-    return best
+    def pairs_of(i, m, why):
+        ps = []
+        while 0 <= i < m:
+            j = why[i]
+            if 0 <= j < m:
+                ps.append((j, i))
+            i = j if j > -2 else -2 - j
+        return ps
 
-
-def schedule(ops):
-    pred, mate = graph(ops)
-    base = greedy(ops, pred, mate)
-    total, pairs, start, hold, order, key = anneal(ops, pred, timer(ops, pred, mate, base), base)
-    REAL.clear()
-    for i, b in hold.items():
-        REAL[ops[i]["any"]] = BIGB[b]
-    last, other = {}, {}
-    for i in order:
-        o = ops[i]
-        o["start"] = start[i]
-        for b in o["B"]:
-            r = REAL.get(b, b)
-            if r in last and ops[last[r]]["q"] != o["q"]:
-                other[r] = last[r]
-            if r in other:
-                o["D"].add(other[r])
-            last[r] = i
-    return order, total
-
-
-def clock(ops, pred, mate, goal=None):
-    n, NB = len(ops), len(BIGB)
-    res = {r: k for k, r in enumerate(list("VSPGYN") + ["pz0", "pz1", "pt0", "pt1"])}
-    second = {j: i for i, j in mate.items()}
-    J, I = np.array([[j, i] for i in range(n) for j, l in pred[i]]).T
-    kinds = sorted(set(o["kind"] for o in ops))
-    num = {w: k for k, w in enumerate(kinds)}
-    ci, base = np.array([num[o["kind"]] for o in ops]), np.array([HALF * o["j"] for o in ops])
-    row = [(pred[i], res[o["q"]], o["c"], o["occ"] if o["q"] != "N" else -1e9, [res[b] for b in o["fix"]], i in mate, second.get(i, -1)) for i, o in enumerate(ops)]
-
-    def run(turns, soon):
-        key = turns[ci] + base
-        while True:
-            bad = np.nonzero(key[J] >= key[I])[0]
-            if not len(bad):
-                break
-            np.maximum.at(key, I[bad], key[J[bad]] + 1e-5)
-        order = np.argsort(key, kind="stable").tolist()
-        end, why, dep = [0.0] * (n + 1), [-1] * n, [True] * n
-        free, who, lq, big, hold, idle = [-1.0] * 10, [n] * 10, [-1] * 10, [(0.0, -1)] * NB, {}, list(range(NB))
-        for i in order:
-            pr, qi, c, occ, fix, first, sec = row[i]
-            t, w, d = free[qi], who[qi], False
-            for j, l in pr:
-                u = end[j] + l
-                if u > t:
-                    t, w, d = u, j, True
-            for b in fix:
-                u = free[b] if lq[b] == qi else free[b] + LAT
-                if u > t:
-                    t, w, d = u, who[b], False
-            if first:
-                if not idle:
-                    return None
-                b = min(idle, key=lambda b: big[b])
-                idle.remove(b)
-                hold[i] = b
-                if big[b][0] > t:
-                    t, w = big[b]
-                    d = False
-            if t < soon[i]:
-                t, w = soon[i], -1
-            free[qi], who[qi] = t + occ, i
-            t += c
-            for b in fix:
-                free[b], who[b], lq[b] = t, i, qi
-            end[i], why[i], dep[i] = t, w, d
-            if sec >= 0:
-                big[hold[sec]] = (t + LAT, i)
-                idle.append(hold[sec])
-        i = goal if goal is not None else end.index(max(end))
-        total, pairs = end[i], []
-        while i < n and why[i] >= 0:
-            if not dep[i] and why[i] < n:
-                pairs.append((why[i], i))
-            i = why[i]
-        return total, pairs, end, hold, order, key
-    return run, kinds, ci.tolist(), base
-
-
-def improve(ops, pred, mate, given, keep, free, n, half=None):
-    ix = [i for i, o in enumerate(ops) if keep(o)]
-    m = {i: k for k, i in enumerate(ix)}
-    ops, pred, mate = [ops[i] for i in ix], [[(m[j], l) for j, l in pred[i] if j in m] for i in ix], {m[i]: m[j] for i, j in mate.items() if i in m}
-    marks = [i for i, o in enumerate(ops) if o["kind"][:2] == ("w", 7)]
-    goal = marks[-2] if ops[-1]["part"][0] != "o" else None
-    run, kinds, cls, base = clock(ops, pred, mate, goal)
-    parts, tries, heat = {}, OPT["tries"][n], OPT["heat"][n]
-    for k, w in enumerate(kinds):
-        parts.setdefault((w[0], w[2]), []).append(k)
-    rep = [i for i, o in enumerate(ops) if free(o)]
-    at, cost, held = np.array(cls)[rep], np.array([o["c"] for o in ops]), np.ones(len(kinds), bool)
-    held[at] = False
-    rest = np.nonzero(held[cls])[0]
-
-
-    def score(g):
-        return g[0] if half else 1.3 * g[0] - g[2][marks[-4]]
-    rnd = np.random.default_rng(OPT["seed"][n])
-    turns, soon = np.array([given[w] for w in kinds]), [0.0] * len(ops)
-    got = run(turns, soon)
-    now = score(got)
-    best = (now, got, turns)
-    for it in range(tries + 1):
-        if it == tries:
-            now, got, turns = best
-        h = half or (got[0] - got[2][marks[-4]]) / 2
-        if it == tries:
-            OPT.get("log", []).append(round(now if half else 2 * h, 2))
-            turns[at] = (got[5] - base)[rep]
-            return given | dict(zip(kinds, turns.tolist())), h
-        if it % OPT["norm"] == 0:
-            key = (np.array(got[2][:-1]) - cost) * (HALF / h)
-            new = turns.copy()
-            new[at] = (key + (np.median((got[5] - key)[rest]) if len(rest) else 0.0) - base)[rep]
-            g2 = run(new, soon)
-            if g2 is not None and score(g2) <= now + OPT["tol"]:
-                turns, got, now = new, g2, score(g2)
-        r = rnd.random(6).tolist()
-        pairs = [p for p in got[1] if not (held[cls[p[0]]] and held[cls[p[1]]])] if half else got[1]
-        j, i = pairs[int(r[0] * len(pairs))]
-        key, new = got[5], turns.copy()
-        more = 0.5 * r[2] if r[2] > 0.5 else 0.0
-        if r[4] < 0.1:
-            a, sign = (i, -1) if r[1] < 0.5 else (j, 1)
-            w = kinds[cls[a]]
-            for k in parts[(w[0], w[2])]:
-                if r[5] >= 0.5 or sign * (kinds[k][1] - w[1]) >= 0:
-                    new[k] += sign * (key[i] - key[j] + 1e-3 + 2 * r[2] ** 2)
-        elif r[1] < 0.5:
-            todo, count = [(i, key[j] - 1e-4 - more)], 0
-            while todo and count < 40:
-                a, l = todo.pop()
-                count += 1
-                if key[a] > l:
-                    new[cls[a]] = min(new[cls[a]], l - base[a])
-                    todo += [(p, l - 1e-4) for p, _ in pred[a]]
-        else:
-            new[cls[j]] = key[i] + 1e-4 + more - base[j]
-        new[held] = turns[held]
-        g2 = run(new, soon)
-        if g2 is not None:
-            s2 = score(g2)
-            if s2 <= now - heat * max(0.03, 1.0 - it / tries) * math.log(1.0 - r[3]):
-                turns, got, now = new, g2, s2
-                if now < best[0]:
-                    best = (now, got, turns)
-
-
-def fit(ops, pred, mate, key):
-    n, first = len(ops), {j: i for i, j in mate.items()}
-    lines, start, end = {}, [0.0] * n, [None] * n
-
-    def slot(r, t, c, q):
-        for a, b, w in lines.setdefault(r, []):
-            pad = 0.0 if w == q else LAT
-            if t + c + pad <= a + 1e-9:
-                break
-            t = max(t, b + pad)
-        return t
-
-    def room(i, t):
-        o = ops[i]
-        while o["q"] != "N":
-            u = slot(o["q"], t, o["occ"], o["q"])
-            for b in o["fix"]:
-                u = slot(b, u, o["c"], o["q"])
-            if u <= t + 1e-9:
-                break
-            t = u
-        return t
-
-    def take(i, t):
-        o = ops[i]
-        start[i], end[i] = t, t + o["c"]
-        for r, c in [(o["q"], o["occ"])] * (o["q"] != "N") + [(b, o["c"]) for b in o["fix"]]:
-            lines[r] = sorted(lines.get(r, []) + [(t, t + c, o["q"])])
-
-    def needs(i):
-        return [(j, l) for j, l in pred[i] + pred[mate.get(i, i)] if j != i]
-    todo = sorted((i for i in range(n) if i not in first), key=lambda i: key[i])
-    while todo:
-        i = next(i for i in todo if all(end[j] is not None for j, l in needs(i)))
-        todo.remove(i)
-        t = room(i, max([end[j] + l for j, l in pred[i]], default=0.0))
-        while i in mate:
-            j, c = mate[i], ops[i]["c"]
-            u = room(j, max([t + c + LAT] + [end[k] + l for k, l in pred[j] if k != i]))
-            v = room(i, max(t, u - LAT - c - 0.3))
-            t = v if v + c + LAT <= u + 1e-9 else t
-            w, b = min((slot(b, t, u + ops[j]["c"] - t, ""), b) for b in BIGB)
-            if w <= t + 1e-9:
-                lines[b] = sorted(lines[b] + [(t, u + ops[j]["c"], "*")])
-                take(j, u)
-                break
-            t = room(i, w)
-        take(i, t)
-    return start
-
-
-def steady_turns(ops, pred, mate):
-    off, turns, seen = [0.0] * len(ops), {}, {}
-    for i, o in enumerate(ops):
-        off[i] = max([off[j] + ops[j]["c"] + l for j, l in pred[i] if (ops[j]["part"], ops[j]["t"]) == (o["part"], o["t"])], default=0.0)
-        if o["t"] == 2:
-            turns[o["kind"]] = LEAD[o["kind"][0]] + off[i] + 1e-3 * o["kind"][1]
-    for i in sorted(mate):
-        if ops[i]["j"] == 4 + (ops[i]["part"] == "c1"):
-            w = ops[i]["part"]
-            turns[ops[i]["kind"]] += 0.55 * seen.get(w, 0)
-            turns[ops[mate[i]]["kind"]] = turns[ops[i]["kind"]] + 0.6
-            seen[w] = seen.get(w, 0) + 1
-    return improve(ops, pred, mate, turns, lambda o: 2 <= o["j"] <= 6 + (o["part"][:1] in AHEAD), lambda o: o["j"] == (5 if o["part"] == "c1" else OPT["at"] + 2 * (o["part"][:1] in AHEAD)), 0)
+    ends, whys = [0.0] * n + [-LAT], [-1] * (n + 1)
+    empty = ([0.0] * NR, [-1] * NR, [-1] * NR, [n] * NB, 0, -1.0, -1)
+    for size, tries, heat in OPT["sweeps"]:
+        u = forward(seq, empty, whole, [], ends, whys, 1e9)[5]
+        OPT.get("log", []).append(round(u, 2))
+        timed = sorted(seq, key=lambda i: ends[i] - C[i])
+        s = forward(timed, empty, whole, [], ends, whys, 1e9)
+        if s and s[5] <= u + 0.1:
+            seq = timed
+        cuts = list(range(-int(rnd.integers(size // 2)), n - size // 2, size // 2))
+        for a in cuts[::-1] if rnd.random() < 0.5 else cuts:
+            a, b = max(a, 0), min(a + size, n)
+            tail, nxt = tails(seq, b)
+            st = forward(seq[:a], empty, whole, [], ends, whys, 1e9)
+            m, held = b - a, st[3][st[4]:]
+            st = (st[0], [-1] * NR, st[2], list(range(m, m + len(held))), 0, -1.0, -1)
+            own = {i: k for k, i in enumerate(seq[a:b])}
+            row, lb = [None] * m, [0.0] * m
+            for i, k in reversed(own.items()):
+                xt = max([l + tail[j] for j, l in succ[i] if j not in own], default=0.0)
+                lb[k] = max([xt] + [l + C[j] + lb[own[j]] for j, l in succ[i] if j in own])
+                row[k] = ([(own[j], l) for j, l in pred[i] if j in own], max([ends[j] + l for j, l in pred[i] if j not in own], default=0.0),
+                          Q[i], C[i], OCC[i], FIX[i], POOL[i], xt, lb[k])
+            PS = [set(j for j, l in r[0]) for r in row]
+            SS = [set(own[j] for j, l in succ[i] if j in own) for i in own]
+            out = ([(q, tail[j], Q[j]) for q, j in enumerate(nxt) if j is not None and q != 5], [i for i in seq[b:] if POOL[i] == 1][:NB], tail)
+            part, pos, snaps = list(range(m)), list(range(m)), []
+            end, why = [0.0] * m + [ends[i] for i in held], [-1] * m
+            now = close(forward(part, st, row, snaps, end, why, 1e9), end, *out)
+            ps = pairs_of(now[0], m, why)
+            rr = rnd.random((tries, 5))
+            rr[:, 4] = -heat * np.log(1.0 - rr[:, 4])
+            for r in rr.tolist():
+                if ps and r[3] > 0.15:
+                    j, i = ps[int(r[0] * len(ps))]
+                    pj, pi = pos[j], pos[i]
+                    if r[2] > 0.6:
+                        x = int((r[2] - 0.6) * 40)
+                        pj, pi = max(0, pj - x * (r[1] < 0.5)), min(m - 1, pi + x * (r[1] >= 0.5))
+                else:
+                    pi = 1 + int(r[0] * (m - 1))
+                    i, pj = part[pi], pi - 1
+                    while pj > 0 and row[part[pj]][2] != row[i][2]:
+                        pj -= 1
+                    j = part[pj]
+                up = r[1] < 0.5
+                near = PS if up else SS
+                need, mv, rest = near[i if up else j], [i if up else j], []
+                for k in part[pj:pi][::-1] if up else part[pj + 1:pi + 1]:
+                    if k in need:
+                        mv.append(k)
+                        need = need | near[k]
+                    else:
+                        rest.append(k)
+                if not rest:
+                    continue
+                new = mv[::-1] + rest[::-1] if up else rest + mv
+                s0 = pj // STEP
+                e2, w2, sn = end[:], why[:], []
+                s = forward(part[s0 * STEP:pj] + new + part[pi + 1:], snaps[s0], row, sn, e2, w2, now[2] + r[4] + 0.03)
+                if s is None:
+                    continue
+                v = close(s, e2, *out)
+                if v[1] <= now[1] + r[4]:
+                    part[pj:pi + 1] = new
+                    for k in range(pj, pi + 1):
+                        pos[part[k]] = k
+                    end, why, now = e2, w2, v
+                    snaps[s0:] = sn
+                    ps = pairs_of(now[0], m, why)
+            seq = seq[:a] + [seq[a + k] for k in part] + seq[b:]
+    s = forward(seq, empty, whole, [], ends, whys, 1e9)
+    return seq, s[5], ends[:n], s[3]
 
 
 def schedule(ops):
-    pred, mate = graph(ops)
-    for o in ops:
-        p = o["part"]
-        o["j"] = 2 * o["t"] + (p[1:2] == "1")
-        o["kind"] = (p if p[:1] in "lrbo" else p[:1] + p[2:], o["cls"][1], 0)
-    steady, half = OPT.get("steady") or steady_turns(ops, pred, mate)
-    key = [steady[o["kind"]] + HALF * o["j"] if o["kind"] in steady else None for o in ops]
-    for i, o in enumerate(ops):
-        if o["j"] in OPT["job"] and (o["kind"][0], 0, 0) in steady:
-            key[i] = max([steady[(o["kind"][0], 0, 0)] + HALF * o["j"]] + [key[j] + ops[j]["c"] + l for j, l in pred[i] if ops[j]["part"] == o["part"] and key[j]])
-    late = [1e9] * len(ops)
-    for i in range(len(ops) - 1, -1, -1):
-        if key[i] is None:
-            key[i] = min(late[i] - ops[i]["c"] - 10.0 * (ops[i]["part"] == "r1"), 0.0 if late[i] == 1e9 or not ops[i]["part"] else 1e9)
-        for j, l in pred[i]:
-            late[j] = min(late[j], key[i] - l)
-    start = fit(ops, pred, mate, key)
-    for a, b, near in ((0, OPT["own"][0] - 1, OPT["own"][0]), (OPT["own"][1] + 1, 9, OPT["own"][1])):
-        shift = float(np.median([key[i] - start[i] * HALF / half for i, o in enumerate(ops) if o["j"] == near]))
-        key = [start[i] * HALF / half + shift if a <= o["j"] <= b else key[i] for i, o in enumerate(ops)]
-    turns = {}
-    for o, k in zip(ops, key):
-        o["kind"] = o["kind"][:2] + (0 if OPT["own"][0] <= o["j"] <= OPT["own"][1] else o["j"] + 1,)
-        turns[o["kind"]] = k - HALF * o["j"]
-    if "hook" in OPT:
-        return OPT["hook"](ops, pred, mate, turns, half)
-    turns = improve(ops, pred, mate, turns, lambda o: o["j"] <= 4 + 2 * (o["part"][:1] in AHEAD), lambda o: o["j"] < OPT["own"][0], 1, half)[0]
-    turns = improve(ops, pred, mate, turns, lambda o: o["j"] >= 5, lambda o: o["j"] > OPT["own"][1], 2, half)[0]
-    run, kinds = clock(ops, pred, mate)[:2]
-    total, pairs, end, hold, order, key = run(np.array([turns[w] for w in kinds]), [0.0] * len(ops))
+    pred, users = graph(ops)
+    order, total, end, freed = refine(ops, pred, users, line_up(ops, pred, users, first_turns(ops, pred)))
     REAL.clear()
-    for i, b in hold.items():
-        REAL[ops[i]["any"]] = BIGB[b]
+    for k, i in enumerate(i for i in order if i in users):
+        REAL[ops[i]["any"]] = BIGB[k] if k < len(BIGB) else REAL[ops[freed[k]]["any"]]
     last, other = {}, {}
     for i in order:
         o = ops[i]

@@ -53,7 +53,7 @@ for _n in ("hl", "zl", "vl"):
     _b(_n, [128, 256], U16)
 for _n in ("c1", "c2", "yvf", "ypf"):
     _b(_n, [128, 256], F32)
-for _n in ("yy", "yeb", "zy", "mk", "mkn", "nsel", "dcon", "rm", "rmn", "zero", "ktile"):
+for _n in ("yy", "yeb", "zy", "mk", "mkn", "nsel", "dcon", "rm", "rmn", "zero", "e18"):
     _b(_n, [128, 256], BF)
 _b("r2", [128, 272], BF)
 for _n in ("adat", "zz", "ee", "parb", "zr", "cm1k"):
@@ -65,18 +65,16 @@ _b("ol", [128, 32], U16)
 _b("zo", [128, 16], U16)
 _b("cs", [128, 2], BF)
 _b("cint", [128, 4], I32)
-for _n in ("ones", "eye", "neye", "blk", "blk1", "c2048", "cm256", "e18", "m64", "vrow"):
+for _n in ("ones", "eye", "neye", "blk", "blk1", "c2048", "cm256", "ktile", "m64", "cmf", "cme"):
     _b(_n, [128, 128], BF)
-for _j in (4, 8):
-    for _n in ("cmf", "ckf", "cme"):
-        _b("%s%d" % (_n, _j), [128, 256], BF)
 _b("zx", [128, 144], BF)
 _b("kcon", [8, 512], BF)
 _b("kval", [128, 32], BF)
 for _n in ("b64", "b4k"):
     _b(_n, [128, 48], BF)
-for _n in ("ptile", "nset", "ns32"):
+for _n in ("ptile", "ns32"):
     _b(_n, [128, 8], BF)
+_b("nset", [128, 16], BF)
 _b("tb", [128, 1040], BF)
 _b("lf", [128, 2048], BF)
 _b("io1", [128, 128], I32)
@@ -89,10 +87,10 @@ _b("thb", [128, 4], F32)
 for _n in BIGB + FIXB:
     _b(_n, [128, 512], F32, "psum")
 
-for _n in ("lim", "wt", "par", "first"):
+for _n in ("lim", "wt", "par", "first", "clear"):
     SEMAPHORES.append("l_" + _n)
 for _z in range(2):
-    for _n in ("who", "est", "plain", "tab", "claim", "again", "yv", "ye", "yp0", "yp1"):
+    for _n in ("who", "est", "plain0", "plain1", "tab", "claim", "again", "yv", "ye", "yp0", "yp1"):
         SEMAPHORES.append("l_%s%d" % (_n, _z))
 for _t in range(1, VIS):
     for _h in range(2):
@@ -116,23 +114,28 @@ HALVES = {"ol": ["ol", "ol0", "ol1"], "la": ["la", "la0", "la1"], "mx": ["mx", "
 for _h in HALVES:
     for _n in HALVES[_h][1:]:
         BUF[_n], PACK[_n] = BUF[_h], (_h, 0)
+for _n in ("ad0", "ad1"):
+    BUF[_n], PACK[_n], HALVES[_n] = BUF["ad"], ("ad", 0), ["ad", _n]
 _CACHE = {}
-CY, PCY, GATH, SCAT = 0.00083 * 1.08, 0.00042 * 1.08, 1.56, 3.8
-VOV, SOV, POV, LAT = 0.04, 0.04, 0.02, 0.2
+CY, PCY, GATH, SCAT = 0.00083 * 1.15, 0.00042 * 1.2, 1.56, 3.8
+VOV, SOV, POV, IOV, LAT = 0.015, 0.015, 0.01, 0.05, 0.225
 OPT = {
-    "onv": ("p1",),
-    "rows": {"f": 4, "e": 4},
+    "onv": ("p1", "p3"),
+    "fv": (1,),
+    "split": (1, 3),
+    "rows": 4,
     "gl": {"x": 32, "p": 32, "g": 32},
     "al": 32,
-    "zv": "VVVVSSSS",
-    "job": {0: {"onv": ("p1", "p3", "x1")}, 9: {"rows": {"f": 8, "e": 8}, "onv": ("p1", "p3")}},
-    "send": (1, 3, 4),
+    "apart": (3,),
+    "zv": "VVVSSSSD",
+    "job": {0: {"onv": ("p1", "p3", "x1")}, 9: {"rows": 8}},
+    "send": (1, 3.3, 4),
     "seed": 0,
-    "sweeps": [(100, 1000, 0.12 * 0.983 ** k) for k in range(100)],
+    "sweeps": [(100, 1000, 0.12 * 0.986 ** k) for k in range(110)] + [(100, 1000, h) for h in (0.018, 0.012, 0.006, 0.003)],
 }
 HALF, ALONE = 15.0, 0.85
 LEAD = {"n": -12.4, "x": -7.9, "y": -2.5, "p0": 0.0, "q0": 0.3, "z0": 2.0, "g0": 4.5, "d0": 5.5, "p1": 0.7, "q1": 0.4, "z1": 3.4, "g1": 6.5, "d1": 7.8,
-        "m0": 8.5, "s0": 11.3, "m1": 10.3, "s1": 12.5, "v0": 10.0, "v1": 11.0, "c": 11.9, "f": 14.5, "t": 14.5, "u": 20.0, "e": 19.5, "a": 21.0, "h": 26.1, "w": 29.6, "o": 10.0}
+        "m0": 8.5, "s0": 11.3, "m1": 10.3, "s1": 12.5, "v0": 10.0, "v1": 11.0, "c": 11.9, "f0": 13.0, "f1": 14.5, "t": 14.5, "u": 20.0, "e": 19.5, "a": 21.0, "h": 26.1, "w": 29.6, "o": 10.0}
 REAL = {}
 R256 = 1.5 * 2 ** 31
 
@@ -192,7 +195,7 @@ def build(nE, vis):
         return len(ops) - 1
 
     def vcost(n, f=1.0):
-        return max(64, n * f) * CY + VOV
+        return max(64, n * f) * CY + (IOV if f in (GATH, SCAT) else VOV)
 
     def tt(out, a, b, op):
         n = width(b)
@@ -234,7 +237,7 @@ def build(nE, vis):
             if scale is not None:
                 kw["scale"] = ap(T, scale) if isinstance(scale, tuple) else scale
             return g.scalar.activation(out=ap(T, out), in_=ap(T, a), func=func, **kw)
-        add("S", [f], R, [out], max(64, width(a) * (GATH if len(a) == 7 else 1.0)) * CY + SOV)
+        add("S", [f], R, [out], max(64, width(a) * (GATH if len(a) == 7 else 1.0)) * CY + (IOV + 0.015 if len(a) == 7 else SOV))
 
     def opt(name):
         return OPT["job"].get(2 * part[1] + (part[0][1:2] == "1"), {}).get(name, OPT[name])
@@ -257,9 +260,9 @@ def build(nE, vis):
         mm([(out, l, r, i == 0, i == len(terms) - 1) for i, (l, r) in enumerate(terms)])
 
     def pile(*lots):
+        ends = set({h: (n, i) for n, terms in enumerate(lots) for i, (o, l, r) in enumerate(terms) for h in range(o[5], o[5] + o[4], 64)}.values())
         for n, terms in enumerate(lots):
-            ends = set({o[5]: i for i, (o, l, r) in enumerate(terms)}.values())
-            mm([(o, l, r, n == 0 and i == 0, n == len(lots) - 1 and i in ends) for i, (o, l, r) in enumerate(terms)],
+            mm([(o, l, r, n == 0 and i == 0, (n, i) in ends) for i, (o, l, r) in enumerate(terms)],
                None if len(lots) == 1 else "first" if n == 0 else "last" if n == len(lots) - 1 else "more")
 
     def dma(q, sem, pairs, R, W, cost):
@@ -322,10 +325,10 @@ def build(nE, vis):
             both(q, "l_%s%d" % (n, z), lambda T, e, to=to: T[to][64 * e:64 * e + 64, c], lambda T, e, n=n: T[n][r, 128 * e:128 * e + 128], S(to, 128 * z, 128 * z + 128), 2.0 + 2 * z)
             in_turn()
 
-    def claims_in(q, sem, z, halves, spans, cost):
+    def claims_in(q, sem, z, halves, spans, cost, R=()):
         cw = "claimw%d" % z
         dma(q, sem, [(lambda T, e=e, a=a, b=b: T[cw][64 * e:64 * e + 64, a:b], lambda T, a=a, b=b: T.claim[64 * z:64 * z + 64, 0:b - a]) for e in halves for a, b in spans],
-            [], [S(cw + ("" if len(halves) > 1 else "_%d" % halves[0]), spans[0][0], spans[-1][1])], cost)
+            list(R), [S(cw + ("" if len(halves) > 1 else "_%d" % halves[0]), spans[0][0], spans[-1][1])], cost)
         in_turn()
 
     part[0] = "l0"
@@ -351,9 +354,7 @@ def build(nE, vis):
         o = S("parw%d" % (e // 4), 1040 * (e % 4), 1040 * (e % 4) + 1040)
         if OPT["zv"][e] == "V":
             fill(o, 0.0)
-        elif OPT["zv"][e] == "G":
-            flat(o, 0)
-        else:
+        elif OPT["zv"][e] == "S":
             act(o, full("tb"), AF.Copy)
     cp(full("wtf"), full("wti"))
     cp(full("limf"), full("limi"))
@@ -364,12 +365,19 @@ def build(nE, vis):
         part[0] = "b%d" % z
         if z:
             objects(1, "Y")
+            byd = [e for e in range(4) if OPT["zv"][4 + e] == "D"]
+            if byd:
+                dma("Y", "l_clear", [(lambda T, e=e: T.parw1[:, 1040 * e:1040 * e + 1040], lambda T: T.tb[:]) for e in byd], [full("tb")],
+                    [S("parw1", 1040 * byd[0], 1040 * byd[-1] + 1040)], 3.5 + 1.1 * len(byd))
+                in_turn()
+            claims_in("Y", "l_claim1", 1, [0, 1], [(0, 4096)], 6.6 + 1.0 * len(byd))
         ts(third("vb0", 128 * z, 128 * z + 128), S("whoi", 128 * z, 128 * z + 128), -2048.0, A.add)
         dma("Y", "l_tab%d" % z, [(lambda T, e=e, h=h, z=z: T["parw%d" % z][64 * h + e:64 * h + 64:16, P0:P0 + 4096],
                                   lambda T, e=e, z=z: T.parb[64 * z:64 * z + 64, 256 * e:256 * e + 256]) for e in range(2) for h in range(2)],
-            [full("parb")], [S("parw%d" % z, P0, P0 + 4096)], 1.7 + 1.5 * z)
+            [full("parb")], [S("parw%d" % z, P0, P0 + 4096)], 1.7 + 3.5 * z)
         in_turn()
-        claims_in("Y", "l_claim%d" % z, z, [0, 1] if z else [1], [(0, 4096)], 3.2 + 3.4 * z)
+        if not z:
+            claims_in("Y", "l_claim0", 0, [1], [(0, 4096)], 3.2)
         part[0] = ""
         mark(full("dup%d" % z), "zero", [[0, 2], [-1, 64]], -64 * z, 1, 1)
         mark(full("exf%d" % z), "zero", [[0, 2], [-1, 4], [0, 16]], -4 * z, 1, 1)
@@ -379,14 +387,14 @@ def build(nE, vis):
         times(S("thb", z, 4, 2), S(b, 2, 4), 1)
         acc(S(b, 4, 5), [(full("wmat%d" % z), S("c2048", 0, 1))])
         times(S("cols", 2 + z, 3 + z), S(b, 4, 5), -0.5)
-    for z in range(2):
-        part[0] = "r%d" % z
-        claims_in("Y", "l_again%d" % z, z, [0, 1], [(4096, 8192), (8192, CW)], 11.0 + 4.5 * z)
+    part[0] = "r0"
+    claims_in("Y", "l_again0", 0, [0, 1], [(4096, 8192), (8192, CW)], 9.5)
     part[0] = ""
     level(full("zx"), 0)
     times(S("zx", 15, 143, 16), SET, 1)
-    for name, c in (("neye", -1), ("e18", 2 ** 18), ("m64", -64)):
+    for name, c in (("neye", -1), ("m64", -64)):
         mark(full(name), "zero", [[-1, 128]], 0, 1, c)
+    mark(full("e18"), "zero", [[0, 2], [-1, 128]], 0, 1, 2 ** 18)
     for e in range(2):
         asel(S("lf", 1024 * e, 1024 * e + 1024), S("tb", 0, 1024), [[-1, 8], [-16, 8], [0, 16]], A.not_equal, -8 * e, 1, -256.0)
         asel(S("lf", 1024 * e, 1024 + 896 * e), S("lf", 1024 * e, 1024 + 896 * e), [[-1, 8 - e], [-16, 8], [0, 16]], A.not_equal, -8 * e - 1, 1, 256.0)
@@ -395,12 +403,11 @@ def build(nE, vis):
         fill(S("sum3", e, 192, 3), w)
     fill(S("mx", 77, 4 * MW, 48), 1024.0)
     ROW = [[0, 16], [1, 16]]
+    band(full("nset"), [[0, 2], [16, 8]], 16)
     for e, w in enumerate((1, 2, -1)):
-        for j in range(2):
-            times(S("b4k", 16 * e + 8 * j, 16 * e + 8 * j + 8), SET, 4096 * w)
+        times(S("b4k", 16 * e, 16 * e + 16), full("nset"), -4096 * w)
     times(full("b64"), full("b4k"), 1.0 / 64)
     iota(S("ktile", 0, 128), [[0, 8], [1, 16]], 0, 0)
-    level(S("ktile", 128, 256), 0)
     mark(full("rm"), "zero", ROW, 0, 0, 1e9)
     flat(full("rmn"), 2 ** 24 - 1)
     mark(full("rmn"), "rmn", ROW, 0, 0, -1e9)
@@ -412,15 +419,9 @@ def build(nE, vis):
     ts(S("mk", 0, 128), S("ktile", 0, 128), K16, A.is_equal, 64.0, A.mult)
     times(S("mk", 128, 256), S("mk", 0, 128), 1.0 / 64)
     times(full("mkn"), full("mk"), -1)
-    rows = sorted(set(n for o in [OPT] + list(OPT["job"].values()) for n in o.get("rows", {}).values()) - {0})
-    if rows:
-        flat(full("cm1k"), -1024)
-    for n in rows:
-        asel(full("ckf%d" % n), full("zero"), [[0, 64], [-1, 4]], A.is_ge, 3 - n // 4, 0, 2.0 ** 20)
-        asel(full("vrow"), BLK, [[0, 32], [1, 4]], A.is_ge, n // 4 - 4, 0)
-        for j in range(2):
-            times(S("cme%d" % n, 128 * j, 128 * j + 128), full("vrow"), -4096)
-        times(full("cmf%d" % n), full("cme%d" % n), 1.0 / 64)
+    flat(full("cm1k"), -1024)
+    times(full("cmf"), BLK, -64)
+    times(full("cme"), BLK, -4096)
     mark(full("kval"), "zero", [[0, 2], [1, 16]], -3, 0, -1088)
     mark(full("kval"), "kval", [[0, 2], [1, 16]], -11, 0, 69632)
     mark(full("kval"), "kval", [[0, 2], [1, 16]], -12, 0, 2112)
@@ -446,7 +447,6 @@ def build(nE, vis):
     ts(full("dcon"), full("dcon"), S("cols", 5, 6), A.is_le, 8192.0, A.mult)
     band(full("nsel"), [[16, 2], [32, 4], [0, 32]], 16)
     band(S("ns32", 0, 4), [[32, 4]], 32)
-    times(full("nset"), SET, -1)
     for e in range(2):
         level(S("dq", e, 768, 3), e)
     for z in range(2):
@@ -511,11 +511,24 @@ def build(nE, vis):
         place(t, p, S("um%d" % (t % 2), *c), S("t4", *c), S("t5", *c), S("c2", *c), S("zl", *c))
         part[0] = "g%d%d" % (z, n)
         for a in range(c0, c1, n2):
-            tt(S("d", 16 * a, 16 * (a + n2)), claims(t, z, "zl", a, n2), S("x%d" % (t % 2), 16 * a, 16 * (a + n2)), A.subtract)
+            if a % 128 // 32 in opt("apart"):
+                act(S("d", 16 * a, 16 * (a + n2)), claims(t, z, "zl", a, n2), AF.Copy)
+            else:
+                tt(S("d", 16 * a, 16 * (a + n2)), claims(t, z, "zl", a, n2), S("x%d" % (t % 2), 16 * a, 16 * (a + n2)), A.subtract)
         part[0] = "d%d%d" % (z, n)
         for a in range(c0, c1, n3):
-            act(S("ad", 16 * a, 16 * (a + n3)), S("d", 16 * a, 16 * (a + n3)), AF.Abs)
-        acc(D, [(sx(k), S("ad", X + k, X2, 16)) for k in range(16)])
+            e = S("d", 16 * a, 16 * (a + n3))
+            if a % 128 // 32 in opt("apart"):
+                w = S(bank(), 0, 16 * n3)
+                pile([(w, NEYE, S("x%d" % (t % 2), 16 * a, 16 * (a + n3)))], [(w, EYE, e)])
+                e = w
+            if a % 128 // 32 in opt("split"):
+                for h in range(2):
+                    act(S("ad%d" % h, 16 * a + h, 16 * (a + n3), 2), S(e[0], e[1] + h, e[2], 2), AF.Abs)
+                ops[-1]["after"] = len(ops) - 2
+            else:
+                act(S("ad", 16 * a, 16 * (a + n3)), e, AF.Abs)
+        pile(*[[(D, sx(k), S("ad%d" % h, X + k, X2, 16)) for k in range(h, 16, 2)] for h in range(2)])
         ts(third("dq", *c), D, S("thc%d" % t if t else "thb", z, z + 1), A.is_lt)
 
     def st_names(t, z, n):
@@ -549,9 +562,9 @@ def build(nE, vis):
         ts(S("cint", 2, 4), S("cint", 0, 2), 31, A.bitwise_and)
         tt(full("thc%d" % (t + 1)), S("cint", 2, 4), S("thb", 0, 2), A.add)
 
-    def distances(t, z, mid, bias, weights):
+    def distances(t, z, mid):
         X, x, b = 2048 * z, "x%d" % (t % 2), "pt%d" % z
-        nv, n = opt("rows")[part[0][0]], width(full(weights)) // 3
+        nv, n, weights = opt("rows"), 16, "b4k"
         onv = range(4 - nv // 4, 4)
         own = [(S(b, k, 256, 16), S(x, X + k, X + 2048, 16), S(weights, 2 * n, 3 * n)) for k in range(16) if k % 4 in onv]
         lots = []
@@ -559,12 +572,9 @@ def build(nE, vis):
             a, rows, out = bank(), S(x, X + q, X + 2048, 4), S("af", X + 512 * q, X + 512 * q + 512)
             if q not in onv:
                 pile([(S(a, 0, 512), EYE, rows)], [(S(a, r, 512, 4), NEYE, mid) for r in range(4)])
-                act(out, S(a, 0, 512), AF.Abs, bias)
+                act(out, S(a, 0, 512), AF.Abs)
             else:
-                if bias:
-                    pile([(S(a, 0, 512), EYE, full("cm1k"))], [(S(a, r, 512, 4), EYE, mid) for r in range(4)])
-                else:
-                    mm([(S(a, r, 512, 4), EYE, mid, True, True) for r in range(4)])
+                mm([(S(a, r, 512, 4), EYE, mid, True, True) for r in range(4)])
                 tt(out, rows, S(a, 0, 512), A.max)
             w = S(weights, n, 2 * n) if q in onv else S(weights, 0, n)
             lots.append([(S(b, 4 * r + q, 256, 16), S("af", out[1] + r, out[2], 4), w) for r in range(4)])
@@ -572,15 +582,27 @@ def build(nE, vis):
 
     def st_truth(t, z):
         c, b, q = (128 * z, 128 * z + 128), "pt%d" % z, 8 * z
-        key, mid = S(b, 0, 256), third("mm_", *c)
-        part[0] = "f%d" % z
-        nv, own, lots = distances(t, z, mid, 1024.0, "b64")
+        key, x = S(b, 0, 256), "x%d" % (t % 2)
+        first, mids = [(key, third("dq", *c), full("e18")), (S(b, 0, 128), EYE, full("ktile"))], []
+        for n, e in ((0, 0), (0, 1), (1, 1), (1, 0)):
+            part[0] = "f%d%d" % (z, n)
+            X, mid, a = 2048 * z + 1024 * n, third("mm_", c[0] + 64 * n, c[0] + 64 * n + 64), bank()
+            onv = e and n in opt("fv")
+            pile([(S(a, 0, 512), EYE, full("cm1k") if onv else S(x, X + e, X + 1024, 2))], [(S(a, r, 512, 8), EYE if onv else NEYE, mid) for r in range(8)])
+            for h in range(2):
+                o = 2048 * z + 512 * (e + 2 * h) + 256 * n
+                if onv:
+                    tt(S("af", o, o + 256), S(x, X + e + 2 * h, X + 1024, 4), S(a, h, 512, 2), A.max)
+                else:
+                    act(S("af", o, o + 256), S(a, h, 512, 2), AF.Abs, 512.0, 0.5)
+            ops[-1]["after"] = len(ops) - 2
+            if onv:
+                first += [(S(b, j + 1, j + 128, 2, 64, 64 * n), S("cm1k", 0, 64), S("cmf", 0, 128, 2)) for j in (0, 128)]
+                first += [(S(b, k, 256, 16, 64, 64 * n), S(x, X + k, X + 1024, 16), S("b64", 32, 48)) for k in range(1, 16, 2)]
+                mids += [(S(b, j + 1, j + 128, 2, 64, 64 * n), mid, S("cmf", 0, 128, 2)) for j in (0, 128)]
         part[0] = "t%d" % z
-        first = [(key, EYE, full("ktile"))] + own + [(S(b, e, e + 128), third("dq", *c), full("e18")) for e in (0, 128)]
-        if nv:
-            first.append((key, EYE, full("ckf%d" % nv)))
-            lots[0] = [(key, mid, full("cmf%d" % nv))] + lots[0]
-        pile(first, *lots)
+        lots = [[(S(b, 4 * r + e, 256, 16), S("af", 2048 * z + 512 * e + r, 2048 * z + 512 * e + 512, 4), S("b64", 16, 32)) for r in range(4)] for e in range(4)]
+        pile(first, mids, lots[1] + lots[0], lots[3] + lots[2]) if mids else pile(first, lots[1] + lots[0], lots[3] + lots[2])
         scan(full("km%d" % z), full("rm"), key, 0.0, A.max, A.min)
         tt(S("ct%d" % z, 0, 8), S("km%d" % z, 15, 128, 16), S("km%d" % z, 143, 256, 16), A.subtract)
         tt(S("zy", *c), IND("ct%d" % z, 0, 8, "zo", 0, 8), S("mk", 128, 256), A.mult)
@@ -599,13 +621,13 @@ def build(nE, vis):
         part[0] = "e%d" % z
         v = third("vb%d" % t, *c)
         ts(S("vh", *c), v, 1.0 / 64, A.mult, 1120.5078125, A.add)
-        nv, own, lots = distances(t, z, S("yy", *c), None, "b4k")
+        nv, own, lots = distances(t, z, S("yy", *c))
         part[0] = "a%d" % z
         key, hi, lo = S(b, 0, 256), S(b, 0, 128), S(b, 128, 256)
         first = [(key, S("ones", 0, 128, 1, 8), S("kcon", c2, c2 + 256, 1, 8))] + own
         names = [(lo, S("vh", *c), full("m64")), (lo, v, EYE), (hi, S("vh", *c), EYE)]
         if nv:
-            first.append((key, S("yy", *c), full("cme%d" % nv)))
+            first += [(S(b, j + q, j + 128, 4), S("yy", *c), S("cme", 0, 128, 4)) for j in (0, 128) for q in range(4 - nv // 4, 4)]
             late = 1 if nv == 4 else 3
             lots[late] = names + lots[late]
         else:
@@ -636,7 +658,7 @@ def build(nE, vis):
         O = bank()
         both2 = [(e, h) for h in range(2) for e in range(2)]
         pile([(S(O, 0, 16), EYE, S("zero", 0, 16))] +
-             [(S(O, 8 * e, 8 * e + 8, 1, 64, 64 * h), S("zz", c2 + 128 * j + 64 * e, c2 + 128 * j + 64 * e + 64), full("nset")) for e, h in both2 for j in range(2)],
+             [(S(O, 8 * e, 8 * e + 8, 1, 64, 64 * h), S("zz", c2 + 128 * j + 64 * e, c2 + 128 * j + 64 * e + 64), S("nset", 0, 8)) for e, h in both2 for j in range(2)],
              [(S(O, 8 * e + j, 8 * e + 8, 2, 64, 64 * h), S("ee", c2 + 128 * j + 64 * e, c2 + 128 * j + 64 * e + 64), S("ns32", 0, 4)) for e, h in both2 for j in range(2)])
         for j in range(2):
             ts(S("ol%d" % j, 16 * z + j, 16 * z + 16, 2), S(O, j, 16, 2), P0 - 64.0, A.add, ASIDE[j], A.max)
@@ -649,13 +671,11 @@ def build(nE, vis):
         return T["plain%d" % z][64 * e:64 * e + 64:16, P0 + 2048 * e:P0 + 2048 * e + 2048]
 
     def st_plain(z):
-        c = (128 * z, 128 * z + 128)
         part[0] = "o%d" % z
-        b = S(bank(), 0, 128)
-        mm([(S(b[0], 0, 128, 1, 64, 64 * e), S("zx", 15 - k, 79 - k), S("parw%d" % z, P0 + 2048 * e + 128 * k, P0 + 2048 * e + 128 * k + 128), k == 0, k == 15)
-            for e in range(2) for k in range(16)])
-        move("o", S("ypf", *c), b)
-        both("Y", "l_plain%d" % z, lambda T, e: halves(z, T, e), lambda T, e: T.ypf[64 * e:64 * e + 64, c[0]:c[1]], full("plain%d" % z), 2.5, [S("ypf", *c)])
+        for j in range(2):
+            kw = {"accum_op": A.add} if j else {}
+            add("G", [lambda g, T, e=e, j=j, kw=kw: g.dma_start(halves(z, T, e), T["parw%d" % z][64 * e + j:64 * e + 64:16, P0 + 2048 * e:P0 + 2048 * e + 2048], **kw) for e in range(2)],
+                [full("parw%d" % z)], [full("plain%d" % z)], 5.0 - 1.5 * (z + j > 0), sem="l_plain%d%d" % (j, z), val=32)
 
     def st_store(z):
         c, t = (128 * z, 128 * z + 128), vis - 1
@@ -682,6 +702,9 @@ def build(nE, vis):
             if t < vis - 1:
                 send("v", t, z)
             st_truth(t, z)
+            if t == z == 0:
+                part[0] = "r0"
+                claims_in("Y", "l_again1", 1, [0, 1], [(4096, 8192), (8192, CW)], 6.0, [S("yb1", 0, 128)])
             st_ask(t, z)
             if t == vis - 1:
                 st_store(z)
@@ -719,7 +742,9 @@ def build(nE, vis):
                     l.append(i)
         dep.discard(i)
         o["O"] = set(j for j in dep if o["q"] == "P" and ops[j]["q"] == "P")
-        if "after" in o:
+        if o["q"] == "S" and not o["part"]:
+            o["after"] = issued["S"]
+        if "after" in o and o["after"] not in dep:
             dep.add(o["after"])
             o["O"].add(o["after"])
         o["D"], o["i"], o["j"] = dep, i, 2 * o["t"] + (o["part"][1:2] == "1")
@@ -730,17 +755,18 @@ def graph(ops):
     n = len(ops)
     pred, users, above = [sorted(o["D"]) for o in ops], {}, [0] * n
     for i, o in enumerate(ops):
-        o["occ"] = 0.15 * len(o["f"]) if o["sem"] and o["q"] in "YS" else o["c"]
+        o["occ"] = (1.0 if o["q"] == "G" else 0.15) * len(o["f"]) if o["sem"] and o["f"] else o["c"]
         o["fix"] = [b for b in o["B"] if b in SCRATCH]
         for b in o["B"]:
             if b not in SCRATCH:
                 o["any"] = b
                 users.setdefault(b, []).append(i)
         far = 0
-        for j in pred[i]:
+        done = [j for j in pred[i] if not (j in o["O"] and ops[j]["sem"])]
+        for j in done:
             far |= above[j]
         above[i] = far
-        for j in pred[i]:
+        for j in done:
             above[i] |= 1 << j
         pred[i] = [(j, ops[j]["occ"] - ops[j]["c"] if j in o["O"] else LAT) for j in pred[i] if not far >> j & 1]
     return pred, {u[0]: u for u in users.values()}
@@ -1009,9 +1035,9 @@ def plan(nE):
             o["ev"] = (s, count[s])
         out.append((o, sorted(waits.items())))
     ends = {}
-    for o in ops:
+    for o in sorted(ops, key=lambda o: o["start"] + o["c"]):
         s, v = o["ev"]
-        ends[s] = max(ends.get(s, 0), v)
+        ends[s] = max(ends.pop(s, 0), v)
     _CACHE[nE] = (out, ends, total)
     return _CACHE[nE]
 
@@ -1045,5 +1071,5 @@ def rank_program(g, core, T, topo):
         else:
             for f in o["f"]:
                 f(g, T).then_inc(T.sem[SEMQ[q]], 1)
-    for s, v in sorted(ends.items()):
+    for s, v in ends.items():
         g.wait_ge(T.sem[s], v)

import numpy as np
from concourse.mybir import AluOpType, ActivationFunctionType

A = AluOpType
AF = ActivationFunctionType
VIS = 5
BUF = {}
SEMAPHORES = ["vv", "ss", "pp", "gg"]
BIGB = ["pa0", "pa1", "pa2", "pa3"]
FIXB = ["pz0", "pz1", "pt0", "pt1"]


def _b(name, shape, dtype="float32", where="sbuf"):
    BUF[name] = (where, shape, dtype)


BF, F16, F32, I32, U16 = "bfloat16", "float16", "float32", "int32", "uint16"
CW = 8512
PW, P0 = 4160, 32
WIDE = {"y": 128, "v": 384}
_b("dq", [128, 768], BF)
for _z in range(2):
    _b("claimw%d" % _z, [128, CW], BF)
    _b("parw%d" % _z, [128, PW], BF)
    _b("plain%d" % _z, [128, PW], F32)
    _b("adf%d" % _z, [128, 256], F32)
    _b("km%d" % _z, [128, 256], F32)
    _b("pm%d" % _z, [128, 512], F32)
    _b("tt%d" % _z, [128, 256], F32)
    _b("rr%d" % _z, [128, 48], F32)
    _b("ct%d" % _z, [128, 16], BF)
    _b("ca%d" % _z, [128, 512], BF)
    for _n in ("wmat", "en", "enf"):
        _b("%s%d" % (_n, _z), [128, 128], BF)
    _b("dup%d" % _z, [128, 128], F32)
    _b("exf%d" % _z, [8, 128], F32)
_b("yb0", [128, 256], BF)
for _t in range(VIS):
    if _t:
        _b("yb%d" % _t, [128, 256], F16)
    for _n in ("vb", "yn", "vn"):
        _b("%s%d" % (_n, _t), [128, 2 * WIDE[_n[0]]], F16)
    _b("thc%d" % _t, [128, 2], F32)
for _n in ("x0", "x1", "d", "ad", "la", "af"):
    _b(_n, [128, 4096], BF)
MW = 3120
_b("mx", [128, 4 * MW], F16)
_b("sum3", [128, 192], F16)
_b("mm_", [128, 768], F16)
for _n in ("um0", "um1", "t1", "t2", "t3", "t4", "t5", "whoi", "pari"):
    _b(_n, [128, 256], I32)
for _n in ("hl", "zl", "vl"):
    _b(_n, [128, 256], U16)
for _n in ("c1", "c2", "yvf", "ypf"):
    _b(_n, [128, 256], F32)
for _n in ("yy", "yeb", "zy", "mk", "mkn", "nsel", "dcon", "rm", "rmn", "zero", "e18"):
    _b(_n, [128, 256], BF)
_b("r2", [128, 272], BF)
for _n in ("adat", "zz", "ee", "parb", "zr", "cm1k"):
    _b(_n, [128, 512], BF)
_b("vh", [128, 256], F16)
_b("kt32", [32, 256], BF)
_b("yl", [128, 16], U16)
_b("ol", [128, 32], U16)
_b("zo", [128, 16], U16)
_b("cs", [128, 2], BF)
_b("cint", [128, 4], I32)
for _n in ("ones", "eye", "neye", "blk", "blk1", "c2048", "cm256", "ktile", "m64", "cmf", "cme"):
    _b(_n, [128, 128], BF)
_b("zx", [128, 144], BF)
_b("kcon", [8, 512], BF)
_b("kval", [128, 32], BF)
for _n in ("b64", "b4k"):
    _b(_n, [128, 48], BF)
for _n in ("ptile", "ns32"):
    _b(_n, [128, 8], BF)
_b("nset", [128, 16], BF)
_b("tb", [128, 1040], BF)
_b("lf", [128, 2048], BF)
_b("io1", [128, 128], I32)
_b("cols", [128, 16], F32)
_b("wti", [128, 1], I32)
_b("wtf", [128, 1], F32)
_b("limi", [8, 2], I32)
_b("limf", [8, 2], F32)
_b("thb", [128, 4], F32)
for _n in BIGB + FIXB:
    _b(_n, [128, 512], F32, "psum")

for _n in ("lim", "wt", "par", "first", "clear"):
    SEMAPHORES.append("l_" + _n)
for _z in range(2):
    for _n in ("who", "est", "plain0", "plain1", "tab", "claim", "again", "yv", "ye", "yp0", "yp1"):
        SEMAPHORES.append("l_%s%d" % (_n, _z))
for _t in range(1, VIS):
    for _h in range(2):
        for _k in "yv":
            SEMAPHORES += ["a%s%d%d" % (_k, _t, _h), "o%s%d%d" % (_k, _t, _h)]

PACK = {}
SCRATCH = {}
_ROOM = {}
_KEEP = ("whoi", "pari", "parb", "ypf", "yvf", "yeb", "wti", "limi", "hl", "zl", "vl", "yl", "ol", "zo", "adat", "yy", "zy", "mk", "ct0", "ct1", "adf0", "adf1")
for _n, (_w, _sh, _d) in BUF.items():
    if _w == "sbuf" and _n not in _KEEP and _n[:2] not in ("yb", "vb", "yn", "vn") and _sh[1] <= 512:
        PACK[_n] = ("pack_" + _d, _ROOM.get(_d, 0))
        _ROOM[_d] = _ROOM.get(_d, 0) + (_sh[1] + 15) // 16 * 16
    else:
        SCRATCH[_n] = BUF[_n]
for _d in _ROOM:
    SCRATCH["pack_" + _d] = ("sbuf", [128, _ROOM[_d]], _d)

HALVES = {"ol": ["ol", "ol0", "ol1"], "la": ["la", "la0", "la1"], "mx": ["mx", "mx0", "mx1"], "claimw0": ["claimw0", "claimw0_0", "claimw0_1"]}
for _h in HALVES:
    for _n in HALVES[_h][1:]:
        BUF[_n], PACK[_n] = BUF[_h], (_h, 0)
for _n in ("ad0", "ad1"):
    BUF[_n], PACK[_n], HALVES[_n] = BUF["ad"], ("ad", 0), ["ad", _n]
_CACHE = {}
CY, PCY, GATH, SCAT = 0.00083 * 1.15, 0.00042 * 1.2, 1.56, 3.8
VOV, SOV, POV, IOV, LAT = 0.015, 0.015, 0.01, 0.05, 0.225
OPT = {
    "onv": ("p1", "p3"),
    "fv": (1,),
    "split": (1, 3),
    "rows": 4,
    "gl": {"x": 32, "p": 32, "g": 32},
    "al": 32,
    "apart": (3,),
    "zv": "VVVSSSSD",
    "job": {0: {"onv": ("p1", "p3", "x1")}, 9: {"rows": 8}},
    "send": (1, 3.3, 4),
    "seed": 0,
    "sweeps": [(100, 1000, 0.12 * 0.986 ** k) for k in range(110)] + [(100, 1000, h) for h in (0.018, 0.012, 0.006, 0.003)],
}
HALF, ALONE = 15.0, 0.85
LEAD = {"n": -12.4, "x": -7.9, "y": -2.5, "p0": 0.0, "q0": 0.3, "z0": 2.0, "g0": 4.5, "d0": 5.5, "p1": 0.7, "q1": 0.4, "z1": 3.4, "g1": 6.5, "d1": 7.8,
        "m0": 8.5, "s0": 11.3, "m1": 10.3, "s1": 12.5, "v0": 10.0, "v1": 11.0, "c": 11.9, "f0": 13.0, "f1": 14.5, "t": 14.5, "u": 20.0, "e": 19.5, "a": 21.0, "h": 26.1, "w": 29.6, "o": 10.0}
REAL = {}
R256 = 1.5 * 2 ** 31


def S(name, a, b, step=1, p=128, p0=0):
    return (name, a, b, step, p, p0)


def IND(name, a, b, off, c, d):
    return (name, a, b, off, c, d, "ind")


def ap(T, s):
    if len(s) == 7:
        return T[s[0]][:, s[1]:s[2]].indirect(T[s[3]][:, s[4]:s[5]])
    r, o = PACK.get(s[0], (REAL.get(s[0], s[0]), 0))
    if s[3] == 1:
        return T[r][s[5]:s[5] + s[4], o + s[1]:o + s[2]]
    return T[r][s[5]:s[5] + s[4], o + s[1]:o + s[2]:s[3]]


def regs(s):
    if len(s) == 7:
        return [(n, s[1], s[2]) for n in HALVES.get(s[0], [s[0]])] + [(n, s[4], s[5]) for n in HALVES.get(s[3], [s[3]])]
    return [(n, s[1], s[2]) for n in HALVES.get(s[0], [s[0]])]


def width(s):
    if len(s) == 7:
        return 16 * (s[5] - s[4])
    return (s[2] - s[1] + s[3] - 1) // s[3]


def half(*ss):
    return all(BUF[s[0]][2] in (BF, F16, U16) for s in ss)


def send_sides(Tto, Tfrom, what):
    k, t, z = what
    c = slice(WIDE[k] * z, WIDE[k] * (z + 1))
    return Tto["%sb%d" % (k, t)][:, c], Tfrom["%sn%d" % (k, t - 1)][:, c]


def third(name, a, b):
    return S(name, 3 * a + 2, 3 * b, 3)


def build(nE, vis):
    ops = []
    part = ["", 0]

    def add(q, fns, R, W, cost, sem=None, val=0, send=None, lot=None):
        rr = [r for s in R for r in regs(s)]
        ww = [(s[0], s[1], s[2]) for s in W]
        offs = [r for s in W if len(s) == 7 for r in regs(s)[1:]]
        ops.append({"q": q, "f": fns, "R": rr + offs, "W": ww, "c": cost, "sem": sem, "val": val, "send": send, "part": part[0], "t": part[1], "lot": lot})
        return len(ops) - 1

    def vcost(n, f=1.0):
        return max(64, n * f) * CY + (IOV if f in (GATH, SCAT) else VOV)

    def tt(out, a, b, op):
        n = width(b)
        if len(a) == 7:
            f = GATH
        else:
            f = 1.0 if "psum" in (BUF[a[0]][0], BUF[b[0]][0]) else 2.0
        add("V", [lambda g, T: g.vector.tensor_tensor(out=ap(T, out), in0=ap(T, a), in1=ap(T, b), op=op)], [a, b], [out], vcost(n, f))

    def cp(out, a):
        f = SCAT if len(out) == 7 else GATH if len(a) == 7 else 0.5 if half(out, a) else 1.0
        add("V", [lambda g, T: g.vector.tensor_copy(out=ap(T, out), in_=ap(T, a))], [a], [out], vcost(width(a), f))

    def ts(out, a, s1, op0, s2=None, op1=None):
        R = [a] + [s for s in (s1, s2) if isinstance(s, tuple)]

        def f(g, T):
            x1 = ap(T, s1) if isinstance(s1, tuple) else s1
            x2 = ap(T, s2) if isinstance(s2, tuple) else s2
            if op1 is None:
                return g.vector.tensor_scalar(out=ap(T, out), in0=ap(T, a), scalar1=x1, scalar2=None, op0=op0)
            return g.vector.tensor_scalar(out=ap(T, out), in0=ap(T, a), scalar1=x1, scalar2=x2, op0=op0, op1=op1)
        add("V", [f], R, [out], vcost(width(a), 0.5 if half(out, a) else 1.0))

    def scan(out, d0, d1, init, op0, op1):
        add("V", [lambda g, T: g.vector.tensor_tensor_scan(out=ap(T, out), data0=ap(T, d0), data1=ap(T, d1), initial=init, op0=op0, op1=op1)],
            [d0, d1], [out], vcost(width(d1), 0.5 if half(out, d0, d1) else 1.0))

    def fill(out, c):
        add("V", [lambda g, T: g.vector.memset(ap(T, out), c)], [], [out], vcost(width(out), 0.5 if half(out) else 1.0))

    def act(out, a, func, bias=None, scale=None):
        R = [a] + [s for s in (bias, scale) if isinstance(s, tuple)]

        def f(g, T):
            kw = {}
            if bias is not None:
                kw["bias"] = ap(T, bias) if isinstance(bias, tuple) else bias
            if scale is not None:
                kw["scale"] = ap(T, scale) if isinstance(scale, tuple) else scale
            return g.scalar.activation(out=ap(T, out), in_=ap(T, a), func=func, **kw)
        add("S", [f], R, [out], max(64, width(a) * (GATH if len(a) == 7 else 1.0)) * CY + (IOV + 0.015 if len(a) == 7 else SOV))

    def opt(name):
        return OPT["job"].get(2 * part[1] + (part[0][1:2] == "1"), {}).get(name, OPT[name])

    def move(tag, out, a):
        if tag in opt("onv"):
            cp(out, a)
        else:
            act(out, a, AF.Copy)

    def mm(groups, lot=None):
        fns = []
        c = POV
        for (o, l, r, st, sp) in groups:
            fns.append(lambda g, T, o=o, l=l, r=r, st=st, sp=sp: g.tensor.matmul(out=ap(T, o), lhsT=ap(T, l), rhs=ap(T, r), start=st, stop=sp))
            c += max(min(64, width(l)), width(r)) * PCY * (4 if BUF[r[0]][2] == F32 else 1)
        add("P", fns, [r for (o, l, r2, st, sp) in groups for r in (l, r2)], [x[0] for x in groups], c, lot=lot)

    def acc(out, terms):
        mm([(out, l, r, i == 0, i == len(terms) - 1) for i, (l, r) in enumerate(terms)])

    def pile(*lots):
        ends = set({h: (n, i) for n, terms in enumerate(lots) for i, (o, l, r) in enumerate(terms) for h in range(o[5], o[5] + o[4], 64)}.values())
        for n, terms in enumerate(lots):
            mm([(o, l, r, n == 0 and i == 0, (n, i) in ends) for i, (o, l, r) in enumerate(terms)],
               None if len(lots) == 1 else "first" if n == 0 else "last" if n == len(lots) - 1 else "more")

    def dma(q, sem, pairs, R, W, cost):
        add(q, [lambda g, T, o=o, i=i: (g.sync if q == "Y" else g.scalar).dma_start(o(T), i(T)) for (o, i) in pairs], R, W, cost, sem=sem, val=16 * len(pairs))

    def iota(out, pattern, base, cm):
        kw = {"allow_small_or_imprecise_dtypes": True} if BUF[out[0]][2] in (BF, F32) else {}
        add("G", [lambda g, T: g.iota(ap(T, out), pattern, base, cm, **kw)], [], [out], 0.13 + 2 * width(out) * CY)

    def asel(out, a, pattern, op, base, cm, fill=0.0):
        add("G", [lambda g, T: g.affine_select(ap(T, out), ap(T, a), pattern, op, fill, base, cm)], [a], [out], 0.17 + 2 * width(out) * CY)

    def full(name):
        sh = BUF[name][1]
        return S(name, 0, sh[1], 1, sh[0])

    EYE, NEYE, BLK = full("eye"), full("neye"), full("blk")
    SET = S("blk", 0, 128, 16)

    def sx(k):
        return S("zx", 15 - k, 143 - k)

    turn = [0]

    def bank():
        turn[0] += 1
        _b("bank%d" % turn[0], [128, 512], F32, "psum")
        return "bank%d" % turn[0]

    def flat(out, c):
        iota(out, [[0, width(out)]], c, 0)

    def mark(out, a, pattern, base, cm, c):
        asel(out, S(a, 0, width(out), 1, out[4]), pattern, A.not_equal, base, cm, float(c))

    def band(out, pattern, n):
        asel(out, S("zero", 0, width(out)), pattern, A.is_gt, 0, -1, -1.0)
        asel(out, out, pattern, A.is_ge, n - 1, -1)

    def times(out, a, c):
        act(out, a, AF.Identity, None, float(c))

    def level(out, c):
        act(out, S("zero", 0, width(out)), AF.Identity, float(c) if c else None)

    def both(q, sem, out, in_, W, cost, R=()):
        dma(q, sem, [(lambda T, e=e: out(T, e), lambda T, e=e: in_(T, e)) for e in range(2)], list(R), [W], cost)

    issued = {}

    def in_turn():
        q = ops[-1]["q"]
        if q in issued:
            ops[-1]["after"] = issued[q]
        issued[q] = len(ops) - 1

    def objects(z, q):
        r, c = slice(64 * z, 64 * z + 64), slice(128 * z, 128 * z + 128)
        for q, n, to in ((q, "est", "yb0"), ("Y", "who", "whoi")):
            both(q, "l_%s%d" % (n, z), lambda T, e, to=to: T[to][64 * e:64 * e + 64, c], lambda T, e, n=n: T[n][r, 128 * e:128 * e + 128], S(to, 128 * z, 128 * z + 128), 2.0 + 2 * z)
            in_turn()

    def claims_in(q, sem, z, halves, spans, cost, R=()):
        cw = "claimw%d" % z
        dma(q, sem, [(lambda T, e=e, a=a, b=b: T[cw][64 * e:64 * e + 64, a:b], lambda T, a=a, b=b: T.claim[64 * z:64 * z + 64, 0:b - a]) for e in halves for a, b in spans],
            list(R), [S(cw + ("" if len(halves) > 1 else "_%d" % halves[0]), spans[0][0], spans[-1][1])], cost)
        in_turn()

    part[0] = "l0"
    for n, to in (("par", "pari"), ("wt", "wti"), ("lim", "limi")):
        dma("Y", "l_" + n, [(lambda T, to=to: T[to][:], lambda T, n=n: T[n][:])], [], [full(to)], 2.0)
        in_turn()
    objects(0, "S")
    claims_in("S", "l_first", 0, [0], [(0, 4096)], 3.9)
    part[0] = ""
    fill(full("ones"), 1.0)
    iota(S("io1", 0, 1), [[0, 1]], 0, 1)
    asel(full("blk1"), full("ones"), [[-16, 8], [0, 16]], A.is_ge, 0, 1)
    asel(BLK, full("blk1"), [[16, 8], [0, 16]], A.is_ge, 15, -1)
    asel(EYE, full("ones"), [[-1, 128]], A.is_equal, 0, 1)
    ts(S("io1", 16, 17), S("io1", 0, 1), 15, A.bitwise_and)
    K16 = S("cols", 0, 1)
    NCOL = S("cols", 1, 2)
    cp(K16, S("io1", 16, 17))
    fill(full("zero"), 0.0)
    level(full("c2048"), 2048)
    fill(full("tb"), 0.0)
    for e in range(8):
        o = S("parw%d" % (e // 4), 1040 * (e % 4), 1040 * (e % 4) + 1040)
        if OPT["zv"][e] == "V":
            fill(o, 0.0)
        elif OPT["zv"][e] == "S":
            act(o, full("tb"), AF.Copy)
    cp(full("wtf"), full("wti"))
    cp(full("limf"), full("limi"))
    part[0] = "b0"
    cp(S("parb", 0, 256), full("pari"))
    tt(S("parb", 256, 512), full("pari"), S("parb", 0, 256), A.subtract)
    for z in range(2):
        part[0] = "b%d" % z
        if z:
            objects(1, "Y")
            byd = [e for e in range(4) if OPT["zv"][4 + e] == "D"]
            if byd:
                dma("Y", "l_clear", [(lambda T, e=e: T.parw1[:, 1040 * e:1040 * e + 1040], lambda T: T.tb[:]) for e in byd], [full("tb")],
                    [S("parw1", 1040 * byd[0], 1040 * byd[-1] + 1040)], 3.5 + 1.1 * len(byd))
                in_turn()
            claims_in("Y", "l_claim1", 1, [0, 1], [(0, 4096)], 6.6 + 1.0 * len(byd))
        ts(third("vb0", 128 * z, 128 * z + 128), S("whoi", 128 * z, 128 * z + 128), -2048.0, A.add)
        dma("Y", "l_tab%d" % z, [(lambda T, e=e, h=h, z=z: T["parw%d" % z][64 * h + e:64 * h + 64:16, P0:P0 + 4096],
                                  lambda T, e=e, z=z: T.parb[64 * z:64 * z + 64, 256 * e:256 * e + 256]) for e in range(2) for h in range(2)],
            [full("parb")], [S("parw%d" % z, P0, P0 + 4096)], 1.7 + 3.5 * z)
        in_turn()
        if not z:
            claims_in("Y", "l_claim0", 0, [1], [(0, 4096)], 3.2)
        part[0] = ""
        mark(full("dup%d" % z), "zero", [[0, 2], [-1, 64]], -64 * z, 1, 1)
        mark(full("exf%d" % z), "zero", [[0, 2], [-1, 4], [0, 16]], -4 * z, 1, 1)
        b = "pt%d" % z
        mm([(S(b, 0, 1), full("dup%d" % z), full("wtf"), True, True), (S(b, 2, 4), full("exf%d" % z), full("limf"), True, True)])
        ts(full("wmat%d" % z), BLK, S(b, 0, 1), A.mult)
        times(S("thb", z, 4, 2), S(b, 2, 4), 1)
        acc(S(b, 4, 5), [(full("wmat%d" % z), S("c2048", 0, 1))])
        times(S("cols", 2 + z, 3 + z), S(b, 4, 5), -0.5)
    part[0] = "r0"
    claims_in("Y", "l_again0", 0, [0, 1], [(4096, 8192), (8192, CW)], 9.5)
    part[0] = ""
    level(full("zx"), 0)
    times(S("zx", 15, 143, 16), SET, 1)
    for name, c in (("neye", -1), ("m64", -64)):
        mark(full(name), "zero", [[-1, 128]], 0, 1, c)
    mark(full("e18"), "zero", [[0, 2], [-1, 128]], 0, 1, 2 ** 18)
    for e in range(2):
        asel(S("lf", 1024 * e, 1024 * e + 1024), S("tb", 0, 1024), [[-1, 8], [-16, 8], [0, 16]], A.not_equal, -8 * e, 1, -256.0)
        asel(S("lf", 1024 * e, 1024 + 896 * e), S("lf", 1024 * e, 1024 + 896 * e), [[-1, 8 - e], [-16, 8], [0, 16]], A.not_equal, -8 * e - 1, 1, 256.0)
    level(full("cm256"), -256)
    for e, w in enumerate((0.0, 1.0, 0.5 - 2.0 ** -11)):
        fill(S("sum3", e, 192, 3), w)
    fill(S("mx", 77, 4 * MW, 48), 1024.0)
    ROW = [[0, 16], [1, 16]]
    band(full("nset"), [[0, 2], [16, 8]], 16)
    for e, w in enumerate((1, 2, -1)):
        times(S("b4k", 16 * e, 16 * e + 16), full("nset"), -4096 * w)
    times(full("b64"), full("b4k"), 1.0 / 64)
    iota(S("ktile", 0, 128), [[0, 8], [1, 16]], 0, 0)
    mark(full("rm"), "zero", ROW, 0, 0, 1e9)
    flat(full("rmn"), 2 ** 24 - 1)
    mark(full("rmn"), "rmn", ROW, 0, 0, -1e9)
    asel(full("r2"), S("tb", 0, 272), [[0, 17], [1, 16]], A.is_equal, -1, 0, 1.0)
    iota(S("io1", 32, 40), [[16, 8]], 0, 0)
    ts(full("ptile"), S("io1", 32, 40), K16, A.add, 16.0, A.mult)
    iota(S("io1", 48, 64), [[1, 16]], 0, 0)
    cp(full("zo"), S("io1", 48, 64))
    ts(S("mk", 0, 128), S("ktile", 0, 128), K16, A.is_equal, 64.0, A.mult)
    times(S("mk", 128, 256), S("mk", 0, 128), 1.0 / 64)
    times(full("mkn"), full("mk"), -1)
    flat(full("cm1k"), -1024)
    times(full("cmf"), BLK, -64)
    times(full("cme"), BLK, -4096)
    mark(full("kval"), "zero", [[0, 2], [1, 16]], -3, 0, -1088)
    mark(full("kval"), "kval", [[0, 2], [1, 16]], -11, 0, 69632)
    mark(full("kval"), "kval", [[0, 2], [1, 16]], -12, 0, 2112)
    act(S("kval", 0, 32, 8), S("cm256", 0, 4), AF.Identity, 3840.0, K16)
    times(S("cols", 6, 8), S("thb", 2, 4), -4096)
    for e in (1, 9):
        times(S("kval", e, 32, 16), S("cols", 6, 8), 1)
        tt(S("kval", e + 1, 32, 16), S("cols", 6, 8), S("kval", e, 32, 16), A.subtract)
    b = bank()
    mm([(S(b, 128 * e, 128 * e + 128, 1, 8), S("kval", 8 * e, 8 * e + 8), EYE, True, True) for e in range(4)])
    times(full("kcon"), S(b, 0, 512, 1, 8), 1)
    for e in range(2):
        for name, base in (("en%d", 992), ("enf%d", -8)):
            o = S(name % e, 0, 128, 1, 32)
            mark(o, "zero", [[0, 2], [-1, 4], [-1000, 16]], -4 * e, 1, 64)
            mark(o, o[0], [[0, 2], [-1, 4], [-1000, 16]], base - 4 * e, 1, 1)
    ts(NCOL, K16, 0.0, A.is_equal, -64.0, A.mult)
    ASIDE = [K16, S("cols", 4, 5)]
    act(ASIDE[1], K16, AF.Identity, 16.0)
    ts(S("io1", 65, 66), S("io1", 0, 1), 31, A.bitwise_and)
    cp(S("cols", 5, 6), S("io1", 65, 66))
    iota(full("dcon"), [[16, 2], [0, 8], [1, 16]], 0, 0)
    ts(full("dcon"), full("dcon"), S("cols", 5, 6), A.is_le, 8192.0, A.mult)
    band(full("nsel"), [[16, 2], [32, 4], [0, 32]], 16)
    band(S("ns32", 0, 4), [[32, 4]], 32)
    for e in range(2):
        level(S("dq", e, 768, 3), e)
    for z in range(2):
        flat(full("ca%d" % z), 0)

    def send(what, t, z):
        c = (WIDE[what] * z, WIDE[what] * (z + 1))
        key = "%s%d%d" % (what, t + 1, z)
        i = add("G", None, [S("%sn%d" % (what, t), *c)], [], OPT["send"][0] + OPT["send"][2] * (key == "v10"), sem="o" + key, val=nE, send=(what, t + 1, z))
        add("N", None, [], [S("%sb%d" % (what, t + 1), *c)], OPT["send"][1], sem="a" + key, val=nE, send=i)

    def place(t, s, um, a, b, c, out):
        tt(a, s, um, A.mult)
        ts(b, a, 5, A.arith_shift_right, 4095, A.bitwise_and)
        if t == 0:
            tt(a, s, b, A.add)
            ts(b, a, 4095, A.bitwise_and)
            cp(out, b)
        else:
            tt(c, s, b, A.add)
            ts(out, c, 77.0 * t, A.add)

    def claims(t, z, off, a, n):
        return IND("claimw%d" % z, 0, 4096 if t == 0 else CW, off, a, a + n)

    def block(z, n):
        return 128 * z + 64 * n, 128 * z + 64 * n + 64, ("pz%d", "pt%d")[n] % z, 256 * n

    def st_hash(t, z):
        c0, c1, b = 128 * z, 128 * z + 128, "pz%d" % z
        c = (c0, c1)
        part[0] = "n%d" % z
        ts(S("vl", *c), third("vb%d" % t, *c), 2048.0, A.add)
        part[0] = "x%d" % z
        um = S("um%d" % (t % 2), *c)
        U, s = S(b, 256, 384), S(b, 384, 512)
        acc(s, [(EYE, third("vb%d" % t, *c)), (EYE, full("c2048"))])
        acc(U, [(full("wmat%d" % z), S("yb%d" % t, *c))])
        if t == 0:
            cp(S("t1", *c), U)
        else:
            ts(S("t1", *c), U, S("cols", 2 + z, 3 + z), A.add)
        ts(um, S("t1", *c), 4095, A.bitwise_and)
        place(t, s, um, S("t2", *c), S("t3", *c), S("c1", *c), S("hl", *c))
        part[0] = "y%d" % z
        n = opt("gl")["x"]
        for a in range(c0, c1, n):
            move("x%d" % ((a - c0) // 32), S("x%d" % (t % 2), 16 * a, 16 * (a + n)), claims(t, z, "hl", a, n))

    def st_z(t, z, n):
        c0, c1, b, o = block(z, n)
        c, L, X, X2 = (c0, c1), c1 - c0, 16 * c0, 16 * c1
        p, D, v = S(b, o, o + 192, 3), S(b, o + 192, o + 256), third("vb%d" % t, *c)
        part[0] = "p%d%d" % (z, n)
        n1, n2, n3 = opt("gl")["p"], opt("gl")["g"], opt("al")
        for a in range(c0, c1, n1):
            move("p%d" % (a % 128 // 32), S("d", 16 * a, 16 * (a + n1)), IND("parw%d" % z, P0, P0 + 4096, "vl", a, a + n1))
        part[0] = "q%d%d" % (z, n)
        mm([(S(b, o + 1, o + 192, 3), NEYE, v, True, False), (S(b, o + 1, o + 192, 3), NEYE, S("c2048", 0, L), False, True), (S(b, o + 2, o + 192, 3), EYE, v, True, True)])
        part[0] = "z%d%d" % (z, n)
        acc(p, [(sx(k), S("d", X + k, X2, 16)) for k in range(16)])
        place(t, p, S("um%d" % (t % 2), *c), S("t4", *c), S("t5", *c), S("c2", *c), S("zl", *c))
        part[0] = "g%d%d" % (z, n)
        for a in range(c0, c1, n2):
            if a % 128 // 32 in opt("apart"):
                act(S("d", 16 * a, 16 * (a + n2)), claims(t, z, "zl", a, n2), AF.Copy)
            else:
                tt(S("d", 16 * a, 16 * (a + n2)), claims(t, z, "zl", a, n2), S("x%d" % (t % 2), 16 * a, 16 * (a + n2)), A.subtract)
        part[0] = "d%d%d" % (z, n)
        for a in range(c0, c1, n3):
            e = S("d", 16 * a, 16 * (a + n3))
            if a % 128 // 32 in opt("apart"):
                w = S(bank(), 0, 16 * n3)
                pile([(w, NEYE, S("x%d" % (t % 2), 16 * a, 16 * (a + n3)))], [(w, EYE, e)])
                e = w
            if a % 128 // 32 in opt("split"):
                for h in range(2):
                    act(S("ad%d" % h, 16 * a + h, 16 * (a + n3), 2), S(e[0], e[1] + h, e[2], 2), AF.Abs)
                ops[-1]["after"] = len(ops) - 2
            else:
                act(S("ad", 16 * a, 16 * (a + n3)), e, AF.Abs)
        pile(*[[(D, sx(k), S("ad%d" % h, X + k, X2, 16)) for k in range(h, 16, 2)] for h in range(2)])
        ts(third("dq", *c), D, S("thc%d" % t if t else "thb", z, z + 1), A.is_lt)

    def st_names(t, z, n):
        c0, c1, b, o = block(z, n)
        part[0] = "v%d%d" % (z, n)
        scan(S("vn%d" % t, 3 * c0, 3 * c1), S("dq", 3 * c0, 3 * c1), S(b, o, o + 192), 0.0, A.mult, A.add)

    def st_m(t, z, n):
        c0, c1, b, o = block(z, n)
        c, L, X, X2 = (c0, c1), c1 - c0, 16 * c0, 16 * c1
        x = "x%d" % (t % 2)
        part[0] = "m%d%d" % (z, n)
        for e in range(2):
            a = bank()
            mm([(S(a, k // 2, 512, 8), S("lf", 128 * k, 128 * k + 128), third("dq", *c), True, k < 15) for k in range(e, 16, 2)] +
               [(S(a, 7, 512, 8), EYE, S("cm256", 0, L), False, True)] * e)
            move("l%d" % (2 * n + e), S("la%d" % e, X + e, X2, 2), S(a, 0, 512))
        part[0] = "s%d%d" % (z, n)
        a = MW * (c0 // 64)
        scan(S("mx0", a, a + 3072, 3), S(x, X, X2), S("la", X, X2), -1.0, A.max, A.add)
        scan(S("mx1", a + 16, a + 3088, 3), S(x, X, X2), S("la", X, X2), 256.0, A.min, A.subtract)
        scan(S("mm_", 3 * c0, 3 * c1), full("sum3"), S("mx", a + 45, a + 3104, 16), 0.0, A.mult, A.add)

    def st_count(t):
        part[0] = "c1"
        a, b = S(bank(), 0, 2), S(bank(), 0, 2)
        acc(a, [(third("dq", 128, 256), S("ones", 0, 2)), (third("dq", 0, 128), S("ones", 0, 2))])
        move("c", full("cs"), a)
        acc(b, [(full("ones"), full("cs"))])
        cp(S("cint", 0, 2), b)
        ts(S("cint", 2, 4), S("cint", 0, 2), 31, A.bitwise_and)
        tt(full("thc%d" % (t + 1)), S("cint", 2, 4), S("thb", 0, 2), A.add)

    def distances(t, z, mid):
        X, x, b = 2048 * z, "x%d" % (t % 2), "pt%d" % z
        nv, n, weights = opt("rows"), 16, "b4k"
        onv = range(4 - nv // 4, 4)
        own = [(S(b, k, 256, 16), S(x, X + k, X + 2048, 16), S(weights, 2 * n, 3 * n)) for k in range(16) if k % 4 in onv]
        lots = []
        for q in (3, 0, 2, 1) if nv else range(4):
            a, rows, out = bank(), S(x, X + q, X + 2048, 4), S("af", X + 512 * q, X + 512 * q + 512)
            if q not in onv:
                pile([(S(a, 0, 512), EYE, rows)], [(S(a, r, 512, 4), NEYE, mid) for r in range(4)])
                act(out, S(a, 0, 512), AF.Abs)
            else:
                mm([(S(a, r, 512, 4), EYE, mid, True, True) for r in range(4)])
                tt(out, rows, S(a, 0, 512), A.max)
            w = S(weights, n, 2 * n) if q in onv else S(weights, 0, n)
            lots.append([(S(b, 4 * r + q, 256, 16), S("af", out[1] + r, out[2], 4), w) for r in range(4)])
        return nv, own, lots

    def st_truth(t, z):
        c, b, q = (128 * z, 128 * z + 128), "pt%d" % z, 8 * z
        key, x = S(b, 0, 256), "x%d" % (t % 2)
        first, mids = [(key, third("dq", *c), full("e18")), (S(b, 0, 128), EYE, full("ktile"))], []
        for n, e in ((0, 0), (0, 1), (1, 1), (1, 0)):
            part[0] = "f%d%d" % (z, n)
            X, mid, a = 2048 * z + 1024 * n, third("mm_", c[0] + 64 * n, c[0] + 64 * n + 64), bank()
            onv = e and n in opt("fv")
            pile([(S(a, 0, 512), EYE, full("cm1k") if onv else S(x, X + e, X + 1024, 2))], [(S(a, r, 512, 8), EYE if onv else NEYE, mid) for r in range(8)])
            for h in range(2):
                o = 2048 * z + 512 * (e + 2 * h) + 256 * n
                if onv:
                    tt(S("af", o, o + 256), S(x, X + e + 2 * h, X + 1024, 4), S(a, h, 512, 2), A.max)
                else:
                    act(S("af", o, o + 256), S(a, h, 512, 2), AF.Abs, 512.0, 0.5)
            ops[-1]["after"] = len(ops) - 2
            if onv:
                first += [(S(b, j + 1, j + 128, 2, 64, 64 * n), S("cm1k", 0, 64), S("cmf", 0, 128, 2)) for j in (0, 128)]
                first += [(S(b, k, 256, 16, 64, 64 * n), S(x, X + k, X + 1024, 16), S("b64", 32, 48)) for k in range(1, 16, 2)]
                mids += [(S(b, j + 1, j + 128, 2, 64, 64 * n), mid, S("cmf", 0, 128, 2)) for j in (0, 128)]
        part[0] = "t%d" % z
        lots = [[(S(b, 4 * r + e, 256, 16), S("af", 2048 * z + 512 * e + r, 2048 * z + 512 * e + 512, 4), S("b64", 16, 32)) for r in range(4)] for e in range(4)]
        pile(first, mids, lots[1] + lots[0], lots[3] + lots[2]) if mids else pile(first, lots[1] + lots[0], lots[3] + lots[2])
        scan(full("km%d" % z), full("rm"), key, 0.0, A.max, A.min)
        tt(S("ct%d" % z, 0, 8), S("km%d" % z, 15, 128, 16), S("km%d" % z, 143, 256, 16), A.subtract)
        tt(S("zy", *c), IND("ct%d" % z, 0, 8, "zo", 0, 8), S("mk", 128, 256), A.mult)
        acc(S(b, 448, 456), [(EYE, full("ptile")), (S("zy", *c), SET)])
        cp(S("yl", q, q + 8), S(b, 448, 456))
        move("y", S("yy", *c), IND("x%d" % (t % 2), 16 * c[0], 16 * c[1], "yl", q, q + 8))
        part[0] = "u%d" % z
        e = S("pz%d" % z, 128, 256)
        acc(e, [(EYE, S("yb%d" % t, *c)), (EYE, S("yy", *c))])
        ts(S("yn%d" % t, *c), e, 0.5, A.mult, 511.75 if t else 1023.75, A.add)
        if t < vis - 1:
            send("y", t, z)

    def st_ask(t, z):
        c, b, c2 = (128 * z, 128 * z + 128), "pt%d" % z, 256 * z
        part[0] = "e%d" % z
        v = third("vb%d" % t, *c)
        ts(S("vh", *c), v, 1.0 / 64, A.mult, 1120.5078125, A.add)
        nv, own, lots = distances(t, z, S("yy", *c))
        part[0] = "a%d" % z
        key, hi, lo = S(b, 0, 256), S(b, 0, 128), S(b, 128, 256)
        first = [(key, S("ones", 0, 128, 1, 8), S("kcon", c2, c2 + 256, 1, 8))] + own
        names = [(lo, S("vh", *c), full("m64")), (lo, v, EYE), (hi, S("vh", *c), EYE)]
        if nv:
            first += [(S(b, j + q, j + 128, 4), S("yy", *c), S("cme", 0, 128, 4)) for j in (0, 128) for q in range(4 - nv // 4, 4)]
            late = 1 if nv == 4 else 3
            lots[late] = names + lots[late]
        else:
            first += names
        pile(first, *lots)
        pm, t2, k = "pm%d" % z, S("tt%d" % z, 1, 256), S("ca%d" % z, 0, 512, 16)
        scan(S(pm, 0, 256), full("rmn"), key, 0.0, A.min, A.max)
        tt(t2, S(b, 1, 256), S(pm, 0, 255), A.min)
        scan(S(pm, 257, 512), S("r2", 1, 256), t2, 0.0, A.mult, A.max)
        m, r = S(pm, 15, 512, 16), S("rr%d" % z, 16, 48)
        ts(r, m, R256, A.add, -R256, A.add)
        tt(k, m, r, A.subtract)
        part[0] = "h%d" % z
        scan(S("zr", c2, c2 + 256), S("r2", 1, 257), S(k[0], 256, 512), 0.0, A.mult, A.add)
        scan(S("zz", c2, c2 + 256), S("zr", c2, c2 + 256), full("mkn"), 0.0, A.max, A.mult)
        kt = S(bank(), 0, 128, 1, 32)
        acc(kt, [(k, EYE)])
        move("j", S("kt32", *c, 1, 32), kt)
        N = bank()
        last = t == vis - 1
        ad, a0, table = ("adf%d" % z, 0, "plain%d" % z) if last else ("adat", c2, "parw%d" % z)
        mm([(S(N, 128 * e, 128 * e + 128), S(("enf%d" if last else "en%d") % e, 0, 128, 1, 32), S("kt32", *c, 1, 32), True, True) for e in range(2)])
        act(S(ad, a0, a0 + 256), S(N, 0, 256), AF.Identity, NCOL)
        pile([(key, EYE, full("dcon"))],
             [(S(b, 128 * j, 128 * j + 128), (full("m64"), NEYE)[e], S("zr", c2 + 128 * e, c2 + 128 * e + 128)) for j in range(2) for e in range(2)],
             [(S(b, 128 * j, 128 * j + 128), S("nsel", 128 * j, 128 * j + 128), S("zz", c2 + 128 * e, c2 + 128 * e + 128)) for j in range(2) for e in range(2)])
        ts(S("ee", c2, c2 + 256), key, 0.0, A.is_equal, 8192.0, A.mult)
        O = bank()
        both2 = [(e, h) for h in range(2) for e in range(2)]
        pile([(S(O, 0, 16), EYE, S("zero", 0, 16))] +
             [(S(O, 8 * e, 8 * e + 8, 1, 64, 64 * h), S("zz", c2 + 128 * j + 64 * e, c2 + 128 * j + 64 * e + 64), S("nset", 0, 8)) for e, h in both2 for j in range(2)],
             [(S(O, 8 * e + j, 8 * e + 8, 2, 64, 64 * h), S("ee", c2 + 128 * j + 64 * e, c2 + 128 * j + 64 * e + 64), S("ns32", 0, 4)) for e, h in both2 for j in range(2)])
        for j in range(2):
            ts(S("ol%d" % j, 16 * z + j, 16 * z + 16, 2), S(O, j, 16, 2), P0 - 64.0, A.add, ASIDE[j], A.max)
        ops[-1]["after"] = len(ops) - 2
        part[0] = "w%d" % z
        for a in range(7, -1, -1):
            cp(IND(table, 0, PW, "ol", 16 * z + 2 * a, 16 * z + 2 * a + 2), S(ad, a0 + 32 * a, a0 + 32 * a + 32))

    def halves(z, T, e):
        return T["plain%d" % z][64 * e:64 * e + 64:16, P0 + 2048 * e:P0 + 2048 * e + 2048]

    def st_plain(z):
        part[0] = "o%d" % z
        for j in range(2):
            kw = {"accum_op": A.add} if j else {}
            add("G", [lambda g, T, e=e, j=j, kw=kw: g.dma_start(halves(z, T, e), T["parw%d" % z][64 * e + j:64 * e + 64:16, P0 + 2048 * e:P0 + 2048 * e + 2048], **kw) for e in range(2)],
                [full("parw%d" % z)], [full("plain%d" % z)], 5.0 - 1.5 * (z + j > 0), sem="l_plain%d%d" % (j, z), val=32)

    def st_store(z):
        c, t = (128 * z, 128 * z + 128), vis - 1
        r = slice(64 * z, 64 * z + 64)
        part[0] = "o%d" % z
        ts(S("yvf", *c), third("vn%d" % t, *c), 2048.0, A.add)
        ts(S("yeb", *c), S("yn%d" % t, *c), -1024.0, A.add)
        for n, b in (("yv", "yvf"), ("ye", "yeb")):
            dma("Y", "l_%s%d" % (n, z), [(lambda T, e=e, n=n: T[n][r, 128 * e:128 * e + 128], lambda T, e=e, b=b: T[b][64 * e:64 * e + 64, c[0]:c[1]]) for e in range(2)],
                [S(b, *c)], [], 2.0)
        for e in range(2):
            dma("YS"[e], "l_yp%d%d" % (e, z), [(lambda T, e=e: T.yp[4 * z:4 * z + 4, 2048 * e:2048 * e + 2048], lambda T, e=e: halves(z, T, e))],
                [full("plain%d" % z)], [], 2.0)

    for t in range(vis):
        part[1] = t
        for z in range(2):
            st_hash(t, z)
            if t == vis - 1:
                st_plain(z)
            for f in (st_z, st_m, st_names):
                for n in range(2):
                    f(t, z, n)
            if t < vis - 1:
                send("v", t, z)
            st_truth(t, z)
            if t == z == 0:
                part[0] = "r0"
                claims_in("Y", "l_again1", 1, [0, 1], [(4096, 8192), (8192, CW)], 6.0, [S("yb1", 0, 128)])
            st_ask(t, z)
            if t == vis - 1:
                st_store(z)
        if t < vis - 1:
            st_count(t)

    hist, sums = {}, {}
    for i, o in enumerate(ops):
        dep = set()
        for (n, a, b) in o["R"]:
            for (j, a2, b2, w) in hist.get(n, ()):
                if w and a < b2 and a2 < b:
                    dep.add(j)
        for (n, a, b) in o["W"]:
            for (j, a2, b2, w) in hist.get(n, ()):
                if a < b2 and a2 < b:
                    dep.add(j)
        for (n, a, b) in o["R"]:
            hist.setdefault(n, []).append((i, a, b, False))
        for (n, a, b) in o["W"]:
            l = hist.setdefault(n, [])
            l[:] = [e for e in l if not (a <= e[1] and e[2] <= b)]
            l.append((i, a, b, True))
        if o["q"] == "N":
            dep = {o["send"]}
        o["B"] = sorted(set(r[0] for r in o["R"] + o["W"] if BUF[r[0]][0] == "psum"))
        for b in o["B"]:
            if o["q"] == "P":
                l = sums.setdefault(b, [])
                if o["lot"]:
                    dep.update(l)
                    l[:] = [i]
                else:
                    dep.update(l[:1])
                    l.append(i)
        dep.discard(i)
        o["O"] = set(j for j in dep if o["q"] == "P" and ops[j]["q"] == "P")
        if o["q"] == "S" and not o["part"]:
            o["after"] = issued["S"]
        if "after" in o and o["after"] not in dep:
            dep.add(o["after"])
            o["O"].add(o["after"])
        o["D"], o["i"], o["j"] = dep, i, 2 * o["t"] + (o["part"][1:2] == "1")
    return ops


def graph(ops):
    n = len(ops)
    pred, users, above = [sorted(o["D"]) for o in ops], {}, [0] * n
    for i, o in enumerate(ops):
        o["occ"] = (1.0 if o["q"] == "G" else 0.15) * len(o["f"]) if o["sem"] and o["f"] else o["c"]
        o["fix"] = [b for b in o["B"] if b in SCRATCH]
        for b in o["B"]:
            if b not in SCRATCH:
                o["any"] = b
                users.setdefault(b, []).append(i)
        far = 0
        done = [j for j in pred[i] if not (j in o["O"] and ops[j]["sem"])]
        for j in done:
            far |= above[j]
        above[i] = far
        for j in done:
            above[i] |= 1 << j
        pred[i] = [(j, ops[j]["occ"] - ops[j]["c"] if j in o["O"] else LAT) for j in pred[i] if not far >> j & 1]
    return pred, {u[0]: u for u in users.values()}


def first_turns(ops, pred):
    n = len(ops)
    off, key, late = [0.0] * n, [None] * n, [1e9] * n
    for i, o in enumerate(ops):
        p = o["part"]
        off[i] = max([off[j] + ops[j]["c"] + l for j, l in pred[i] if (ops[j]["part"], ops[j]["t"]) == (p, o["t"])], default=0.0)
        if p[:1] + p[2:] in LEAD:
            lead, j = LEAD[p[:1] + p[2:]] + off[i], o["j"]
            key[i] = max([lead * (ALONE if j in (0, 2 * VIS - 1) and lead > 0 else 1.0) + HALF * j - (j > 0) * (1 - ALONE) * 2 * HALF] + [key[j] + 1e-3 for j, l in pred[i] if key[j] is not None])
    for i in range(n - 1, -1, -1):
        if key[i] is None:
            key[i] = min(late[i] - ops[i]["c"], 0.0) - 20.0 * (ops[i]["part"][:1] == "l")
        for j, l in pred[i]:
            late[j] = min(late[j], key[i] - l)
    return key


def line_up(ops, pred, users, key, early=False):
    n = len(ops)
    need = [set(j for j, l in pred[i]) for i in range(n)]
    safe = {i: set(j for k in u for j, l in pred[k]) - set(u) for i, u in users.items()}
    last = set(u[-1] for u in users.values())
    todo, done, seq, free = sorted(range(n), key=lambda i: key[i]), set(), [], len(BIGB)
    while todo:
        i = next(i for i in todo if need[i] <= done and (i not in users or free > (1 if early else len(BIGB)) or free and safe[i] <= done))
        todo.remove(i)
        done.add(i)
        seq.append(i)
        free += (i in last) - (i in users)
    return seq


def refine(ops, pred, users, seq):
    n, NB, STEP = len(ops), len(BIGB), 20
    res = {r: k for k, r in enumerate(list("VSPGYN") + FIXB)}
    NR = len(res)
    last = set(u[-1] for u in users.values())
    Q = [res[o["q"]] for o in ops]
    C = [o["c"] for o in ops]
    OCC = [o["occ"] if o["q"] != "N" else -1e9 for o in ops]
    FIX = [[res[b] for b in o["fix"]] for o in ops]
    POOL = [1 if i in users else 2 if i in last else 0 for i in range(n)]
    succ = [[] for _ in range(n)]
    for i in range(n):
        for j, l in pred[i]:
            succ[j].append((i, l))
    whole = [(pred[i], 0.0, Q[i], C[i], OCC[i], FIX[i], POOL[i], 0.0, 0.0) for i in range(n)]
    rnd = np.random.default_rng(OPT["seed"])

    def tails(seq, b):
        tail = [0.0] * n
        nq, acq = [None] * NR, [i for i in seq if POOL[i] == 1]
        r = len(acq)
        for i in reversed(seq[b:]):
            t = max([l + tail[j] for j, l in succ[i]], default=0.0)
            for k in FIX[i]:
                j = nq[k]
                if j is not None:
                    t = max(t, tail[j] + (LAT if Q[j] != Q[i] else 0.0))
                nq[k] = i
            if POOL[i] == 2:
                r -= 1
                if r + NB < len(acq):
                    t = max(t, LAT + tail[acq[r + NB]])
            t += C[i]
            j = nq[Q[i]]
            if j is not None:
                t = max(t, OCC[i] + tail[j])
            nq[Q[i]] = i
            tail[i] = t
        return tail, nq

    def forward(part, st, row, snaps, end, why, thr):
        free, who, lq, rel, na, best, arg = st[0][:], st[1][:], st[2][:], st[3][:], st[4], st[5], st[6]
        for k in range(0, len(part), STEP):
            snaps.append((free[:], who[:], lq[:], rel[:], na, best, arg))
            for i in part[k:k + STEP]:
                pr, soon, qi, c, occ, fix, pool, xt, lb = row[i]
                t, w = free[qi], who[qi]
                if soon > t:
                    t, w = soon, -1
                for j, l in pr:
                    u = end[j] + l
                    if u > t:
                        t, w = u, -2 - j
                if pool:
                    if pool == 2:
                        rel.append(i)
                    else:
                        if na >= len(rel):
                            return None
                        j = rel[na]
                        na += 1
                        if end[j] + LAT > t:
                            t, w = end[j] + LAT, j
                if fix:
                    for b in fix:
                        u = free[b] if lq[b] == qi else free[b] + LAT
                        if u > t:
                            t, w = u, who[b]
                    for b in fix:
                        free[b], who[b], lq[b] = t + c, i, qi
                free[qi], who[qi] = t + occ, i
                t += c
                end[i], why[i] = t, w
                if t + lb > best:
                    if t + lb > thr:
                        return None
                    if t + xt > best:
                        best, arg = t + xt, i
        return free, who, lq, rel, na, best, arg

    def close(s, end, exits, after, tail):
        free, who, lq, rel, na, best, arg = s
        soft = 0.0
        for q, t, e in exits:
            u = free[q] + t + (LAT if q > 5 and lq[q] != e else 0.0)
            if q < 3:
                soft += u
            if u > best:
                best, arg = u, who[q]
        for r, j in zip(rel[na:], after):
            if end[r] + LAT + tail[j] > best:
                best, arg = end[r] + LAT + tail[j], r
        return arg, best + 0.02 * soft, best

    def pairs_of(i, m, why):
        ps = []
        while 0 <= i < m:
            j = why[i]
            if 0 <= j < m:
                ps.append((j, i))
            i = j if j > -2 else -2 - j
        return ps

    ends, whys = [0.0] * n + [-LAT], [-1] * (n + 1)
    empty = ([0.0] * NR, [-1] * NR, [-1] * NR, [n] * NB, 0, -1.0, -1)
    for size, tries, heat in OPT["sweeps"]:
        u = forward(seq, empty, whole, [], ends, whys, 1e9)[5]
        OPT.get("log", []).append(round(u, 2))
        timed = sorted(seq, key=lambda i: ends[i] - C[i])
        s = forward(timed, empty, whole, [], ends, whys, 1e9)
        if s and s[5] <= u + 0.1:
            seq = timed
        cuts = list(range(-int(rnd.integers(size // 2)), n - size // 2, size // 2))
        for a in cuts[::-1] if rnd.random() < 0.5 else cuts:
            a, b = max(a, 0), min(a + size, n)
            tail, nxt = tails(seq, b)
            st = forward(seq[:a], empty, whole, [], ends, whys, 1e9)
            m, held = b - a, st[3][st[4]:]
            st = (st[0], [-1] * NR, st[2], list(range(m, m + len(held))), 0, -1.0, -1)
            own = {i: k for k, i in enumerate(seq[a:b])}
            row, lb = [None] * m, [0.0] * m
            for i, k in reversed(own.items()):
                xt = max([l + tail[j] for j, l in succ[i] if j not in own], default=0.0)
                lb[k] = max([xt] + [l + C[j] + lb[own[j]] for j, l in succ[i] if j in own])
                row[k] = ([(own[j], l) for j, l in pred[i] if j in own], max([ends[j] + l for j, l in pred[i] if j not in own], default=0.0),
                          Q[i], C[i], OCC[i], FIX[i], POOL[i], xt, lb[k])
            PS = [set(j for j, l in r[0]) for r in row]
            SS = [set(own[j] for j, l in succ[i] if j in own) for i in own]
            out = ([(q, tail[j], Q[j]) for q, j in enumerate(nxt) if j is not None and q != 5], [i for i in seq[b:] if POOL[i] == 1][:NB], tail)
            part, pos, snaps = list(range(m)), list(range(m)), []
            end, why = [0.0] * m + [ends[i] for i in held], [-1] * m
            now = close(forward(part, st, row, snaps, end, why, 1e9), end, *out)
            ps = pairs_of(now[0], m, why)
            rr = rnd.random((tries, 5))
            rr[:, 4] = -heat * np.log(1.0 - rr[:, 4])
            for r in rr.tolist():
                if ps and r[3] > 0.15:
                    j, i = ps[int(r[0] * len(ps))]
                    pj, pi = pos[j], pos[i]
                    if r[2] > 0.6:
                        x = int((r[2] - 0.6) * 40)
                        pj, pi = max(0, pj - x * (r[1] < 0.5)), min(m - 1, pi + x * (r[1] >= 0.5))
                else:
                    pi = 1 + int(r[0] * (m - 1))
                    i, pj = part[pi], pi - 1
                    while pj > 0 and row[part[pj]][2] != row[i][2]:
                        pj -= 1
                    j = part[pj]
                up = r[1] < 0.5
                near = PS if up else SS
                need, mv, rest = near[i if up else j], [i if up else j], []
                for k in part[pj:pi][::-1] if up else part[pj + 1:pi + 1]:
                    if k in need:
                        mv.append(k)
                        need = need | near[k]
                    else:
                        rest.append(k)
                if not rest:
                    continue
                new = mv[::-1] + rest[::-1] if up else rest + mv
                s0 = pj // STEP
                e2, w2, sn = end[:], why[:], []
                s = forward(part[s0 * STEP:pj] + new + part[pi + 1:], snaps[s0], row, sn, e2, w2, now[2] + r[4] + 0.03)
                if s is None:
                    continue
                v = close(s, e2, *out)
                if v[1] <= now[1] + r[4]:
                    part[pj:pi + 1] = new
                    for k in range(pj, pi + 1):
                        pos[part[k]] = k
                    end, why, now = e2, w2, v
                    snaps[s0:] = sn
                    ps = pairs_of(now[0], m, why)
            seq = seq[:a] + [seq[a + k] for k in part] + seq[b:]
    s = forward(seq, empty, whole, [], ends, whys, 1e9)
    return seq, s[5], ends[:n], s[3]


def schedule(ops):
    pred, users = graph(ops)
    order, total, end, freed = refine(ops, pred, users, line_up(ops, pred, users, first_turns(ops, pred)))
    REAL.clear()
    for k, i in enumerate(i for i in order if i in users):
        REAL[ops[i]["any"]] = BIGB[k] if k < len(BIGB) else REAL[ops[freed[k]]["any"]]
    last, other = {}, {}
    for i in order:
        o = ops[i]
        o["start"] = end[i] - o["c"]
        for b in o["B"]:
            r = REAL.get(b, b)
            if r in last and ops[last[r]]["q"] != o["q"]:
                other[r] = last[r]
            if r in other:
                o["D"].add(other[r])
            last[r] = i
    return order, total


SEMQ = {"V": "vv", "S": "ss", "P": "pp", "G": "gg"}


def plan(nE):
    if nE in _CACHE:
        return _CACHE[nE]
    ops = build(nE, VIS)
    order, total = schedule(ops)
    count = {s: 0 for s in SEMQ.values()}
    know, kq, out = {}, {}, []
    for i in order:
        o = ops[i]
        q = o["q"]
        mine = kq.setdefault(q, {})
        waits = {}
        if q != "N":
            for j in sorted(o["D"] - o["O"], key=lambda j: -ops[j]["start"]):
                s, v = ops[j]["ev"]
                if mine.get(s, 0) >= v:
                    continue
                waits[s] = max(waits.get(s, 0), v)
                for s2, v2 in know[j].items():
                    mine[s2] = max(mine.get(s2, 0), v2)
                mine[s] = max(mine.get(s, 0), v)
        know[i] = dict(mine) if q != "N" else {}
        if o["sem"]:
            o["ev"] = (o["sem"], o["val"])
        else:
            s = SEMQ[q]
            count[s] += len(o["f"])
            o["ev"] = (s, count[s])
        out.append((o, sorted(waits.items())))
    ends = {}
    for o in sorted(ops, key=lambda o: o["start"] + o["c"]):
        s, v = o["ev"]
        ends[s] = max(ends.pop(s, 0), v)
    _CACHE[nE] = (out, ends, total)
    return _CACHE[nE]


def rank_program(g, core, T, topo):
    rank = T.rank_of(core)
    if rank is None:
        return
    nxt = T.cores[(rank + 1) % len(T.cores)]
    eng = topo.engines(core, nxt)
    mask = 0
    for e in eng:
        mask |= 1 << e
    rid, pid, _ = topo.addr(nxt)
    steps, ends, _ = plan(len(eng))
    queue = {"V": g.vector, "S": g.scalar, "P": g.tensor, "G": g, "Y": g.sync}
    for o, waits in steps:
        q = o["q"]
        if q == "N":
            continue
        for s, v in waits:
            queue[q].wait_ge(T.sem[s], v)
        if o["send"]:
            k, t, h = o["send"]
            dst, src = send_sides(T, T, o["send"])
            g.remote_dma(out_ap=dst, in_ap=src, remote_sem=T.sem["a%s%d%d" % (k, t, h)],
                         local_sem=T.sem["o%s%d%d" % (k, t, h)], pid=pid, routing_id=rid, dma_engine_mask=mask)
        elif o["sem"]:
            for f in o["f"]:
                f(g, T).then_inc(T.sem[o["sem"]], 16)
        else:
            for f in o["f"]:
                f(g, T).then_inc(T.sem[SEMQ[q]], 1)
    for s, v in ends.items():
        g.wait_ge(T.sem[s], v)
